import numpy as np, ml_dtypes
CORES = [23,119,17,113]
N = 4
BF = ml_dtypes.bfloat16
def gentries(a):
    return np.ascontiguousarray(a.reshape(8, 16, -1).transpose(0, 2, 1)).reshape(8, -1)
def gtable(e):
    e = np.asarray(e); return np.ascontiguousarray(e.reshape(8, -1, 16).transpose(0, 2, 1)).reshape(128, -1).astype(np.int32)
W, P, RO = 3072, 256, 3
def parts(rng):
    X = rng.integers(0, 128, (N, 8, 16, W)); G = rng.integers(-127, 128, (N, 8, 16, W)); E = rng.integers(0, 2 ** 20, (N, 8, W)); B = rng.integers(0, W, (N, 8, 16, W))
    return X, G, E, B, rng.integers(0, W, (N, 8, P, 16)), rng.integers(0, W, (N, 8, P, 16)), rng.integers(0, 9, (N, 8, P, 16))
def pack(X, G, E, B, a, b, l):
    return {"xrec": np.ascontiguousarray(X.reshape(N, 128, W)).astype(np.float32).astype(BF), "grec": np.ascontiguousarray(G.reshape(N, 128, W)).astype(np.float32).astype(BF),
            "erec": np.ascontiguousarray(E.reshape(N, 8, W)).astype(np.int32), "nbr": np.ascontiguousarray(B.reshape(N, 128, W)).astype(np.int32),
            "pa": np.stack([gtable(t.reshape(8, -1)) for t in a]), "pb": np.stack([gtable(t.reshape(8, -1)) for t in b]), "lam": np.stack([gtable(t.reshape(8, -1)) for t in l])}
def setup_inputs(rng):
    X, G, E, B, a, b, l = parts(rng)
    X[:, 1::2] = (X[:, 1::2] * rng.choice(np.array([1, 4, 16, 16]), (N, 4, 1, W))) >> 4
    E[:, 2::3] &= 2 ** 20 - 2 ** 18
    r = rng.integers(0, W, (N, 8, 1)); a[:, :, 5] = r; b[:, :, 5] = r
    return pack(X, G, E, B, a, b, l)
def setup_inputs_corners(rng):
    X, G, E, B, a, b, l = parts(rng); h = P // 2; sh = int(rng.integers(0, 8)); J = np.arange(16)
    for q in range(N):
        for g in range(8):
            c = (g + q + sh) % 8
            if c == 0:
                z = h // 2; r = rng.integers(0, W, (z, 1)); a[q, g, :z] = r; b[q, g, :z] = r
                rec = rng.permutation(W)[:16]; X[q, g][:, rec] = X[q, g][:, rec[:1]]
                a[q, g, z:h] = rec[rng.integers(0, 16, (h - z, 16))]; b[q, g, z:h] = rec[rng.integers(0, 16, (h - z, 16))]
            elif c == 1:
                B[q, g] = np.arange(W); l[q, g] = 8 * rng.integers(0, 2, (P, 16))
            elif c == 2:
                B[q, g] = (W - 1) * rng.integers(0, 2, (16, W)); l[q, g] = 8 * rng.integers(0, 2, (P, 16))
                a[q, g, :, ::3] = (W - 1) * rng.integers(0, 2, (P, 6)); b[q, g, :, 1::3] = (W - 1) * rng.integers(0, 2, (P, 5))
            elif c == 3:
                l[q, g] = rng.integers(3, 6, (P, 16))
                rec = rng.permutation(W)[:48].reshape(3, 16); o = rng.permutation(16)
                v = 2 * rng.integers(51, 62, (16, 16)); v[o[1]] = v[o[0]]; v[o[2]] = v[o[0]] + 4 * rng.integers(0, 2, 16) - 2
                s = v.copy(); s[o[0]] += 1; s[o[1]] -= 1; u = v >> 1; u[o[0]] += 1; u[o[2]] -= 1
                X[q, g][:, rec[0]] = 0; X[q, g][:, rec[1]] = v; X[q, g][:, rec[2]] = s; G[q, g][:, rec[0]] = u; E[q, g, rec[2]] = 2 ** 20 - 1
                i = np.arange(h) % 16; a[q, g, :h, 0] = rec[0][i]; b[q, g, :h, 0] = rec[1][i]; l[q, g, :h, 0] = 0
                a[q, g, :h, 1] = rec[2][i]; b[q, g, :h, 1] = rec[2][i]
            elif c == 4:
                if q % 2 == 0: E[q, g] = rng.integers(0, 2 ** 20)
                else: E[q, g] = 4096 * int(rng.integers(128, 256)) + 1025 + 8 * int(rng.integers(0, 127)) + rng.integers(0, 2, W)
            elif c == 5:
                G[q, g] = 0; r = rng.integers(0, W, (h, 2))[:, J % 2]; a[q, g, :h] = r; b[q, g, :h] = r
                rec = rng.permutation(W)[:128].reshape(8, 16); inc = np.zeros((16, 16), np.int64); inc[:, 1] = 1; size = rng.permutation(20)[:8] + 1
                for i in range(2, 16): inc[i, i] = 3 if i == 15 else 2
                for i in range(8): X[q, g][:, rec[i]] = 40 + int(size[i]) * np.add.accumulate(inc, axis=1)
                k = rec[np.arange(P - h) % 8]; a[q, g, h:] = k; b[q, g, h:] = k
            elif c == 6:
                r = rng.integers(0, W, (P, 2)); a[q, g] = np.take_along_axis(r, rng.integers(0, 2, (P, 16)), 1); b[q, g] = np.take_along_axis(r, rng.integers(0, 2, (P, 16)), 1)
            else:
                u = rng.integers(0, W, (P, 2)); cut = rng.integers(0, 15, (P, 1)); r = np.where(J <= cut, u[:, :1], u[:, 1:]); a[q, g] = r; k = b[q, g].copy(); b[q, g] = r
                b[q, g, h:, 0] = k[h:, 0]; b[q, g, h:, 15] = k[h:, 15]; l[q, g, h:, 0] = 0; l[q, g, h:, 15] = 0
    return pack(X, G, E, B, a, b, l)
def setup_inputs_crowd(rng):
    X, G, E, B, a, b, l = parts(rng); sh = int(rng.integers(0, 8)); J = np.arange(16)
    for q in range(N):
        for g in range(8):
            c = (g + sh) % 8; one = int(rng.choice(np.array([0, W - 1, int(rng.integers(0, W))])))
            if c < 2:
                B[q, g] = one; l[q, g] = 8 * rng.integers(0, 2, (P, 16))
                if c == 1: B[q, g, int(rng.integers(0, 16)), a[q, g, P - 1, 15]] = (one + 1) % W
            elif c in (2, 3, 6):
                cut = 14 if c == 2 else 13 if c == 3 else 0
                u = rng.integers(0, W, (P, 2)); r = np.where(J <= cut, u[:, :1], u[:, 1:]); k = b[q, g].copy(); a[q, g] = r; b[q, g] = r
                b[q, g, 1::2, 0] = k[1::2, 0]; b[q, g, 1::2, 15] = k[1::2, 15]; l[q, g, 1::2, 0] = 0; l[q, g, 1::2, 15] = 0
            elif c == 4:
                a[q, g] = one; b[q, g] = one; i = int(rng.integers(0, 16)); a[q, g, P - 1, i] = (one + 1) % W; b[q, g, P - 1, i] = (one + 2) % W
            elif c == 5:
                r = rng.integers(0, W, 4); a[q, g] = r[rng.integers(0, 4, (P, 16))]; b[q, g] = r[rng.integers(0, 4, (P, 16))]; B[q, g] = r[rng.integers(0, 4, (16, W))]
            else:
                b[q, g] = one; l[q, g] = 8
    return pack(X, G, E, B, a, b, l)
def setup_inputs_ends(rng):
    X, G, E, B, a, b, l = parts(rng)
    X = 127 * rng.integers(0, 2, X.shape); G = 254 * rng.integers(0, 2, G.shape) - 127; E = (2 ** 20 - 1) * rng.integers(0, 2, E.shape)
    E[:, :, 0] = (2 ** 20 - 1) * rng.integers(0, 2, (N, 8)); E[:, ::2, W - 1] = 2 ** 20 - 1 - E[:, ::2, 0]
    B = np.where(rng.random(B.shape) < 0.3, B, (W - 1) * rng.integers(0, 2, B.shape))
    a = np.where(rng.random(a.shape) < 0.33, a, (W - 1) * rng.integers(0, 2, a.shape)); b = np.where(rng.random(b.shape) < 0.33, b, (W - 1) * rng.integers(0, 2, b.shape))
    l = np.where(rng.random(l.shape) < 0.2, l, 8 * rng.integers(0, 2, l.shape)); alt = (W - 1) * (np.arange(16) % 2)
    for g in (0, 2, 5, 7):
        o = rng.integers(0, 2, (N, 1)); X[:, g, :, 0] = 127 * o; X[:, g, :, W - 1] = 127 * (1 - o)
        s = 254 * rng.integers(0, 2, (N, 2)) - 127
        if g == 7: s[:] = 127
        if g == 0: s[:] = -127
        G[:, g, :, 0] = s[:, :1]; G[:, g, :, W - 1] = s[:, 1:]
        a[:, g, 7::8] = alt; b[:, g, 7::8] = alt
    return pack(X, G, E, B, a, b, l)
def setup_inputs_spread(rng):
    X, G, E, B, a, b, l = parts(rng)
    X = (np.exp2(7 * rng.random((N, 8, 1, W))) * rng.random(X.shape)).astype(np.int64); X[:, 1::2] = 127 - X[:, 1::2]
    G = np.minimum((np.exp2(7 * rng.random((N, 8, 1, W))) * rng.random(G.shape)).astype(np.int64), 127) * (2 * rng.integers(0, 2, G.shape) - 1)
    E = np.minimum(np.exp2(20 * rng.random(E.shape)).astype(np.int64) - 1, 2 ** 20 - 1)
    a = np.minimum((W * rng.random(a.shape) ** 3).astype(np.int64), W - 1); b = np.minimum((W * rng.random(b.shape) ** 2).astype(np.int64), W - 1)
    B = W - 1 - np.minimum((W * rng.random(B.shape) ** 3).astype(np.int64), W - 1)
    l = rng.choice(np.array([0, 0, 0, 1, 2, 3, 4, 4, 5, 6, 7, 8, 8, 8]), l.shape)
    return pack(np.minimum(np.maximum(X, 0), 127), G, E, B, a, b, l)
def check_inputs(d):
    bad = []
    for k, lo, hi in (("xrec", 0, 127), ("grec", -127, 127), ("erec", 0, 2 ** 20 - 1), ("nbr", 0, W - 1), ("pa", 0, W - 1), ("pb", 0, W - 1), ("lam", 0, 8)):
        v = np.asarray(d[k]).astype(np.float64)
        if not (np.min(v) >= lo and np.max(v) <= hi): bad.append("range of " + k)
        elif not np.all(v == np.rint(v)): bad.append("whole numbers in " + k)
    return bad
def pick(t, i):
    return np.take_along_axis(t, i.reshape(N, 8, 1, P * 16), 3).reshape(N, 8, 16, P, 16)
def dot(u, v):
    return np.add.reduce(u * v, axis=2)
def reference(xrec, grec, erec, nbr, pa, pb, lam):
    X = xrec.astype(np.float32).astype(np.int64).reshape(N, 8, 16, W); G = grec.astype(np.float32).astype(np.int64).reshape(N, 8, 16, W)
    E = erec.astype(np.int64); B = nbr.astype(np.int64).reshape(N, 8, 16, W); J = np.arange(16); mid = (J > 0) & (J < 15)
    a, b, l = [np.stack([gentries(t) for t in v]).astype(np.int64).reshape(N, 8, P, 16) for v in (pa, pb, lam)]
    for rnd in range(RO):
        w = l[:, :, None]; xa = pick(X, a); d = pick(X, b) - xa; R = 8 * xa + w * d
        g = (8 - w) * pick(G, a) + w * pick(G, b)
        ea = np.take_along_axis(E, a.reshape(N, 8, P * 16), 2).reshape(N, 8, P, 16); eb = np.take_along_axis(E, b.reshape(N, 8, P * 16), 2).reshape(N, 8, P, 16)
        e = (8 - l) * ea + l * eb
        Rx = np.concatenate([np.roll(R[..., 15:], 1, axis=0), R, np.roll(R[..., :1], -1, axis=0)], axis=4)
        ex = np.concatenate([np.roll(e[..., 15:], 1, axis=0), e, np.roll(e[..., :1], -1, axis=0)], axis=3)
        D = Rx[..., 1:] - Rx[..., :-1]; fwd = ex[..., 2:] >= ex[..., :-2]
        tau = np.where(fwd[:, :, None], D[..., 1:], D[..., :-1])
        p = dot(g, d).astype(np.float32) * dot(tau, tau).astype(np.float32)
        q = dot(g, tau).astype(np.float32) * dot(tau, d).astype(np.float32)
        l = l - (p > q).astype(np.int64) + (p < q).astype(np.int64)
        up = l > 8; dn = l < 0; z = np.where(up, b, a)
        n = np.take_along_axis(B, z.transpose(0, 1, 3, 2), 3).transpose(0, 1, 3, 2)
        a, b, l = np.where(up, b, np.where(dn, n, a)), np.where(up, n, np.where(dn, a, b)), np.where(up, 1, np.where(dn, 7, l))
        xa = pick(X, a); R = 8 * xa + l[:, :, None] * (pick(X, b) - xa)
        H = np.add.reduce(np.abs(R[..., 1:] - R[..., :-1]), axis=2)
        C = np.concatenate([np.zeros((N, 8, P, 1), np.int64), np.add.accumulate(H, axis=3)], axis=3); S = C[..., 15:]
        c = np.where(l <= 4, a, b)
        j = np.add.reduce((15 * C[..., None, :15] <= J[:, None] * S[..., None]).astype(np.int64), axis=4) - 1
        lo = np.take_along_axis(C, j, 3); gap = 15 * (np.take_along_axis(C, j + 1, 3) - lo); rest = 16 * (J * S - 15 * lo); m = np.zeros((N, 8, P, 16), np.int64)
        for i in range(1, 9): m = m + ((2 * i - 1) * gap <= rest)
        a, b, l = np.where(mid, np.take_along_axis(c, j, 3), a), np.where(mid, np.take_along_axis(c, j + 1, 3), b), np.where(mid, m, l)
    ya, yb, yl = [np.stack([gtable(t.reshape(8, -1)) for t in v]).astype(np.float32) for v in (a, b, l)]
    return {"ya": ya, "yb": yb, "yl": yl}

@@ -1,0 +1,745 @@
+import numpy as np
+from concourse.bass import DstId, RemoteDMATransfer
+from concourse.mybir import AluOpType, AxisListType, ActivationFunctionType
+
+AL = AluOpType
+AF = ActivationFunctionType
+W, RO = 3072, 3
+HS = 136
+R0 = 3 * HS
+GC = 1024
+NPR = 6
+MAGIC_H = 1.5 * 2 ** 30
+MAGIC_1 = 1.5 * 2 ** 23
+BIAS = [15000.0, 0.0]
+DADD = {"dd": False, "dg": False}
+XW2 = False
+PC = 2
+PEN = [3.0]
+SEARCH = [0, 350, 200.0, 1.005, 4]
+
+SCRATCH = {
+    "xt": ("sbuf", [128, W], "bfloat16"), "gt": ("sbuf", [128, W], "bfloat16"),
+    "nt": ("sbuf", [128, 2 * W], "int32"), "et": ("sbuf", [128, W], "int32"),
+    "pin": ("sbuf", [128, 768], "int32"), "p16": ("sbuf", [128, 768], "float16"),
+    "ones": ("sbuf", [128, 2048], "bfloat16"), "bk": ("sbuf", [128, 2048], "bfloat16"),
+    "wk": ("sbuf", [128, 1792], "bfloat16"),
+    "xh": ("sbuf", [128, 896], "bfloat16"), "xl": ("sbuf", [128, 896], "bfloat16"),
+    "cb": ("sbuf", [128, 13, 144], "bfloat16"), "c32": ("sbuf", [128, 3, 128], "float32"),
+    "xaw": ("sbuf", [128, 32], "bfloat16"), "col": ("sbuf", [128, 64], "float32"), "coli": ("sbuf", [128, 8], "int32"),
+}
+for _i in range(NPR):
+    SCRATCH["pr%d" % _i] = ("sbuf", [128, 2048], "float32")
+for _h in range(2):
+    for _n in ("xa", "dd", "ga", "dg", "ld", "lg", "tv"):
+        SCRATCH["%s%d" % (_n, _h)] = ("sbuf", [128, 2064 if _n in ("ga", "lg") else 2048], "float16")
+    SCRATCH["eg%d" % _h] = ("sbuf", [128, 256], "float32")
+    SCRATCH["rw%d" % _h] = ("sbuf", [128, 2048 + 6 * HS], "float32")
+    SCRATCH["q%d" % _h] = ("sbuf", [128, 144, 16], "float16")
+    SCRATCH["of%d" % _h] = ("sbuf", [128, 912], "uint16")
+    SCRATCH["lb%d" % _h] = ("sbuf", [128, 384], "bfloat16")
+    SCRATCH["st%d" % _h] = ("sbuf", [128, 32, 16], "float32")
+    SCRATCH["sf%d" % _h] = ("sbuf", [128, 64, 16], "float32")
+    SCRATCH["sh%d" % _h] = ("sbuf", [128, 88, 16], "float16")
+    SCRATCH["ed%d" % _h] = ("sbuf", [128, 10, 32], "float32")
+    SCRATCH["sb%d" % _h] = ("sbuf", [128, 2, HS], "float32")
+for _i in range(8):
+    SCRATCH["ps%d" % _i] = ("psum", [128, 32, 16], "float32")
+NDMA = 72
+SEMAPHORES = ["cD", "cA", "cP", "cG"] + ["dm%d" % i for i in range(NDMA)] \
+    + ["ar%d" % i for i in range(2 * RO)] + ["lo%d" % i for i in range(2 * RO)]
+
+S = slice
+ALLP = S(None)
+CY, PCY, GCY, LAT = 1.0, 0.5, 1.56, 100.0
+
+
+def ap(name, *idx, p=ALLP):
+    return (name, (p,) + idx)
+
+
+def fl(name, k=ALLP, p=S(0, 128), shift=0):
+    a, b = 16 * p.start, 16 * p.stop
+    if isinstance(k, tuple):
+        return ap(name, S(a + k[0], b, k[1]))
+    return ap(name, S(a + shift, b + shift)) if k == ALLP else ap(name, S(a + k, b, 16))
+
+
+def ind(win, off):
+    return ("IND", win, off)
+
+
+_IDX = {}
+
+
+def region(a):
+    name, idx = a
+    if name not in SCRATCH:
+        return None
+    if name not in _IDX:
+        fs = SCRATCH[name][1][1:]
+        _IDX[name] = np.arange(int(np.prod(fs))).reshape(fs)
+    return _IDX[name][idx[1:]].ravel()
+
+
+def nel(a):
+    return len(region(a[2])) * 16 if a[0] == "IND" else len(region(a))
+
+
+def two(a):
+    return a[0] != "IND" and SCRATCH[a[0]][2] in ("bfloat16", "float16", "uint16")
+
+
+def psum(a):
+    return a[0] != "IND" and SCRATCH[a[0]][0] == "psum"
+
+
+def real(T, a):
+    if not isinstance(a, tuple):
+        return a
+    if a[0] == "IND":
+        return real(T, a[1]).indirect(real(T, a[2]))
+    return T[a[0]][a[1]]
+
+
+def parts(a):
+    if not isinstance(a, tuple):
+        return []
+    return [a[1], a[2]] if a[0] == "IND" else [a]
+
+
+def build():
+    ops = []
+
+    def add(eng, cost, reads, writes, emit, **kw):
+        o = dict(eng=eng, cost=cost, reads=[x for r in reads for x in parts(r)], writes=writes, emit=emit, half=cur[0])
+        o.update(kw)
+        ops.append(o)
+        return len(ops) - 1
+    cur = [None]
+
+    def vcost(n, k):
+        return 60 + max(64, n * k) * CY
+
+    def tt(out, a, b, op):
+        k = GCY if a[0] == "IND" else 1 if psum(a) or psum(b) else 2
+        add("D", {"D": vcost(nel(a), k)}, [a, b], [out], lambda e: [lambda g, T: g.vector.tensor_tensor(real(T, out), real(T, a), real(T, b), op)])
+
+    def ts(out, a, s1, op0, s2=None, op1=None):
+        k = 0.5 if two(a) and two(out) else 1
+        if op1 is None:
+            f = lambda g, T: g.vector.tensor_scalar(real(T, out), real(T, a), real(T, s1), None, op0)
+        else:
+            f = lambda g, T: g.vector.tensor_scalar(real(T, out), real(T, a), real(T, s1), real(T, s2), op0, op1)
+        add("D", {"D": vcost(nel(a), k)}, [a, s1, s2], [out], lambda e: [f])
+
+    def cp(out, a):
+        add("D", {"D": vcost(nel(a), 0.5 if two(a) and two(out) else 1)}, [a], [out], lambda e: [lambda g, T: g.vector.tensor_copy(real(T, out), real(T, a))])
+
+    def mset(out, v):
+        add("D", {"D": vcost(nel(out), 0.5 if two(out) else 1)}, [], [out], lambda e: [lambda g, T: g.vector.memset(real(T, out), v)])
+
+    def act(out, a, fn, scale=1.0, bias=0.0):
+        add("A", {"A": vcost(nel(a), 1)}, [a], [out], lambda e: [lambda g, T: g.scalar.activation(real(T, out), real(T, a), fn, bias=bias, scale=scale)])
+
+    def aff(out, a, scale=1.0, bias=0.0, eng="DA"):
+        k = GCY if a[0] == "IND" else 1
+
+        def emit(e):
+            if e == "A":
+                return [lambda g, T: g.scalar.activation(real(T, out), real(T, a), AF.Identity, bias=bias, scale=scale)]
+            if scale == 1.0 and bias == 0.0:
+                return [lambda g, T: g.vector.tensor_copy(real(T, out), real(T, a))]
+            return [lambda g, T: g.vector.tensor_scalar(real(T, out), real(T, a), scale, bias, AL.mult, AL.add)]
+        kd = 0.5 if two(a) and two(out) else k
+        add(eng, {"D": vcost(nel(a), kd), "A": vcost(nel(a), k)}, [a], [out], emit)
+
+    def mm(lst):
+        fs, cost, rd, wr = [], 30, [], []
+        for out, terms in lst:
+            wr.append(out)
+            for i, tm in enumerate(terms):
+                l, r = tm[0], tm[1]
+                o = tm[2] if len(tm) > 2 else out
+                cost += max(64, nel(r)) * (1 if two(l) else 4) * PCY
+                rd += [l, r]
+                fs.append(lambda g, T, o=o, l=l, r=r, a=(i == 0), b=(i == len(terms) - 1): g.tensor.matmul(real(T, o), real(T, l), real(T, r), a, b))
+        add("P", {"P": cost}, rd, wr, lambda e: fs)
+
+    def iota(out, pat, base, cm):
+        if SCRATCH[out[0]][2] == "int32":
+            f = lambda g, T: g.iota(real(T, out), pat, base, cm)
+        else:
+            f = lambda g, T: g.iota(real(T, out), pat, base, cm, allow_small_or_imprecise_dtypes=True)
+        add("G", {"G": 130 + 2 * nel(out) * CY}, [], [out], lambda e: [f])
+
+    def sel(out, a, pat, cmp, fill, base, cm):
+        add("G", {"G": 170 + 2 * nel(a) * CY}, [a], [out], lambda e: [lambda g, T: g.affine_select(real(T, out), real(T, a), pat, cmp, fill, base, cm)])
+
+    nd = [0]
+
+    def dma(out, a, nbytes, q="S"):
+        sem = "dm%d" % nd[0]
+        nd[0] += 1
+        if q == "G":
+            f = lambda g, T: g.dma_start(real(T, out), real(T, a), accum_op=AL.add)
+            return add(q, {q: 1000.0}, [a, out], [out], lambda e: [f], sem=sem, inc=16, late=2000 + nbytes / 125.0)
+        if q == "S":
+            f = lambda g, T: g.sync.dma_start(real(T, out), real(T, a))
+        else:
+            f = lambda g, T: g.scalar.dma_start(real(T, out), real(T, a))
+        add(q, {q: 80.0}, [a], [out], lambda e: [f], sem=sem, inc=16, late=2000 + nbytes / 250.0)
+
+    EQ, GE = AL.is_equal, AL.is_ge
+    dma(ap("pin", S(0, 256)), ap("pa", ALLP), 131072)
+    dma(ap("pin", S(256, 512)), ap("pb", ALLP), 131072, "A")
+    dma(ap("xt", ALLP), ap("xrec", ALLP), 786432 * 1.5)
+    dma(ap("pin", S(512, 768)), ap("lam", ALLP), 131072, "A")
+    dma(ap("gt", ALLP), ap("grec", ALLP), 786432 * 2.2, "A")
+    I, NI, I2, IN, TRI, G15, ZC, Z0, Z15, PI, P64, BC = [ap("cb", j, S(0, 128)) for j in range(12)]
+    I32, I8, ONE32 = [ap("c32", j, ALLP) for j in range(3)]
+    mset(ap("ones", ALLP), 1.0)
+    mset(ONE32, 1.0)
+    on = lambda n: ap("ones", S(0, n))
+    dg_ = [[-1, 128]]
+    sel(I, on(128), dg_, EQ, 0.0, 0, 1)
+    sel(ap("bk", ALLP), on(2048), [[-1, 16], [-16, 8], [0, 16]], EQ, 0.0, 0, 1)
+    sel(I32, ONE32, dg_, EQ, 0.0, 0, 1)
+    mset(ap("et", ALLP), 0)
+    dma(ap("et", ALLP, p=S(0, 128, 16)), ap("erec", ALLP), 98304 * 4)
+    dma(ap("nt", S(0, W)), ap("nbr", ALLP), 1572864 * 2)
+    ts(NI, I, -1.0, AL.mult)
+    ts(I2, I, 2.0, AL.mult)
+    E8 = ap("cb", 12, S(0, 128))
+    ts(E8, I, 8.0, AL.mult)
+    ts(IN, I, -1536.0, AL.mult)
+    ts(I8, I32, 8.0, AL.mult)
+    cl = lambda a, n=1: ap("col", S(a, a + n))
+    GS, SE8, SEN = cl(32, 8), cl(40, 8), cl(48, 8)
+    I32c = ap("c32", 0, S(0, 128, 16))
+    ts(SE8, I32c, 0.125, AL.mult)
+    ts(SEN, I32c, -0.125, AL.mult)
+    sel(GS, ap("c32", 2, S(0, 8)), [[-16, 8]], GE, 0.0, 0, 1)
+    sel(GS, GS, [[16, 8]], GE, 0.0, 15, -1)
+    iota(PI, [[1, 128]], 0, 0)
+    iota(ap("coli", S(0, 1)), [[0, 1]], 0, 1)
+    iota(cl(0, 3), [[HS, 3]], HS + 1, 15)
+    iota(cl(3, 3), [[HS, 3]], 2034, -15)
+    iota(cl(6, 3), [[HS, 3]], HS - 1, 0)
+    iota(cl(9, 3), [[-HS, 3]], 1025 - HS, 0)
+    ts(cl(0, 6), cl(0, 6), 0.5, AL.mult)
+    ts(ap("coli", S(4, 5)), ap("coli", S(0, 1)), 15, AL.bitwise_and)
+    cp(cl(12), ap("coli", S(4, 5)))
+    ts(cl(13), cl(12), 0.0, EQ)
+    ts(cl(14), cl(12), 15.0, EQ, 1024.0, AL.mult)
+    ts(cl(9, 3), cl(9, 3), cl(13), AL.mult, cl(14), AL.add)
+    ts(cl(6, 3), cl(6, 3), cl(12), AL.add)
+    tt(cl(16, 3), cl(6, 3), cl(9, 3), AL.add)
+    ts(cl(15), cl(13), -15.0, AL.mult, 16.0, AL.add)
+    ts(BC, PI, cl(15), AL.mult)
+    ts(P64, PI, 1.0 / 64, AL.mult)
+    ts(ap("p16", S(0, 512)), ap("pin", S(0, 512)), -1536.0, AL.add)
+    cp(ap("p16", S(512, 768)), ap("pin", S(512, 768)))
+    late = []
+
+    def late_consts():
+        cur[0] = None
+        iota(ap("nt", S(W, 2 * W)), [[1, W]], 0, 0)
+        zc = lambda j: ap("cb", j, ALLP)
+        sel(zc(6), on(144), [[0, 9], [1, 16]], EQ, 0.0, -15, 0)
+        sel(zc(7), zc(6), [[-16, 9], [0, 16]], EQ, 0.0, 0, 1)
+        sel(zc(8), zc(6), [[-16, 9], [0, 16]], EQ, 0.0, -15, 1)
+        sel(zc(6), zc(6), [[-16, 9], [0, 16]], GE, 0.0, 0, 1)
+        sel(zc(6), zc(6), [[16, 9], [0, 16]], GE, 0.0, 15, -1)
+        ts(TRI, on(128), 1.0 / 128, AL.mult)
+        sel(G15, TRI, [[-16, 8], [0, 16]], GE, 0.0, 0, 1)
+        sel(TRI, G15, [[16, 8], [1, 16]], GE, 0.0, -1, -1)
+        sel(G15, G15, [[16, 8], [0, 16]], GE, 0.0, 14, -1)
+        sel(ap("ones", ALLP), ap("bk", ALLP), [[-1, 16], [0, 8], [1, 16]], EQ, 0.0, 0, 0)
+        wk = ap("wk", ALLP)
+        iota(wk, [[1, 14], [0, 128]], 1, 0)
+        for k in range(1, 15):
+            b = ap("wk", S(128 * (k - 1), 128 * k))
+            sel(b, b, [[-16, 8], [-1, 16]], GE, float(k - 15), 0, 1)
+        sel(wk, wk, [[0, 14], [-16, 8], [0, 16]], GE, 0.0, 0, 1)
+        sel(wk, wk, [[0, 14], [16, 8], [0, 16]], GE, 0.0, 14, -1)
+        xh, xl = ap("xh", ALLP), ap("xl", ALLP)
+        pat = [[0, 112], [-16, 8]]
+        iota(xh, [[0, 14], [3840, 8], [0, 8]], -28800, 0)
+        sel(xh, xh, pat, EQ, 0.0, -3, 1)
+        iota(xl, [[0, 14], [-3840, 8], [0, 8]], -1920, 0)
+        sel(xl, xl, pat, EQ, 0.0, -10, 1)
+        dma(ap("xh", ALLP, p=S(10, 128, 16)), ap("xl", ALLP, p=S(10, 128, 16)), 20000)
+        iota(xl, [[2048, 14], [0, 64]], 2048, 0)
+        sel(xl, xl, pat, EQ, 0.0, -5, 1)
+        dma(ap("xh", ALLP, p=S(5, 128, 16)), ap("xl", ALLP, p=S(5, 128, 16)), 20000)
+        dma(ap("xl", ALLP, p=S(1, 128)), ap("xh", ALLP, p=S(0, 127)), 230000)
+        dma(ap("xl", ALLP, p=S(0, 1)), ap("xh", ALLP, p=S(127, 128)), 2000)
+        ic = lambda q: ap("cb", 0, S(q, 128, 16))
+        xw = lambda q: ap("xaw", S(8 * q, 8 * q + 8))
+        cp(xw(0), ic(0))
+        tt(xw(1), ic(1), ic(2), AL.add)
+        tt(xw(2), ic(7), ic(0), AL.subtract)
+        tt(xw(3), ic(8), ic(9), AL.add)
+        tt(xw(3), xw(3), xw(1), AL.subtract)
+        ts(ap("xaw", S(16, 32)), ap("xaw", S(16, 32)), 0.125, AL.mult)
+        for h in range(2):
+            for a in range(0, 144, 48):
+                ts(ap("q%d" % h, S(a, a + 48), ALLP), ap("xt", S(0, 768)), 0.0, AL.mult)
+            for n in ("ga", "lg"):
+                ts(ap("%s%d" % (n, h), S(2048, 2064)), ap("xt", S(0, 16)), 0.0, AL.mult)
+
+    rot, prn = [0, 0], [0]
+
+    def names(h):
+        H = str(h)
+        c = lambda n, k=ALLP, p=S(0, 128), shift=0: fl(n + H, k, p, shift)
+        of = lambda j, a=0, b=128: ap("of" + H, S(128 * j + a, 128 * j + b))
+        blk = lambda n, j, k=ALLP, w=1: ap(n, S(8 * j, 8 * (j + w)), k)
+        return H, c, of, blk, "ps%d" % (4 * h + 3)
+
+    def bank(h):
+        rot[h] = (rot[h] + 1) % 3
+        return "ps%d" % (4 * h + rot[h])
+
+    def newpr():
+        prn[0] = (prn[0] + 1) % NPR
+        return "pr%d" % prn[0]
+
+    MID, EDG = S(1, 15), S(0, 16, 15)
+
+    def gathers(dst, win, oj, h, scale=1.0, bias=0.0, eng="DA"):
+        H, c, of, blk, sm = names(h)
+        for a in range(0, 2048, GC):
+            aff(ap(dst, S(a, a + GC)), ind(win, of(oj, a // 16, (a + GC) // 16)), scale, bias, eng)
+
+    def gather_tt(dst, win, oj, other, o0, op, h):
+        H, c, of, blk, sm = names(h)
+        for a in range(0, 2048, GC):
+            tt(ap(dst, S(a, a + GC)), ind(win, of(oj, a // 16, (a + GC) // 16)), ap(other, S(o0 + a, o0 + a + GC)), op)
+
+    XT, GT = ap("xt", ALLP), ap("gt", ALLP)
+
+    def first(h):
+        cur[0] = h
+        H, c, of, blk, sm = names(h)
+        st, sh = "st" + H, "sh" + H
+        cp(of(0), ap("pin", S(128 * h, 128 * h + 128)))
+        cp(of(1), ap("pin", S(256 + 128 * h, 256 + 128 * h + 128)))
+        pa_, pb_, pl_ = [ap("p16", S(256 * j + 128 * h, 256 * j + 128 * h + 128)) for j in range(3)]
+        aff(ap("lb" + H, S(0, 128)), pl_, -0.125)
+        mm([(blk(sm, 0), [(pa_, I)]), (blk(sm, 1), [(pb_, I), (pa_, NI)]), (blk(sm, 2), [(pl_, I)])])
+        aff(blk(st, 0), blk(sm, 0))
+        aff(blk(sh, 0), blk(sm, 0))
+        aff(blk(st, 2), blk(sm, 1), 0.125)
+        aff(blk(sh, 1), blk(sm, 2))
+        ea, eb = newpr(), newpr()
+        gathers(ea, ap("et", ALLP), 0, h, 1.0 / 1024)
+        gathers(eb, ap("et", ALLP), 1, h, 1.0 / 1024)
+        mm([(blk(sm, 0, k), [(fl(ea, k), SE8)]) for k in range(16)])
+        aff(blk(st, 1), blk(sm, 0), 8.0)
+        aff(blk(st, 3), blk(sm, 0))
+        mm([(blk(sm, 1, k), [(fl(eb, k), SE8)]) for k in range(16)])
+        tt(blk(st, 3), blk(sm, 1), blk(st, 3), AL.subtract)
+
+    def send(h, r):
+        rw, hl, hr = "rw%d" % h, R0 - HS * (r + 1), R0 + 2048 + HS * r
+        i = add("G", {"G": 1000.0}, [ap("sb%d" % h, ALLP, ALLP)], [], None, sem="lo%d" % (2 * r + h), inc=8, late=2500.0, send=(h, r, hl, hr))
+        add("X", {"X": 0.0}, [], [ap(rw, S(hl, hl + HS)), ap(rw, S(hr, hr + HS))], None, sem="ar%d" % (2 * r + h), inc=8, late=2000.0, after=i)
+
+    def step1(h, r):
+        cur[0] = h
+        H, c, of, blk, sm = names(h)
+        st, sf, sh, rw = "st" + H, "sf" + H, "sh" + H, "rw" + H
+        hl, hr = R0 - HS * (r + 1), R0 + 2048 + HS * r
+        for na, nd_, tab in (("xa", "dd", XT), ("ga", "dg", GT)):
+            gathers(na + H, tab, 0, h, -1.0)
+            if DADD[nd_]:
+                gathers(nd_ + H, tab, 1, h)
+                for a in range(0, 128, GC // 16):
+                    pp = S(a, a + GC // 16)
+                    dma(c(nd_, p=pp), c(na, p=pp), 256 * GC, "G")
+            else:
+                gather_tt(nd_ + H, tab, 1, na + H, 0, AL.add, h)
+        e, tx = blk(sf, 0), blk(sh, 2)
+        tt(blk(sf, 1), blk(sh, 1), blk(st, 3), AL.mult)
+        tt(e, blk(sf, 1), blk(st, 1), AL.add)
+        for a in range(4):
+            pl, ks = bank(h), (a, 4)
+            mm([(ap(pl, ALLP, S(k, 16, 4)), [(ap("bk", S(128 * (a + 4 * k), 128 * (a + 4 * k) + 128)), ap("lb" + H, S(0, 128)))]) for k in range(4)])
+            tt(c("ld", ks), c("dd", ks), ap(pl, ALLP, ALLP), AL.mult)
+            tt(c("lg", ks), c("dg", ks), ap(pl, ALLP, ALLP), AL.mult)
+        for a in range(0, 128, 32):
+            p2, pp = bank(h), S(a, a + 32)
+            mm([(ap(p2, ALLP, ALLP), [(I, c("xa", p=pp)), (I, c("ld", p=pp))])])
+            aff(ap(rw, S(R0 + 16 * a, R0 + 16 * a + 512)), ap(p2, ALLP, ALLP), -8.0)
+        dma(c("lg"), c("ga"), 524288, "G")
+        if r == 0:
+            for j, k in ((0, 15), (1, 0)):
+                aff(ap("sb" + H, j, S(0, 128)), ap(rw, S(R0 + k, R0 + 2048, 16)))
+                aff(ap("sb" + H, j, S(128, HS)), blk(sf, 0, k))
+            send(h, 0)
+        tt(blk(sh, 2, MID), blk(sf, 0, S(2, 16)), blk(sf, 0, S(0, 14)), GE)
+        tt(blk(sf, 1, 0), blk(sf, 0, 1), ap(rw, S(hl + 128, hl + HS)), GE)
+        tt(blk(sf, 1, 15), ap(rw, S(hr + 128, hr + HS)), blk(sf, 0, 14), GE)
+        ts(blk(sh, 2, 0), blk(sf, 1, 0), cl(r), AL.mult, -512.0, AL.add)
+        ts(blk(sh, 2, 15), blk(sf, 1, 15), cl(3 + r), AL.mult, -512.0, AL.add)
+        mm([(blk(sm, 3), [(tx, I2), (I, BC)])])
+        ts(of(2), blk(sm, 3), cl(16 + r), AL.add)
+        gathers("tv" + H, ap(rw, S(hl, hr + HS)), 2, h)
+        pgd, pgt, ptt, ptd = newpr(), newpr(), newpr(), newpr()
+        red = lambda j, pr, a: mm([(blk(sm, j, k), [(fl(pr, k), GS)]) for k in range(a, 16, 4)])
+        for a in range(4):
+            pg, ks = bank(h), (a, 4)
+            mm([(ap(pg, ALLP, ALLP), [(I, c("dd", ks))])])
+            tt(fl(pgd, ks), c("lg", ks), ap(pg, ALLP, ALLP), AL.mult)
+            red(0, pgd, a)
+        for a in range(4):
+            pt, ks = bank(h), (a, 4)
+            mm([(ap(pt, ALLP, ALLP), [(E8, c("xa", ks)), (E8, c("ld", ks)), (I, c("tv", ks))])])
+            tt(fl(ptd, ks), c("dd", ks), ap(pt, ALLP, ALLP), AL.mult)
+            tt(fl(pgt, ks), c("lg", ks), ap(pt, ALLP, ALLP), AL.mult)
+            act(fl(ptt, ks), ap(pt, ALLP, ALLP), AF.Square)
+            for j, pr in ((3, ptd), (1, pgt), (2, ptt)):
+                red(j, pr, a)
+
+    def step23(h, r):
+        cur[0] = h
+        H, c, of, blk, sm = names(h)
+        st, sf, sh, rw, q, ed, lb = "st" + H, "sf" + H, "sh" + H, "rw" + H, "q" + H, "ed" + H, "lb" + H
+        last = r == RO - 1
+        a16, l16, dl, lp, m8, mu8, ab, ov, sg_, mw8, uf = [blk(sh, j) for j in (0, 1, 2, 3, 4, 5, 6, 7, 8, 9, 10)]
+        va, ve, da, de = [blk(st, j) for j in range(4)]
+        qr = lambda j: ap(q, S(16 + j, 144, 16), ALLP)
+        aff(blk(sf, 2, w=2), blk(sm, 2, w=2), eng="A")
+        tt(blk(sf, 4, w=2), blk(sf, 2, w=2), blk(sm, 0, w=2), AL.mult)
+        tt(blk(sf, 2), blk(sf, 4), blk(sf, 5), AL.subtract)
+        act(dl, blk(sf, 2), AF.Sign)
+        tt(lp, l16, dl, AL.add)
+        act(mu8, dl, AF.Relu, 8.0)
+        act(ab, lp, AF.Abs, 1.0, -4.0)
+        act(ov, ab, AF.Sign, 1.0, -4.5)
+        tt(blk(sf, 3), mu8, da, AL.mult)
+        tt(sg_, dl, ov, AL.mult)
+        act(mw8, sg_, AF.Relu, 8.0)
+        tt(blk(sf, 4), mw8, da, AL.mult)
+        mm([(blk(sm, 0), [(a16, I), (ov, IN), (blk(sf, 3), I32)])])
+        ts(of(3), blk(sm, 0), 3072.0, AL.add)
+        mm([(blk(sm, 1), [(a16, I), (blk(sf, 4), I32)])])
+        ts(of(4), blk(sm, 1), 1536.0, AL.add)
+        gathers("ld" + H, ap("nt", ALLP), 3, h, 1.0, -1536.0)
+        if XW2:
+            gather_tt("tv" + H, XT, 4, rw, R0, AL.subtract, h)
+        else:
+            gathers("ga" + H, XT, 4, h, -1.0)
+        pw = 128 // PC
+        for a in range(0, 128, pw):
+            pu = ap(sm, S(16 + a // 16, 16 + (a + pw) // 16), ALLP)
+            mm([(pu, [(ap("ones", S(128 * k, 128 * k + 128)), c("ld", k, S(a, a + pw))) for k in range(16)])])
+            ts(of(5, a, a + pw), pu, 1536.0, AL.add)
+        if XW2:
+            gather_tt("lg" + H, XT, 5, "tv" + H, 0, AL.subtract, h)
+        else:
+            gather_tt("lg" + H, XT, 5, rw, R0, AL.add, h)
+        ts(m8, lp, 5.0, GE, 8.0, AL.mult)
+        tt(blk(sf, 5), m8, da, AL.mult)
+        tt(qr(0), blk(sf, 5), va, AL.add)
+        if not last:
+            tt(blk(sf, 6), m8, de, AL.mult)
+            tt(blk(sf, 7), blk(sf, 6), ve, AL.add)
+            ts(qr(1), blk(sf, 7), MAGIC_1, AL.add, -MAGIC_1, AL.add)
+            tt(qr(2), blk(sf, 7), qr(1), AL.subtract)
+            aff(uf, blk(sm, 2))
+        nq = 1 if last else 2
+        grp = [(ap(sm, S(0, 8), e), [(c("ld", k), ap("cb", 0, S(k, 128, 16)))]) for e, k in ((0, 0), (1, 15))]
+        if not last:
+            mm([(ap(sm, 24, S(8 * e, 8 * e + 8)), [(ap("cb", 7 + e, S(15 - j, 143 - j)), ap(sh, S(80, 88), j)) for j in range(16)]) for e in range(2)])
+            ts(of(7, 0, 16), ap(sm, 24, ALLP), 1536.0, AL.add)
+            aff(ap("eg" + H, ALLP), ind(ap("et", ALLP), of(7, 0, 16)), 1.0 / 1024)
+            grp += [(ap(sm, S(8, 16), e), [(ap("eg" + H, S(128 * e, 128 * e + 128)), I32c)]) for e in range(2)]
+        mm(grp)
+        eb = lambda j, a=0, b=16 * nq: ap(ed, j, S(a, b))
+        V, DV, U = ap(st, S(0, 8 * nq), EDG), ap(st, S(16, 16 + 8 * nq), EDG), ap(sm, S(0, 8 * nq), S(0, 2))
+        for j in range(nq):
+            aff(eb(0, 16 * j, 16 * j + 16), blk(sh, 9, EDG), eng="A")
+            act(eb(1, 16 * j, 16 * j + 16), blk(sh, 2, EDG), AF.Relu, -1.0)
+            aff(eb(2, 16 * j, 16 * j + 16), blk(sh, 2, EDG), 0.125, eng="A")
+        act(eb(9, 0, 16), blk(sh, 2, EDG), AF.Relu, -8.0)
+        ts(eb(3), eb(2), 0.0, EQ)
+        tt(eb(4), eb(0), DV, AL.mult)
+        tt(eb(5), eb(4), V, AL.add)
+        tt(eb(7), eb(3), DV, AL.mult)
+        tt(eb(9, 16, 32), blk(sh, 3, EDG), eb(0, 0, 16), AL.subtract)
+        tt(blk(sh, 1, EDG), eb(9, 16, 32), eb(9, 0, 16), AL.add)
+        tt(eb(6), U, eb(5), AL.subtract)
+        tt(eb(4), eb(1), eb(6), AL.mult)
+        tt(eb(8), eb(2), eb(6), AL.mult)
+        tt(V, eb(4), eb(5), AL.add)
+        tt(DV, eb(8), eb(7), AL.add)
+        aff(blk(sh, 0, EDG), blk(st, 0, EDG))
+        if not last:
+            if XW2:
+                for j, k in ((0, 15), (1, 0)):
+                    aff(ap("sb" + H, j, S(0, 128)), c("lg", k))
+            else:
+                pe = bank(h)
+                mm([(blk(pe, j), [(I, c("ga", k)), (I, c("lg", k))]) for j, k in ((0, 15), (1, 0))])
+                aff(ap("sb" + H, ALLP, S(0, 128)), blk(pe, 0, w=2))
+            tt(blk(sf, 6, EDG), blk(sh, 1, EDG), blk(st, 3, EDG), AL.mult)
+            for j, k in ((0, 15), (1, 0)):
+                tt(ap("sb" + H, j, S(128, HS)), blk(sf, 6, k), blk(st, 1, k), AL.add)
+            send(h, r + 1)
+        zc = lambda k: ap("cb", 6, S(15 - k, 143 - k))
+        k0, k1 = S(0, 15), S(1, 16)
+        nr = pw // 16
+        for p0 in range(0, 128, pw):
+            for a in range(p0, p0 + pw, 32):
+                pd, pp = ap(bank(h), ALLP, ALLP), S(a, a + 32)
+                mm([(pd, ([] if XW2 else [(I, c("ga", p=pp, shift=1)), (NI, c("ga", p=pp))]) + [(I, c("lg", p=pp, shift=1)), (NI, c("lg", p=pp))])])
+                act(c("tv", p=pp), pd, AF.Abs)
+            ph = ap(bank(h), S(0, nr), ALLP)
+            mm([(ph, [(zc(k), c("tv", k, S(p0, p0 + pw))) for k in range(15)])])
+            hh, hl = ap(lb, S(128 + p0, 128 + p0 + pw)), ap(lb, S(256 + p0, 256 + p0 + pw))
+            ts(hh, ph, MAGIC_H, AL.add, -MAGIC_H, AL.add)
+            tt(hl, ph, hh, AL.subtract)
+        hh, hl = ap(lb, S(128, 256)), ap(lb, S(256, 384))
+        pq = bank(h)
+        mm([(blk(pq, 0), [(hh, TRI)]), (blk(pq, 1), [(hl, TRI)]), (blk(pq, 2), [(hh, G15)]), (blk(pq, 3), [(hl, G15)])])
+        for j in range(4):
+            aff(qr(3 + j), blk(pq, j))
+        for p0 in range(0, 128, pw):
+            hh, hl = ap(lb, S(128 + p0, 128 + p0 + pw)), ap(lb, S(256 + p0, 256 + p0 + pw))
+            sg = lambda k, n=1: c("dg", p=S(p0 + nr * k, p0 + nr * (k + n)))
+            step = 7 if PC == 2 else 4
+            for a in range(0, 14, step):
+                n = min(step, 14 - a)
+                pk = bank(h)
+                mm([(ap(pk, S(nr * j, nr * j + nr), ALLP), [(ap("wk", S(128 * (a + j), 128 * (a + j + 1))), x) for x in (hh, hl)]) for j in range(n)])
+                act(sg(a, n), ap(pk, S(0, nr * n), ALLP), AF.Sign, 1.0, 0.5)
+            pc = ap(bank(h), S(0, nr), ALLP)
+            mm([(pc, [(I, ap("cb", 10, S(p0, p0 + pw)))] + [(zc(k), sg(k - 1)) for k in range(1, 15)])])
+            ts(of(6, p0, p0 + pw), pc, 14.0, AL.add, 64.0, AL.mult)
+        for a in range(0, 16, 4):
+            pt = bank(h)
+            mm([(blk(pt, j), [(ap(q, S(16, 144), min(a + j, 14)), I), (ap(q, S(9, 137), min(a + j, 14) + 1), I)]) for j in range(4)])
+            aff(ap(rw, S(R0 + 128 * a, R0 + 128 * a + 512)), ap(pt, ALLP, ALLP))
+        gathers("ld" + H, ap(rw, S(R0, R0 + 2048)), 6, h)
+        px = bank(h)
+        mm([(ap(px, ALLP, k), [(c("ld", k), ap("xaw", ALLP))]) for k in range(1, 15)])
+        aff(blk(sh, 0, MID), blk(px, 0, MID))
+        if last:
+            aff(blk(st, 2, MID), blk(px, 2, MID))
+        else:
+            aff(ap(st, ALLP, MID), ap(px, ALLP, MID))
+        mm([(blk(sm, 0), [(a16, I)]), (blk(sm, 1), [(a16, I), (da, I8)])])
+        if not last:
+            ts(of(0, 0, 256), blk(sm, 0, w=2), 1536.0, AL.add)
+        else:
+            aff(blk(sf, 0, w=2), blk(sm, 0, w=2), 1.0, 1536.0)
+            dma(ap("ya", S(128 * h, 128 * h + 128)), blk(sf, 0), 65536)
+            dma(ap("yb", S(128 * h, 128 * h + 128)), blk(sf, 1), 65536)
+        for b in range(2):
+            px = bank(h)
+            mm([(ap(px, ALLP, k), [(c("ld", k), ap(x, S(64 * (k - 1) + 32 * b, 64 * (k - 1) + 32 * b + 32))) for x in ("xh", "xl")]) for k in range(1, 15)])
+            act(ap(sh, S(16 + 32 * b, 48 + 32 * b), MID), ap(px, ALLP, MID), AF.Sign, 1.0, 0.5)
+        mm([(blk(sm, 3, MID), [(I, blk(sh, 2 + m, MID)) for m in range(8)])])
+        aff(blk(sh, 1, MID), blk(sm, 3, MID), 0.5, 4.0)
+        mm([(blk(sm, 2), [(l16, I)])])
+        if not last:
+            aff(ap(lb, S(0, 128)), blk(sm, 2), -0.125)
+        else:
+            aff(blk(sf, 2), blk(sm, 2))
+            dma(ap("yl", S(128 * h, 128 * h + 128)), blk(sf, 2), 65536)
+
+    for h in range(2):
+        first(h)
+    for r in range(RO):
+        for h in range(2):
+            step1(h, r)
+        if r == 0:
+            late_consts()
+        for h in range(2):
+            step23(h, r)
+    return ops
+
+
+def depend(ops):
+    lastw, readers, bankacc = {}, {}, {}
+    for i, o in enumerate(ops):
+        d = set()
+        for a in o["reads"]:
+            rg = region(a)
+            if rg is None:
+                continue
+            if a[0] in lastw:
+                d.update(int(x) for x in np.unique(lastw[a[0]][rg]) if x >= 0)
+        for a in o["writes"]:
+            rg = region(a)
+            if rg is None:
+                continue
+            n = a[0]
+            if n not in lastw:
+                lastw[n] = np.full(_IDX[n].size, -1)
+            d.update(int(x) for x in np.unique(lastw[n][rg]) if x >= 0)
+            m = np.zeros(_IDX[n].size, bool)
+            m[rg] = True
+            keep = []
+            for j, mj in readers.get(n, []):
+                if (mj & m).any():
+                    d.add(j)
+                    mj = mj & ~m
+                if mj.any():
+                    keep.append((j, mj))
+            readers[n] = keep
+        for a in o["writes"]:
+            if region(a) is not None:
+                lastw[a[0]][region(a)] = i
+        rd = {}
+        for a in o["reads"]:
+            if region(a) is not None:
+                rd.setdefault(a[0], np.zeros(_IDX[a[0]].size, bool))[region(a)] = True
+        for n, m in rd.items():
+            readers.setdefault(n, []).append((i, m))
+        for n in set(a[0] for a in o["reads"] + o["writes"] if a[0].startswith("ps")):
+            acc = bankacc.setdefault(n, [None, [], []])
+            if acc[0] != o["eng"] or len(o["eng"]) > 1:
+                acc[:] = [o["eng"], [], acc[1]]
+            d.update(acc[2])
+            acc[1].append(i)
+        d.discard(i)
+        o["deps"] = d
+
+
+def schedule(ops):
+    n = len(ops)
+    succ = [[] for _ in ops]
+    for i, o in enumerate(ops):
+        o["tdeps"] = set(o["deps"]) | ({o["after"]} if "after" in o else set())
+        for j in o["tdeps"]:
+            succ[j].append(i)
+    pri = [0.0] * n
+    for i in range(n - 1, -1, -1):
+        o = ops[i]
+        pri[i] = min(o["cost"][e] for e in o["eng"]) + o.get("late", LAT) + max([pri[j] for j in succ[i]] + [0.0])
+    for i, o in enumerate(ops):
+        if o["half"] is not None:
+            pri[i] += BIAS[o["half"]]
+    pred = [sorted(o["tdeps"]) for o in ops]
+    late = [o.get("late", LAT) for o in ops]
+
+    def place(key, pen, back=False):
+        before, after = (succ, pred) if back else (pred, succ)
+        left = [len(x) for x in before]
+        rdy = [0.0] * n
+        ready = set(i for i in range(n) if not left[i])
+        busy = {e: [] for e in "DAPGSX"}
+        res = [None] * n
+        while ready:
+            i = min(ready, key=lambda j: (key[j], j))
+            ready.remove(i)
+            o, best = ops[i], None
+            for x in o["eng"]:
+                c, st, b = o["cost"][x], rdy[i] + (late[i] if back else 0.0), busy[x]
+                k = len(b)
+                while k > 0 and b[k - 1][1] > st:
+                    k -= 1
+                while k < len(b) and b[k][0] < st + c:
+                    st = max(st, b[k][1])
+                    k += 1
+                f = st + c * (pen[i] if x == "D" else 1.0)
+                if best is None or f < best[0]:
+                    best = (f, st, x, k)
+            f, st, x, k = best
+            busy[x].insert(k, (st, st + o["cost"][x]))
+            res[i] = (x, st, st + o["cost"][x] + (0.0 if back else late[i]))
+            for j in after[i]:
+                rdy[j] = max(rdy[j], res[i][2])
+                left[j] -= 1
+                if not left[j]:
+                    ready.add(j)
+        return max(r[2] for r in res), res
+
+    rng = np.random.default_rng(SEARCH[0])
+    key = [-p for p in pri]
+    pen = bp = [PEN[0]] * n
+    flex = [i for i in range(n) if ops[i]["eng"] == "DA" and ops[i]["cost"]["A"] > 400]
+    best = place(key, pen)
+    now = best
+    for it in range(SEARCH[1]):
+        z = rng.normal(0.0, SEARCH[2], (2, n))
+        p2 = list(pen)
+        for i in rng.choice(flex, SEARCH[4]):
+            p2[int(i)] = float(rng.choice([0.3, PEN[0], 30.0]))
+        b = place([-now[1][i][2] + float(z[0, i]) for i in range(n)], p2, True)
+        t = place([-b[1][i][2] + float(z[1, i]) for i in range(n)], p2)
+        if t[0] < best[0]:
+            best, bp = t, p2
+        now, pen = (t, p2) if t[0] < best[0] * SEARCH[3] else (best, bp)
+    for o, r in zip(ops, best[1]):
+        o["q"], o["t0"], o["t1"] = r
+    return sorted(range(n), key=lambda i: (ops[i]["t0"], i))
+
+
+def plan():
+    ops = build()
+    depend(ops)
+    order = schedule(ops)
+    cnt, known, prog = {}, {e: {} for e in "DAPGSX"}, []
+    for i in order:
+        o = ops[i]
+        q = o["q"]
+        kn = known[q]
+        waits = {}
+        for j in sorted(o["deps"], key=lambda j: -ops[j]["t1"]):
+            p = ops[j]
+            if q == "P" and p["q"] == "P":
+                continue
+            s, c = p["mark"]
+            if kn.get(s, 0) < c:
+                waits[s] = max(waits.get(s, 0), c)
+                for s2, c2 in p["clock"].items():
+                    kn[s2] = max(kn.get(s2, 0), c2)
+        fs = o["emit"](q) if o["emit"] else [None]
+        s = o.get("sem", "c" + q)
+        cnt[s] = cnt.get(s, 0) + o.get("inc", len(fs))
+        o["mark"] = (s, cnt[s])
+        o["clock"] = dict(kn) if q != "X" else {}
+        o["clock"][s] = cnt[s]
+        prog.append((q, waits, fs, s, o))
+    return prog, cnt, ops
+
+
+_PLAN = []
+
+
+def rank_program(g, core, T, topo):
+    rank = T.rank_of(core)
+    if rank is None:
+        return
+    if not _PLAN:
+        _PLAN.append(plan())
+    prog, cnt, _ = _PLAN[0]
+    Q = {"D": g.vector, "A": g.scalar, "P": g.tensor, "G": g, "S": g.sync}
+    n = len(T.cores)
+    nxt, prv = T.cores[(rank + 1) % n], T.cores[(rank - 1) % n]
+    for q, waits, fs, s, o in prog:
+        if q == "X":
+            continue
+        for w, c in waits.items():
+            Q[q].wait_ge(T.sem[w], c)
+        if "send" in o:
+            h, r, hl, hr = o["send"]
+            trs = []
+            for j, (dst, at) in enumerate(((nxt, hl), (prv, hr))):
+                rid, pid, _ = topo.addr(dst)
+                eng = topo.engines(core, dst)
+                k = len(eng) // 2
+                mask = sum(1 << e for e in eng[j * k:j * k + 4])
+                trs.append(RemoteDMATransfer(dst_ids=[DstId(rid=rid, pnc=pid)], dma_engine_mask=mask, remote_sem=T.sem["ar%d" % (2 * r + h)],
+                                             src=T["sb%d" % h][:, j, :], dst=T["rw%d" % h][:, at:at + HS]))
+            g.remote_dma_fused(trs, local_sem=T.sem[s])
+            continue
+        for f in fs:
+            f(g, T).then_inc(T.sem[s], o.get("inc", 1))
+    for s, c in cnt.items():
+        g.wait_ge(T.sem[s], c)

@@ -11,12 +11,15 @@ GC = 1024
 NPR = 6
 MAGIC_H = 1.5 * 2 ** 30
 MAGIC_1 = 1.5 * 2 ** 23
-BIAS = [15000.0, 0.0]
+BIAS = [6000.0, 0.0]
 DADD = {"dd": False, "dg": False}
-XW2 = False
+SPEEDS = [((1.3, 1.3), 1.0, 60, 120.0, 1.0, 0.9), ((0.75, 1.28), 1.15, 80, 250.0, 1.6, 1.0)]
+POLISH = [24000, 80.0]
+RDMA = False
+XW2 = True
 PC = 2
 PEN = [3.0]
-SEARCH = [0, 350, 200.0, 1.005, 4]
+SEARCH = [3, 300, 120.0, 1.003, 3]
 
 SCRATCH = {
     "xt": ("sbuf", [128, W], "bfloat16"), "gt": ("sbuf", [128, W], "bfloat16"),
@@ -51,7 +54,7 @@ SEMAPHORES = ["cD", "cA", "cP", "cG"] + ["dm%d" % i for i in range(NDMA)] \
 
 S = slice
 ALLP = S(None)
-CY, PCY, GCY, LAT = 1.0, 0.5, 1.56, 100.0
+CY, PCY, GCY, LAT = 0.9, 0.4, 1.56, 120.0
 
 
 def ap(name, *idx, p=ALLP):
@@ -183,7 +186,7 @@ def build():
         nd[0] += 1
         if q == "G":
             f = lambda g, T: g.dma_start(real(T, out), real(T, a), accum_op=AL.add)
-            return add(q, {q: 1000.0}, [a, out], [out], lambda e: [f], sem=sem, inc=16, late=2000 + nbytes / 125.0)
+            return add(q, {q: 1000.0}, [a, out], [out], lambda e: [f], sem=sem, inc=16, late=2500 + nbytes / 100.0)
         if q == "S":
             f = lambda g, T: g.sync.dma_start(real(T, out), real(T, a))
         else:
@@ -205,9 +208,11 @@ def build():
     sel(I, on(128), dg_, EQ, 0.0, 0, 1)
     sel(ap("bk", ALLP), on(2048), [[-1, 16], [-16, 8], [0, 16]], EQ, 0.0, 0, 1)
     sel(I32, ONE32, dg_, EQ, 0.0, 0, 1)
-    mset(ap("et", ALLP), 0)
+    mset(ap("et", S(0, 1536)), 0)
+    iota(ap("et", S(1536, W)), [[0, W - 1536]], 0, 0)
     dma(ap("et", ALLP, p=S(0, 128, 16)), ap("erec", ALLP), 98304 * 4)
     dma(ap("nt", S(0, W)), ap("nbr", ALLP), 1572864 * 2)
+    ops[-1]["reads"] += [ap("gt", S(0, 8)), ap("et", S(0, 8))]
     ts(NI, I, -1.0, AL.mult)
     ts(I2, I, 2.0, AL.mult)
     E8 = ap("cb", 12, S(0, 128))
@@ -356,9 +361,9 @@ def build():
             gathers(na + H, tab, 0, h, -1.0)
             if DADD[nd_]:
                 gathers(nd_ + H, tab, 1, h)
-                for a in range(0, 128, GC // 16):
-                    pp = S(a, a + GC // 16)
-                    dma(c(nd_, p=pp), c(na, p=pp), 256 * GC, "G")
+                for a in range(0, 128, 64):
+                    pp = S(a, a + 64)
+                    dma(c(nd_, p=pp), c(na, p=pp), 262144, "G")
             else:
                 gather_tt(nd_ + H, tab, 1, na + H, 0, AL.add, h)
         e, tx = blk(sf, 0), blk(sh, 2)
@@ -369,7 +374,11 @@ def build():
             mm([(ap(pl, ALLP, S(k, 16, 4)), [(ap("bk", S(128 * (a + 4 * k), 128 * (a + 4 * k) + 128)), ap("lb" + H, S(0, 128)))]) for k in range(4)])
             tt(c("ld", ks), c("dd", ks), ap(pl, ALLP, ALLP), AL.mult)
             tt(c("lg", ks), c("dg", ks), ap(pl, ALLP, ALLP), AL.mult)
-        for a in range(0, 128, 32):
+        for a in range(0, 128, 64) if RDMA else []:
+            pp = S(a, a + 64)
+            dma(c("ld", p=pp), c("xa", p=pp), 262144, "G")
+            aff(ap(rw, S(R0 + 16 * a, R0 + 16 * a + 1024)), c("ld", p=pp), -8.0)
+        for a in [] if RDMA else range(0, 128, 32):
             p2, pp = bank(h), S(a, a + 32)
             mm([(ap(p2, ALLP, ALLP), [(I, c("xa", p=pp)), (I, c("ld", p=pp))])])
             aff(ap(rw, S(R0 + 16 * a, R0 + 16 * a + 512)), ap(p2, ALLP, ALLP), -8.0)
@@ -396,7 +405,7 @@ def build():
             red(0, pgd, a)
         for a in range(4):
             pt, ks = bank(h), (a, 4)
-            mm([(ap(pt, ALLP, ALLP), [(E8, c("xa", ks)), (E8, c("ld", ks)), (I, c("tv", ks))])])
+            mm([(ap(pt, ALLP, ALLP), ([] if RDMA else [(E8, c("xa", ks))]) + [(E8, c("ld", ks)), (I, c("tv", ks))])])
             tt(fl(ptd, ks), c("dd", ks), ap(pt, ALLP, ALLP), AL.mult)
             tt(fl(pgt, ks), c("lg", ks), ap(pt, ALLP, ALLP), AL.mult)
             act(fl(ptt, ks), ap(pt, ALLP, ALLP), AF.Square)
@@ -607,7 +616,13 @@ def depend(ops):
             d.update(acc[2])
             acc[1].append(i)
         d.discard(i)
-        o["deps"] = d
+        anc = 0
+        for j in d:
+            anc |= ops[j]["anc"]
+        o["deps"] = set(j for j in d if not anc >> j & 1)
+        for j in d:
+            anc |= 1 << j
+        o["anc"] = anc
 
 
 def schedule(ops):
@@ -631,12 +646,17 @@ def schedule(ops):
         before, after = (succ, pred) if back else (pred, succ)
         left = [len(x) for x in before]
         rdy = [0.0] * n
-        ready = set(i for i in range(n) if not left[i])
+        rank = [0] * n
+        byrank = [int(j) for j in np.argsort(np.array(key), kind="stable")]
+        for k, j in enumerate(byrank):
+            rank[j] = k
+        ready = set(rank[i] for i in range(n) if not left[i])
         busy = {e: [] for e in "DAPGSX"}
         res = [None] * n
         while ready:
-            i = min(ready, key=lambda j: (key[j], j))
-            ready.remove(i)
+            k = min(ready)
+            ready.remove(k)
+            i = byrank[k]
             o, best = ops[i], None
             for x in o["eng"]:
                 c, st, b = o["cost"][x], rdy[i] + (late[i] if back else 0.0), busy[x]
@@ -656,8 +676,33 @@ def schedule(ops):
                 rdy[j] = max(rdy[j], res[i][2])
                 left[j] -= 1
                 if not left[j]:
-                    ready.add(j)
-        return max(r[2] for r in res), res
+                    ready.add(rank[j])
+        if back:
+            return 0.0, res
+        order = sorted(range(n), key=lambda i: (res[i][1], i))
+        tot = max(r[2] for r in res)
+        for cs, w in alt:
+            free, fin = {e: 0.0 for e in "DAPGSX"}, [0.0] * n
+            for i in order:
+                x = res[i][0]
+                st = free[x]
+                for j in pred[i]:
+                    if fin[j] > st:
+                        st = fin[j]
+                free[x] = st + cs[i][x]
+                fin[i] = free[x] + cs[i]["late"]
+            tot += w * max(fin)
+        return tot, res
+
+    alt = []
+    for fg, fp, ovh, lat, fd, w in SPEEDS:
+        cs = []
+        for o in ops:
+            c = {e: (v - 60) * ((fg[o["eng"] == "D"]) if any(a[0].startswith("of") for a in o["reads"]) else 1.0) + ovh if e in "DA" else v * (fp if e == "P" else 1.0)
+                 for e, v in o["cost"].items()}
+            c["late"] = o["late"] * fd if "late" in o else lat
+            cs.append(c)
+        alt.append((cs, w))
 
     rng = np.random.default_rng(SEARCH[0])
     key = [-p for p in pri]
@@ -675,6 +720,58 @@ def schedule(ops):
         if t[0] < best[0]:
             best, bp = t, p2
         now, pen = (t, p2) if t[0] < best[0] * SEARCH[3] else (best, bp)
+    base = [dict(o["cost"], late=late[i]) for i, o in enumerate(ops)]
+    allc = [(base, 1.0)] + alt
+
+    def run(order, q, cs):
+        free, last, fin, sta, why = {e: 0.0 for e in "DAPGSX"}, {}, [0.0] * n, [0.0] * n, [None] * n
+        for i in order:
+            x = q[i]
+            st, w = free[x], (last.get(x), 1)
+            for j in pred[i]:
+                if fin[j] > st:
+                    st, w = fin[j], (j, 0)
+            free[x] = st + cs[i][x]
+            fin[i], sta[i], why[i], last[x] = free[x] + cs[i]["late"], st, w, i
+        return max(fin), fin, sta, why
+
+    q = [r[0] for r in best[1]]
+    order = sorted(range(n), key=lambda i: (best[1][i][1], i))
+    runs = [run(order, q, cs) for cs, w in allc]
+    val = sum(r[0] * w for r, (cs, w) in zip(runs, allc))
+    keep = (val, order, q)
+    for it in range(POLISH[0]):
+        r = runs[it % len(runs)]
+        i, moves = int(np.argmax(r[1])), []
+        while i is not None:
+            j, onq = r[3][i]
+            if onq and j is not None:
+                moves.append((j, i))
+            if ops[i]["eng"] == "DA":
+                moves.append((i, None))
+            i = j
+        u, v = moves[int(rng.integers(len(moves)))]
+        o2, q2 = order, q
+        if v is None:
+            q2 = list(q)
+            q2[u] = "A" if q[u] == "D" else "D"
+        else:
+            a, b = order.index(u), order.index(v)
+            between = order[a + 1:b + 1]
+            if any(u in ops[j]["tdeps"] for j in between):
+                continue
+            o2 = order[:a] + between + [u] + order[b + 1:]
+        r2 = [run(o2, q2, cs) for cs, w in allc]
+        v2 = sum(x[0] * w for x, (cs, w) in zip(r2, allc))
+        if v2 < val + POLISH[1] * (1.0 - it / POLISH[0]) * float(rng.exponential()):
+            pos = {j: k for k, j in enumerate(o2)}
+            order, q, runs, val = sorted(o2, key=lambda j: (r2[0][2][j], pos[j])), q2, r2, v2
+            if val < keep[0]:
+                keep = (val, order, q)
+    r = run(keep[1], keep[2], base)
+    for i, o in enumerate(ops):
+        o["q"], o["t0"], o["t1"] = keep[2][i], r[2][i], r[1][i]
+    return keep[1]
     for o, r in zip(ops, best[1]):
         o["q"], o["t0"], o["t1"] = r
     return sorted(range(n), key=lambda i: (ops[i]["t0"], i))

@@ -5,56 +5,59 @@ from concourse.mybir import AluOpType, AxisListType, ActivationFunctionType
 AL = AluOpType
 AF = ActivationFunctionType
 W, RO = 3072, 3
-HS = 136
-R0 = 3 * HS
+HS = 272
 GC = 1024
 NPR = 6
-MAGIC_H = 1.5 * 2 ** 30
-MAGIC_1 = 1.5 * 2 ** 23
+OFF = 1536.0
+CY, PCY, GCY, LAT = 0.9, 0.4, 1.56, 120.0
 BIAS = [6000.0, 0.0]
-DADD = {"dd": False, "dg": False}
 SPEEDS = [((1.3, 1.3), 1.0, 60, 120.0, 1.0, 0.9), ((0.75, 1.28), 1.15, 80, 250.0, 1.6, 1.0)]
-POLISH = [24000, 80.0]
-RDMA = False
-XW2 = True
-PC = 2
+POLISH = [16000, 80.0]
 PEN = [3.0]
-SEARCH = [3, 300, 120.0, 1.003, 3]
+SEARCH = [3, 200, 120.0, 1.003, 3]
+PW = 64
+RD = "GG"
+TF = False
+DENG = "G"
+WENG = "G"
 
 SCRATCH = {
-    "xt": ("sbuf", [128, W], "bfloat16"), "gt": ("sbuf", [128, W], "bfloat16"),
-    "nt": ("sbuf", [128, 2 * W], "int32"), "et": ("sbuf", [128, W], "int32"),
-    "pin": ("sbuf", [128, 768], "int32"), "p16": ("sbuf", [128, 768], "float16"),
-    "ones": ("sbuf", [128, 2048], "bfloat16"), "bk": ("sbuf", [128, 2048], "bfloat16"),
-    "wk": ("sbuf", [128, 1792], "bfloat16"),
-    "xh": ("sbuf", [128, 896], "bfloat16"), "xl": ("sbuf", [128, 896], "bfloat16"),
-    "cb": ("sbuf", [128, 13, 144], "bfloat16"), "c32": ("sbuf", [128, 3, 128], "float32"),
-    "xaw": ("sbuf", [128, 32], "bfloat16"), "col": ("sbuf", [128, 64], "float32"), "coli": ("sbuf", [128, 8], "int32"),
+    "vt": ("sbuf", [128, W], "float32"), "xt": ("sbuf", [128, W], "bfloat16"), "gt": ("sbuf", [128, W], "bfloat16"),
+    "nt": ("sbuf", [128, W], "int32"), "et": ("sbuf", [128, W], "int32"),
+    "bk": ("sbuf", [128, 2048], "bfloat16"), "wk": ("sbuf", [128, 1792], "bfloat16"),
+    "xw": ("sbuf", [128, 182, 8], "float32"), "ct": ("sbuf", [128, 14, 13], "float32"), "c2": ("sbuf", [128, 14, 9], "float32"),
+    "cb": ("sbuf", [128, 160, 16], "bfloat16"), "zz": ("sbuf", [128, 4, 144], "bfloat16"), "c32": ("sbuf", [128, 8, 128], "float32"),
+    "col": ("sbuf", [128, 80], "float32"), "coli": ("sbuf", [128, 8], "int32"),
 }
 for _i in range(NPR):
-    SCRATCH["pr%d" % _i] = ("sbuf", [128, 2048], "float32")
+    SCRATCH["pr%d" % _i] = ("sbuf", [128, 128, 4], "float32")
 for _h in range(2):
-    for _n in ("xa", "dd", "ga", "dg", "ld", "lg", "tv"):
-        SCRATCH["%s%d" % (_n, _h)] = ("sbuf", [128, 2064 if _n in ("ga", "lg") else 2048], "float16")
+    SCRATCH["va%d" % _h] = ("sbuf", [128, 2048], "float32")
+    SCRATCH["d8%d" % _h] = ("sbuf", [128, 2048], "float32")
+    SCRATCH["tb%d" % _h] = ("sbuf", [128, 2176], "float32")
+    SCRATCH["di%d" % _h] = ("sbuf", [128, 2048], "int32")
+    SCRATCH["rw%d" % _h] = ("sbuf", [128, 2048 + RO * HS], "float32")
+    for _n in ("g16", "t16", "ld", "y16"):
+        SCRATCH["%s%d" % (_n, _h)] = ("sbuf", [128, 2064 if _n in ("y16", "ld") else 2048], "float16")
     SCRATCH["eg%d" % _h] = ("sbuf", [128, 256], "float32")
-    SCRATCH["rw%d" % _h] = ("sbuf", [128, 2048 + 6 * HS], "float32")
-    SCRATCH["q%d" % _h] = ("sbuf", [128, 144, 16], "float16")
-    SCRATCH["of%d" % _h] = ("sbuf", [128, 912], "uint16")
-    SCRATCH["lb%d" % _h] = ("sbuf", [128, 384], "bfloat16")
+    SCRATCH["of%d" % _h] = ("sbuf", [128, 656], "uint16")
     SCRATCH["st%d" % _h] = ("sbuf", [128, 32, 16], "float32")
-    SCRATCH["sf%d" % _h] = ("sbuf", [128, 64, 16], "float32")
-    SCRATCH["sh%d" % _h] = ("sbuf", [128, 88, 16], "float16")
-    SCRATCH["ed%d" % _h] = ("sbuf", [128, 10, 32], "float32")
-    SCRATCH["sb%d" % _h] = ("sbuf", [128, 2, HS], "float32")
-for _i in range(8):
-    SCRATCH["ps%d" % _i] = ("psum", [128, 32, 16], "float32")
-NDMA = 72
+    SCRATCH["sf%d" % _h] = ("sbuf", [128, 112, 16], "float32")
+    SCRATCH["sh%d" % _h] = ("sbuf", [128, 48, 16], "bfloat16")
+    SCRATCH["uf%d" % _h] = ("sbuf", [128, 8, 16], "float16")
+    SCRATCH["sg%d" % _h] = ("sbuf", [128, 72, 16], "bfloat16")
+    SCRATCH["ed%d" % _h] = ("sbuf", [128, 144], "float32")
+    SCRATCH["eb%d" % _h] = ("sbuf", [128, 16], "bfloat16")
+    SCRATCH["sb%d" % _h] = ("sbuf", [128, HS], "float32")
+    for _i in range(3):
+        SCRATCH["ps%d" % (4 * _h + _i)] = ("psum", [128, 128, 4], "float32")
+    SCRATCH["ps%d" % (4 * _h + 3)] = ("psum", [128, 32, 16], "float32")
+NDMA = 110
 SEMAPHORES = ["cD", "cA", "cP", "cG"] + ["dm%d" % i for i in range(NDMA)] \
     + ["ar%d" % i for i in range(2 * RO)] + ["lo%d" % i for i in range(2 * RO)]
 
 S = slice
 ALLP = S(None)
-CY, PCY, GCY, LAT = 0.9, 0.4, 1.56, 120.0
 
 
 def ap(name, *idx, p=ALLP):
@@ -112,14 +115,13 @@ def parts(a):
 
 
 def build():
-    ops = []
+    ops, cur = [], [None]
 
     def add(eng, cost, reads, writes, emit, **kw):
         o = dict(eng=eng, cost=cost, reads=[x for r in reads for x in parts(r)], writes=writes, emit=emit, half=cur[0])
         o.update(kw)
         ops.append(o)
         return len(ops) - 1
-    cur = [None]
 
     def vcost(n, k):
         return 60 + max(64, n * k) * CY
@@ -128,13 +130,14 @@ def build():
         k = GCY if a[0] == "IND" else 1 if psum(a) or psum(b) else 2
         add("D", {"D": vcost(nel(a), k)}, [a, b], [out], lambda e: [lambda g, T: g.vector.tensor_tensor(real(T, out), real(T, a), real(T, b), op)])
 
+    def tsf(out, a, s1, op0, s2, op1):
+        if op1 is None:
+            return lambda g, T: g.vector.tensor_scalar(real(T, out), real(T, a), real(T, s1), None, op0)
+        return lambda g, T: g.vector.tensor_scalar(real(T, out), real(T, a), real(T, s1), real(T, s2), op0, op1)
+
     def ts(out, a, s1, op0, s2=None, op1=None):
         k = 0.5 if two(a) and two(out) else 1
-        if op1 is None:
-            f = lambda g, T: g.vector.tensor_scalar(real(T, out), real(T, a), real(T, s1), None, op0)
-        else:
-            f = lambda g, T: g.vector.tensor_scalar(real(T, out), real(T, a), real(T, s1), real(T, s2), op0, op1)
-        add("D", {"D": vcost(nel(a), k)}, [a, s1, s2], [out], lambda e: [f])
+        add("D", {"D": vcost(nel(a), k)}, [a, s1, s2], [out], lambda e: [tsf(out, a, s1, op0, s2, op1)])
 
     def cp(out, a):
         add("D", {"D": vcost(nel(a), 0.5 if two(a) and two(out) else 1)}, [a], [out], lambda e: [lambda g, T: g.vector.tensor_copy(real(T, out), real(T, a))])
@@ -142,31 +145,38 @@ def build():
     def mset(out, v):
         add("D", {"D": vcost(nel(out), 0.5 if two(out) else 1)}, [], [out], lambda e: [lambda g, T: g.vector.memset(real(T, out), v)])
 
-    def act(out, a, fn, scale=1.0, bias=0.0):
-        add("A", {"A": vcost(nel(a), 1)}, [a], [out], lambda e: [lambda g, T: g.scalar.activation(real(T, out), real(T, a), fn, bias=bias, scale=scale)])
-
-    def aff(out, a, scale=1.0, bias=0.0, eng="DA"):
+    def act(out, a, fn, scale=1.0, bias=0.0, alt=None, eng="DA"):
         k = GCY if a[0] == "IND" else 1
 
         def emit(e):
             if e == "A":
-                return [lambda g, T: g.scalar.activation(real(T, out), real(T, a), AF.Identity, bias=bias, scale=scale)]
-            if scale == 1.0 and bias == 0.0:
+                return [lambda g, T: g.scalar.activation(real(T, out), real(T, a), fn, bias=real(T, bias), scale=real(T, scale))]
+            if e == "G":
+                return [lambda g, T: g.affine_select(real(T, out), real(T, a), [[0, nel(a)]], AL.is_equal, 0.0, 0, 0)]
+            if alt == ():
                 return [lambda g, T: g.vector.tensor_copy(real(T, out), real(T, a))]
-            return [lambda g, T: g.vector.tensor_scalar(real(T, out), real(T, a), scale, bias, AL.mult, AL.add)]
+            return [tsf(out, a, *alt)]
         kd = 0.5 if two(a) and two(out) else k
-        add(eng, {"D": vcost(nel(a), kd), "A": vcost(nel(a), k)}, [a], [out], emit)
+        add("A" if alt is None else eng, {"D": vcost(nel(a), kd), "A": vcost(nel(a), k), "G": 170 + 2 * nel(a) * CY}, [a, scale, bias], [out], emit)
 
-    def mm(lst):
+    def aff(out, a, scale=1.0, bias=0.0, eng="DA"):
+        act(out, a, AF.Identity, scale, bias, () if scale == 1.0 and bias == 0.0 else (scale, AL.mult, bias, AL.add), eng)
+
+    def relu(out, a, scale=1.0):
+        act(out, a, AF.Relu, scale, 0.0, (scale, AL.mult, 0.0, AL.max))
+
+    def mm(lst, start=True, stop=True):
         fs, cost, rd, wr = [], 30, [], []
         for out, terms in lst:
             wr.append(out)
+            if not start:
+                rd.append(out)
             for i, tm in enumerate(terms):
                 l, r = tm[0], tm[1]
                 o = tm[2] if len(tm) > 2 else out
                 cost += max(64, nel(r)) * (1 if two(l) else 4) * PCY
                 rd += [l, r]
-                fs.append(lambda g, T, o=o, l=l, r=r, a=(i == 0), b=(i == len(terms) - 1): g.tensor.matmul(real(T, o), real(T, l), real(T, r), a, b))
+                fs.append(lambda g, T, o=o, l=l, r=r, a=(start and i == 0), b=(stop and i == len(terms) - 1): g.tensor.matmul(real(T, o), real(T, l), real(T, r), a, b))
         add("P", {"P": cost}, rd, wr, lambda e: fs)
 
     def iota(out, pat, base, cm):
@@ -186,122 +196,75 @@ def build():
         nd[0] += 1
         if q == "G":
             f = lambda g, T: g.dma_start(real(T, out), real(T, a), accum_op=AL.add)
-            return add(q, {q: 1000.0}, [a, out], [out], lambda e: [f], sem=sem, inc=16, late=2500 + nbytes / 100.0)
+            return add(q, {q: 1000.0}, [a, out], [out], lambda e: [f], sem=sem, inc=16, late=2500 + nbytes / 150.0)
         if q == "S":
             f = lambda g, T: g.sync.dma_start(real(T, out), real(T, a))
         else:
             f = lambda g, T: g.scalar.dma_start(real(T, out), real(T, a))
         add(q, {q: 80.0}, [a], [out], lambda e: [f], sem=sem, inc=16, late=2000 + nbytes / 250.0)
 
+    def dmas(lst, nbytes):
+        nd[0] += 1
+        fs = [lambda g, T, o=o, a=a: g.sync.dma_start(real(T, o), real(T, a)) for o, a in lst]
+        add("S", {"S": 80.0 * len(lst)}, [a for o, a in lst], [o for o, a in lst], lambda e: fs, sem="dm%d" % (nd[0] - 1), inc=16, late=2000 + nbytes / 250.0)
+
     EQ, GE = AL.is_equal, AL.is_ge
-    dma(ap("pin", S(0, 256)), ap("pa", ALLP), 131072)
-    dma(ap("pin", S(256, 512)), ap("pb", ALLP), 131072, "A")
-    dma(ap("xt", ALLP), ap("xrec", ALLP), 786432 * 1.5)
-    dma(ap("pin", S(512, 768)), ap("lam", ALLP), 131072, "A")
-    dma(ap("gt", ALLP), ap("grec", ALLP), 786432 * 2.2, "A")
-    I, NI, I2, IN, TRI, G15, ZC, Z0, Z15, PI, P64, BC = [ap("cb", j, S(0, 128)) for j in range(12)]
-    I32, I8, ONE32 = [ap("c32", j, ALLP) for j in range(3)]
-    mset(ap("ones", ALLP), 1.0)
-    mset(ONE32, 1.0)
-    on = lambda n: ap("ones", S(0, n))
-    dg_ = [[-1, 128]]
-    sel(I, on(128), dg_, EQ, 0.0, 0, 1)
-    sel(ap("bk", ALLP), on(2048), [[-1, 16], [-16, 8], [0, 16]], EQ, 0.0, 0, 1)
-    sel(I32, ONE32, dg_, EQ, 0.0, 0, 1)
-    mset(ap("et", S(0, 1536)), 0)
-    iota(ap("et", S(1536, W)), [[0, W - 1536]], 0, 0)
+    MID, EDG = S(1, 15), S(0, 16, 15)
+    blk = lambda n, j, k=ALLP, w=1: ap(n, S(8 * j, 8 * (j + w)), k)
+    rb = lambda n, j, w=1: ap(n, S(32 * j, 32 * (j + w)), ALLP)
+    pin = lambda j, h: ap("di0", S(256 * j + 128 * h, 256 * j + 128 * h + 128))
+    dma(ap("di0", S(0, 256)), ap("pa", ALLP), 131072)
+    dma(ap("di0", S(256, 512)), ap("pb", ALLP), 131072, "A")
+    dma(ap("di0", S(512, 768)), ap("lam", ALLP), 131072)
+    for a in range(0, W, 1024):
+        dma(ap("xt", S(a, a + 1024)), ap("xrec", S(a, a + 1024)), 400000 + 512 * (a + 1024), "A")
+        dma(ap("gt", S(a, a + 1024)), ap("grec", S(a, a + 1024)), 400000 + 512 * (a + 1024))
+    mset(ap("et", S(0, 2048)), 0)
+    iota(ap("et", S(2048, W)), [[0, W - 2048]], 0, 0)
     dma(ap("et", ALLP, p=S(0, 128, 16)), ap("erec", ALLP), 98304 * 4)
-    dma(ap("nt", S(0, W)), ap("nbr", ALLP), 1572864 * 2)
-    ops[-1]["reads"] += [ap("gt", S(0, 8)), ap("et", S(0, 8))]
-    ts(NI, I, -1.0, AL.mult)
-    ts(I2, I, 2.0, AL.mult)
-    E8 = ap("cb", 12, S(0, 128))
-    ts(E8, I, 8.0, AL.mult)
-    ts(IN, I, -1536.0, AL.mult)
-    ts(I8, I32, 8.0, AL.mult)
+    dma(ap("nt", ALLP), ap("nbr", ALLP), 1572864 * 2)
+    ops[-1]["reads"] += [ap("gt", S(1024, 1032)), ap("et", S(0, 8))]
+    cb = lambda j, k=ALLP: blk("cb", j, k)
+    I, ONE, BC, P64, G15 = [cb(j) for j in range(5)]
+    sc = {}
+    I32, ONE32 = ap("c32", 0, ALLP), ap("c32", 1, ALLP)
+    mset(ONE, 1.0)
+    mset(ONE32, 1.0)
+    sel(I, ONE, [[-1, 128]], EQ, 0.0, 0, 1)
+    sel(I32, ONE32, [[-1, 128]], EQ, 0.0, 0, 1)
+    for j, v in enumerate((1.0 / 2048, -1.0, -2.0, 2.0, -0.25, 1.0 / 16, -7.0 / 16, 8.0, 4.0, 0.5, -4.0)):
+        sc[v] = 5 + j
+        aff(cb(5 + j), I, v)
+    Ib = lambda v, k=ALLP: cb(sc[v], k)
+    sf32 = {}
+    for j, v in enumerate((-1.0, 2.0, -0.5, 0.5)):
+        sf32[v] = ap("c32", 2 + j, ALLP)
+        aff(sf32[v], I32, v)
+    If = lambda v: sf32[v]
     cl = lambda a, n=1: ap("col", S(a, a + n))
-    GS, SE8, SEN = cl(32, 8), cl(40, 8), cl(48, 8)
-    I32c = ap("c32", 0, S(0, 128, 16))
-    ts(SE8, I32c, 0.125, AL.mult)
-    ts(SEN, I32c, -0.125, AL.mult)
-    sel(GS, ap("c32", 2, S(0, 8)), [[-16, 8]], GE, 0.0, 0, 1)
+    GS, SE4, EQ8 = cl(32, 8), cl(40, 8), cl(56, 8)
+    aff(SE4, ap("c32", 0, S(0, 128, 16)), 4.0)
+    sel(GS, ap("c32", 1, S(0, 8)), [[-16, 8]], GE, 0.0, 0, 1)
     sel(GS, GS, [[16, 8]], GE, 0.0, 15, -1)
-    iota(PI, [[1, 128]], 0, 0)
+    mset(ap("bk", ALLP), -1.0)
+    sel(ap("bk", ALLP), ap("bk", ALLP), [[-1, 16], [-16, 8], [0, 16]], EQ, 0.0, 0, 1)
+    iota(P64, [[1, 128]], 0, 0)
     iota(ap("coli", S(0, 1)), [[0, 1]], 0, 1)
-    iota(cl(0, 3), [[HS, 3]], HS + 1, 15)
-    iota(cl(3, 3), [[HS, 3]], 2034, -15)
-    iota(cl(6, 3), [[HS, 3]], HS - 1, 0)
-    iota(cl(9, 3), [[-HS, 3]], 1025 - HS, 0)
-    ts(cl(0, 6), cl(0, 6), 0.5, AL.mult)
+    iota(cl(0, 3), [[-HS, 3]], 1 - 2048, 15)
+    iota(cl(3, 3), [[HS, 3]], 2048 + 144 - 14, -15)
+    iota(cl(6, 3), [[HS, 3]], 1025, 0)
+    aff(cl(0, 6), cl(0, 6), 0.5)
     ts(ap("coli", S(4, 5)), ap("coli", S(0, 1)), 15, AL.bitwise_and)
     cp(cl(12), ap("coli", S(4, 5)))
     ts(cl(13), cl(12), 0.0, EQ)
     ts(cl(14), cl(12), 15.0, EQ, 1024.0, AL.mult)
-    ts(cl(9, 3), cl(9, 3), cl(13), AL.mult, cl(14), AL.add)
-    ts(cl(6, 3), cl(6, 3), cl(12), AL.add)
-    tt(cl(16, 3), cl(6, 3), cl(9, 3), AL.add)
-    ts(cl(15), cl(13), -15.0, AL.mult, 16.0, AL.add)
-    ts(BC, PI, cl(15), AL.mult)
-    ts(P64, PI, 1.0 / 64, AL.mult)
-    ts(ap("p16", S(0, 512)), ap("pin", S(0, 512)), -1536.0, AL.add)
-    cp(ap("p16", S(512, 768)), ap("pin", S(512, 768)))
-    late = []
-
-    def late_consts():
-        cur[0] = None
-        iota(ap("nt", S(W, 2 * W)), [[1, W]], 0, 0)
-        zc = lambda j: ap("cb", j, ALLP)
-        sel(zc(6), on(144), [[0, 9], [1, 16]], EQ, 0.0, -15, 0)
-        sel(zc(7), zc(6), [[-16, 9], [0, 16]], EQ, 0.0, 0, 1)
-        sel(zc(8), zc(6), [[-16, 9], [0, 16]], EQ, 0.0, -15, 1)
-        sel(zc(6), zc(6), [[-16, 9], [0, 16]], GE, 0.0, 0, 1)
-        sel(zc(6), zc(6), [[16, 9], [0, 16]], GE, 0.0, 15, -1)
-        ts(TRI, on(128), 1.0 / 128, AL.mult)
-        sel(G15, TRI, [[-16, 8], [0, 16]], GE, 0.0, 0, 1)
-        sel(TRI, G15, [[16, 8], [1, 16]], GE, 0.0, -1, -1)
-        sel(G15, G15, [[16, 8], [0, 16]], GE, 0.0, 14, -1)
-        sel(ap("ones", ALLP), ap("bk", ALLP), [[-1, 16], [0, 8], [1, 16]], EQ, 0.0, 0, 0)
-        wk = ap("wk", ALLP)
-        iota(wk, [[1, 14], [0, 128]], 1, 0)
-        for k in range(1, 15):
-            b = ap("wk", S(128 * (k - 1), 128 * k))
-            sel(b, b, [[-16, 8], [-1, 16]], GE, float(k - 15), 0, 1)
-        sel(wk, wk, [[0, 14], [-16, 8], [0, 16]], GE, 0.0, 0, 1)
-        sel(wk, wk, [[0, 14], [16, 8], [0, 16]], GE, 0.0, 14, -1)
-        xh, xl = ap("xh", ALLP), ap("xl", ALLP)
-        pat = [[0, 112], [-16, 8]]
-        iota(xh, [[0, 14], [3840, 8], [0, 8]], -28800, 0)
-        sel(xh, xh, pat, EQ, 0.0, -3, 1)
-        iota(xl, [[0, 14], [-3840, 8], [0, 8]], -1920, 0)
-        sel(xl, xl, pat, EQ, 0.0, -10, 1)
-        dma(ap("xh", ALLP, p=S(10, 128, 16)), ap("xl", ALLP, p=S(10, 128, 16)), 20000)
-        iota(xl, [[2048, 14], [0, 64]], 2048, 0)
-        sel(xl, xl, pat, EQ, 0.0, -5, 1)
-        dma(ap("xh", ALLP, p=S(5, 128, 16)), ap("xl", ALLP, p=S(5, 128, 16)), 20000)
-        dma(ap("xl", ALLP, p=S(1, 128)), ap("xh", ALLP, p=S(0, 127)), 230000)
-        dma(ap("xl", ALLP, p=S(0, 1)), ap("xh", ALLP, p=S(127, 128)), 2000)
-        ic = lambda q: ap("cb", 0, S(q, 128, 16))
-        xw = lambda q: ap("xaw", S(8 * q, 8 * q + 8))
-        cp(xw(0), ic(0))
-        tt(xw(1), ic(1), ic(2), AL.add)
-        tt(xw(2), ic(7), ic(0), AL.subtract)
-        tt(xw(3), ic(8), ic(9), AL.add)
-        tt(xw(3), xw(3), xw(1), AL.subtract)
-        ts(ap("xaw", S(16, 32)), ap("xaw", S(16, 32)), 0.125, AL.mult)
-        for h in range(2):
-            for a in range(0, 144, 48):
-                ts(ap("q%d" % h, S(a, a + 48), ALLP), ap("xt", S(0, 768)), 0.0, AL.mult)
-            for n in ("ga", "lg"):
-                ts(ap("%s%d" % (n, h), S(2048, 2064)), ap("xt", S(0, 16)), 0.0, AL.mult)
+    ts(cl(14), cl(14), cl(12), AL.add, -1.0, AL.add)
+    ts(cl(16, 3), cl(6, 3), cl(13), AL.mult, cl(14), AL.add)
+    aff(cl(15), cl(13), -15.0, 16.0)
+    aff(BC, P64, cl(15))
+    aff(P64, P64, 2.0 / PW)
 
     rot, prn = [0, 0], [0]
-
-    def names(h):
-        H = str(h)
-        c = lambda n, k=ALLP, p=S(0, 128), shift=0: fl(n + H, k, p, shift)
-        of = lambda j, a=0, b=128: ap("of" + H, S(128 * j + a, 128 * j + b))
-        blk = lambda n, j, k=ALLP, w=1: ap(n, S(8 * j, 8 * (j + w)), k)
-        return H, c, of, blk, "ps%d" % (4 * h + 3)
 
     def bank(h):
         rot[h] = (rot[h] + 1) % 3
@@ -311,257 +274,333 @@ def build():
         prn[0] = (prn[0] + 1) % NPR
         return "pr%d" % prn[0]
 
-    MID, EDG = S(1, 15), S(0, 16, 15)
+    def table():
+        cur[0] = None
+        for a in range(0, W, 512):
+            pv = ap(bank(a // 512 % 2), ALLP, ALLP)
+            mm([(pv, [(I, ap("xt", S(a, a + 512))), (Ib(1.0 / 2048), ap("gt", S(a, a + 512)))])])
+            aff(ap("vt", S(a, a + 512)), pv, 1.0, 128.125)
+
+    def late_consts():
+        cur[0] = None
+        zc = lambda j: ap("zz", j, ALLP)
+        mset(zc(3), 1.0)
+        sel(zc(0), zc(3), [[0, 9], [1, 16]], EQ, 0.0, -15, 0)
+        sel(zc(1), zc(0), [[-16, 9], [0, 16]], EQ, 0.0, 0, 1)
+        sel(zc(2), zc(0), [[-16, 9], [0, 16]], EQ, 0.0, -15, 1)
+        sel(zc(0), zc(0), [[-16, 9], [0, 16]], GE, 0.0, 0, 1)
+        sel(zc(0), zc(0), [[16, 9], [0, 16]], GE, 0.0, 15, -1)
+        sel(G15, ONE, [[-16, 8], [0, 16]], GE, 0.0, 0, 1)
+        sel(G15, G15, [[16, 8], [0, 16]], GE, 0.0, 14, -1)
+        wk = ap("wk", ALLP)
+        iota(wk, [[1, 14], [0, 128]], 1, 0)
+        for k in range(1, 15):
+            b = ap("wk", S(128 * (k - 1), 128 * k))
+            sel(b, b, [[-16, 8], [-1, 16]], GE, float(k - 15), 0, 1)
+        sel(wk, wk, [[0, 14], [-16, 8], [0, 16]], GE, 0.0, 0, 1)
+        sel(wk, wk, [[0, 14], [16, 8], [0, 16]], GE, 0.0, 14, -1)
+        mset(ap("wk", S(15, 1792, 16)), 0.0)
+        iota(EQ8, [[1, 8]], 0, 0)
+        ts(EQ8, EQ8, cl(12), EQ)
+        iota(ap("ct", ALLP, S(0, 8)), [[0, 14], [2, 8]], 1, 0)
+        iota(ap("ct", ALLP, S(8, 9)), [[0, 14]], 15, 0)
+        iota(ap("c2", ALLP, ALLP), [[0, 2], [1, 7], [0, 9]], -3, 0)
+        aff(cl(64, 4), cl(60, 4), 16.0)
+        aff(cl(66), cl(62), -15.0)
+        for j in range(2):
+            x = ap("ct", S(7 * j, 7 * j + 7), S(0, 9))
+            aff(x, x, cl(66), cl(64 + j))
+        aff(ap("c2", ALLP, ALLP), ap("c2", ALLP, ALLP), cl(67))
+        tt(ap("ct", ALLP, S(0, 9)), ap("ct", ALLP, S(0, 9)), ap("c2", ALLP, ALLP), AL.add)
+        aff(cl(56, 4), cl(56, 4), 0.5)
+        tt(cl(68, 2), ap("col", S(57, 60, 2)), ap("col", S(56, 60, 2)), AL.subtract)
+        tt(cl(70, 2), ap("col", S(57, 60, 2)), ap("col", S(56, 60, 2)), AL.add)
+        for j in range(4):
+            aff(ap("ct", ALLP, 9 + j), ap("c32", 1, S(0, 14)), cl(68 + j))
+        for j in range(8):
+            aff(ap("xw", ALLP, j), ap("ct", ALLP, ALLP), cl(32 + j))
+        for h in range(2):
+            mset(ap("sg%d" % h, ALLP, EDG), 0.0)
+            mset(ap("ld%d" % h, S(2048, 2064)), 0.0)
+            mset(ap("y16%d" % h, S(2048, 2064)), 0.0)
+            dma(ap("tb%d" % h, ALLP), ap("vt", S(0, 2176)), 1114112)
+
+    def names(h):
+        H = str(h)
+        c = lambda n, k=ALLP, p=S(0, 128), shift=0: fl(n + H, k, p, shift)
+        of = lambda j, a=0, b=128: ap("of" + H, S(128 * j + a, 128 * j + b))
+        return H, c, of, "ps%d" % (4 * h + 3)
 
     def gathers(dst, win, oj, h, scale=1.0, bias=0.0, eng="DA"):
-        H, c, of, blk, sm = names(h)
+        H, c, of, sm = names(h)
         for a in range(0, 2048, GC):
             aff(ap(dst, S(a, a + GC)), ind(win, of(oj, a // 16, (a + GC) // 16)), scale, bias, eng)
 
-    def gather_tt(dst, win, oj, other, o0, op, h):
-        H, c, of, blk, sm = names(h)
+    def gather_tt(dst, win, oj, other, op, h):
+        H, c, of, sm = names(h)
         for a in range(0, 2048, GC):
-            tt(ap(dst, S(a, a + GC)), ind(win, of(oj, a // 16, (a + GC) // 16)), ap(other, S(o0 + a, o0 + a + GC)), op)
+            tt(ap(dst, S(a, a + GC)), ind(win, of(oj, a // 16, (a + GC) // 16)), ap(other, S(a, a + GC)), op)
 
-    XT, GT = ap("xt", ALLP), ap("gt", ALLP)
+    XT, VT, NT, ET = ap("xt", ALLP), ap("vt", ALLP), ap("nt", ALLP), ap("et", ALLP)
 
     def first(h):
         cur[0] = h
-        H, c, of, blk, sm = names(h)
-        st, sh = "st" + H, "sh" + H
-        cp(of(0), ap("pin", S(128 * h, 128 * h + 128)))
-        cp(of(1), ap("pin", S(256 + 128 * h, 256 + 128 * h + 128)))
-        pa_, pb_, pl_ = [ap("p16", S(256 * j + 128 * h, 256 * j + 128 * h + 128)) for j in range(3)]
-        aff(ap("lb" + H, S(0, 128)), pl_, -0.125)
-        mm([(blk(sm, 0), [(pa_, I)]), (blk(sm, 1), [(pb_, I), (pa_, NI)]), (blk(sm, 2), [(pl_, I)])])
+        H, c, of, sm = names(h)
+        st, sf, sh, ed = "st" + H, "sf" + H, "sh" + H, "ed" + H
+        f, da, fd, z, y = [blk(sf, j) for j in range(5)]
+        ts(f, pin(2, h), 8.0, EQ)
+        tt(da, pin(1, h), pin(0, h), AL.subtract)
+        tt(fd, f, da, AL.mult)
+        tt(z, pin(0, h), fd, AL.add)
+        tt(y, pin(1, h), fd, AL.subtract)
+        cp(of(0, 0, 256), blk(sf, 3, w=2))
+        ts(pin(2, h), pin(2, h), 7, AL.bitwise_and)
+        aff(blk(sh, 0), pin(2, h), 0.125)
+        gathers("d8" + H, ET, 1, h)
+        gathers("rw" + H, ET, 0, h)
+        mm([(blk(sm, 2), [(y, I32)]), (blk(sm, 0), [(z, If(0.5)), (y, If(-0.5))]), (blk(sm, 1), [(f, I32)])])
+        aff(blk(st, 2), blk(sm, 2), 1.0, -OFF)
         aff(blk(st, 0), blk(sm, 0))
-        aff(blk(sh, 0), blk(sm, 0))
-        aff(blk(st, 2), blk(sm, 1), 0.125)
-        aff(blk(sh, 1), blk(sm, 2))
-        ea, eb = newpr(), newpr()
-        gathers(ea, ap("et", ALLP), 0, h, 1.0 / 1024)
-        gathers(eb, ap("et", ALLP), 1, h, 1.0 / 1024)
-        mm([(blk(sm, 0, k), [(fl(ea, k), SE8)]) for k in range(16)])
-        aff(blk(st, 1), blk(sm, 0), 8.0)
-        aff(blk(st, 3), blk(sm, 0))
-        mm([(blk(sm, 1, k), [(fl(eb, k), SE8)]) for k in range(16)])
-        tt(blk(st, 3), blk(sm, 1), blk(st, 3), AL.subtract)
+        aff(ap(ed, S(96, 112)), blk(sm, 1, EDG), 2.0, -1.0)
+        aff(ap(ed, S(112, 128)), blk(sm, 1, EDG), -4.0, 2.0)
+        mm([(blk(sm, 3, k), [(c("d8", k), SE4)]) for k in range(16)])
+        aff(blk(st, 3), blk(sm, 3), 2.0)
+        aff(blk(sf, 8), blk(sm, 3))
+        mm([(blk(sm, 1, k), [(c("rw", k), SE4)]) for k in range(16)])
+        tt(blk(st, 1), blk(sm, 1), blk(sf, 8), AL.subtract)
+
+    def spread(h, x, p0, a):
+        pl = bank(h)
+        mm([(ap(pl, S(k // 4, 128, 2), k % 4), [(ap("bk", S(128 * (a + 2 * k), 128 * (a + 2 * k) + 128)), ap(x[0], S(x[1] + p0 // 16, x[1] + p0 // 16 + 4), ALLP))]) for k in range(8)])
+        return ap(pl, ALLP, ALLP), dict(k=(a, 2), p=S(p0, p0 + 64))
 
     def send(h, r):
-        rw, hl, hr = "rw%d" % h, R0 - HS * (r + 1), R0 + 2048 + HS * r
-        i = add("G", {"G": 1000.0}, [ap("sb%d" % h, ALLP, ALLP)], [], None, sem="lo%d" % (2 * r + h), inc=8, late=2500.0, send=(h, r, hl, hr))
-        add("X", {"X": 0.0}, [], [ap(rw, S(hl, hl + HS)), ap(rw, S(hr, hr + HS))], None, sem="ar%d" % (2 * r + h), inc=8, late=2000.0, after=i)
+        rw, sb, a = "rw%d" % h, "sb%d" % h, 2048 + HS * r
+        tr = [(ap(sb, S(0, 136)), ap(rw, S(a, a + 136))), (ap(sb, S(136, HS)), ap(rw, S(a + 136, a + HS)))]
+        i = add("G", {"G": 1000.0}, [ap(sb, ALLP)], [], None, sem="lo%d" % (2 * r + h), inc=8, late=2500.0, send=tr, arr="ar%d" % (2 * r + h))
+        add("X", {"X": 0.0}, [], [ap(rw, S(a, a + HS))], None, sem="ar%d" % (2 * r + h), inc=8, late=2000.0, after=i)
 
     def step1(h, r):
         cur[0] = h
-        H, c, of, blk, sm = names(h)
-        st, sf, sh, rw = "st" + H, "sf" + H, "sh" + H, "rw" + H
-        hl, hr = R0 - HS * (r + 1), R0 + 2048 + HS * r
-        for na, nd_, tab in (("xa", "dd", XT), ("ga", "dg", GT)):
-            gathers(na + H, tab, 0, h, -1.0)
-            if DADD[nd_]:
-                gathers(nd_ + H, tab, 1, h)
-                for a in range(0, 128, 64):
-                    pp = S(a, a + 64)
-                    dma(c(nd_, p=pp), c(na, p=pp), 262144, "G")
-            else:
-                gather_tt(nd_ + H, tab, 1, na + H, 0, AL.add, h)
-        e, tx = blk(sf, 0), blk(sh, 2)
-        tt(blk(sf, 1), blk(sh, 1), blk(st, 3), AL.mult)
-        tt(e, blk(sf, 1), blk(st, 1), AL.add)
-        for a in range(4):
-            pl, ks = bank(h), (a, 4)
-            mm([(ap(pl, ALLP, S(k, 16, 4)), [(ap("bk", S(128 * (a + 4 * k), 128 * (a + 4 * k) + 128)), ap("lb" + H, S(0, 128)))]) for k in range(4)])
-            tt(c("ld", ks), c("dd", ks), ap(pl, ALLP, ALLP), AL.mult)
-            tt(c("lg", ks), c("dg", ks), ap(pl, ALLP, ALLP), AL.mult)
-        for a in range(0, 128, 64) if RDMA else []:
-            pp = S(a, a + 64)
-            dma(c("ld", p=pp), c("xa", p=pp), 262144, "G")
-            aff(ap(rw, S(R0 + 16 * a, R0 + 16 * a + 1024)), c("ld", p=pp), -8.0)
-        for a in [] if RDMA else range(0, 128, 32):
-            p2, pp = bank(h), S(a, a + 32)
-            mm([(ap(p2, ALLP, ALLP), [(I, c("xa", p=pp)), (I, c("ld", p=pp))])])
-            aff(ap(rw, S(R0 + 16 * a, R0 + 16 * a + 512)), ap(p2, ALLP, ALLP), -8.0)
-        dma(c("lg"), c("ga"), 524288, "G")
+        H, c, of, sm = names(h)
+        st, sf, sh, rw, ed = "st" + H, "sf" + H, "sh" + H, "rw" + H, "ed" + H
+        hz, hE, z, Ez = [blk(st, j) for j in range(4)]
+        lb = blk(sh, 0)
+        gathers("va" + H, VT, 0, h, -1.0)
+        gather_tt("d8" + H, VT, 1, "va" + H, AL.add, h)
+        pq = rb(bank(h), 0)
+        mm([(pq, [(lb, Ib(-2.0)), (Ib(2.0), ONE)])])
+        tt(pq, pq, hE, AL.mult)
+        tt(blk(sf, 0), pq, Ez, AL.add)
+        for p0 in (0, 64):
+            cols = S(16 * p0, 16 * p0 + 1024)
+            aff(ap("di" + H, cols), ap("d8" + H, cols), eng=DENG)
+            for a in range(2):
+                pw, ks = spread(h, (sh, 0), p0, a)
+                tt(pw, c("d8", **ks), pw, AL.mult)
+                tt(pw, c("va", **ks), pw, AL.add)
+                aff(c("y16", **ks), pw)
+                tt(c("g16", **ks), pw, c("y16", **ks), AL.subtract)
+            aff(ap(rw, cols), ap("y16" + H, cols), eng=WENG)
         if r == 0:
-            for j, k in ((0, 15), (1, 0)):
-                aff(ap("sb" + H, j, S(0, 128)), ap(rw, S(R0 + k, R0 + 2048, 16)))
-                aff(ap("sb" + H, j, S(128, HS)), blk(sf, 0, k))
+            aff(ap("sb" + H, S(128, 136)), blk(sf, 0, 15))
+            aff(ap("sb" + H, S(136, 144)), blk(sf, 0, 0))
+            aff(ap("sb" + H, S(0, 128)), c("y16", 15))
+            aff(ap("sb" + H, S(144, HS)), c("y16", 0))
             send(h, 0)
-        tt(blk(sh, 2, MID), blk(sf, 0, S(2, 16)), blk(sf, 0, S(0, 14)), GE)
-        tt(blk(sf, 1, 0), blk(sf, 0, 1), ap(rw, S(hl + 128, hl + HS)), GE)
-        tt(blk(sf, 1, 15), ap(rw, S(hr + 128, hr + HS)), blk(sf, 0, 14), GE)
-        ts(blk(sh, 2, 0), blk(sf, 1, 0), cl(r), AL.mult, -512.0, AL.add)
-        ts(blk(sh, 2, 15), blk(sf, 1, 15), cl(3 + r), AL.mult, -512.0, AL.add)
-        mm([(blk(sm, 3), [(tx, I2), (I, BC)])])
-        ts(of(2), blk(sm, 3), cl(16 + r), AL.add)
-        gathers("tv" + H, ap(rw, S(hl, hr + HS)), 2, h)
-        pgd, pgt, ptt, ptd = newpr(), newpr(), newpr(), newpr()
-        red = lambda j, pr, a: mm([(blk(sm, j, k), [(fl(pr, k), GS)]) for k in range(a, 16, 4)])
+        gathers("ld" + H, NT, 0, h, 1.0, -OFF)
+        sl = 2048 + HS * r
+        mo = lambda k=ALLP: ap("uf" + H, ALLP, k)
+        tt(mo(MID), blk(sf, 0, S(2, 16)), blk(sf, 0, S(0, 14)), GE)
+        tt(blk(sf, 1, 0), blk(sf, 0, 1), ap(rw, S(sl + 128, sl + 136)), GE)
+        tt(blk(sf, 1, 15), ap(rw, S(sl + 136, sl + 144)), blk(sf, 0, 14), GE)
+        aff(mo(0), blk(sf, 1, 0), cl(r), 512.0)
+        aff(mo(15), blk(sf, 1, 15), cl(3 + r), -512.0)
+        po = bank(h)
+        mm([(rb(po, 0), [(mo(), Ib(2.0)), (I, BC)])])
+        ts(of(2), rb(po, 0), cl(16 + r), AL.add)
+        red = lambda j, pr, a: mm([(blk(sm, j, a + 4 * k), [(ap(pr, ALLP, k), GS)]) for k in range(4)])
         for a in range(4):
-            pg, ks = bank(h), (a, 4)
-            mm([(ap(pg, ALLP, ALLP), [(I, c("dd", ks))])])
-            tt(fl(pgd, ks), c("lg", ks), ap(pg, ALLP, ALLP), AL.mult)
-            red(0, pgd, a)
+            pg, ks, pr = ap(bank(h), ALLP, ALLP), (a, 4), newpr()
+            mm([(pg, [(I, c("g16", ks))])])
+            tt(ap(pr, ALLP, ALLP), c("di", ks), pg, AL.mult)
+            red(0, pr, a)
+        if TF:
+            gather_tt("t16" + H, ap(rw, S(0, sl + HS)), 2, "y16" + H, AL.subtract, h)
+        else:
+            gathers("t16" + H, ap(rw, S(0, sl + HS)), 2, h)
         for a in range(4):
-            pt, ks = bank(h), (a, 4)
-            mm([(ap(pt, ALLP, ALLP), ([] if RDMA else [(E8, c("xa", ks))]) + [(E8, c("ld", ks)), (I, c("tv", ks))])])
-            tt(fl(ptd, ks), c("dd", ks), ap(pt, ALLP, ALLP), AL.mult)
-            tt(fl(pgt, ks), c("lg", ks), ap(pt, ALLP, ALLP), AL.mult)
-            act(fl(ptt, ks), ap(pt, ALLP, ALLP), AF.Square)
-            for j, pr in ((3, ptd), (1, pgt), (2, ptt)):
+            pt, ks = ap(bank(h), ALLP, ALLP), (a, 4)
+            ptd, pgt, ptt = newpr(), newpr(), newpr()
+            mm([(pt, [(I, c("t16", ks))] + ([] if TF else [(Ib(-1.0), c("y16", ks))]))])
+            act(ap(ptt, ALLP, ALLP), c("t16", ks) if TF else pt, AF.Square)
+            tt(ap(ptd, ALLP, ALLP), c("di", ks), pt, AL.mult)
+            tt(ap(pgt, ALLP, ALLP), c("g16", ks), pt, AL.mult)
+            for j, pr in ((2, ptt), (3, ptd), (1, pgt)):
                 red(j, pr, a)
 
     def step23(h, r):
         cur[0] = h
-        H, c, of, blk, sm = names(h)
-        st, sf, sh, rw, q, ed, lb = "st" + H, "sf" + H, "sh" + H, "rw" + H, "q" + H, "ed" + H, "lb" + H
+        H, c, of, sm = names(h)
+        st, sf, sh, rw, ed, sg, va = "st" + H, "sf" + H, "sh" + H, "rw" + H, "ed" + H, "sg" + H, "va" + H
         last = r == RO - 1
-        a16, l16, dl, lp, m8, mu8, ab, ov, sg_, mw8, uf = [blk(sh, j) for j in (0, 1, 2, 3, 4, 5, 6, 7, 8, 9, 10)]
-        va, ve, da, de = [blk(st, j) for j in range(4)]
-        qr = lambda j: ap(q, S(16 + j, 144, 16), ALLP)
-        aff(blk(sf, 2, w=2), blk(sm, 2, w=2), eng="A")
-        tt(blk(sf, 4, w=2), blk(sf, 2, w=2), blk(sm, 0, w=2), AL.mult)
-        tt(blk(sf, 2), blk(sf, 4), blk(sf, 5), AL.subtract)
-        act(dl, blk(sf, 2), AF.Sign)
-        tt(lp, l16, dl, AL.add)
-        act(mu8, dl, AF.Relu, 8.0)
-        act(ab, lp, AF.Abs, 1.0, -4.0)
-        act(ov, ab, AF.Sign, 1.0, -4.5)
-        tt(blk(sf, 3), mu8, da, AL.mult)
-        tt(sg_, dl, ov, AL.mult)
-        act(mw8, sg_, AF.Relu, 8.0)
-        tt(blk(sf, 4), mw8, da, AL.mult)
-        mm([(blk(sm, 0), [(a16, I), (ov, IN), (blk(sf, 3), I32)])])
-        ts(of(3), blk(sm, 0), 3072.0, AL.add)
-        mm([(blk(sm, 1), [(a16, I), (blk(sf, 4), I32)])])
-        ts(of(4), blk(sm, 1), 1536.0, AL.add)
-        gathers("ld" + H, ap("nt", ALLP), 3, h, 1.0, -1536.0)
-        if XW2:
-            gather_tt("tv" + H, XT, 4, rw, R0, AL.subtract, h)
-        else:
-            gathers("ga" + H, XT, 4, h, -1.0)
-        pw = 128 // PC
-        for a in range(0, 128, pw):
-            pu = ap(sm, S(16 + a // 16, 16 + (a + pw) // 16), ALLP)
-            mm([(pu, [(ap("ones", S(128 * k, 128 * k + 128)), c("ld", k, S(a, a + pw))) for k in range(16)])])
-            ts(of(5, a, a + pw), pu, 1536.0, AL.add)
-        if XW2:
-            gather_tt("lg" + H, XT, 5, "tv" + H, 0, AL.subtract, h)
-        else:
-            gather_tt("lg" + H, XT, 5, rw, R0, AL.add, h)
-        ts(m8, lp, 5.0, GE, 8.0, AL.mult)
-        tt(blk(sf, 5), m8, da, AL.mult)
-        tt(qr(0), blk(sf, 5), va, AL.add)
-        if not last:
-            tt(blk(sf, 6), m8, de, AL.mult)
-            tt(blk(sf, 7), blk(sf, 6), ve, AL.add)
-            ts(qr(1), blk(sf, 7), MAGIC_1, AL.add, -MAGIC_1, AL.add)
-            tt(qr(2), blk(sf, 7), qr(1), AL.subtract)
-            aff(uf, blk(sm, 2))
         nq = 1 if last else 2
-        grp = [(ap(sm, S(0, 8), e), [(c("ld", k), ap("cb", 0, S(k, 128, 16)))]) for e, k in ((0, 0), (1, 15))]
+        hz, hE, z, Ez = [blk(st, j) for j in range(4)]
+        lb, dl, ov, lam, hh, hl = [blk(sh, j) for j in range(6)]
+        aff(blk(sf, 2, w=2), blk(sm, 2, w=2))
+        pn = bank(h)
+        mm([(rb(pn, 0), [(If(-1.0), z)] + [(c("ld", k), ap("cb", S(0, 8), k), ap(pn, S(k // 4, 32, 4), k % 4)) for k in range(16)])])
+        tt(blk(sf, 4), blk(sm, 0), blk(sf, 2), AL.mult)
+        tt(blk(sm, 1), blk(sm, 1), blk(sf, 3), AL.mult)
+        tt(blk(sm, 1), blk(sm, 1), blk(sf, 4), AL.subtract)
+        act(dl, blk(sm, 1), AF.Sign, -1.0)
+        mm([(blk(sm, j), [(I, dl), (lb, Ib(8.0))]) for j in range(nq)])
+        relu(ov, blk(sm, 0), -1.0)
+        prod = blk(sf, 2)
+        tt(prod, rb(pn, 0), ov, AL.mult)
+        pu = bank(h)
+        mm([(rb(pu, 0), [(z, I32), (prod, I32)]), (rb(pu, 1), [(dl, I), (ov, Ib(2.0))])])
+        ts(of(3), rb(pu, 0), OFF, AL.add)
+        aff(lam, rb(pu, 1), 0.125)
         if not last:
-            mm([(ap(sm, 24, S(8 * e, 8 * e + 8)), [(ap("cb", 7 + e, S(15 - j, 143 - j)), ap(sh, S(80, 88), j)) for j in range(16)]) for e in range(2)])
-            ts(of(7, 0, 16), ap(sm, 24, ALLP), 1536.0, AL.add)
-            aff(ap("eg" + H, ALLP), ind(ap("et", ALLP), of(7, 0, 16)), 1.0 / 1024)
-            grp += [(ap(sm, S(8, 16), e), [(ap("eg" + H, S(128 * e, 128 * e + 128)), I32c)]) for e in range(2)]
-        mm(grp)
-        eb = lambda j, a=0, b=16 * nq: ap(ed, j, S(a, b))
-        V, DV, U = ap(st, S(0, 8 * nq), EDG), ap(st, S(16, 16 + 8 * nq), EDG), ap(sm, S(0, 8 * nq), S(0, 2))
-        for j in range(nq):
-            aff(eb(0, 16 * j, 16 * j + 16), blk(sh, 9, EDG), eng="A")
-            act(eb(1, 16 * j, 16 * j + 16), blk(sh, 2, EDG), AF.Relu, -1.0)
-            aff(eb(2, 16 * j, 16 * j + 16), blk(sh, 2, EDG), 0.125, eng="A")
-        act(eb(9, 0, 16), blk(sh, 2, EDG), AF.Relu, -8.0)
-        ts(eb(3), eb(2), 0.0, EQ)
-        tt(eb(4), eb(0), DV, AL.mult)
-        tt(eb(5), eb(4), V, AL.add)
-        tt(eb(7), eb(3), DV, AL.mult)
-        tt(eb(9, 16, 32), blk(sh, 3, EDG), eb(0, 0, 16), AL.subtract)
-        tt(blk(sh, 1, EDG), eb(9, 16, 32), eb(9, 0, 16), AL.add)
-        tt(eb(6), U, eb(5), AL.subtract)
-        tt(eb(4), eb(1), eb(6), AL.mult)
-        tt(eb(8), eb(2), eb(6), AL.mult)
-        tt(V, eb(4), eb(5), AL.add)
-        tt(DV, eb(8), eb(7), AL.add)
-        aff(blk(sh, 0, EDG), blk(st, 0, EDG))
+            aff(ap("uf" + H, ALLP, ALLP), rb(pu, 0))
+        gather_tt("di" + H, VT, 3, va, AL.add, h)
+        for p0 in (0, 64):
+            for a in range(2):
+                pw, ks = spread(h, (sh, 24), p0, a)
+                if RD[p0 // 64] == "D":
+                    tt(pw, c("di", **ks), pw, AL.mult)
+                    tt(c("ld", **ks), c("y16", **ks), pw, AL.add)
+                else:
+                    tt(c("ld", **ks), c("di", **ks), pw, AL.mult)
+            if RD[p0 // 64] == "G":
+                dma(c("ld", p=S(p0, p0 + 64)), c("y16", p=S(p0, p0 + 64)), 262144, "G")
+        mu = ap("eb" + H, ALLP)
         if not last:
-            if XW2:
-                for j, k in ((0, 15), (1, 0)):
-                    aff(ap("sb" + H, j, S(0, 128)), c("lg", k))
-            else:
-                pe = bank(h)
-                mm([(blk(pe, j), [(I, c("ga", k)), (I, c("lg", k))]) for j, k in ((0, 15), (1, 0))])
-                aff(ap("sb" + H, ALLP, S(0, 128)), blk(pe, 0, w=2))
-            tt(blk(sf, 6, EDG), blk(sh, 1, EDG), blk(st, 3, EDG), AL.mult)
+            ts(mu, blk(sm, 0, EDG), 8.0, EQ, -2.0, AL.mult)
+        ts(blk(sm, 0, w=nq), blk(sm, 0, w=nq), 5.0, AL.is_lt, 2.0, AL.mult)
+        tt(blk(sf, 3, w=nq), blk(sm, 0, w=nq), blk(st, 0, w=nq), AL.mult)
+        pc = bank(h)
+        mm([(rb(pc, j), [(blk(st, 2 + j), I32), (blk(sf, 3 + j), I32)]) for j in range(nq)])
+        aff(blk(sf, 6, w=nq), rb(pc, 0, nq))
+        row = lambda j, u, a: ap("tb" + H, S(PW * (17 * u + a), PW * (17 * u + a + 16)), p=S(j, 128, 16))
+        for u in range(128 // PW):
+            dmas([(row(j, u, 1 - j % 2), ap(sf, S(48 + 8 * (j // 2) + u * PW // 16, 48 + 8 * (j // 2) + (u + 1) * PW // 16), ALLP)) for j in range(2 * nq)], 1024 * nq * PW)
+        er = lambda j, n=1: ap(sm, S(j, j + n), ALLP)
+        on16, ove = ap("cb", 8, ALLP), blk(sh, 2, EDG)
+        lp = [(I, blk(sh, 1, EDG)), (lb, Ib(8.0, EDG)), (Ib(8.0), ove)]
+        if not last:
+            mm([(er(16 + j), [(I, on16), (Ib(-2.0), ove), (I, mu)]) for j in range(2)] + [(er(18 + j), [(Ib(2.0), ove), (Ib(-1.0), mu)]) for j in range(2)]
+               + [(er(20), lp + [(Ib(4.0), mu)])] + [(er(21 + j), [(I, on16), (I, mu)]) for j in range(2)]
+               + [(er(28), [(Ib(-0.25), blk(sh, 1, EDG)), (lb, Ib(-2.0, EDG)), (Ib(-2.0), ove), (Ib(-1.0), mu), (Ib(2.0), on16)])]
+               + [(ap(sm, 23, S(8 * e, 8 * e + 8)), [(ap("zz", 1 + e, S(15 - j, 143 - j)), ap("uf" + H, ALLP, j)) for j in range(16)]) for e in range(2)])
+            ts(of(5, 0, 16), er(23), OFF, AL.add)
+            aff(ap("eg" + H, ALLP), ind(ET, of(5, 0, 16)))
+            for j in range(2):
+                tt(ap(ed, S(32 * j, 32 * j + 32)), er(16 + 2 * j, 2), blk(st, 0, EDG, 2), AL.mult)
+            tt(ap(ed, S(96, 128)), er(21, 2), ap(ed, S(96, 128)), AL.mult)
+            aff(blk(sg, 0, EDG), er(20), 2.0)
+            eu = lambda e: ap("eg" + H, S(128 * e, 128 * e + 128))
+            mm([(er(24, 4), [(I32, ap(ed, S(0, 64))), (If(0.5), blk(sf, 2, EDG), er(24)), (I32, blk(st, 2, EDG, 2), er(26, 2)), (If(-0.5), blk(st, 3, EDG), er(25))]
+                 + [(eu(e), SE4, ap(sm, 25, S(e, 16, 2))) for e in range(2)])])
+            aff(ap(st, ALLP, EDG), er(24, 4))
+            tt(ap(ed, S(80, 96)), er(28), blk(st, 1, EDG), AL.mult)
             for j, k in ((0, 15), (1, 0)):
-                tt(ap("sb" + H, j, S(128, HS)), blk(sf, 6, k), blk(st, 1, k), AL.add)
+                tt(ap("sb" + H, S(128 + 8 * j, 136 + 8 * j)), ap(ed, S(81 - j, 96, 2)), blk(st, 3, k), AL.add)
+                if "P" in RD:
+                    tt(ap("sb" + H, S(144 * j, 144 * j + 128)), c("ld", k), c("y16", k), AL.add)
+                else:
+                    aff(ap("sb" + H, S(144 * j, 144 * j + 128)), c("ld", k), eng="G")
             send(h, r + 1)
-        zc = lambda k: ap("cb", 6, S(15 - k, 143 - k))
-        k0, k1 = S(0, 15), S(1, 16)
-        nr = pw // 16
-        for p0 in range(0, 128, pw):
-            for a in range(p0, p0 + pw, 32):
-                pd, pp = ap(bank(h), ALLP, ALLP), S(a, a + 32)
-                mm([(pd, ([] if XW2 else [(I, c("ga", p=pp, shift=1)), (NI, c("ga", p=pp))]) + [(I, c("lg", p=pp, shift=1)), (NI, c("lg", p=pp))])])
-                act(c("tv", p=pp), pd, AF.Abs)
-            ph = ap(bank(h), S(0, nr), ALLP)
-            mm([(ph, [(zc(k), c("tv", k, S(p0, p0 + pw))) for k in range(15)])])
-            hh, hl = ap(lb, S(128 + p0, 128 + p0 + pw)), ap(lb, S(256 + p0, 256 + p0 + pw))
-            ts(hh, ph, MAGIC_H, AL.add, -MAGIC_H, AL.add)
-            tt(hl, ph, hh, AL.subtract)
-        hh, hl = ap(lb, S(128, 256)), ap(lb, S(256, 384))
-        pq = bank(h)
-        mm([(blk(pq, 0), [(hh, TRI)]), (blk(pq, 1), [(hl, TRI)]), (blk(pq, 2), [(hh, G15)]), (blk(pq, 3), [(hl, G15)])])
-        for j in range(4):
-            aff(qr(3 + j), blk(pq, j))
-        for p0 in range(0, 128, pw):
-            hh, hl = ap(lb, S(128 + p0, 128 + p0 + pw)), ap(lb, S(256 + p0, 256 + p0 + pw))
-            sg = lambda k, n=1: c("dg", p=S(p0 + nr * k, p0 + nr * (k + n)))
-            step = 7 if PC == 2 else 4
-            for a in range(0, 14, step):
-                n = min(step, 14 - a)
-                pk = bank(h)
-                mm([(ap(pk, S(nr * j, nr * j + nr), ALLP), [(ap("wk", S(128 * (a + j), 128 * (a + j + 1))), x) for x in (hh, hl)]) for j in range(n)])
-                act(sg(a, n), ap(pk, S(0, nr * n), ALLP), AF.Sign, 1.0, 0.5)
-            pc = ap(bank(h), S(0, nr), ALLP)
-            mm([(pc, [(I, ap("cb", 10, S(p0, p0 + pw)))] + [(zc(k), sg(k - 1)) for k in range(1, 15)])])
-            ts(of(6, p0, p0 + pw), pc, 14.0, AL.add, 64.0, AL.mult)
-        for a in range(0, 16, 4):
-            pt = bank(h)
-            mm([(blk(pt, j), [(ap(q, S(16, 144), min(a + j, 14)), I), (ap(q, S(9, 137), min(a + j, 14) + 1), I)]) for j in range(4)])
-            aff(ap(rw, S(R0 + 128 * a, R0 + 128 * a + 512)), ap(pt, ALLP, ALLP))
-        gathers("ld" + H, ap(rw, S(R0, R0 + 2048)), 6, h)
-        px = bank(h)
-        mm([(ap(px, ALLP, k), [(c("ld", k), ap("xaw", ALLP))]) for k in range(1, 15)])
-        aff(blk(sh, 0, MID), blk(px, 0, MID))
-        if last:
-            aff(blk(st, 2, MID), blk(px, 2, MID))
         else:
-            aff(ap(st, ALLP, MID), ap(px, ALLP, MID))
-        mm([(blk(sm, 0), [(a16, I)]), (blk(sm, 1), [(a16, I), (da, I8)])])
-        if not last:
-            ts(of(0, 0, 256), blk(sm, 0, w=2), 1536.0, AL.add)
+            mm([(er(16), [(I, on16), (Ib(-2.0), ove)]), (er(20), lp + [(Ib(-4.0), on16)])])
+            tt(ap(ed, S(0, 16)), er(16), blk(st, 0, EDG), AL.mult)
+            tt(blk(sg, 0, EDG), er(20), ap(ed, S(112, 128)), AL.mult)
+            mm([(er(24), [(I32, ap(ed, S(0, 16))), (If(0.5), blk(sf, 2, EDG))]),
+                (er(25), [(I32, blk(st, 0, EDG)), (If(0.5), blk(sf, 2, EDG)), (I32, blk(st, 2, EDG))])])
+            tt(blk(st, 0, EDG), er(24), ap(ed, S(96, 112)), AL.mult)
+            aff(blk(st, 2, EDG), er(25))
+        zc = lambda k: ap("zz", 0, S(15 - k, 143 - k))
+        wk = lambda k: ap("wk", S(128 * (k - 1), 128 * k))
+
+        def hops(a):
+            pd, pp = ap(bank(h), ALLP, ALLP), S(a, a + 32)
+            tm = []
+            for x in ("ld" + H, "y16" + H)[:2 if RD[a // 64] == "P" else 1]:
+                tm.append((Ib(-1.0), fl(x, p=pp)))
+                if a == 32:
+                    tm += [(I, ap(x, S(513, 1021)), ap(pd[0], S(0, 127), ALLP)), (I, ap(x, S(1021, 1024)), ap(pd[0], 127, S(0, 3)))]
+                else:
+                    tm.append((I, fl(x, p=pp, shift=1)))
+            mm([(pd, tm)])
+            act(c("t16", p=pp), pd, AF.Abs, 8.0)
+
+        nr = PW // 4
+        qb = lambda n, j, w=1: ap(n, S(nr * j, nr * (j + w)), ALLP)
+        part = lambda n, j, p0: ap(n, S(8 * j + p0 // 16, 8 * j + (p0 + PW) // 16), ALLP)
+        sn = lambda p0, k, n=1: ap("g16" + H, S(16 * p0 + PW * k, 16 * p0 + PW * (k + n)))
+
+        def lengths(p0):
+            ph = part(sm, 0, p0)
+            mm([(ph, [(zc(k), c("t16", k, S(p0, p0 + PW))) for k in range(15)])])
+            aff(part(sh, 4, p0), ph)
+            tt(part(sh, 5, p0), ph, part(sh, 4, p0), AL.subtract)
+
+        def rows(p0):
+            pq, s0 = bank(h), 80 + p0 // 4
+            mm([(qb(pq, j), [(w, part(sh, 4, p0)), (w, part(sh, 5, p0))]) for j, w in enumerate((wk(4), wk(11), I, G15))])
+            aff(ap(sf, S(s0, s0 + nr), ALLP), qb(pq, 0, 4))
+            dmas([(row(4 + j, p0 // PW, 1), ap(sf, S(s0 + j * PW // 16, s0 + (j + 1) * PW // 16), ALLP)) for j in range(4)], 2048 * PW)
+
+        def signs(p0, b, n):
+            pk = bank(h)
+            mm([(qb(pk, j), [(wk(b + j), part(sh, 4, p0)), (wk(b + j), part(sh, 5, p0))]) for j in range(n)])
+            act(sn(p0, b, n), qb(pk, 0, n), AF.Sign, 1.0, 0.5)
+
+        def count(p0):
+            pc = part(sm, 1, p0)
+            mm([(pc, [(I, ap("cb", S(24, 24 + PW // 16), ALLP))] + [(zc(k), sn(p0, k)) for k in range(1, 15)])])
+            ts(of(4, p0, p0 + PW), pc, 14.0, AL.add, PW / 2.0, AL.mult)
+            for b in range(16 * p0, 16 * (p0 + PW), GC):
+                aff(ap("d8" + H, S(b, b + GC)), ind(ap("tb" + H, S(17 * p0, 17 * (p0 + PW))), of(4, b // 16, (b + GC) // 16)))
+
+        if PW == 64:
+            for f, *x in ((hops, 0), (hops, 32), (lengths, 0), (hops, 64), (rows, 0), (hops, 96), (signs, 0, 1, 7), (lengths, 64), (signs, 0, 8, 7),
+                          (rows, 64), (count, 0), (signs, 64, 1, 7), (signs, 64, 8, 7), (count, 64)):
+                f(*x)
         else:
-            aff(blk(sf, 0, w=2), blk(sm, 0, w=2), 1.0, 1536.0)
-            dma(ap("ya", S(128 * h, 128 * h + 128)), blk(sf, 0), 65536)
-            dma(ap("yb", S(128 * h, 128 * h + 128)), blk(sf, 1), 65536)
-        for b in range(2):
+            for f, *x in [(hops, a) for a in range(0, 128, 32)] + [(lengths, 0), (rows, 0)] + [(signs, 0, b, min(4, 15 - b)) for b in range(1, 15, 4)] + [(count, 0)]:
+                f(*x)
+        for b in range(4):
             px = bank(h)
-            mm([(ap(px, ALLP, k), [(c("ld", k), ap(x, S(64 * (k - 1) + 32 * b, 64 * (k - 1) + 32 * b + 32))) for x in ("xh", "xl")]) for k in range(1, 15)])
-            act(ap(sh, S(16 + 32 * b, 48 + 32 * b), MID), ap(px, ALLP, MID), AF.Sign, 1.0, 0.5)
-        mm([(blk(sm, 3, MID), [(I, blk(sh, 2 + m, MID)) for m in range(8)])])
-        aff(blk(sh, 1, MID), blk(sm, 3, MID), 0.5, 4.0)
-        mm([(blk(sm, 2), [(l16, I)])])
+            ks = [k for k in range(4 * b, 4 * b + 4) if 0 < k < 15]
+            k4, kk = S(ks[0] % 4, ks[-1] % 4 + 1), S(ks[0], ks[-1] + 1)
+            mm([(ap(px, S(0, 104), k % 4), [(c("d8", k), ap("xw", S(13 * (k - 1), 13 * k), ALLP))]) for k in ks])
+            act(ap(sg, ALLP, kk), ap(px, S(0, 72), k4), AF.Sign, 1.0, 0.5)
+            if last:
+                aff(ap(st, S(0, 24), kk), ap(px, S(72, 96), k4))
+            else:
+                tt(ap(st, S(0, 16), kk), ap(px, S(72, 88), k4), ap(sg, S(56, 72), kk), AL.mult)
+                tt(ap(st, S(16, 32), kk), ap(px, S(88, 104), k4), ap(st, S(0, 16), kk), AL.subtract)
         if not last:
-            aff(ap(lb, S(0, 128)), blk(sm, 2), -0.125)
+            mm([(blk(sm, 0), [(z, I32), (hz, If(2.0))]), (blk(sm, 1), [(z, I32)])])
+            ts(of(0, 0, 256), blk(sm, 0, w=2), OFF, AL.add)
+            pl = rb(bank(h), 0)
+            mm([(pl, [(blk(sg, m), Ib(1.0 / 16 if m < 7 else -7.0 / 16)) for m in range(8)])])
+            aff(lb, pl)
         else:
-            aff(blk(sf, 2), blk(sm, 2))
-            dma(ap("yl", S(128 * h, 128 * h + 128)), blk(sf, 2), 65536)
+            mm([(blk(sm, 0), [(z, I32), (hz, If(-1.0))]), (blk(sm, 1), [(z, I32), (hz, I32)])])
+            aff(blk(sf, 0, w=2), blk(sm, 0, w=2), 1.0, OFF)
+            dma(ap("ya", S(128 * h, 128 * h + 128)), blk(sf, 0), 65536)
+            dma(ap("yb", S(128 * h, 128 * h + 128)), blk(sf, 1), 65536, "A")
+            pl = rb(bank(h), 0)
+            mm([(pl, [(blk(sg, m), Ib(0.5)) for m in range(8)])])
+            aff(blk(sf, 8), pl, 1.0, 4.0)
+            dma(ap("yl", S(128 * h, 128 * h + 128)), blk(sf, 8), 65536)
 
     for h in range(2):
         first(h)
+    table()
     for r in range(RO):
         for h in range(2):
             step1(h, r)
@@ -573,7 +612,7 @@ def build():
 
 
 def depend(ops):
-    lastw, readers, bankacc = {}, {}, {}
+    lastw, readers, bankacc, some = {}, {}, {}, {}
     for i, o in enumerate(ops):
         d = set()
         for a in o["reads"]:
@@ -589,6 +628,7 @@ def depend(ops):
             n = a[0]
             if n not in lastw:
                 lastw[n] = np.full(_IDX[n].size, -1)
+            rows = a[1][0] != ALLP
             d.update(int(x) for x in np.unique(lastw[n][rg]) if x >= 0)
             m = np.zeros(_IDX[n].size, bool)
             m[rg] = True
@@ -596,13 +636,19 @@ def depend(ops):
             for j, mj in readers.get(n, []):
                 if (mj & m).any():
                     d.add(j)
-                    mj = mj & ~m
+                    if not rows:
+                        mj = mj & ~m
                 if mj.any():
                     keep.append((j, mj))
             readers[n] = keep
+        for a in o["reads"]:
+            d.update(j for j, rg in some.get(a[0], []) if np.intersect1d(rg, region(a)).size)
         for a in o["writes"]:
             if region(a) is not None:
-                lastw[a[0]][region(a)] = i
+                if a[1][0] != ALLP:
+                    some.setdefault(a[0], []).append((i, region(a)))
+                else:
+                    lastw[a[0]][region(a)] = i
         rd = {}
         for a in o["reads"]:
             if region(a) is not None:
@@ -623,6 +669,9 @@ def depend(ops):
         for j in d:
             anc |= 1 << j
         o["anc"] = anc
+
+
+PART = {}
 
 
 def schedule(ops):
@@ -772,15 +821,271 @@ def schedule(ops):
     for i, o in enumerate(ops):
         o["q"], o["t0"], o["t1"] = keep[2][i], r[2][i], r[1][i]
     return keep[1]
-    for o, r in zip(ops, best[1]):
-        o["q"], o["t0"], o["t1"] = r
-    return sorted(range(n), key=lambda i: (ops[i]["t0"], i))
+
+
+def graph(ops):
+    pred = [sorted(set(o["deps"]) | ({o["after"]} if "after" in o else set())) for o in ops]
+    succ = [[] for _ in ops]
+    for i, x in enumerate(pred):
+        for j in x:
+            succ[j].append(i)
+    return pred, succ, [o.get("late", LAT) for o in ops]
+
+
+def rightof(s, v, key=None):
+    a, b = 0, len(s)
+    while a < b:
+        m = (a + b) // 2
+        if (s[m] if key is None else key[s[m]]) > v:
+            b = m
+        else:
+            a = m + 1
+    return a
+
+
+def pack(ops, key, iters, rng):
+    n = len(ops)
+    pred, succ, late = graph(ops)
+    engs = [[(x, o["cost"][x]) for x in o["eng"]] for o in ops]
+
+    def place(key, back=False):
+        before, after = (succ, pred) if back else (pred, succ)
+        left, rdy = [len(x) for x in before], [0.0] * n
+        byrank = [int(j) for j in np.argsort(np.array(key), kind="stable")]
+        rank = [0] * n
+        for k, j in enumerate(byrank):
+            rank[j] = k
+        ready = set(rank[i] for i in range(n) if not left[i])
+        bs, be = {e: [] for e in "DAPGSX"}, {e: [] for e in "DAPGSX"}
+        q, t0, t1 = [None] * n, [0.0] * n, [0.0] * n
+        while ready:
+            k = min(ready)
+            ready.remove(k)
+            i, best = byrank[k], None
+            for x, c in engs[i]:
+                s, e, st = bs[x], be[x], rdy[i] + (late[i] if back else 0.0)
+                k, m = rightof(e, st), len(s)
+                while k < m and s[k] < st + c:
+                    st = e[k]
+                    k += 1
+                f = st + c * (3.0 if x == "D" else 1.0)
+                if best is None or f < best[0]:
+                    best = (f, st, x, k, c)
+            f, st, x, k, c = best
+            bs[x].insert(k, st)
+            be[x].insert(k, st + c)
+            q[i], t0[i] = x, st
+            f = t1[i] = st + c + (0.0 if back else late[i])
+            for j in after[i]:
+                if f > rdy[j]:
+                    rdy[j] = f
+                left[j] -= 1
+                if not left[j]:
+                    ready.add(rank[j])
+        return max(t1), q, t0, t1
+
+    if key is None:
+        key = [0.0] * n
+        for i in range(n - 1, -1, -1):
+            key[i] = min([key[j] for j in succ[i]] + [0.0]) - min(c for x, c in engs[i]) - late[i]
+    now = best = place(key)
+    for it in range(iters):
+        z = rng.normal(0, 120.0, (2, n))
+        b = place([-x + float(y) for x, y in zip(now[3], z[0])], True)
+        c = place([-x + float(y) for x, y in zip(b[3], z[1])])
+        if c[0] < best[0]:
+            best = c
+        now = c if c[0] < best[0] * 1.003 else best
+    return best[:3]
+
+
+def shorten(ops, init, iters, rng, reach=30):
+    n = len(ops)
+    pred, succ, late = graph(ops)
+    q = list(init[1])
+    p = [ops[i]["cost"][q[i]] for i in range(n)]
+    seq = {e: [] for e in "DAPGSX"}
+    for i in sorted(range(n), key=lambda i: (init[2][i], i)):
+        seq[q[i]].append(i)
+    npred = [len(x) for x in pred]
+
+    def times():
+        mp, ms, left = [-1] * n, [-1] * n, list(npred)
+        for e in "DAPGS":
+            s = seq[e]
+            for a, b in zip(s, s[1:]):
+                mp[b], ms[a] = a, b
+                left[b] += 1
+        r, rd = [0.0] * n, [0.0] * n
+        order = [i for i in range(n) if not left[i]]
+        for i in order:
+            f, j = r[i] + p[i], ms[i]
+            if j >= 0:
+                if f > r[j]:
+                    r[j] = f
+                left[j] -= 1
+                if not left[j]:
+                    order.append(j)
+            f += late[i]
+            for j in succ[i]:
+                if f > rd[j]:
+                    rd[j] = f
+                    if f > r[j]:
+                        r[j] = f
+                left[j] -= 1
+                if not left[j]:
+                    order.append(j)
+        if len(order) < n:
+            return None
+        t, td = [0.0] * n, [0.0] * n
+        for i in reversed(order):
+            m = 0.0
+            for j in succ[i]:
+                if t[j] > m:
+                    m = t[j]
+            m += late[i]
+            td[i], j = m, ms[i]
+            if j >= 0 and t[j] > m:
+                m = t[j]
+            t[i] = m + p[i]
+        return max(t), r, rd, t, td, mp, ms
+
+    cur = times()
+    best, tb = (cur[0], list(q), list(cur[1])), {}
+    for it in range(iters):
+        C, r, rd, t, td, mp, ms = cur
+        c0 = [i for i in range(n) if r[i] == 0.0 and t[i] > C - 1e-6]
+        i = c0[int(rng.integers(len(c0)))]
+        blocks = [[i]]
+        while True:
+            nx = [j for j in succ[i] if abs(t[j] + late[i] + p[i] - t[i]) < 1e-6]
+            j = ms[i]
+            if j >= 0 and abs(t[j] + p[i] - t[i]) < 1e-6 and (not nx or rng.random() < 0.5):
+                blocks[-1].append(j)
+                i = j
+            elif nx:
+                i = nx[int(rng.integers(len(nx)))]
+                blocks.append([i])
+            else:
+                break
+        cand = []
+        for b in blocks:
+            L = len(b)
+            for a in range(L):
+                u = b[a]
+                lo, hi = max([r[j] for j in pred[u]] + [-1.0]), min([r[j] for j in succ[u]] + [1e18])
+                for x in ops[u]["eng"]:
+                    if x == q[u]:
+                        continue
+                    s, c, bp = seq[x], ops[u]["cost"][x], None
+                    k = rightof(s, lo, r)
+                    while k <= len(s) and not (k and r[s[k - 1]] >= hi):
+                        v = max(rd[u], r[s[k - 1]] + p[s[k - 1]] if k else 0.0) + c + max(td[u], t[s[k]] if k < len(s) else 0.0)
+                        if bp is None or v < bp[0]:
+                            bp = (v, k)
+                        elif v > bp[0] + 3000:
+                            break
+                        k += 1
+                    if bp:
+                        cand.append((bp[0], 2, u, x, bp[1]))
+                h, hs = (r[mp[u]] + p[mp[u]] if mp[u] >= 0 else 0.0), []
+                for k in range(a + 1, min(L, a + reach + 1)):
+                    v = b[k]
+                    if r[v] >= hi:
+                        break
+                    h = max(h, rd[v])
+                    hs.append(h)
+                    h += p[v]
+                    if k == L - 1 or a == 0:
+                        tl = p[u] + max(td[u], t[ms[v]] if ms[v] >= 0 else 0.0)
+                        est = max(h, rd[u]) + tl
+                        for m in range(k, a, -1):
+                            tl = p[b[m]] + max(td[b[m]], tl)
+                            est = max(est, hs[m - a - 1] + tl)
+                        cand.append((est, 0, u, v, 0))
+                tl, ts_ = (t[ms[u]] if ms[u] >= 0 else 0.0), []
+                for k in range(a - 1, max(-1, a - reach - 1), -1):
+                    v = b[k]
+                    if r[v] <= lo:
+                        break
+                    tl = p[v] + max(td[v], tl)
+                    ts_.append(tl)
+                    if (k == 0 or a == L - 1) and (k < a - 1 or (k > 0 and a < L - 1)):
+                        h = max(rd[u], r[mp[v]] + p[mp[v]] if mp[v] >= 0 else 0.0)
+                        est = h + p[u] + max(td[u], tl)
+                        h += p[u]
+                        for m in range(k, a):
+                            h = max(h, rd[b[m]])
+                            est = max(est, h + ts_[a - 1 - m])
+                            h += p[b[m]]
+                        cand.append((est, 1, u, v, 0))
+        done = False
+        for m in np.argsort(np.array([c[0] for c in cand]) + rng.random(len(cand)) * 300.0):
+            est, kind, u, v, k = cand[m]
+            if tb.get((u, v) if kind != 1 else (v, u), -1) >= it and est >= best[0]:
+                continue
+            s, old = seq[q[u]], q[u]
+            a = s.index(u)
+            s.pop(a)
+            if kind == 2:
+                seq[v].insert(k, u)
+                q[u], p[u], back = v, ops[u]["cost"][v], [(u, old)]
+            else:
+                b = s.index(v)
+                s.insert(b + (1 - kind), u)
+                back = [(w, u) for w in s[a:b + 1]] if kind == 0 else [(u, w) for w in s[b + 1:a + 1]]
+            nw = times()
+            if nw is None:
+                seq[q[u]].remove(u)
+                q[u], p[u] = old, ops[u]["cost"][old]
+                s.insert(a, u)
+                continue
+            ten = it + 50 + int(rng.integers(50))
+            for kk in back:
+                tb[kk] = ten
+            cur, done = nw, True
+            break
+        if not done:
+            tb = {}
+        if cur[0] < best[0] - 1e-6:
+            best = (cur[0], list(q), list(cur[1]))
+    return best
+
+
+STARTS = [(a, b) for a in (10000.0, 14000.0, 18000.0, 22000.0) for b in (1.15, 1.3, 1.45)]
+EFFORT = [800, 10, 3, 2500, 1, 8000, 0]
+
+
+def schedule2(ops):
+    rng = np.random.default_rng(EFFORT[6])
+    idx = [i for i, o in enumerate(ops) if o["half"] != 1]
+    at = {j: k for k, j in enumerate(idx)}
+    one = [dict(ops[i]) for i in idx]
+    for o in one:
+        if "after" in o:
+            o["after"] = at[o["after"]]
+    depend(one)
+    t = shorten(one, pack(one, None, EFFORT[1], rng), EFFORT[0], rng)[2]
+    pair = list(zip([i for i, o in enumerate(ops) if o["half"] == 0], [i for i, o in enumerate(ops) if o["half"] == 1]))
+    res = [pack(ops, None, EFFORT[1], rng)]
+    for lag, pace in STARTS:
+        key = [t[at[i]] * pace if i in at else 0.0 for i in range(len(ops))]
+        for a, b in pair:
+            key[b] = key[a] + (lag if t[at[a]] > 9000 else 500.0)
+        res.append(pack(ops, key, EFFORT[1], rng))
+    for keep, iters in (EFFORT[2:4], EFFORT[4:6]):
+        res = [shorten(ops, x, iters, rng) for x in sorted(res, key=lambda x: x[0])[:keep]]
+    best = min(res, key=lambda x: x[0])
+    for i, o in enumerate(ops):
+        o["q"], o["t0"] = best[1][i], best[2][i]
+        o["t1"] = o["t0"] + o["cost"][o["q"]] + o.get("late", LAT)
+    return sorted(range(len(ops)), key=lambda i: (best[2][i], i))
 
 
 def plan():
     ops = build()
     depend(ops)
-    order = schedule(ops)
+    order = schedule2(ops)
     cnt, known, prog = {}, {e: {} for e in "DAPGSX"}, []
     for i in order:
         o = ops[i]
@@ -798,7 +1103,7 @@ def plan():
                     kn[s2] = max(kn.get(s2, 0), c2)
         fs = o["emit"](q) if o["emit"] else [None]
         s = o.get("sem", "c" + q)
-        cnt[s] = cnt.get(s, 0) + o.get("inc", len(fs))
+        cnt[s] = cnt.get(s, 0) + o.get("inc", 1) * len(fs)
         o["mark"] = (s, cnt[s])
         o["clock"] = dict(kn) if q != "X" else {}
         o["clock"][s] = cnt[s]
@@ -825,15 +1130,14 @@ def rank_program(g, core, T, topo):
         for w, c in waits.items():
             Q[q].wait_ge(T.sem[w], c)
         if "send" in o:
-            h, r, hl, hr = o["send"]
             trs = []
-            for j, (dst, at) in enumerate(((nxt, hl), (prv, hr))):
+            for j, dst in enumerate((nxt, prv)):
                 rid, pid, _ = topo.addr(dst)
                 eng = topo.engines(core, dst)
                 k = len(eng) // 2
                 mask = sum(1 << e for e in eng[j * k:j * k + 4])
-                trs.append(RemoteDMATransfer(dst_ids=[DstId(rid=rid, pnc=pid)], dma_engine_mask=mask, remote_sem=T.sem["ar%d" % (2 * r + h)],
-                                             src=T["sb%d" % h][:, j, :], dst=T["rw%d" % h][:, at:at + HS]))
+                trs.append(RemoteDMATransfer(dst_ids=[DstId(rid=rid, pnc=pid)], dma_engine_mask=mask, remote_sem=T.sem[o["arr"]],
+                                             src=real(T, o["send"][j][0]), dst=real(T, o["send"][j][1])))
             g.remote_dma_fused(trs, local_sem=T.sem[s])
             continue
         for f in fs:

@@ -1,63 +1,49 @@
 import numpy as np
 from concourse.bass import DstId, RemoteDMATransfer
-from concourse.mybir import AluOpType, AxisListType, ActivationFunctionType
+from concourse.mybir import AluOpType, ActivationFunctionType
 
 AL = AluOpType
 AF = ActivationFunctionType
 W, RO = 3072, 3
 HS = 272
 GC = 1024
-NPR = 6
-OFF = 1536.0
-CY, PCY, GCY, LAT = 0.9, 0.4, 1.56, 120.0
-BIAS = [6000.0, 0.0]
-SPEEDS = [((1.3, 1.3), 1.0, 60, 120.0, 1.0, 0.9), ((0.75, 1.28), 1.15, 80, 250.0, 1.6, 1.0)]
-POLISH = [16000, 80.0]
-PEN = [3.0]
-SEARCH = [3, 200, 120.0, 1.003, 3]
 PW = 64
-RD = "GG"
-TF = False
-DENG = "G"
-WENG = "G"
+NPR = 7
+OFF = 1536.0
+TB = [1088, 0, 5248, 6336]
+WIN = [(1088, 5248), (0, 5248), (2176, 6336), (2176, 7424)]
+CY, PCY, GCY, LAT = 0.9, 0.42, 1.56, 140.0
+STARTS = [(a, b) for a in (10000.0, 14000.0, 18000.0, 22000.0) for b in (1.15, 1.3, 1.45)]
+PACES = [(1.0, 1.0, 1.0, 1.0), (1.0, 1.0, 1.1, 1.2), (1.2, 1.15, 1.0, 1.0), (1.0, 0.8, 1.05, 0.8)]
+EFFORT = [400, 8, 3, 700, 60, 300, 0]
 
 SCRATCH = {
     "vt": ("sbuf", [128, W], "float32"), "xt": ("sbuf", [128, W], "bfloat16"), "gt": ("sbuf", [128, W], "bfloat16"),
-    "nt": ("sbuf", [128, W], "int32"), "et": ("sbuf", [128, W], "int32"),
+    "nt": ("sbuf", [128, W], "int32"), "tb": ("sbuf", [128, W + 4 * 1088], "int32"),
     "bk": ("sbuf", [128, 2048], "bfloat16"), "wk": ("sbuf", [128, 1792], "bfloat16"),
     "xw": ("sbuf", [128, 182, 8], "float32"), "ct": ("sbuf", [128, 14, 13], "float32"), "c2": ("sbuf", [128, 14, 9], "float32"),
-    "cb": ("sbuf", [128, 160, 16], "bfloat16"), "zz": ("sbuf", [128, 4, 144], "bfloat16"), "c32": ("sbuf", [128, 8, 128], "float32"),
+    "cb": ("sbuf", [128, 144, 16], "bfloat16"), "zz": ("sbuf", [128, 144], "bfloat16"), "c32": ("sbuf", [128, 6, 128], "float32"),
     "col": ("sbuf", [128, 80], "float32"), "coli": ("sbuf", [128, 8], "int32"),
 }
 for _i in range(NPR):
     SCRATCH["pr%d" % _i] = ("sbuf", [128, 128, 4], "float32")
 for _h in range(2):
-    SCRATCH["va%d" % _h] = ("sbuf", [128, 2048], "float32")
-    SCRATCH["d8%d" % _h] = ("sbuf", [128, 2048], "float32")
-    SCRATCH["tb%d" % _h] = ("sbuf", [128, 2176], "float32")
-    SCRATCH["di%d" % _h] = ("sbuf", [128, 2048], "int32")
-    SCRATCH["rw%d" % _h] = ("sbuf", [128, 2048 + RO * HS], "float32")
-    for _n in ("g16", "t16", "ld", "y16"):
-        SCRATCH["%s%d" % (_n, _h)] = ("sbuf", [128, 2064 if _n in ("y16", "ld") else 2048], "float16")
-    SCRATCH["eg%d" % _h] = ("sbuf", [128, 256], "float32")
-    SCRATCH["of%d" % _h] = ("sbuf", [128, 656], "uint16")
-    SCRATCH["st%d" % _h] = ("sbuf", [128, 32, 16], "float32")
-    SCRATCH["sf%d" % _h] = ("sbuf", [128, 112, 16], "float32")
-    SCRATCH["sh%d" % _h] = ("sbuf", [128, 48, 16], "bfloat16")
-    SCRATCH["uf%d" % _h] = ("sbuf", [128, 8, 16], "float16")
-    SCRATCH["sg%d" % _h] = ("sbuf", [128, 72, 16], "bfloat16")
-    SCRATCH["ed%d" % _h] = ("sbuf", [128, 144], "float32")
-    SCRATCH["eb%d" % _h] = ("sbuf", [128, 16], "bfloat16")
-    SCRATCH["sb%d" % _h] = ("sbuf", [128, HS], "float32")
+    for _n, _s, _t in (("va", [2048], "float32"), ("d8", [2048], "float32"), ("di", [2048], "int32"), ("rw", [2048 + RO * HS], "float32"),
+                       ("g16", [2048], "float16"), ("t16", [2048], "float16"), ("ld", [2048], "float16"), ("y16", [2048], "float16"),
+                       ("si", [768], "int32"), ("of", [640], "uint16"), ("st", [32, 16], "float32"), ("sf", [72, 16], "float32"),
+                       ("sh", [48, 16], "bfloat16"), ("yh", [128], "float16"), ("uf", [8, 16], "float16"), ("sg", [72, 16], "bfloat16"),
+                       ("ed", [128], "float32"), ("eb", [16], "bfloat16"), ("sb", [HS], "float32")):
+        SCRATCH["%s%d" % (_n, _h)] = ("sbuf", [128] + _s, _t)
     for _i in range(3):
         SCRATCH["ps%d" % (4 * _h + _i)] = ("psum", [128, 128, 4], "float32")
     SCRATCH["ps%d" % (4 * _h + 3)] = ("psum", [128, 32, 16], "float32")
-NDMA = 110
+NDMA = 56
 SEMAPHORES = ["cD", "cA", "cP", "cG"] + ["dm%d" % i for i in range(NDMA)] \
     + ["ar%d" % i for i in range(2 * RO)] + ["lo%d" % i for i in range(2 * RO)]
 
 S = slice
 ALLP = S(None)
+_IDX, PLACE = {}, {}
 
 
 def ap(name, *idx, p=ALLP):
@@ -75,15 +61,16 @@ def ind(win, off):
     return ("IND", win, off)
 
 
-_IDX = {}
+def spec(name):
+    return SCRATCH.get(PLACE.get(name, name))
 
 
 def region(a):
     name, idx = a
-    if name not in SCRATCH:
+    if spec(name) is None:
         return None
     if name not in _IDX:
-        fs = SCRATCH[name][1][1:]
+        fs = spec(name)[1][1:]
         _IDX[name] = np.arange(int(np.prod(fs))).reshape(fs)
     return _IDX[name][idx[1:]].ravel()
 
@@ -93,11 +80,11 @@ def nel(a):
 
 
 def two(a):
-    return a[0] != "IND" and SCRATCH[a[0]][2] in ("bfloat16", "float16", "uint16")
+    return a[0] != "IND" and spec(a[0])[2] in ("bfloat16", "float16", "uint16")
 
 
 def psum(a):
-    return a[0] != "IND" and SCRATCH[a[0]][0] == "psum"
+    return a[0] != "IND" and spec(a[0])[0] == "psum"
 
 
 def real(T, a):
@@ -105,7 +92,7 @@ def real(T, a):
         return a
     if a[0] == "IND":
         return real(T, a[1]).indirect(real(T, a[2]))
-    return T[a[0]][a[1]]
+    return T[PLACE.get(a[0], a[0])][a[1]]
 
 
 def parts(a):
@@ -115,7 +102,7 @@ def parts(a):
 
 
 def build():
-    ops, cur = [], [None]
+    ops, cur, nd = [], [None], [0]
 
     def add(eng, cost, reads, writes, emit, **kw):
         o = dict(eng=eng, cost=cost, reads=[x for r in reads for x in parts(r)], writes=writes, emit=emit, half=cur[0])
@@ -139,9 +126,6 @@ def build():
         k = 0.5 if two(a) and two(out) else 1
         add("D", {"D": vcost(nel(a), k)}, [a, s1, s2], [out], lambda e: [tsf(out, a, s1, op0, s2, op1)])
 
-    def cp(out, a):
-        add("D", {"D": vcost(nel(a), 0.5 if two(a) and two(out) else 1)}, [a], [out], lambda e: [lambda g, T: g.vector.tensor_copy(real(T, out), real(T, a))])
-
     def mset(out, v):
         add("D", {"D": vcost(nel(out), 0.5 if two(out) else 1)}, [], [out], lambda e: [lambda g, T: g.vector.memset(real(T, out), v)])
 
@@ -162,21 +146,16 @@ def build():
     def aff(out, a, scale=1.0, bias=0.0, eng="DA"):
         act(out, a, AF.Identity, scale, bias, () if scale == 1.0 and bias == 0.0 else (scale, AL.mult, bias, AL.add), eng)
 
-    def relu(out, a, scale=1.0):
-        act(out, a, AF.Relu, scale, 0.0, (scale, AL.mult, 0.0, AL.max))
-
-    def mm(lst, start=True, stop=True):
+    def mm(lst):
         fs, cost, rd, wr = [], 30, [], []
         for out, terms in lst:
             wr.append(out)
-            if not start:
-                rd.append(out)
             for i, tm in enumerate(terms):
                 l, r = tm[0], tm[1]
                 o = tm[2] if len(tm) > 2 else out
                 cost += max(64, nel(r)) * (1 if two(l) else 4) * PCY
                 rd += [l, r]
-                fs.append(lambda g, T, o=o, l=l, r=r, a=(start and i == 0), b=(stop and i == len(terms) - 1): g.tensor.matmul(real(T, o), real(T, l), real(T, r), a, b))
+                fs.append(lambda g, T, o=o, l=l, r=r, a=(i == 0), b=(i == len(terms) - 1): g.tensor.matmul(real(T, o), real(T, l), real(T, r), a, b))
         add("P", {"P": cost}, rd, wr, lambda e: fs)
 
     def iota(out, pat, base, cm):
@@ -188,8 +167,6 @@ def build():
 
     def sel(out, a, pat, cmp, fill, base, cm):
         add("G", {"G": 170 + 2 * nel(a) * CY}, [a], [out], lambda e: [lambda g, T: g.affine_select(real(T, out), real(T, a), pat, cmp, fill, base, cm)])
-
-    nd = [0]
 
     def dma(out, a, nbytes, q="S"):
         sem = "dm%d" % nd[0]
@@ -206,7 +183,7 @@ def build():
     def dmas(lst, nbytes):
         nd[0] += 1
         fs = [lambda g, T, o=o, a=a: g.sync.dma_start(real(T, o), real(T, a)) for o, a in lst]
-        add("S", {"S": 80.0 * len(lst)}, [a for o, a in lst], [o for o, a in lst], lambda e: fs, sem="dm%d" % (nd[0] - 1), inc=16, late=2000 + nbytes / 250.0)
+        add("S", {"S": 80.0 * len(lst)}, [a for o, a in lst], [o for o, a in lst], lambda e: fs, sem="dm%d" % (nd[0] - 1), inc=16, late=2200 + nbytes / 250.0)
 
     EQ, GE = AL.is_equal, AL.is_ge
     MID, EDG = S(1, 15), S(0, 16, 15)
@@ -219,27 +196,26 @@ def build():
     for a in range(0, W, 1024):
         dma(ap("xt", S(a, a + 1024)), ap("xrec", S(a, a + 1024)), 400000 + 512 * (a + 1024), "A")
         dma(ap("gt", S(a, a + 1024)), ap("grec", S(a, a + 1024)), 400000 + 512 * (a + 1024))
-    mset(ap("et", S(0, 2048)), 0)
-    iota(ap("et", S(2048, W)), [[0, W - 2048]], 0, 0)
-    dma(ap("et", ALLP, p=S(0, 128, 16)), ap("erec", ALLP), 98304 * 4)
+    mset(ap("tb", S(2176, 4224)), 0)
+    iota(ap("tb", S(4224, 5248)), [[0, 1024]], 0, 0)
+    dma(ap("tb", S(2176, 5248), p=S(0, 128, 16)), ap("erec", ALLP), 98304 * 4)
     dma(ap("nt", ALLP), ap("nbr", ALLP), 1572864 * 2)
-    ops[-1]["reads"] += [ap("gt", S(1024, 1032)), ap("et", S(0, 8))]
+    ops[-1]["reads"] += [ap("gt", S(1024, 1032)), ap("tb", S(2176, 2184))]
     cb = lambda j, k=ALLP: blk("cb", j, k)
-    I, ONE, BC, P64, G15 = [cb(j) for j in range(5)]
-    sc = {}
+    I, ONE, BC, P32, G15, IE, IM = [cb(j) for j in (0, 1, 2, 3, 4, 16, 17)]
     I32, ONE32 = ap("c32", 0, ALLP), ap("c32", 1, ALLP)
     mset(ONE, 1.0)
     mset(ONE32, 1.0)
     sel(I, ONE, [[-1, 128]], EQ, 0.0, 0, 1)
     sel(I32, ONE32, [[-1, 128]], EQ, 0.0, 0, 1)
-    for j, v in enumerate((1.0 / 2048, -1.0, -2.0, 2.0, -0.25, 1.0 / 16, -7.0 / 16, 8.0, 4.0, 0.5, -4.0)):
+    sc, sf32 = {}, {}
+    for j, v in enumerate((1.0 / 2048, -1.0, -2.0, 2.0, 1.0 / 16, -7.0 / 16, 8.0, 0.5, -4.0)):
         sc[v] = 5 + j
         aff(cb(5 + j), I, v)
-    Ib = lambda v, k=ALLP: cb(sc[v], k)
-    sf32 = {}
     for j, v in enumerate((-1.0, 2.0, -0.5, 0.5)):
         sf32[v] = ap("c32", 2 + j, ALLP)
         aff(sf32[v], I32, v)
+    Ib = lambda v, k=ALLP: cb(sc[v], k)
     If = lambda v: sf32[v]
     cl = lambda a, n=1: ap("col", S(a, a + n))
     GS, SE4, EQ8 = cl(32, 8), cl(40, 8), cl(56, 8)
@@ -248,31 +224,33 @@ def build():
     sel(GS, GS, [[16, 8]], GE, 0.0, 15, -1)
     mset(ap("bk", ALLP), -1.0)
     sel(ap("bk", ALLP), ap("bk", ALLP), [[-1, 16], [-16, 8], [0, 16]], EQ, 0.0, 0, 1)
-    iota(P64, [[1, 128]], 0, 0)
+    iota(P32, [[1, 128]], 0, 0)
     iota(ap("coli", S(0, 1)), [[0, 1]], 0, 1)
     iota(cl(0, 3), [[-HS, 3]], 1 - 2048, 15)
     iota(cl(3, 3), [[HS, 3]], 2048 + 144 - 14, -15)
     iota(cl(6, 3), [[HS, 3]], 1025, 0)
     aff(cl(0, 6), cl(0, 6), 0.5)
     ts(ap("coli", S(4, 5)), ap("coli", S(0, 1)), 15, AL.bitwise_and)
-    cp(cl(12), ap("coli", S(4, 5)))
+    aff(cl(12), ap("coli", S(4, 5)), eng="D")
     ts(cl(13), cl(12), 0.0, EQ)
     ts(cl(14), cl(12), 15.0, EQ, 1024.0, AL.mult)
     ts(cl(14), cl(14), cl(12), AL.add, -1.0, AL.add)
     ts(cl(16, 3), cl(6, 3), cl(13), AL.mult, cl(14), AL.add)
     aff(cl(15), cl(13), -15.0, 16.0)
-    aff(BC, P64, cl(15))
-    aff(P64, P64, 2.0 / PW)
+    aff(BC, P32, cl(15))
+    aff(P32, P32, 1.0 / 32)
 
     rot, prn = [0, 0], [0]
 
     def bank(h):
-        rot[h] = (rot[h] + 1) % 3
-        return "ps%d" % (4 * h + rot[h])
+        rot[h] += 1
+        PLACE["vb%d" % (2 * rot[h] + h)] = "ps%d" % (4 * h + rot[h] % 3)
+        return "vb%d" % (2 * rot[h] + h)
 
     def newpr():
-        prn[0] = (prn[0] + 1) % NPR
-        return "pr%d" % prn[0]
+        prn[0] += 1
+        PLACE["vp%d" % prn[0]] = "pr%d" % (prn[0] % NPR)
+        return "vp%d" % prn[0]
 
     def table():
         cur[0] = None
@@ -283,13 +261,19 @@ def build():
 
     def late_consts():
         cur[0] = None
-        zc = lambda j: ap("zz", j, ALLP)
-        mset(zc(3), 1.0)
-        sel(zc(0), zc(3), [[0, 9], [1, 16]], EQ, 0.0, -15, 0)
-        sel(zc(1), zc(0), [[-16, 9], [0, 16]], EQ, 0.0, 0, 1)
-        sel(zc(2), zc(0), [[-16, 9], [0, 16]], EQ, 0.0, -15, 1)
-        sel(zc(0), zc(0), [[-16, 9], [0, 16]], GE, 0.0, 0, 1)
-        sel(zc(0), zc(0), [[16, 9], [0, 16]], GE, 0.0, 15, -1)
+        zz = ap("zz", ALLP)
+        iota(zz, [[0, 144]], 1, 0)
+        sel(zz, zz, [[0, 9], [1, 16]], EQ, 0.0, -15, 0)
+        ts(cl(24), cl(12), 15.0, EQ, cl(13), AL.add)
+        aff(cl(25), cl(24), 1.0 / 32)
+        aff(cl(26), cl(24), -1.0, 1.0)
+        aff(IE, I, cl(25))
+        aff(IM, I, cl(26))
+        for u in range(4):
+            a, b = 448.0 + TB[u] - WIN[u][0], OFF + 2176 - WIN[u][0]
+            aff(cl(20 + u), cl(24), b - a, a)
+        sel(zz, zz, [[-16, 9], [0, 16]], GE, 0.0, 0, 1)
+        sel(zz, zz, [[16, 9], [0, 16]], GE, 0.0, 15, -1)
         sel(G15, ONE, [[-16, 8], [0, 16]], GE, 0.0, 0, 1)
         sel(G15, G15, [[16, 8], [0, 16]], GE, 0.0, 14, -1)
         wk = ap("wk", ALLP)
@@ -299,7 +283,7 @@ def build():
             sel(b, b, [[-16, 8], [-1, 16]], GE, float(k - 15), 0, 1)
         sel(wk, wk, [[0, 14], [-16, 8], [0, 16]], GE, 0.0, 0, 1)
         sel(wk, wk, [[0, 14], [16, 8], [0, 16]], GE, 0.0, 14, -1)
-        mset(ap("wk", S(15, 1792, 16)), 0.0)
+        iota(ap("wk", S(15, 1792, 16)), [[0, 112]], 0, 0)
         iota(EQ8, [[1, 8]], 0, 0)
         ts(EQ8, EQ8, cl(12), EQ)
         iota(ap("ct", ALLP, S(0, 8)), [[0, 14], [2, 8]], 1, 0)
@@ -320,10 +304,8 @@ def build():
         for j in range(8):
             aff(ap("xw", ALLP, j), ap("ct", ALLP, ALLP), cl(32 + j))
         for h in range(2):
-            mset(ap("sg%d" % h, ALLP, EDG), 0.0)
-            mset(ap("ld%d" % h, S(2048, 2064)), 0.0)
-            mset(ap("y16%d" % h, S(2048, 2064)), 0.0)
-            dma(ap("tb%d" % h, ALLP), ap("vt", S(0, 2176)), 1114112)
+            iota(ap("sg%d" % h, ALLP, EDG), [[0, 144]], 0, 0)
+            dma(ap("tb", S(5248 * h, 5248 * h + 2176)), ap("nt", S(0, 2176)), 1114112)
 
     def names(h):
         H = str(h)
@@ -331,17 +313,17 @@ def build():
         of = lambda j, a=0, b=128: ap("of" + H, S(128 * j + a, 128 * j + b))
         return H, c, of, "ps%d" % (4 * h + 3)
 
-    def gathers(dst, win, oj, h, scale=1.0, bias=0.0, eng="DA"):
+    def gathers(dst, win, oj, h, scale=1.0, bias=0.0):
         H, c, of, sm = names(h)
         for a in range(0, 2048, GC):
-            aff(ap(dst, S(a, a + GC)), ind(win, of(oj, a // 16, (a + GC) // 16)), scale, bias, eng)
+            aff(ap(dst, S(a, a + GC)), ind(win, of(oj, a // 16, (a + GC) // 16)), scale, bias)
 
-    def gather_tt(dst, win, oj, other, op, h):
+    def gather_add(dst, win, oj, other, h):
         H, c, of, sm = names(h)
         for a in range(0, 2048, GC):
-            tt(ap(dst, S(a, a + GC)), ind(win, of(oj, a // 16, (a + GC) // 16)), ap(other, S(a, a + GC)), op)
+            tt(ap(dst, S(a, a + GC)), ind(win, of(oj, a // 16, (a + GC) // 16)), ap(other, S(a, a + GC)), AL.add)
 
-    XT, VT, NT, ET = ap("xt", ALLP), ap("vt", ALLP), ap("nt", ALLP), ap("et", ALLP)
+    VT, NT, ET = ap("vt", ALLP), ap("nt", ALLP), ap("tb", S(2176, 5248))
 
     def first(h):
         cur[0] = h
@@ -353,7 +335,7 @@ def build():
         tt(fd, f, da, AL.mult)
         tt(z, pin(0, h), fd, AL.add)
         tt(y, pin(1, h), fd, AL.subtract)
-        cp(of(0, 0, 256), blk(sf, 3, w=2))
+        aff(of(0, 0, 256), blk(sf, 3, w=2))
         ts(pin(2, h), pin(2, h), 7, AL.bitwise_and)
         aff(blk(sh, 0), pin(2, h), 0.125)
         gathers("d8" + H, ET, 1, h)
@@ -383,57 +365,55 @@ def build():
     def step1(h, r):
         cur[0] = h
         H, c, of, sm = names(h)
-        st, sf, sh, rw, ed = "st" + H, "sf" + H, "sh" + H, "rw" + H, "ed" + H
-        hz, hE, z, Ez = [blk(st, j) for j in range(4)]
+        st, sf, sh, rw = "st" + H, "sf" + H, "sh" + H, "rw" + H
+        hz, hE, y, Ey = [blk(st, j) for j in range(4)]
         lb = blk(sh, 0)
         gathers("va" + H, VT, 0, h, -1.0)
-        gather_tt("d8" + H, VT, 1, "va" + H, AL.add, h)
+        gather_add("d8" + H, VT, 1, "va" + H, h)
+        aff(ap("yh" + H, ALLP), y, eng="DAG")
         pq = rb(bank(h), 0)
         mm([(pq, [(lb, Ib(-2.0)), (Ib(2.0), ONE)])])
         tt(pq, pq, hE, AL.mult)
-        tt(blk(sf, 0), pq, Ez, AL.add)
+        tt(blk(sf, 0), pq, Ey, AL.add)
+        aff(ap("sb" + H, S(128, 136)), blk(sf, 0, 15), eng="DAG")
+        aff(ap("sb" + H, S(136, 144)), blk(sf, 0, 0), eng="DAG")
         for p0 in (0, 64):
             cols = S(16 * p0, 16 * p0 + 1024)
-            aff(ap("di" + H, cols), ap("d8" + H, cols), eng=DENG)
+            aff(ap("di" + H, cols), ap("d8" + H, cols), eng="G")
             for a in range(2):
                 pw, ks = spread(h, (sh, 0), p0, a)
                 tt(pw, c("d8", **ks), pw, AL.mult)
                 tt(pw, c("va", **ks), pw, AL.add)
                 aff(c("y16", **ks), pw)
                 tt(c("g16", **ks), pw, c("y16", **ks), AL.subtract)
-            aff(ap(rw, cols), ap("y16" + H, cols), eng=WENG)
+            aff(ap(rw, cols), ap("y16" + H, cols), eng="G")
         if r == 0:
-            aff(ap("sb" + H, S(128, 136)), blk(sf, 0, 15))
-            aff(ap("sb" + H, S(136, 144)), blk(sf, 0, 0))
             aff(ap("sb" + H, S(0, 128)), c("y16", 15))
             aff(ap("sb" + H, S(144, HS)), c("y16", 0))
-            send(h, 0)
+        send(h, r)
         gathers("ld" + H, NT, 0, h, 1.0, -OFF)
         sl = 2048 + HS * r
         mo = lambda k=ALLP: ap("uf" + H, ALLP, k)
         tt(mo(MID), blk(sf, 0, S(2, 16)), blk(sf, 0, S(0, 14)), GE)
-        tt(blk(sf, 1, 0), blk(sf, 0, 1), ap(rw, S(sl + 128, sl + 136)), GE)
-        tt(blk(sf, 1, 15), ap(rw, S(sl + 136, sl + 144)), blk(sf, 0, 14), GE)
-        aff(mo(0), blk(sf, 1, 0), cl(r), 512.0)
-        aff(mo(15), blk(sf, 1, 15), cl(3 + r), -512.0)
+        tt(mo(0), blk(sf, 0, 1), ap(rw, S(sl + 128, sl + 136)), GE)
+        tt(mo(15), ap(rw, S(sl + 136, sl + 144)), blk(sf, 0, 14), GE)
+        aff(mo(0), mo(0), cl(r), 512.0)
+        aff(mo(15), mo(15), cl(3 + r), -512.0)
         po = bank(h)
         mm([(rb(po, 0), [(mo(), Ib(2.0)), (I, BC)])])
-        ts(of(2), rb(po, 0), cl(16 + r), AL.add)
+        aff(of(2), rb(po, 0), 1.0, cl(16 + r))
         red = lambda j, pr, a: mm([(blk(sm, j, a + 4 * k), [(ap(pr, ALLP, k), GS)]) for k in range(4)])
         for a in range(4):
             pg, ks, pr = ap(bank(h), ALLP, ALLP), (a, 4), newpr()
             mm([(pg, [(I, c("g16", ks))])])
             tt(ap(pr, ALLP, ALLP), c("di", ks), pg, AL.mult)
             red(0, pr, a)
-        if TF:
-            gather_tt("t16" + H, ap(rw, S(0, sl + HS)), 2, "y16" + H, AL.subtract, h)
-        else:
-            gathers("t16" + H, ap(rw, S(0, sl + HS)), 2, h)
+        gathers("t16" + H, ap(rw, S(0, sl + HS)), 2, h)
         for a in range(4):
             pt, ks = ap(bank(h), ALLP, ALLP), (a, 4)
             ptd, pgt, ptt = newpr(), newpr(), newpr()
-            mm([(pt, [(I, c("t16", ks))] + ([] if TF else [(Ib(-1.0), c("y16", ks))]))])
-            act(ap(ptt, ALLP, ALLP), c("t16", ks) if TF else pt, AF.Square)
+            mm([(pt, [(I, c("t16", ks)), (Ib(-1.0), c("y16", ks))])])
+            act(ap(ptt, ALLP, ALLP), pt, AF.Square)
             tt(ap(ptd, ALLP, ALLP), c("di", ks), pt, AL.mult)
             tt(ap(pgt, ALLP, ALLP), c("g16", ks), pt, AL.mult)
             for j, pr in ((2, ptt), (3, ptd), (1, pgt)):
@@ -442,76 +422,62 @@ def build():
     def step23(h, r):
         cur[0] = h
         H, c, of, sm = names(h)
-        st, sf, sh, rw, ed, sg, va = "st" + H, "sf" + H, "sh" + H, "rw" + H, "ed" + H, "sg" + H, "va" + H
+        st, sf, sh, ed, sg, si = "st" + H, "sf" + H, "sh" + H, "ed" + H, "sg" + H, "si" + H
         last = r == RO - 1
         nq = 1 if last else 2
-        hz, hE, z, Ez = [blk(st, j) for j in range(4)]
-        lb, dl, ov, lam, hh, hl = [blk(sh, j) for j in range(6)]
+        hz, hE, y, Ey = [blk(st, j) for j in range(4)]
+        lb, dl, ov, lam = [blk(sh, j) for j in range(4)]
+        yh, prod = ap("yh" + H, ALLP), blk(sf, 2)
         aff(blk(sf, 2, w=2), blk(sm, 2, w=2))
         pn = bank(h)
-        mm([(rb(pn, 0), [(If(-1.0), z)] + [(c("ld", k), ap("cb", S(0, 8), k), ap(pn, S(k // 4, 32, 4), k % 4)) for k in range(16)])])
+        mm([(rb(pn, 0), [(Ib(-1.0), yh)] + [(c("ld", k), ap("cb", S(0, 8), k), ap(pn, S(k // 4, 32, 4), k % 4)) for k in range(16)])])
         tt(blk(sf, 4), blk(sm, 0), blk(sf, 2), AL.mult)
         tt(blk(sm, 1), blk(sm, 1), blk(sf, 3), AL.mult)
         tt(blk(sm, 1), blk(sm, 1), blk(sf, 4), AL.subtract)
         act(dl, blk(sm, 1), AF.Sign, -1.0)
         mm([(blk(sm, j), [(I, dl), (lb, Ib(8.0))]) for j in range(nq)])
-        relu(ov, blk(sm, 0), -1.0)
-        prod = blk(sf, 2)
+        act(ov, blk(sm, 0), AF.Relu, -1.0, 0.0, (-1.0, AL.mult, 0.0, AL.max))
         tt(prod, rb(pn, 0), ov, AL.mult)
         pu = bank(h)
-        mm([(rb(pu, 0), [(z, I32), (prod, I32)]), (rb(pu, 1), [(dl, I), (ov, Ib(2.0))])])
-        ts(of(3), rb(pu, 0), OFF, AL.add)
+        mm([(rb(pu, 0), [(yh, I), (prod, I32)]), (rb(pu, 1), [(dl, I), (ov, Ib(2.0))])])
+        aff(of(3), rb(pu, 0), 1.0, OFF)
         aff(lam, rb(pu, 1), 0.125)
         if not last:
             aff(ap("uf" + H, ALLP, ALLP), rb(pu, 0))
-        gather_tt("di" + H, VT, 3, va, AL.add, h)
-        for p0 in (0, 64):
-            for a in range(2):
-                pw, ks = spread(h, (sh, 24), p0, a)
-                if RD[p0 // 64] == "D":
-                    tt(pw, c("di", **ks), pw, AL.mult)
-                    tt(c("ld", **ks), c("y16", **ks), pw, AL.add)
-                else:
-                    tt(c("ld", **ks), c("di", **ks), pw, AL.mult)
-            if RD[p0 // 64] == "G":
-                dma(c("ld", p=S(p0, p0 + 64)), c("y16", p=S(p0, p0 + 64)), 262144, "G")
+        gather_add("di" + H, VT, 3, "va" + H, h)
+        for a in range(2):
+            pw, ks = spread(h, (sh, 24), 0, a)
+            tt(c("ld", **ks), c("di", **ks), pw, AL.mult)
+        dma(c("ld", p=S(0, 64)), c("y16", p=S(0, 64)), 262144, "G")
+        for a in range(2):
+            pw, ks = spread(h, (sh, 24), 64, a)
+            tt(pw, c("di", **ks), pw, AL.mult)
+            tt(c("ld", **ks), c("y16", **ks), pw, AL.add)
         mu = ap("eb" + H, ALLP)
         if not last:
-            ts(mu, blk(sm, 0, EDG), 8.0, EQ, -2.0, AL.mult)
+            act(mu, blk(sm, 0, EDG), AF.Relu, 2.0, -14.0, (8.0, EQ, 2.0, AL.mult))
         ts(blk(sm, 0, w=nq), blk(sm, 0, w=nq), 5.0, AL.is_lt, 2.0, AL.mult)
         tt(blk(sf, 3, w=nq), blk(sm, 0, w=nq), blk(st, 0, w=nq), AL.mult)
         pc = bank(h)
-        mm([(rb(pc, j), [(blk(st, 2 + j), I32), (blk(sf, 3 + j), I32)]) for j in range(nq)])
-        aff(blk(sf, 6, w=nq), rb(pc, 0, nq))
-        row = lambda j, u, a: ap("tb" + H, S(PW * (17 * u + a), PW * (17 * u + a + 16)), p=S(j, 128, 16))
-        for u in range(128 // PW):
-            dmas([(row(j, u, 1 - j % 2), ap(sf, S(48 + 8 * (j // 2) + u * PW // 16, 48 + 8 * (j // 2) + (u + 1) * PW // 16), ALLP)) for j in range(2 * nq)], 1024 * nq * PW)
+        mm([(rb(pc, j), [(Ey, I32) if j else (yh, I), (blk(sf, 3 + j), I32)]) for j in range(nq)])
+        aff(ap(si, S(0, 128 * nq)), rb(pc, 0, nq))
+        row = lambda j, u, a: ap("tb", S(TB[2 * h + u] + PW * a, TB[2 * h + u] + PW * (a + 16)), p=S(j, 128, 16))
+        for u in range(2):
+            dmas([(row(j, u, 1 - j % 2), ap(si, S(128 * (j // 2) + u * PW, 128 * (j // 2) + (u + 1) * PW))) for j in range(2 * nq)], 1024 * nq * PW)
         er = lambda j, n=1: ap(sm, S(j, j + n), ALLP)
         on16, ove = ap("cb", 8, ALLP), blk(sh, 2, EDG)
         lp = [(I, blk(sh, 1, EDG)), (lb, Ib(8.0, EDG)), (Ib(8.0), ove)]
         if not last:
-            mm([(er(16 + j), [(I, on16), (Ib(-2.0), ove), (I, mu)]) for j in range(2)] + [(er(18 + j), [(Ib(2.0), ove), (Ib(-1.0), mu)]) for j in range(2)]
-               + [(er(20), lp + [(Ib(4.0), mu)])] + [(er(21 + j), [(I, on16), (I, mu)]) for j in range(2)]
-               + [(er(28), [(Ib(-0.25), blk(sh, 1, EDG)), (lb, Ib(-2.0, EDG)), (Ib(-2.0), ove), (Ib(-1.0), mu), (Ib(2.0), on16)])]
-               + [(ap(sm, 23, S(8 * e, 8 * e + 8)), [(ap("zz", 1 + e, S(15 - j, 143 - j)), ap("uf" + H, ALLP, j)) for j in range(16)]) for e in range(2)])
-            ts(of(5, 0, 16), er(23), OFF, AL.add)
-            aff(ap("eg" + H, ALLP), ind(ET, of(5, 0, 16)))
+            mm([(er(16 + j), [(I, on16), (Ib(-2.0), ove), (Ib(-1.0), mu)]) for j in range(2)] + [(er(18 + j), [(Ib(2.0), ove), (I, mu)]) for j in range(2)]
+               + [(er(20), lp + [(Ib(-4.0), mu)])] + [(er(21 + j), [(I, on16), (Ib(-1.0), mu)]) for j in range(2)])
             for j in range(2):
                 tt(ap(ed, S(32 * j, 32 * j + 32)), er(16 + 2 * j, 2), blk(st, 0, EDG, 2), AL.mult)
             tt(ap(ed, S(96, 128)), er(21, 2), ap(ed, S(96, 128)), AL.mult)
             aff(blk(sg, 0, EDG), er(20), 2.0)
-            eu = lambda e: ap("eg" + H, S(128 * e, 128 * e + 128))
-            mm([(er(24, 4), [(I32, ap(ed, S(0, 64))), (If(0.5), blk(sf, 2, EDG), er(24)), (I32, blk(st, 2, EDG, 2), er(26, 2)), (If(-0.5), blk(st, 3, EDG), er(25))]
-                 + [(eu(e), SE4, ap(sm, 25, S(e, 16, 2))) for e in range(2)])])
+            mm([(er(24, 4), [(I32, ap(ed, S(0, 64))), (If(0.5), blk(sf, 2, EDG), er(24)), (I32, blk(st, 2, EDG, 2), er(26, 2)), (If(-0.5), blk(st, 3, EDG), er(25))])])
             aff(ap(st, ALLP, EDG), er(24, 4))
-            tt(ap(ed, S(80, 96)), er(28), blk(st, 1, EDG), AL.mult)
             for j, k in ((0, 15), (1, 0)):
-                tt(ap("sb" + H, S(128 + 8 * j, 136 + 8 * j)), ap(ed, S(81 - j, 96, 2)), blk(st, 3, k), AL.add)
-                if "P" in RD:
-                    tt(ap("sb" + H, S(144 * j, 144 * j + 128)), c("ld", k), c("y16", k), AL.add)
-                else:
-                    aff(ap("sb" + H, S(144 * j, 144 * j + 128)), c("ld", k), eng="G")
-            send(h, r + 1)
+                aff(ap("sb" + H, S(144 * j, 144 * j + 128)), c("ld", k), eng="G")
         else:
             mm([(er(16), [(I, on16), (Ib(-2.0), ove)]), (er(20), lp + [(Ib(-4.0), on16)])])
             tt(ap(ed, S(0, 16)), er(16), blk(st, 0, EDG), AL.mult)
@@ -520,25 +486,21 @@ def build():
                 (er(25), [(I32, blk(st, 0, EDG)), (If(0.5), blk(sf, 2, EDG)), (I32, blk(st, 2, EDG))])])
             tt(blk(st, 0, EDG), er(24), ap(ed, S(96, 112)), AL.mult)
             aff(blk(st, 2, EDG), er(25))
-        zc = lambda k: ap("zz", 0, S(15 - k, 143 - k))
+        zc = lambda k: ap("zz", S(15 - k, 143 - k))
         wk = lambda k: ap("wk", S(128 * (k - 1), 128 * k))
-
-        def hops(a):
-            pd, pp = ap(bank(h), ALLP, ALLP), S(a, a + 32)
-            tm = []
-            for x in ("ld" + H, "y16" + H)[:2 if RD[a // 64] == "P" else 1]:
-                tm.append((Ib(-1.0), fl(x, p=pp)))
-                if a == 32:
-                    tm += [(I, ap(x, S(513, 1021)), ap(pd[0], S(0, 127), ALLP)), (I, ap(x, S(1021, 1024)), ap(pd[0], 127, S(0, 3)))]
-                else:
-                    tm.append((I, fl(x, p=pp, shift=1)))
-            mm([(pd, tm)])
-            act(c("t16", p=pp), pd, AF.Abs, 8.0)
-
-        nr = PW // 4
-        qb = lambda n, j, w=1: ap(n, S(nr * j, nr * (j + w)), ALLP)
+        qb = lambda n, j, w=1: ap(n, S(16 * j, 16 * (j + w)), ALLP)
         part = lambda n, j, p0: ap(n, S(8 * j + p0 // 16, 8 * j + (p0 + PW) // 16), ALLP)
         sn = lambda p0, k, n=1: ap("g16" + H, S(16 * p0 + PW * k, 16 * p0 + PW * (k + n)))
+
+        def hops(a):
+            pd, pp, x = ap(bank(h), ALLP, ALLP), S(a, a + 32), "ld" + H
+            tm = [(Ib(-1.0), fl(x, p=pp))]
+            if a % 64:
+                tm += [(I, ap(x, S(16 * a + 1, 16 * a + 509)), ap(pd[0], S(0, 127), ALLP)), (I, ap(x, S(16 * a + 509, 16 * a + 512)), ap(pd[0], 127, S(0, 3)))]
+            else:
+                tm.append((I, fl(x, p=pp, shift=1)))
+            mm([(pd, tm)])
+            act(c("t16", p=pp), pd, AF.Abs, 8.0)
 
         def lengths(p0):
             ph = part(sm, 0, p0)
@@ -547,35 +509,33 @@ def build():
             tt(part(sh, 5, p0), ph, part(sh, 4, p0), AL.subtract)
 
         def rows(p0):
-            pq, s0 = bank(h), 80 + p0 // 4
+            pq, s0 = bank(h), 256 + 4 * p0
             mm([(qb(pq, j), [(w, part(sh, 4, p0)), (w, part(sh, 5, p0))]) for j, w in enumerate((wk(4), wk(11), I, G15))])
-            aff(ap(sf, S(s0, s0 + nr), ALLP), qb(pq, 0, 4))
-            dmas([(row(4 + j, p0 // PW, 1), ap(sf, S(s0 + j * PW // 16, s0 + (j + 1) * PW // 16), ALLP)) for j in range(4)], 2048 * PW)
+            aff(ap(si, S(s0, s0 + 4 * PW)), qb(pq, 0, 4))
+            dmas([(row(4 + j, p0 // PW, 1), ap(si, S(s0 + j * PW, s0 + (j + 1) * PW))) for j in range(4)], 2048 * PW)
 
-        def signs(p0, b, n):
+        def signs(p0, b):
             pk = bank(h)
-            mm([(qb(pk, j), [(wk(b + j), part(sh, 4, p0)), (wk(b + j), part(sh, 5, p0))]) for j in range(n)])
-            act(sn(p0, b, n), qb(pk, 0, n), AF.Sign, 1.0, 0.5)
+            mm([(qb(pk, j), [(wk(b + j), part(sh, 4, p0)), (wk(b + j), part(sh, 5, p0))]) for j in range(7)])
+            act(sn(p0, b, 7), qb(pk, 0, 7), AF.Sign, 1.0, 0.5)
 
         def count(p0):
-            pc = part(sm, 1, p0)
-            mm([(pc, [(I, ap("cb", S(24, 24 + PW // 16), ALLP))] + [(zc(k), sn(p0, k)) for k in range(1, 15)])])
-            ts(of(4, p0, p0 + PW), pc, 14.0, AL.add, PW / 2.0, AL.mult)
-            for b in range(16 * p0, 16 * (p0 + PW), GC):
-                aff(ap("d8" + H, S(b, b + GC)), ind(ap("tb" + H, S(17 * p0, 17 * (p0 + PW))), of(4, b // 16, (b + GC) // 16)))
+            pc, u = part(sm, 1, p0), 2 * h + p0 // PW
+            mm([(pc, [(I if last else IM, ap("cb", S(24, 28), ALLP))] + ([] if last else [(IE, part("uf" + H, 0, p0))]) + [(zc(k), sn(p0, k)) for k in range(1, 15)])])
+            aff(of(4, p0, p0 + PW), pc, 32.0, 448.0 + TB[u] - WIN[u][0] if last else cl(20 + u))
+            aff(ap("d8" + H, S(16 * p0, 16 * p0 + 1024)), ind(ap("tb", S(*WIN[u])), of(4, p0, p0 + PW)))
 
-        if PW == 64:
-            for f, *x in ((hops, 0), (hops, 32), (lengths, 0), (hops, 64), (rows, 0), (hops, 96), (signs, 0, 1, 7), (lengths, 64), (signs, 0, 8, 7),
-                          (rows, 64), (count, 0), (signs, 64, 1, 7), (signs, 64, 8, 7), (count, 64)):
-                f(*x)
-        else:
-            for f, *x in [(hops, a) for a in range(0, 128, 32)] + [(lengths, 0), (rows, 0)] + [(signs, 0, b, min(4, 15 - b)) for b in range(1, 15, 4)] + [(count, 0)]:
-                f(*x)
+        for f, *x in ((hops, 0), (hops, 32), (lengths, 0), (hops, 64), (rows, 0), (hops, 96), (signs, 0, 1), (lengths, 64), (signs, 0, 8),
+                      (rows, 64), (count, 0), (signs, 64, 1), (signs, 64, 8), (count, 64)):
+            f(*x)
+        if not last:
+            mm([(ap(sm, 29, S(e, 16, 2)), [(c("d8", 15 * e), SE4)]) for e in range(2)])
+            tt(blk(st, 1, EDG), er(29), blk(st, 1, EDG), AL.add)
         for b in range(4):
             px = bank(h)
             ks = [k for k in range(4 * b, 4 * b + 4) if 0 < k < 15]
             k4, kk = S(ks[0] % 4, ks[-1] % 4 + 1), S(ks[0], ks[-1] + 1)
-            mm([(ap(px, S(0, 104), k % 4), [(c("d8", k), ap("xw", S(13 * (k - 1), 13 * k), ALLP))]) for k in ks])
+            mm([(ap(px, S(0, 96 if last else 104), k % 4), [(c("d8", k), ap("xw", S(13 * (k - 1), 13 * k - last), ALLP))]) for k in ks])
             act(ap(sg, ALLP, kk), ap(px, S(0, 72), k4), AF.Sign, 1.0, 0.5)
             if last:
                 aff(ap(st, S(0, 24), kk), ap(px, S(72, 96), k4))
@@ -583,13 +543,13 @@ def build():
                 tt(ap(st, S(0, 16), kk), ap(px, S(72, 88), k4), ap(sg, S(56, 72), kk), AL.mult)
                 tt(ap(st, S(16, 32), kk), ap(px, S(88, 104), k4), ap(st, S(0, 16), kk), AL.subtract)
         if not last:
-            mm([(blk(sm, 0), [(z, I32), (hz, If(2.0))]), (blk(sm, 1), [(z, I32)])])
-            ts(of(0, 0, 256), blk(sm, 0, w=2), OFF, AL.add)
+            mm([(blk(sm, 0), [(y, I32), (hz, If(2.0))]), (blk(sm, 1), [(y, I32)])])
+            aff(of(0, 0, 256), blk(sm, 0, w=2), 1.0, OFF)
             pl = rb(bank(h), 0)
             mm([(pl, [(blk(sg, m), Ib(1.0 / 16 if m < 7 else -7.0 / 16)) for m in range(8)])])
             aff(lb, pl)
         else:
-            mm([(blk(sm, 0), [(z, I32), (hz, If(-1.0))]), (blk(sm, 1), [(z, I32), (hz, I32)])])
+            mm([(blk(sm, 0), [(y, I32), (hz, If(-1.0))]), (blk(sm, 1), [(y, I32), (hz, I32)])])
             aff(blk(sf, 0, w=2), blk(sm, 0, w=2), 1.0, OFF)
             dma(ap("ya", S(128 * h, 128 * h + 128)), blk(sf, 0), 65536)
             dma(ap("yb", S(128 * h, 128 * h + 128)), blk(sf, 1), 65536, "A")
@@ -616,16 +576,12 @@ def depend(ops):
     for i, o in enumerate(ops):
         d = set()
         for a in o["reads"]:
-            rg = region(a)
-            if rg is None:
-                continue
             if a[0] in lastw:
-                d.update(int(x) for x in np.unique(lastw[a[0]][rg]) if x >= 0)
+                d.update(int(x) for x in np.unique(lastw[a[0]][region(a)]) if x >= 0)
         for a in o["writes"]:
-            rg = region(a)
+            rg, n = region(a), a[0]
             if rg is None:
                 continue
-            n = a[0]
             if n not in lastw:
                 lastw[n] = np.full(_IDX[n].size, -1)
             rows = a[1][0] != ALLP
@@ -655,7 +611,7 @@ def depend(ops):
                 rd.setdefault(a[0], np.zeros(_IDX[a[0]].size, bool))[region(a)] = True
         for n, m in rd.items():
             readers.setdefault(n, []).append((i, m))
-        for n in set(a[0] for a in o["reads"] + o["writes"] if a[0].startswith("ps")):
+        for n in set(a[0] for a in o["reads"] + o["writes"] if a[0][:2] in ("ps", "vb")):
             acc = bankacc.setdefault(n, [None, [], []])
             if acc[0] != o["eng"] or len(o["eng"]) > 1:
                 acc[:] = [o["eng"], [], acc[1]]
@@ -665,162 +621,29 @@ def depend(ops):
         anc = 0
         for j in d:
             anc |= ops[j]["anc"]
-        o["deps"] = set(j for j in d if not anc >> j & 1)
+        o["data"] = set(j for j in d if not anc >> j & 1)
         for j in d:
             anc |= 1 << j
         o["anc"] = anc
+    lend(ops)
 
 
-PART = {}
-
-
-def schedule(ops):
-    n = len(ops)
-    succ = [[] for _ in ops]
+def lend(ops, at=None):
+    uses = {}
     for i, o in enumerate(ops):
-        o["tdeps"] = set(o["deps"]) | ({o["after"]} if "after" in o else set())
-        for j in o["tdeps"]:
-            succ[j].append(i)
-    pri = [0.0] * n
-    for i in range(n - 1, -1, -1):
-        o = ops[i]
-        pri[i] = min(o["cost"][e] for e in o["eng"]) + o.get("late", LAT) + max([pri[j] for j in succ[i]] + [0.0])
-    for i, o in enumerate(ops):
-        if o["half"] is not None:
-            pri[i] += BIAS[o["half"]]
-    pred = [sorted(o["tdeps"]) for o in ops]
-    late = [o.get("late", LAT) for o in ops]
-
-    def place(key, pen, back=False):
-        before, after = (succ, pred) if back else (pred, succ)
-        left = [len(x) for x in before]
-        rdy = [0.0] * n
-        rank = [0] * n
-        byrank = [int(j) for j in np.argsort(np.array(key), kind="stable")]
-        for k, j in enumerate(byrank):
-            rank[j] = k
-        ready = set(rank[i] for i in range(n) if not left[i])
-        busy = {e: [] for e in "DAPGSX"}
-        res = [None] * n
-        while ready:
-            k = min(ready)
-            ready.remove(k)
-            i = byrank[k]
-            o, best = ops[i], None
-            for x in o["eng"]:
-                c, st, b = o["cost"][x], rdy[i] + (late[i] if back else 0.0), busy[x]
-                k = len(b)
-                while k > 0 and b[k - 1][1] > st:
-                    k -= 1
-                while k < len(b) and b[k][0] < st + c:
-                    st = max(st, b[k][1])
-                    k += 1
-                f = st + c * (pen[i] if x == "D" else 1.0)
-                if best is None or f < best[0]:
-                    best = (f, st, x, k)
-            f, st, x, k = best
-            busy[x].insert(k, (st, st + o["cost"][x]))
-            res[i] = (x, st, st + o["cost"][x] + (0.0 if back else late[i]))
-            for j in after[i]:
-                rdy[j] = max(rdy[j], res[i][2])
-                left[j] -= 1
-                if not left[j]:
-                    ready.add(rank[j])
-        if back:
-            return 0.0, res
-        order = sorted(range(n), key=lambda i: (res[i][1], i))
-        tot = max(r[2] for r in res)
-        for cs, w in alt:
-            free, fin = {e: 0.0 for e in "DAPGSX"}, [0.0] * n
-            for i in order:
-                x = res[i][0]
-                st = free[x]
-                for j in pred[i]:
-                    if fin[j] > st:
-                        st = fin[j]
-                free[x] = st + cs[i][x]
-                fin[i] = free[x] + cs[i]["late"]
-            tot += w * max(fin)
-        return tot, res
-
-    alt = []
-    for fg, fp, ovh, lat, fd, w in SPEEDS:
-        cs = []
-        for o in ops:
-            c = {e: (v - 60) * ((fg[o["eng"] == "D"]) if any(a[0].startswith("of") for a in o["reads"]) else 1.0) + ovh if e in "DA" else v * (fp if e == "P" else 1.0)
-                 for e, v in o["cost"].items()}
-            c["late"] = o["late"] * fd if "late" in o else lat
-            cs.append(c)
-        alt.append((cs, w))
-
-    rng = np.random.default_rng(SEARCH[0])
-    key = [-p for p in pri]
-    pen = bp = [PEN[0]] * n
-    flex = [i for i in range(n) if ops[i]["eng"] == "DA" and ops[i]["cost"]["A"] > 400]
-    best = place(key, pen)
-    now = best
-    for it in range(SEARCH[1]):
-        z = rng.normal(0.0, SEARCH[2], (2, n))
-        p2 = list(pen)
-        for i in rng.choice(flex, SEARCH[4]):
-            p2[int(i)] = float(rng.choice([0.3, PEN[0], 30.0]))
-        b = place([-now[1][i][2] + float(z[0, i]) for i in range(n)], p2, True)
-        t = place([-b[1][i][2] + float(z[1, i]) for i in range(n)], p2)
-        if t[0] < best[0]:
-            best, bp = t, p2
-        now, pen = (t, p2) if t[0] < best[0] * SEARCH[3] else (best, bp)
-    base = [dict(o["cost"], late=late[i]) for i, o in enumerate(ops)]
-    allc = [(base, 1.0)] + alt
-
-    def run(order, q, cs):
-        free, last, fin, sta, why = {e: 0.0 for e in "DAPGSX"}, {}, [0.0] * n, [0.0] * n, [None] * n
-        for i in order:
-            x = q[i]
-            st, w = free[x], (last.get(x), 1)
-            for j in pred[i]:
-                if fin[j] > st:
-                    st, w = fin[j], (j, 0)
-            free[x] = st + cs[i][x]
-            fin[i], sta[i], why[i], last[x] = free[x] + cs[i]["late"], st, w, i
-        return max(fin), fin, sta, why
-
-    q = [r[0] for r in best[1]]
-    order = sorted(range(n), key=lambda i: (best[1][i][1], i))
-    runs = [run(order, q, cs) for cs, w in allc]
-    val = sum(r[0] * w for r, (cs, w) in zip(runs, allc))
-    keep = (val, order, q)
-    for it in range(POLISH[0]):
-        r = runs[it % len(runs)]
-        i, moves = int(np.argmax(r[1])), []
-        while i is not None:
-            j, onq = r[3][i]
-            if onq and j is not None:
-                moves.append((j, i))
-            if ops[i]["eng"] == "DA":
-                moves.append((i, None))
-            i = j
-        u, v = moves[int(rng.integers(len(moves)))]
-        o2, q2 = order, q
-        if v is None:
-            q2 = list(q)
-            q2[u] = "A" if q[u] == "D" else "D"
-        else:
-            a, b = order.index(u), order.index(v)
-            between = order[a + 1:b + 1]
-            if any(u in ops[j]["tdeps"] for j in between):
-                continue
-            o2 = order[:a] + between + [u] + order[b + 1:]
-        r2 = [run(o2, q2, cs) for cs, w in allc]
-        v2 = sum(x[0] * w for x, (cs, w) in zip(r2, allc))
-        if v2 < val + POLISH[1] * (1.0 - it / POLISH[0]) * float(rng.exponential()):
-            pos = {j: k for k, j in enumerate(o2)}
-            order, q, runs, val = sorted(o2, key=lambda j: (r2[0][2][j], pos[j])), q2, r2, v2
-            if val < keep[0]:
-                keep = (val, order, q)
-    r = run(keep[1], keep[2], base)
-    for i, o in enumerate(ops):
-        o["q"], o["t0"], o["t1"] = keep[2][i], r[2][i], r[1][i]
-    return keep[1]
+        o["deps"] = set(o["data"])
+        for n in sorted(set(a[0] for a in o["reads"] + o["writes"] if a[0][:2] in ("vb", "vp"))):
+            uses.setdefault(n, []).append(i)
+    names = sorted(uses, key=lambda n: uses[n][0] if at is None else (at[2][uses[n][0]], uses[n][0]))
+    free = {"vb": {"ps%d" % j: -1.0 for j in range(8) if j % 4 < 3}, "vp": {"pr%d" % j: -1.0 for j in range(NPR)}}
+    last = {}
+    for n in names:
+        if at is not None:
+            f = free[n[:2]]
+            PLACE[n] = min(f, key=f.get)
+            f[PLACE[n]] = max(at[2][i] + ops[i]["cost"][at[1][i]] for i in uses[n])
+        ops[uses[n][0]]["deps"].update(last.get(PLACE[n], []))
+        last[PLACE[n]] = uses[n]
 
 
 def graph(ops):
@@ -868,7 +691,7 @@ def pack(ops, key, iters, rng):
                 while k < m and s[k] < st + c:
                     st = e[k]
                     k += 1
-                f = st + c * (3.0 if x == "D" else 1.0)
+                f = st + c * (1.0 if x == engs[i][-1][0] else 3.0 if x == "D" else 6.0)
                 if best is None or f < best[0]:
                     best = (f, st, x, k, c)
             f, st, x, k, c = best
@@ -899,7 +722,7 @@ def pack(ops, key, iters, rng):
     return best[:3]
 
 
-def shorten(ops, init, iters, rng, reach=30):
+def shorten(ops, init, iters, rng, reach=14):
     n = len(ops)
     pred, succ, late = graph(ops)
     q = list(init[1])
@@ -973,6 +796,8 @@ def shorten(ops, init, iters, rng, reach=30):
             L = len(b)
             for a in range(L):
                 u = b[a]
+                if len(ops[u]["eng"]) == 1 and (L == 1 or reach < a < L - 1 - reach):
+                    continue
                 lo, hi = max([r[j] for j in pred[u]] + [-1.0]), min([r[j] for j in succ[u]] + [1e18])
                 for x in ops[u]["eng"]:
                     if x == q[u]:
@@ -989,7 +814,7 @@ def shorten(ops, init, iters, rng, reach=30):
                     if bp:
                         cand.append((bp[0], 2, u, x, bp[1]))
                 h, hs = (r[mp[u]] + p[mp[u]] if mp[u] >= 0 else 0.0), []
-                for k in range(a + 1, min(L, a + reach + 1)):
+                for k in range(a + 1, min(L, a + reach + 1) if a == 0 or a + reach >= L - 1 else 0):
                     v = b[k]
                     if r[v] >= hi:
                         break
@@ -1004,7 +829,7 @@ def shorten(ops, init, iters, rng, reach=30):
                             est = max(est, hs[m - a - 1] + tl)
                         cand.append((est, 0, u, v, 0))
                 tl, ts_ = (t[ms[u]] if ms[u] >= 0 else 0.0), []
-                for k in range(a - 1, max(-1, a - reach - 1), -1):
+                for k in range(a - 1, max(-1, a - reach - 1) if a == L - 1 or a <= reach else a, -1):
                     v = b[k]
                     if r[v] <= lo:
                         break
@@ -1020,7 +845,7 @@ def shorten(ops, init, iters, rng, reach=30):
                             h += p[b[m]]
                         cand.append((est, 1, u, v, 0))
         done = False
-        for m in np.argsort(np.array([c[0] for c in cand]) + rng.random(len(cand)) * 300.0):
+        for m in np.argsort(np.array([c[0] for c in cand]) + rng.random(len(cand)) * 200.0):
             est, kind, u, v, k = cand[m]
             if tb.get((u, v) if kind != 1 else (v, u), -1) >= it and est >= best[0]:
                 continue
@@ -1040,7 +865,7 @@ def shorten(ops, init, iters, rng, reach=30):
                 q[u], p[u] = old, ops[u]["cost"][old]
                 s.insert(a, u)
                 continue
-            ten = it + 50 + int(rng.integers(50))
+            ten = it + 100 + int(rng.integers(100))
             for kk in back:
                 tb[kk] = ten
             cur, done = nw, True
@@ -1052,11 +877,7 @@ def shorten(ops, init, iters, rng, reach=30):
     return best
 
 
-STARTS = [(a, b) for a in (10000.0, 14000.0, 18000.0, 22000.0) for b in (1.15, 1.3, 1.45)]
-EFFORT = [800, 10, 3, 2500, 1, 8000, 0]
-
-
-def schedule2(ops):
+def schedule(ops):
     rng = np.random.default_rng(EFFORT[6])
     idx = [i for i, o in enumerate(ops) if o["half"] != 1]
     at = {j: k for k, j in enumerate(idx)}
@@ -1073,19 +894,52 @@ def schedule2(ops):
         for a, b in pair:
             key[b] = key[a] + (lag if t[at[a]] > 9000 else 500.0)
         res.append(pack(ops, key, EFFORT[1], rng))
-    for keep, iters in (EFFORT[2:4], EFFORT[4:6]):
-        res = [shorten(ops, x, iters, rng) for x in sorted(res, key=lambda x: x[0])[:keep]]
-    best = min(res, key=lambda x: x[0])
+    res = [shorten(ops, x, EFFORT[3], rng) for x in sorted(res, key=lambda x: x[0])[:EFFORT[2]]]
+    plain = [(o["cost"], o.get("late")) for o in ops]
+
+    def speed(fv, fg, fp, fd):
+        for o, (c, late) in zip(ops, plain):
+            g = fg if any(a[0][:2] == "of" for a in o["reads"]) else 1.0
+            o["cost"] = c if late else {e: v * (fp if e == "P" else fv * g) for e, v in c.items()}
+            if late:
+                o["late"] = late * fd
+
+    def mean(x):
+        tot = 0.0
+        for s in PACES:
+            speed(*s)
+            tot += shorten(ops, x, 0, rng)[0] / s[0]
+        return tot / len(PACES)
+
+    def back(x):
+        PLACE.update(x[1])
+        for o, d in zip(ops, x[2]):
+            o["deps"] = set(d)
+        return x[0]
+
+    now, best, val = min(res, key=lambda x: x[0]), None, 1e18
+    for it in range(EFFORT[4]):
+        speed(*PACES[it % len(PACES)])
+        now = shorten(ops, now, 0, rng)
+        lend(ops, now)
+        now = shorten(ops, now, EFFORT[5], rng)
+        v = mean(now)
+        if v < val:
+            best, val = (now, dict(PLACE), [set(o["deps"]) for o in ops]), v
+        elif v > val + 2500.0:
+            now = back(best)
+    speed(*PACES[0])
+    now = shorten(ops, back(best), 0, rng)
     for i, o in enumerate(ops):
-        o["q"], o["t0"] = best[1][i], best[2][i]
+        o["q"], o["t0"] = now[1][i], now[2][i]
         o["t1"] = o["t0"] + o["cost"][o["q"]] + o.get("late", LAT)
-    return sorted(range(len(ops)), key=lambda i: (best[2][i], i))
+    return sorted(range(len(ops)), key=lambda i: (now[2][i], i))
 
 
 def plan():
     ops = build()
     depend(ops)
-    order = schedule2(ops)
+    order = schedule(ops)
     cnt, known, prog = {}, {e: {} for e in "DAPGSX"}, []
     for i in order:
         o = ops[i]

@@ -8,7 +8,11 @@ W, RO = 3072, 3
 HS = 272
 GC = 1024
 PW = 64
-NPR = 7
+NPR = 6
+HB = 64
+GA = 0
+GB = 1024
+RND, RNDE = 1.5 * 2 ** 23, 1.5 * 2 ** 33
 OFF = 1536.0
 TB = [1088, 0, 5248, 6336]
 WIN = [(1088, 5248), (0, 5248), (2176, 6336), (2176, 7424)]
@@ -18,26 +22,27 @@ PACES = [(1.0, 1.0, 1.0, 1.0), (1.0, 1.0, 1.1, 1.2), (1.2, 1.15, 1.0, 1.0), (1.0
 EFFORT = [400, 8, 3, 700, 60, 300, 0]
 
 SCRATCH = {
-    "vt": ("sbuf", [128, W], "float32"), "xt": ("sbuf", [128, W], "bfloat16"), "gt": ("sbuf", [128, W], "bfloat16"),
-    "nt": ("sbuf", [128, W], "int32"), "tb": ("sbuf", [128, W + 4 * 1088], "int32"),
-    "bk": ("sbuf", [128, 2048], "bfloat16"), "wk": ("sbuf", [128, 1792], "bfloat16"),
-    "xw": ("sbuf", [128, 182, 8], "float32"), "ct": ("sbuf", [128, 14, 13], "float32"), "c2": ("sbuf", [128, 14, 9], "float32"),
+    "vt": ("sbuf", [128, W], "float32"), "uw": ("sbuf", [128, W + 4096], "float32"), "xb": ("sbuf", [128, 2 * W], "bfloat16"),
+    "nt": ("sbuf", [128, W], "int32"), "tb": ("sbuf", [128, W + 4 * 1088], "float32"),
+    "bk": ("sbuf", [128, 2048], "bfloat16"), "ct": ("sbuf", [128, 14, 13], "bfloat16"), "c2": ("sbuf", [128, 14, 9], "bfloat16"),
     "cb": ("sbuf", [128, 144, 16], "bfloat16"), "zz": ("sbuf", [128, 144], "bfloat16"), "c32": ("sbuf", [128, 6, 128], "float32"),
-    "col": ("sbuf", [128, 80], "float32"), "coli": ("sbuf", [128, 8], "int32"),
+    "col": ("sbuf", [128, 112], "float32"), "coli": ("sbuf", [128, 8], "int32"), "se": ("sbuf", [128, 16], "bfloat16"),
 }
+BASE = {"d80": ("uw", 0), "ut": ("uw", 2048), "d81": ("uw", 2048 + W), "xt": ("xb", 0), "gt": ("xb", W),
+        "gd0": ("tb", 0), "gd1": ("tb", 5248), "wk": ("xb", 0), "x1": ("xb", 1792), "x2": ("xb", 3248), "cm": ("xb", 4256)}
 for _i in range(NPR):
     SCRATCH["pr%d" % _i] = ("sbuf", [128, 128, 4], "float32")
 for _h in range(2):
-    for _n, _s, _t in (("va", [2048], "float32"), ("d8", [2048], "float32"), ("di", [2048], "int32"), ("rw", [2048 + RO * HS], "float32"),
+    for _n, _s, _t in (("va", [2048], "float32"), ("di", [2048], "int32"), ("rw", [2048 + RO * HS], "float32"),
                        ("g16", [2048], "float16"), ("t16", [2048], "float16"), ("ld", [2048], "float16"), ("y16", [2048], "float16"),
-                       ("si", [768], "int32"), ("of", [640], "uint16"), ("st", [32, 16], "float32"), ("sf", [72, 16], "float32"),
-                       ("sh", [48, 16], "bfloat16"), ("yh", [128], "float16"), ("uf", [8, 16], "float16"), ("sg", [72, 16], "bfloat16"),
-                       ("ed", [128], "float32"), ("eb", [16], "bfloat16"), ("sb", [HS], "float32")):
+                       ("si", [896], "float32"), ("of", [640], "uint16"), ("st", [32, 16], "float32"), ("sf", [48, 16], "float32"),
+                       ("sh", [48, 16], "bfloat16"), ("yh", [8, 16], "float16"), ("uf", [8, 16], "float16"), ("ue", [8, 16], "float16"),
+                       ("sg", [72, 16], "bfloat16"), ("ed", [128], "float32"), ("eb", [32], "bfloat16"), ("sb", [2, 136], "float32")):
         SCRATCH["%s%d" % (_n, _h)] = ("sbuf", [128] + _s, _t)
     for _i in range(3):
         SCRATCH["ps%d" % (4 * _h + _i)] = ("psum", [128, 128, 4], "float32")
     SCRATCH["ps%d" % (4 * _h + 3)] = ("psum", [128, 32, 16], "float32")
-NDMA = 56
+NDMA = 72
 SEMAPHORES = ["cD", "cA", "cP", "cG"] + ["dm%d" % i for i in range(NDMA)] \
     + ["ar%d" % i for i in range(2 * RO)] + ["lo%d" % i for i in range(2 * RO)]
 
@@ -47,6 +52,9 @@ _IDX, PLACE = {}, {}
 
 
 def ap(name, *idx, p=ALLP):
+    if name in BASE:
+        (name, b), s = BASE[name], idx[0]
+        idx = (S(s.start + b, s.stop + b, s.step),)
     return (name, (p,) + idx)
 
 
@@ -102,10 +110,10 @@ def parts(a):
 
 
 def build():
-    ops, cur, nd = [], [None], [0]
+    ops, cur, nd = [], [None, -1], [0]
 
     def add(eng, cost, reads, writes, emit, **kw):
-        o = dict(eng=eng, cost=cost, reads=[x for r in reads for x in parts(r)], writes=writes, emit=emit, half=cur[0])
+        o = dict(eng=eng, cost=cost, reads=[x for r in reads for x in parts(r)], writes=writes, emit=emit, half=cur[0], rnd=cur[1])
         o.update(kw)
         ops.append(o)
         return len(ops) - 1
@@ -146,8 +154,8 @@ def build():
     def aff(out, a, scale=1.0, bias=0.0, eng="DA"):
         act(out, a, AF.Identity, scale, bias, () if scale == 1.0 and bias == 0.0 else (scale, AL.mult, bias, AL.add), eng)
 
-    def mm(lst):
-        fs, cost, rd, wr = [], 30, [], []
+    def mm(lst, begin=True, end=True):
+        fs, cost, rd, wr = [], 30, [] if begin else [lst[0][0]], []
         for out, terms in lst:
             wr.append(out)
             for i, tm in enumerate(terms):
@@ -155,7 +163,7 @@ def build():
                 o = tm[2] if len(tm) > 2 else out
                 cost += max(64, nel(r)) * (1 if two(l) else 4) * PCY
                 rd += [l, r]
-                fs.append(lambda g, T, o=o, l=l, r=r, a=(i == 0), b=(i == len(terms) - 1): g.tensor.matmul(real(T, o), real(T, l), real(T, r), a, b))
+                fs.append(lambda g, T, o=o, l=l, r=r, a=(begin and i == 0), b=(end and i == len(terms) - 1): g.tensor.matmul(real(T, o), real(T, l), real(T, r), a, b))
         add("P", {"P": cost}, rd, wr, lambda e: fs)
 
     def iota(out, pat, base, cm):
@@ -198,18 +206,23 @@ def build():
         dma(ap("gt", S(a, a + 1024)), ap("grec", S(a, a + 1024)), 400000 + 512 * (a + 1024))
     mset(ap("tb", S(2176, 4224)), 0)
     iota(ap("tb", S(4224, 5248)), [[0, 1024]], 0, 0)
-    dma(ap("tb", S(2176, 5248), p=S(0, 128, 16)), ap("erec", ALLP), 98304 * 4)
+    ee = lambda j: ap("va1" if j else "di1", S(192 * j, 192 * j + 192))
+    dma(ee(0), ap("erec", ALLP), 98304, "A")
+    ts(ee(1), ee(0), RNDE, AL.add, -RNDE, AL.add)
+    tt(ee(2), ee(0), ee(1), AL.subtract)
+    dmas([(ap("tb", S(2176, 5248), p=S(2 * j, 128, 16)), ee(1 + j)) for j in range(2)], 98304 * 4)
     dma(ap("nt", ALLP), ap("nbr", ALLP), 1572864 * 2)
     ops[-1]["reads"] += [ap("gt", S(1024, 1032)), ap("tb", S(2176, 2184))]
     cb = lambda j, k=ALLP: blk("cb", j, k)
-    I, ONE, BC, P32, G15, IE, IM = [cb(j) for j in (0, 1, 2, 3, 4, 16, 17)]
+    I, ONE, BC, P32, G15, IM = [cb(j) for j in (0, 1, 2, 3, 4, 17)]
+    cm = lambda j, p=ALLP: ap("cm", S(128 * j, 128 * j + 128), p=p)
     I32, ONE32 = ap("c32", 0, ALLP), ap("c32", 1, ALLP)
     mset(ONE, 1.0)
     mset(ONE32, 1.0)
     sel(I, ONE, [[-1, 128]], EQ, 0.0, 0, 1)
     sel(I32, ONE32, [[-1, 128]], EQ, 0.0, 0, 1)
     sc, sf32 = {}, {}
-    for j, v in enumerate((1.0 / 2048, -1.0, -2.0, 2.0, 1.0 / 16, -7.0 / 16, 8.0, 0.5, -4.0)):
+    for j, v in enumerate((1.0 / 2048, -1.0, -2.0, 2.0, 1.0 / 16, -7.0 / 16, 8.0, 0.5, -4.0, 1.0 / 32)):
         sc[v] = 5 + j
         aff(cb(5 + j), I, v)
     for j, v in enumerate((-1.0, 2.0, -0.5, 0.5)):
@@ -218,8 +231,11 @@ def build():
     Ib = lambda v, k=ALLP: cb(sc[v], k)
     If = lambda v: sf32[v]
     cl = lambda a, n=1: ap("col", S(a, a + n))
-    GS, SE4, EQ8 = cl(32, 8), cl(40, 8), cl(56, 8)
-    aff(SE4, ap("c32", 0, S(0, 128, 16)), 4.0)
+    GS, SCL = cl(32, 8), cl(27)
+    SEH, SEN = ap("se", S(0, 8)), ap("se", S(8, 16))
+    aff(cl(40, 8), ap("c32", 0, S(0, 128, 16)), 16.0)
+    tt(SEH, cl(40, 8), ap("cb", S(8 * sc[0.5], 8 * sc[0.5] + 8), 2), AL.add)
+    aff(SEN, SEH, -1.0)
     sel(GS, ap("c32", 1, S(0, 8)), [[-16, 8]], GE, 0.0, 0, 1)
     sel(GS, GS, [[16, 8]], GE, 0.0, 15, -1)
     mset(ap("bk", ALLP), -1.0)
@@ -227,12 +243,13 @@ def build():
     iota(P32, [[1, 128]], 0, 0)
     iota(ap("coli", S(0, 1)), [[0, 1]], 0, 1)
     iota(cl(0, 3), [[-HS, 3]], 1 - 2048, 15)
-    iota(cl(3, 3), [[HS, 3]], 2048 + 144 - 14, -15)
+    iota(cl(3, 3), [[HS, 3]], 2048 + 136 - 14, -15)
     iota(cl(6, 3), [[HS, 3]], 1025, 0)
     aff(cl(0, 6), cl(0, 6), 0.5)
     ts(ap("coli", S(4, 5)), ap("coli", S(0, 1)), 15, AL.bitwise_and)
     aff(cl(12), ap("coli", S(4, 5)), eng="D")
     ts(cl(13), cl(12), 0.0, EQ)
+    ts(SCL, cl(12), 2.0, GE, 1.0 / 32, AL.max)
     ts(cl(14), cl(12), 15.0, EQ, 1024.0, AL.mult)
     ts(cl(14), cl(14), cl(12), AL.add, -1.0, AL.add)
     ts(cl(16, 3), cl(6, 3), cl(13), AL.mult, cl(14), AL.add)
@@ -258,6 +275,8 @@ def build():
             pv = ap(bank(a // 512 % 2), ALLP, ALLP)
             mm([(pv, [(I, ap("xt", S(a, a + 512))), (Ib(1.0 / 2048), ap("gt", S(a, a + 512)))])])
             aff(ap("vt", S(a, a + 512)), pv, 1.0, 128.125)
+        for a in range(0, W, 1024):
+            aff(ap("ut", S(a, a + 1024)), ap("vt", S(a, a + 1024)), -1.0)
 
     def late_consts():
         cur[0] = None
@@ -265,10 +284,15 @@ def build():
         iota(zz, [[0, 144]], 1, 0)
         sel(zz, zz, [[0, 9], [1, 16]], EQ, 0.0, -15, 0)
         ts(cl(24), cl(12), 15.0, EQ, cl(13), AL.add)
-        aff(cl(25), cl(24), 1.0 / 32)
         aff(cl(26), cl(24), -1.0, 1.0)
-        aff(IE, I, cl(25))
         aff(IM, I, cl(26))
+        iota(cm(3), [[16, 128]], 0, 0)
+        sel(cm(3), cm(3), [[0, 128]], EQ, 1.0, 0, 1)
+        aff(cm(4), cm(3), -1.0)
+        iota(cm(5), [[0, 8], [1, 16]], 0, 0)
+        sel(cm(5), cm(5), [[0, 128]], EQ, 1.0, -1, 1)
+        sel(cm(6), cm(5), [[0, 128]], AL.not_equal, W - OFF, -2, 1)
+        sel(cm(5), cm(5), [[0, 128]], AL.not_equal, -2048 - OFF, -2, 1)
         for u in range(4):
             a, b = 448.0 + TB[u] - WIN[u][0], OFF + 2176 - WIN[u][0]
             aff(cl(20 + u), cl(24), b - a, a)
@@ -276,7 +300,10 @@ def build():
         sel(zz, zz, [[16, 9], [0, 16]], GE, 0.0, 15, -1)
         sel(G15, ONE, [[-16, 8], [0, 16]], GE, 0.0, 0, 1)
         sel(G15, G15, [[16, 8], [0, 16]], GE, 0.0, 14, -1)
-        wk = ap("wk", ALLP)
+        sel(cm(0), G15, [[16, 8], [1, 16]], AL.is_gt, 0.0, 0, -1)
+        aff(cm(1), cm(0), 128.0)
+        aff(cm(2), G15, 128.0)
+        wk = ap("wk", S(0, 1792))
         iota(wk, [[1, 14], [0, 128]], 1, 0)
         for k in range(1, 15):
             b = ap("wk", S(128 * (k - 1), 128 * k))
@@ -284,28 +311,39 @@ def build():
         sel(wk, wk, [[0, 14], [-16, 8], [0, 16]], GE, 0.0, 0, 1)
         sel(wk, wk, [[0, 14], [16, 8], [0, 16]], GE, 0.0, 14, -1)
         iota(ap("wk", S(15, 1792, 16)), [[0, 112]], 0, 0)
-        iota(EQ8, [[1, 8]], 0, 0)
-        ts(EQ8, EQ8, cl(12), EQ)
-        iota(ap("ct", ALLP, S(0, 8)), [[0, 14], [2, 8]], 1, 0)
-        iota(ap("ct", ALLP, S(8, 9)), [[0, 14]], 15, 0)
-        iota(ap("c2", ALLP, ALLP), [[0, 2], [1, 7], [0, 9]], -3, 0)
-        aff(cl(64, 4), cl(60, 4), 16.0)
-        aff(cl(66), cl(62), -15.0)
-        for j in range(2):
-            x = ap("ct", S(7 * j, 7 * j + 7), S(0, 9))
-            aff(x, x, cl(66), cl(64 + j))
-        aff(ap("c2", ALLP, ALLP), ap("c2", ALLP, ALLP), cl(67))
-        tt(ap("ct", ALLP, S(0, 9)), ap("ct", ALLP, S(0, 9)), ap("c2", ALLP, ALLP), AL.add)
-        aff(cl(56, 4), cl(56, 4), 0.5)
-        tt(cl(68, 2), ap("col", S(57, 60, 2)), ap("col", S(56, 60, 2)), AL.subtract)
-        tt(cl(70, 2), ap("col", S(57, 60, 2)), ap("col", S(56, 60, 2)), AL.add)
-        for j in range(4):
-            aff(ap("ct", ALLP, 9 + j), ap("c32", 1, S(0, 14)), cl(68 + j))
+        iota(cl(56, 12), [[1, 12]], 0, 0)
+        ts(cl(56, 12), cl(56, 12), cl(12), EQ)
+        iota(ap("ct", ALLP, S(0, 8)), [[0, 14], [30, 8]], 15, 0)
+        iota(ap("ct", ALLP, S(8, 9)), [[0, 14]], 225, 0)
+        iota(ap("c2", ALLP, ALLP), [[16, 14], [0, 9]], 16, 0)
+        aff(cl(56, 2), cl(56, 2), 16.0)
+        aff(cl(58, 4), cl(58, 4), 0.5)
+        tt(cl(68, 6), ap("col", S(56, 68, 2)), ap("col", S(57, 68, 2)), AL.subtract)
+        tt(cl(74, 6), ap("col", S(56, 68, 2)), ap("col", S(57, 68, 2)), AL.add)
+        tt(cl(80), cl(71), cl(72), AL.add)
+        ts(cl(81), cl(62), cl(64), AL.add, -240.0, AL.mult)
+        x = ap("ct", ALLP, S(0, 9))
+        aff(x, x, cl(80), cl(81))
+        aff(ap("c2", ALLP, ALLP), ap("c2", ALLP, ALLP), cl(79))
+        tt(x, x, ap("c2", ALLP, ALLP), AL.add)
+        ts(cl(82), cl(68), cl(69), AL.add, -1.0, AL.mult)
+        for j, (a, b) in enumerate(((-1.0, cl(70)), (1.0, cl(82)), (1.0, cl(76)), (cl(74), cl(75)))):
+            if j == 3:
+                aff(ap("ct", ALLP, 12), ap("c32", 1, S(0, 14)), a, b)
+            else:
+                ts(ap("ct", ALLP, 9 + j), ap("c32", 1, S(0, 14)), b, AL.mult, a, AL.mult)
+        ts(cl(83), cl(77), cl(66), AL.add, 128.0, AL.mult)
+        ts(cl(83), cl(12), 6.0, AL.is_lt, cl(83), AL.add)
+        tt(cl(84), cl(78), cl(67), AL.add)
+        aff(cl(88, 8), GS, cl(83))
+        aff(cl(96, 8), GS, cl(84))
         for j in range(8):
-            aff(ap("xw", ALLP, j), ap("ct", ALLP, ALLP), cl(32 + j))
+            aff(ap("x1", S(j, 1456, 8)), ap("ct", ALLP, ALLP), cl(88 + j))
+            aff(ap("x2", S(j, 1008, 8)), x, cl(96 + j))
         for h in range(2):
+            aff(ap("ue%d" % h, ALLP, ALLP), ONE, 0.0)
             iota(ap("sg%d" % h, ALLP, EDG), [[0, 144]], 0, 0)
-            dma(ap("tb", S(5248 * h, 5248 * h + 2176)), ap("nt", S(0, 2176)), 1114112)
+            iota(ap("tb", S(5248 * h + 2048, 5248 * h + 2176)), [[0, 128]], 0, 0)
 
     def names(h):
         H = str(h)
@@ -318,10 +356,10 @@ def build():
         for a in range(0, 2048, GC):
             aff(ap(dst, S(a, a + GC)), ind(win, of(oj, a // 16, (a + GC) // 16)), scale, bias)
 
-    def gather_add(dst, win, oj, other, h):
+    def gather_add(dst, win, oj, other, h, op=AL.add):
         H, c, of, sm = names(h)
         for a in range(0, 2048, GC):
-            tt(ap(dst, S(a, a + GC)), ind(win, of(oj, a // 16, (a + GC) // 16)), ap(other, S(a, a + GC)), AL.add)
+            tt(ap(dst, S(a, a + GC)), ind(win, of(oj, a // 16, (a + GC) // 16)), ap(other, S(a, a + GC)), op)
 
     VT, NT, ET = ap("vt", ALLP), ap("nt", ALLP), ap("tb", S(2176, 5248))
 
@@ -338,28 +376,28 @@ def build():
         aff(of(0, 0, 256), blk(sf, 3, w=2))
         ts(pin(2, h), pin(2, h), 7, AL.bitwise_and)
         aff(blk(sh, 0), pin(2, h), 0.125)
-        gathers("d8" + H, ET, 1, h)
-        gathers("rw" + H, ET, 0, h)
+        gathers("t16" + H, ET, 1, h, SCL)
+        gathers("g16" + H, ET, 0, h, SCL)
         mm([(blk(sm, 2), [(y, I32)]), (blk(sm, 0), [(z, If(0.5)), (y, If(-0.5))]), (blk(sm, 1), [(f, I32)])])
         aff(blk(st, 2), blk(sm, 2), 1.0, -OFF)
         aff(blk(st, 0), blk(sm, 0))
         aff(ap(ed, S(96, 112)), blk(sm, 1, EDG), 2.0, -1.0)
         aff(ap(ed, S(112, 128)), blk(sm, 1, EDG), -4.0, 2.0)
-        mm([(blk(sm, 3, k), [(c("d8", k), SE4)]) for k in range(16)])
+        mm([(blk(sm, 3, k), [(c("t16", k), SEH)]) for k in range(16)])
         aff(blk(st, 3), blk(sm, 3), 2.0)
-        aff(blk(sf, 8), blk(sm, 3))
-        mm([(blk(sm, 1, k), [(c("rw", k), SE4)]) for k in range(16)])
-        tt(blk(st, 1), blk(sm, 1), blk(sf, 8), AL.subtract)
+        mm([(blk(sm, 1, k), [(c("g16", k), SEH), (c("t16", k), SEN)]) for k in range(16)])
+        aff(blk(st, 1), blk(sm, 1))
 
     def spread(h, x, p0, a):
         pl = bank(h)
-        mm([(ap(pl, S(k // 4, 128, 2), k % 4), [(ap("bk", S(128 * (a + 2 * k), 128 * (a + 2 * k) + 128)), ap(x[0], S(x[1] + p0 // 16, x[1] + p0 // 16 + 4), ALLP))]) for k in range(8)])
+        mm([(ap(pl, ALLP, ALLP), [(ap("bk", S(128 * (a + 2 * k), 128 * (a + 2 * k) + 128)), ap(x[0], S(x[1] + p0 // 16, x[1] + p0 // 16 + 4), ALLP),
+                                   ap(pl, S(k // 4, 128, 2), k % 4)) for k in range(8)])])
         return ap(pl, ALLP, ALLP), dict(k=(a, 2), p=S(p0, p0 + 64))
 
     def send(h, r):
         rw, sb, a = "rw%d" % h, "sb%d" % h, 2048 + HS * r
-        tr = [(ap(sb, S(0, 136)), ap(rw, S(a, a + 136))), (ap(sb, S(136, HS)), ap(rw, S(a + 136, a + HS)))]
-        i = add("G", {"G": 1000.0}, [ap(sb, ALLP)], [], None, sem="lo%d" % (2 * r + h), inc=8, late=2500.0, send=tr, arr="ar%d" % (2 * r + h))
+        tr = [(ap(sb, 0, ALLP), ap(rw, S(a, a + 136))), (ap(sb, 1, ALLP), ap(rw, S(a + 136, a + HS)))]
+        i = add("G", {"G": 1000.0}, [ap(sb, ALLP, ALLP)], [], None, sem="lo%d" % (2 * r + h), inc=8, late=2500.0, send=tr, arr="ar%d" % (2 * r + h))
         add("X", {"X": 0.0}, [], [ap(rw, S(a, a + HS))], None, sem="ar%d" % (2 * r + h), inc=8, late=2000.0, after=i)
 
     def step1(h, r):
@@ -370,33 +408,46 @@ def build():
         lb = blk(sh, 0)
         gathers("va" + H, VT, 0, h, -1.0)
         gather_add("d8" + H, VT, 1, "va" + H, h)
-        aff(ap("yh" + H, ALLP), y, eng="DAG")
-        pq = rb(bank(h), 0)
-        mm([(pq, [(lb, Ib(-2.0)), (Ib(2.0), ONE)])])
+        if r == 0:
+            aff(ap("yh" + H, ALLP, ALLP), y, eng="DAG")
+        pb = bank(h)
+        pq = rb(pb, 0)
+        mm([(pq, [(lb, Ib(-2.0)), (Ib(2.0), ONE)]), (rb(pb, 1), [(lb, Ib(8.0))])])
         tt(pq, pq, hE, AL.mult)
         tt(blk(sf, 0), pq, Ey, AL.add)
-        aff(ap("sb" + H, S(128, 136)), blk(sf, 0, 15), eng="DAG")
-        aff(ap("sb" + H, S(136, 144)), blk(sf, 0, 0), eng="DAG")
+        act(blk(sh, 3), rb(pb, 1), AF.Relu, -1.0, 1.0, (0.0, EQ, 1.0, AL.mult))
+        aff(ap("sb" + H, 0, S(128, 136)), blk(sf, 0, 15), eng="DAG")
+        aff(ap("sb" + H, 1, S(128, 136)), blk(sf, 0, 0), eng="DAG")
         for p0 in (0, 64):
             cols = S(16 * p0, 16 * p0 + 1024)
             aff(ap("di" + H, cols), ap("d8" + H, cols), eng="G")
             for a in range(2):
                 pw, ks = spread(h, (sh, 0), p0, a)
                 tt(pw, c("d8", **ks), pw, AL.mult)
-                tt(pw, c("va", **ks), pw, AL.add)
-                aff(c("y16", **ks), pw)
-                tt(c("g16", **ks), pw, c("y16", **ks), AL.subtract)
-            aff(ap(rw, cols), ap("y16" + H, cols), eng="G")
+                tt(c("rw", **ks), pw, c("va", **ks), AL.add)
+            aff(ap("y16" + H, cols), ap(rw, cols), eng="DAG")
+            for a in range(2):
+                pw, ks = ap(bank(h), ALLP, ALLP), dict(k=(a, 2), p=S(p0, p0 + 64))
+                mm([(pw, [(Ib(-1.0), c("y16", **ks))])])
+                if a + p0 // 32 < GA:
+                    tt(pw, pw, c("rw", **ks), AL.add)
+                    aff(c("g16", **ks), pw)
+                else:
+                    tt(c("g16", **ks), pw, c("rw", **ks), AL.add)
+                    pw = ap(bank(h), ALLP, ALLP)
+                    mm([(pw, [(I, c("g16", **ks))])])
+                tt(c("gd", **ks), pw, c("di", **ks), AL.mult)
         if r == 0:
-            aff(ap("sb" + H, S(0, 128)), c("y16", 15))
-            aff(ap("sb" + H, S(144, HS)), c("y16", 0))
+            aff(ap("sb" + H, 0, S(0, 128)), c("rw", 15), eng="DAG")
+            aff(ap("sb" + H, 1, S(0, 128)), c("rw", 0), eng="DAG")
         send(h, r)
+        dma(ap("d8" + H, S(0, 2048)), ap("va" + H, ALLP), 1048576, "G")
         gathers("ld" + H, NT, 0, h, 1.0, -OFF)
         sl = 2048 + HS * r
         mo = lambda k=ALLP: ap("uf" + H, ALLP, k)
         tt(mo(MID), blk(sf, 0, S(2, 16)), blk(sf, 0, S(0, 14)), GE)
         tt(mo(0), blk(sf, 0, 1), ap(rw, S(sl + 128, sl + 136)), GE)
-        tt(mo(15), ap(rw, S(sl + 136, sl + 144)), blk(sf, 0, 14), GE)
+        tt(mo(15), ap(rw, S(sl + 264, sl + 272)), blk(sf, 0, 14), GE)
         aff(mo(0), mo(0), cl(r), 512.0)
         aff(mo(15), mo(15), cl(3 + r), -512.0)
         po = bank(h)
@@ -404,11 +455,11 @@ def build():
         aff(of(2), rb(po, 0), 1.0, cl(16 + r))
         red = lambda j, pr, a: mm([(blk(sm, j, a + 4 * k), [(ap(pr, ALLP, k), GS)]) for k in range(4)])
         for a in range(4):
-            pg, ks, pr = ap(bank(h), ALLP, ALLP), (a, 4), newpr()
-            mm([(pg, [(I, c("g16", ks))])])
-            tt(ap(pr, ALLP, ALLP), c("di", ks), pg, AL.mult)
-            red(0, pr, a)
+            mm([(blk(sm, 0, k), [(c("gd", k), GS)]) for k in range(a, 16, 4)])
         gathers("t16" + H, ap(rw, S(0, sl + HS)), 2, h)
+        for a in range(0, 2048, GB):
+            aff(ap(rw, S(a, a + GB)), ap("y16" + H, S(a, a + GB)), -8.0)
+            dma(ap(rw, S(a, a + GB)), ap("va" + H, S(a, a + GB)), 512 * GB, "G")
         for a in range(4):
             pt, ks = ap(bank(h), ALLP, ALLP), (a, 4)
             ptd, pgt, ptt = newpr(), newpr(), newpr()
@@ -426,64 +477,60 @@ def build():
         last = r == RO - 1
         nq = 1 if last else 2
         hz, hE, y, Ey = [blk(st, j) for j in range(4)]
-        lb, dl, ov, lam = [blk(sh, j) for j in range(4)]
-        yh, prod = ap("yh" + H, ALLP), blk(sf, 2)
+        lb, eq, dn, m0 = [blk(sh, j) for j in range(4)]
+        yh = ap("yh" + H, ALLP, ALLP)
+        pn, pw, lh = bank(h), bank(h), lambda j: cm(j, S(0, 3))
+        mm([(rb(pn, 0), [(lh(4), lh(5 + h))] + [(c("ld", k), ap("cb", S(0, 8), k), ap(pn, S(k // 4, 32, 4), k % 4)) for k in range(16)])])
+        tt(blk(sf, 5), rb(pn, 0), m0, AL.mult)
+        mm([(rb(pw, 0), [(If(2.0), hz)]), (rb(pw, 1), [(lh(3), lh(5 + h)), (Ib(-1.0), yh), (I32, blk(sf, 5))])])
         aff(blk(sf, 2, w=2), blk(sm, 2, w=2))
-        pn = bank(h)
-        mm([(rb(pn, 0), [(Ib(-1.0), yh)] + [(c("ld", k), ap("cb", S(0, 8), k), ap(pn, S(k // 4, 32, 4), k % 4)) for k in range(16)])])
         tt(blk(sf, 4), blk(sm, 0), blk(sf, 2), AL.mult)
         tt(blk(sm, 1), blk(sm, 1), blk(sf, 3), AL.mult)
-        tt(blk(sm, 1), blk(sm, 1), blk(sf, 4), AL.subtract)
-        act(dl, blk(sm, 1), AF.Sign, -1.0)
-        mm([(blk(sm, j), [(I, dl), (lb, Ib(8.0))]) for j in range(nq)])
-        act(ov, blk(sm, 0), AF.Relu, -1.0, 0.0, (-1.0, AL.mult, 0.0, AL.max))
-        tt(prod, rb(pn, 0), ov, AL.mult)
+        tt(eq, blk(sm, 1), blk(sf, 4), EQ)
+        tt(dn, blk(sm, 1), blk(sf, 4), AL.is_gt)
+        tt(blk(sf, 0, w=2), rb(pw, 0, 2), blk(sh, 1, w=2), AL.mult)
         pu = bank(h)
-        mm([(rb(pu, 0), [(yh, I), (prod, I32)]), (rb(pu, 1), [(dl, I), (ov, Ib(2.0))])])
-        aff(of(3), rb(pu, 0), 1.0, OFF)
-        aff(lam, rb(pu, 1), 0.125)
+        mm([(rb(pu, 0), [(yh, I), (blk(sf, 0), I32), (blk(sf, 1), I32)])])
+        aff(of(3), rb(pu, 0), 1.0, OFF + 2048 * (1 - h))
+        gather_add("ld" + H, ap("uw", S(2048 * h, 2048 * h + 2048 + W)), 3, "rw" + H, h, AL.subtract)
+        mm([(blk(sm, j), [(lb, Ib(8.0)), (Ib(-1.0), eq), (Ib(-2.0), dn)]) for j in range(1)])
+        mu, ove = ap("eb" + H, S(0, 16)), ap("eb" + H, S(16, 32))
+        act(ove, blk(sm, 0, EDG), AF.Relu, -1.0, -1.0, (-2.0, EQ, 1.0, AL.mult))
         if not last:
-            aff(ap("uf" + H, ALLP, ALLP), rb(pu, 0))
-        gather_add("di" + H, VT, 3, "va" + H, h)
-        for a in range(2):
-            pw, ks = spread(h, (sh, 24), 0, a)
-            tt(c("ld", **ks), c("di", **ks), pw, AL.mult)
-        dma(c("ld", p=S(0, 64)), c("y16", p=S(0, 64)), 262144, "G")
-        for a in range(2):
-            pw, ks = spread(h, (sh, 24), 64, a)
-            tt(pw, c("di", **ks), pw, AL.mult)
-            tt(c("ld", **ks), c("y16", **ks), pw, AL.add)
-        mu = ap("eb" + H, ALLP)
-        if not last:
-            act(mu, blk(sm, 0, EDG), AF.Relu, 2.0, -14.0, (8.0, EQ, 2.0, AL.mult))
-        ts(blk(sm, 0, w=nq), blk(sm, 0, w=nq), 5.0, AL.is_lt, 2.0, AL.mult)
-        tt(blk(sf, 3, w=nq), blk(sm, 0, w=nq), blk(st, 0, w=nq), AL.mult)
+            act(mu, blk(sm, 0, EDG), AF.Relu, 2.0, -12.0, (7.0, EQ, 2.0, AL.mult))
+        ts(blk(sm, 0), blk(sm, 0), 4.0, AL.is_lt, 2.0, AL.mult)
+        for j in range(nq):
+            tt(blk(sf, 3 + j), blk(sm, 0), blk(st, j), AL.mult)
         pc = bank(h)
         mm([(rb(pc, j), [(Ey, I32) if j else (yh, I), (blk(sf, 3 + j), I32)]) for j in range(nq)])
-        aff(ap(si, S(0, 128 * nq)), rb(pc, 0, nq))
+        aff(ap(si, S(256, 384)), rb(pc, 0))
+        if not last:
+            ts(ap(si, S(0, 128)), rb(pc, 1), RNDE, AL.add, -RNDE, AL.add)
+            tt(ap(si, S(128, 256)), rb(pc, 1), ap(si, S(0, 128)), AL.subtract)
         row = lambda j, u, a: ap("tb", S(TB[2 * h + u] + PW * a, TB[2 * h + u] + PW * (a + 16)), p=S(j, 128, 16))
         for u in range(2):
-            dmas([(row(j, u, 1 - j % 2), ap(si, S(128 * (j // 2) + u * PW, 128 * (j // 2) + (u + 1) * PW))) for j in range(2 * nq)], 1024 * nq * PW)
+            dmas([(row(j, u, 1 - j % 2), ap(si, S(128 * (j // 2) + u * PW, 128 * (j // 2) + (u + 1) * PW))) for j in range(4 * last, 6)], 1024 * nq * PW)
         er = lambda j, n=1: ap(sm, S(j, j + n), ALLP)
-        on16, ove = ap("cb", 8, ALLP), blk(sh, 2, EDG)
-        lp = [(I, blk(sh, 1, EDG)), (lb, Ib(8.0, EDG)), (Ib(8.0), ove)]
+        on16, pe = ap("cb", 8, ALLP), ap(ed, S(64, 80))
+        tt(pe, blk(sf, 1, EDG), blk(sh, 3, EDG), AL.mult)
+        lp = [(lb, Ib(8.0, EDG)), (Ib(-1.0), blk(sh, 1, EDG)), (Ib(-2.0), blk(sh, 2, EDG)), (I, on16), (Ib(8.0), ove)]
         if not last:
+            tt(ap("ue" + H, ALLP, EDG), pe, blk(st, 2, EDG), AL.add)
+            for j, k in ((0, 15), (1, 0)):
+                aff(ap("sb" + H, j, S(0, 128)), c("ld", k), 0.125)
             mm([(er(16 + j), [(I, on16), (Ib(-2.0), ove), (Ib(-1.0), mu)]) for j in range(2)] + [(er(18 + j), [(Ib(2.0), ove), (I, mu)]) for j in range(2)]
                + [(er(20), lp + [(Ib(-4.0), mu)])] + [(er(21 + j), [(I, on16), (Ib(-1.0), mu)]) for j in range(2)])
             for j in range(2):
                 tt(ap(ed, S(32 * j, 32 * j + 32)), er(16 + 2 * j, 2), blk(st, 0, EDG, 2), AL.mult)
             tt(ap(ed, S(96, 128)), er(21, 2), ap(ed, S(96, 128)), AL.mult)
             aff(blk(sg, 0, EDG), er(20), 2.0)
-            mm([(er(24, 4), [(I32, ap(ed, S(0, 64))), (If(0.5), blk(sf, 2, EDG), er(24)), (I32, blk(st, 2, EDG, 2), er(26, 2)), (If(-0.5), blk(st, 3, EDG), er(25))])])
+            mm([(er(24, 4), [(I32, ap(ed, S(0, 64))), (If(0.5), pe, er(24)), (I32, blk(st, 2, EDG, 2), er(26, 2)), (If(-0.5), blk(st, 3, EDG), er(25))])])
             aff(ap(st, ALLP, EDG), er(24, 4))
-            for j, k in ((0, 15), (1, 0)):
-                aff(ap("sb" + H, S(144 * j, 144 * j + 128)), c("ld", k), eng="G")
         else:
             mm([(er(16), [(I, on16), (Ib(-2.0), ove)]), (er(20), lp + [(Ib(-4.0), on16)])])
             tt(ap(ed, S(0, 16)), er(16), blk(st, 0, EDG), AL.mult)
             tt(blk(sg, 0, EDG), er(20), ap(ed, S(112, 128)), AL.mult)
-            mm([(er(24), [(I32, ap(ed, S(0, 16))), (If(0.5), blk(sf, 2, EDG))]),
-                (er(25), [(I32, blk(st, 0, EDG)), (If(0.5), blk(sf, 2, EDG)), (I32, blk(st, 2, EDG))])])
+            mm([(er(24), [(I32, ap(ed, S(0, 16))), (If(0.5), pe)]), (er(25), [(I32, blk(st, 0, EDG)), (If(0.5), pe), (I32, blk(st, 2, EDG))])])
             tt(blk(st, 0, EDG), er(24), ap(ed, S(96, 112)), AL.mult)
             aff(blk(st, 2, EDG), er(25))
         zc = lambda k: ap("zz", S(15 - k, 143 - k))
@@ -493,49 +540,53 @@ def build():
         sn = lambda p0, k, n=1: ap("g16" + H, S(16 * p0 + PW * k, 16 * p0 + PW * (k + n)))
 
         def hops(a):
-            pd, pp, x = ap(bank(h), ALLP, ALLP), S(a, a + 32), "ld" + H
-            tm = [(Ib(-1.0), fl(x, p=pp))]
-            if a % 64:
-                tm += [(I, ap(x, S(16 * a + 1, 16 * a + 509)), ap(pd[0], S(0, 127), ALLP)), (I, ap(x, S(16 * a + 509, 16 * a + 512)), ap(pd[0], 127, S(0, 3)))]
-            else:
-                tm.append((I, fl(x, p=pp, shift=1)))
+            pd, pp, tm = ap(bank(h), ALLP, ALLP), S(a, a + 32), []
+            for x, w0, w1 in (("ld" + H, Ib(-1.0), I),):
+                tm.append((w0, fl(x, p=pp)))
+                if a % HB == HB - 32:
+                    tm += [(w1, ap(x, S(16 * a + 1, 16 * a + 509)), ap(pd[0], S(0, 127), ALLP)), (w1, ap(x, S(16 * a + 509, 16 * a + 512)), ap(pd[0], 127, S(0, 3)))]
+                else:
+                    tm.append((w1, fl(x, p=pp, shift=1)))
             mm([(pd, tm)])
-            act(c("t16", p=pp), pd, AF.Abs, 8.0)
+            act(c("t16", p=pp), pd, AF.Abs, 1.0 / 128)
 
         def lengths(p0):
             ph = part(sm, 0, p0)
             mm([(ph, [(zc(k), c("t16", k, S(p0, p0 + PW))) for k in range(15)])])
-            aff(part(sh, 4, p0), ph)
+            ts(part(sh, 4, p0), ph, RND, AL.add, -RND, AL.add)
             tt(part(sh, 5, p0), ph, part(sh, 4, p0), AL.subtract)
 
         def rows(p0):
-            pq, s0 = bank(h), 256 + 4 * p0
-            mm([(qb(pq, j), [(w, part(sh, 4, p0)), (w, part(sh, 5, p0))]) for j, w in enumerate((wk(4), wk(11), I, G15))])
+            pq, s0 = bank(h), 384 + 4 * p0
+            mm([(qb(pq, j), [(w, part(sh, 4 + j % 2, p0))]) for j, w in enumerate((cm(0), cm(1), G15, cm(2)))])
             aff(ap(si, S(s0, s0 + 4 * PW)), qb(pq, 0, 4))
-            dmas([(row(4 + j, p0 // PW, 1), ap(si, S(s0 + j * PW, s0 + (j + 1) * PW))) for j in range(4)], 2048 * PW)
+            dmas([(row(6 + j, p0 // PW, a), ap(si, S(s0 + b * PW, s0 + (b + 1) * PW))) for j, (a, b) in enumerate(((1, 0), (0, 0), (1, 1), (0, 1), (1, 2), (1, 3)))], 3072 * PW)
 
         def signs(p0, b):
             pk = bank(h)
             mm([(qb(pk, j), [(wk(b + j), part(sh, 4, p0)), (wk(b + j), part(sh, 5, p0))]) for j in range(7)])
-            act(sn(p0, b, 7), qb(pk, 0, 7), AF.Sign, 1.0, 0.5)
+            act(sn(p0, b, 7), qb(pk, 0, 7), AF.Sign, 1.0, 1.0 / 256)
 
         def count(p0):
-            pc, u = part(sm, 1, p0), 2 * h + p0 // PW
-            mm([(pc, [(I if last else IM, ap("cb", S(24, 28), ALLP))] + ([] if last else [(IE, part("uf" + H, 0, p0))]) + [(zc(k), sn(p0, k)) for k in range(1, 15)])])
+            pc, u, pp = part(sm, 1, p0), 2 * h + p0 // PW, S(p0, p0 + PW)
+            b = 8 * sc[1.0 / 32] + p0 // 16
+            ends = [] if last else [(ap("ue" + H, ALLP, ALLP, p=pp), ap("cb", S(b, b + 4), ALLP, p=pp))]
+            mm([(pc, [(I if last else IM, ap("cb", S(24, 28), ALLP))] + ends + [(zc(k), sn(p0, k)) for k in range(1, 15)])])
             aff(of(4, p0, p0 + PW), pc, 32.0, 448.0 + TB[u] - WIN[u][0] if last else cl(20 + u))
-            aff(ap("d8" + H, S(16 * p0, 16 * p0 + 1024)), ind(ap("tb", S(*WIN[u])), of(4, p0, p0 + PW)))
+            aff(ap("t16" + H, S(16 * p0, 16 * p0 + 1024)), ind(ap("tb", S(*WIN[u])), of(4, p0, p0 + PW)), SCL)
 
         for f, *x in ((hops, 0), (hops, 32), (lengths, 0), (hops, 64), (rows, 0), (hops, 96), (signs, 0, 1), (lengths, 64), (signs, 0, 8),
                       (rows, 64), (count, 0), (signs, 64, 1), (signs, 64, 8), (count, 64)):
             f(*x)
         if not last:
-            mm([(ap(sm, 29, S(e, 16, 2)), [(c("d8", 15 * e), SE4)]) for e in range(2)])
+            mm([(ap(sm, 29, S(e, 16, 2)), [(c("t16", 15 * e), SEH)]) for e in range(2)])
             tt(blk(st, 1, EDG), er(29), blk(st, 1, EDG), AL.add)
         for b in range(4):
             px = bank(h)
             ks = [k for k in range(4 * b, 4 * b + 4) if 0 < k < 15]
             k4, kk = S(ks[0] % 4, ks[-1] % 4 + 1), S(ks[0], ks[-1] + 1)
-            mm([(ap(px, S(0, 96 if last else 104), k % 4), [(c("d8", k), ap("xw", S(13 * (k - 1), 13 * k - last), ALLP))]) for k in ks])
+            mm([(ap(px, S(0, 96 if last else 104), k % 4), [(c("t16", k), ap("x1", S(104 * (k - 1), 104 * k - 8 * last))),
+                                                           (c("t16", k), ap("x2", S(72 * (k - 1), 72 * k)), ap(px, S(0, 72), k % 4))]) for k in ks])
             act(ap(sg, ALLP, kk), ap(px, S(0, 72), k4), AF.Sign, 1.0, 0.5)
             if last:
                 aff(ap(st, S(0, 24), kk), ap(px, S(72, 96), k4))
@@ -543,7 +594,8 @@ def build():
                 tt(ap(st, S(0, 16), kk), ap(px, S(72, 88), k4), ap(sg, S(56, 72), kk), AL.mult)
                 tt(ap(st, S(16, 32), kk), ap(px, S(88, 104), k4), ap(st, S(0, 16), kk), AL.subtract)
         if not last:
-            mm([(blk(sm, 0), [(y, I32), (hz, If(2.0))]), (blk(sm, 1), [(y, I32)])])
+            aff(yh, y, eng="DAG")
+            mm([(blk(sm, 0), [(hz, If(2.0)), (yh, I)]), (blk(sm, 1), [(yh, I)])])
             aff(of(0, 0, 256), blk(sm, 0, w=2), 1.0, OFF)
             pl = rb(bank(h), 0)
             mm([(pl, [(blk(sg, m), Ib(1.0 / 16 if m < 7 else -7.0 / 16)) for m in range(8)])])
@@ -555,13 +607,14 @@ def build():
             dma(ap("yb", S(128 * h, 128 * h + 128)), blk(sf, 1), 65536, "A")
             pl = rb(bank(h), 0)
             mm([(pl, [(blk(sg, m), Ib(0.5)) for m in range(8)])])
-            aff(blk(sf, 8), pl, 1.0, 4.0)
-            dma(ap("yl", S(128 * h, 128 * h + 128)), blk(sf, 8), 65536)
+            aff(blk(sf, 5), pl, 1.0, 4.0)
+            dma(ap("yl", S(128 * h, 128 * h + 128)), blk(sf, 5), 65536)
 
     for h in range(2):
         first(h)
     table()
     for r in range(RO):
+        cur[1] = r
         for h in range(2):
             step1(h, r)
         if r == 0:

@@ -6,11 +6,13 @@ AL = AluOpType
 AF = ActivationFunctionType
 W, RO = 3072, 3
 HS = 272
-GC = 1024
+TWO, FOUR = (0, 1024, 2048), (0, 512, 1024, 1536, 2048)
+GC = {"va": (0, 512, 1024, 2048), "va+": (0, 512, 1024, 2048), "ld": TWO, "t1": FOUR, "g1": TWO, "rw+": FOUR, "tb": (0, 512, 1024)}
 PW = 64
 NPR = 6
-HB = 64
-GA = 0
+HB = 32
+TH = 2
+GD, GY = 1024, 1024
 GB = 1024
 RND, RNDE = 1.5 * 2 ** 23, 1.5 * 2 ** 33
 OFF = 1536.0
@@ -18,29 +20,29 @@ TB = [1088, 0, 5248, 6336]
 WIN = [(1088, 5248), (0, 5248), (2176, 6336), (2176, 7424)]
 CY, PCY, GCY, LAT = 0.9, 0.42, 1.56, 140.0
 STARTS = [(a, b) for a in (10000.0, 14000.0, 18000.0, 22000.0) for b in (1.15, 1.3, 1.45)]
-PACES = [(1.0, 1.0, 1.0, 1.0), (1.0, 1.0, 1.1, 1.2), (1.2, 1.15, 1.0, 1.0), (1.0, 0.8, 1.05, 0.8)]
-EFFORT = [400, 8, 3, 700, 60, 300, 0]
+PACES = [(1.0, 1.0, 1.0, 1.0), (1.0, 1.3, 1.0, 1.2), (1.0, 0.72, 1.05, 0.8), (1.2, 1.15, 1.0, 1.0), (1.0, 1.0, 1.1, 1.5), (1.3, 1.0, 1.3, 1.0)]
+EFFORT = [300, 4, 4, 200, 36, 200, 1]
 
 SCRATCH = {
-    "vt": ("sbuf", [128, W], "float32"), "uw": ("sbuf", [128, W + 4096], "float32"), "xb": ("sbuf", [128, 2 * W], "bfloat16"),
+    "vt": ("sbuf", [128, W], "float32"), "uw": ("sbuf", [128, W + 8192], "float32"), "xb": ("sbuf", [128, 2 * W], "bfloat16"),
     "nt": ("sbuf", [128, W], "int32"), "tb": ("sbuf", [128, W + 4 * 1088], "float32"),
-    "bk": ("sbuf", [128, 2048], "bfloat16"), "ct": ("sbuf", [128, 14, 13], "bfloat16"), "c2": ("sbuf", [128, 14, 9], "bfloat16"),
+    "bk": ("sbuf", [128, 2048], "bfloat16"), "ct": ("sbuf", [128, 14, 15], "bfloat16"), "c2": ("sbuf", [128, 14, 9], "bfloat16"),
     "cb": ("sbuf", [128, 144, 16], "bfloat16"), "zz": ("sbuf", [128, 144], "bfloat16"), "c32": ("sbuf", [128, 6, 128], "float32"),
-    "col": ("sbuf", [128, 112], "float32"), "coli": ("sbuf", [128, 8], "int32"), "se": ("sbuf", [128, 16], "bfloat16"),
+    "cf": ("sbuf", [128, 336], "bfloat16"), "col": ("sbuf", [128, 88], "float32"), "coli": ("sbuf", [128, 8], "int32"), "se": ("sbuf", [128, 16], "bfloat16"),
 }
-BASE = {"d80": ("uw", 0), "ut": ("uw", 2048), "d81": ("uw", 2048 + W), "xt": ("xb", 0), "gt": ("xb", W),
-        "gd0": ("tb", 0), "gd1": ("tb", 5248), "wk": ("xb", 0), "x1": ("xb", 1792), "x2": ("xb", 3248), "cm": ("xb", 4256)}
+BASE = {"va0": ("uw", 0), "d80": ("uw", 2048), "ut": ("uw", 4096), "d81": ("uw", 4096 + W), "va1": ("uw", 6144 + W), "xt": ("xb", 0), "gt": ("xb", W),
+        "gd0": ("tb", 0), "gd1": ("tb", 5248), "wk": ("xb", 0), "x1": ("xb", 1792), "x2": ("xb", 3472), "cm": ("xb", 4480)}
 for _i in range(NPR):
     SCRATCH["pr%d" % _i] = ("sbuf", [128, 128, 4], "float32")
 for _h in range(2):
-    for _n, _s, _t in (("va", [2048], "float32"), ("di", [2048], "int32"), ("rw", [2048 + RO * HS], "float32"),
+    for _n, _s, _t in (("di", [2048], "int32"), ("rw", [2048 + RO * HS], "float32"),
                        ("g16", [2048], "float16"), ("t16", [2048], "float16"), ("ld", [2048], "float16"), ("y16", [2048], "float16"),
-                       ("si", [896], "float32"), ("of", [640], "uint16"), ("st", [32, 16], "float32"), ("sf", [48, 16], "float32"),
-                       ("sh", [48, 16], "bfloat16"), ("yh", [8, 16], "float16"), ("uf", [8, 16], "float16"), ("ue", [8, 16], "float16"),
+                       ("si", [896], "float32"), ("of", [640], "uint16"), ("st", [32, 16], "float32"), ("sf", [40, 16], "float32"),
+                       ("sh", [48, 16], "bfloat16"), ("yh", [16, 16], "float16"), ("uf", [8, 16], "float16"), ("ue", [8, 16], "float16"), ("en", [8, 18], "float32"),
                        ("sg", [72, 16], "bfloat16"), ("ed", [128], "float32"), ("eb", [32], "bfloat16"), ("sb", [2, 136], "float32")):
         SCRATCH["%s%d" % (_n, _h)] = ("sbuf", [128] + _s, _t)
     for _i in range(3):
-        SCRATCH["ps%d" % (4 * _h + _i)] = ("psum", [128, 128, 4], "float32")
+        SCRATCH["ps%d" % (4 * _h + _i)] = ("psum", [128, 512], "float32")
     SCRATCH["ps%d" % (4 * _h + 3)] = ("psum", [128, 32, 16], "float32")
 NDMA = 72
 SEMAPHORES = ["cD", "cA", "cP", "cG"] + ["dm%d" % i for i in range(NDMA)] \
@@ -135,7 +137,9 @@ def build():
         add("D", {"D": vcost(nel(a), k)}, [a, s1, s2], [out], lambda e: [tsf(out, a, s1, op0, s2, op1)])
 
     def mset(out, v):
-        add("D", {"D": vcost(nel(out), 0.5 if two(out) else 1)}, [], [out], lambda e: [lambda g, T: g.vector.memset(real(T, out), v)])
+        fs = {"D": lambda g, T: g.vector.memset(real(T, out), v),
+              "G": lambda g, T: g.iota(real(T, out), [[0, nel(out)]], int(v), 0, allow_small_or_imprecise_dtypes=True)}
+        add("GD", {"D": vcost(nel(out), 0.5 if two(out) else 1), "G": 130 + 2 * nel(out) * CY}, [], [out], lambda e: [fs[e]])
 
     def act(out, a, fn, scale=1.0, bias=0.0, alt=None, eng="DA"):
         k = GCY if a[0] == "IND" else 1
@@ -163,7 +167,7 @@ def build():
                 o = tm[2] if len(tm) > 2 else out
                 cost += max(64, nel(r)) * (1 if two(l) else 4) * PCY
                 rd += [l, r]
-                fs.append(lambda g, T, o=o, l=l, r=r, a=(begin and i == 0), b=(end and i == len(terms) - 1): g.tensor.matmul(real(T, o), real(T, l), real(T, r), a, b))
+                fs.append(lambda g, T, o=o, l=l, r=r, a=(i == 0 and (begin or len(wr) > 1)), b=(end and i == len(terms) - 1): g.tensor.matmul(real(T, o), real(T, l), real(T, r), a, b))
         add("P", {"P": cost}, rd, wr, lambda e: fs)
 
     def iota(out, pat, base, cm):
@@ -196,7 +200,7 @@ def build():
     EQ, GE = AL.is_equal, AL.is_ge
     MID, EDG = S(1, 15), S(0, 16, 15)
     blk = lambda n, j, k=ALLP, w=1: ap(n, S(8 * j, 8 * (j + w)), k)
-    rb = lambda n, j, w=1: ap(n, S(32 * j, 32 * (j + w)), ALLP)
+    rb = lambda n, j, w=1: ap(n, S(128 * j, 128 * (j + w)))
     pin = lambda j, h: ap("di0", S(256 * j + 128 * h, 256 * j + 128 * h + 128))
     dma(ap("di0", S(0, 256)), ap("pa", ALLP), 131072)
     dma(ap("di0", S(256, 512)), ap("pb", ALLP), 131072, "A")
@@ -204,13 +208,13 @@ def build():
     for a in range(0, W, 1024):
         dma(ap("xt", S(a, a + 1024)), ap("xrec", S(a, a + 1024)), 400000 + 512 * (a + 1024), "A")
         dma(ap("gt", S(a, a + 1024)), ap("grec", S(a, a + 1024)), 400000 + 512 * (a + 1024))
-    mset(ap("tb", S(2176, 4224)), 0)
-    iota(ap("tb", S(4224, 5248)), [[0, 1024]], 0, 0)
+    for a in range(2176, 5248, 768):
+        mset(ap("tb", S(a, a + 768)), 0)
     ee = lambda j: ap("va1" if j else "di1", S(192 * j, 192 * j + 192))
     dma(ee(0), ap("erec", ALLP), 98304, "A")
     ts(ee(1), ee(0), RNDE, AL.add, -RNDE, AL.add)
     tt(ee(2), ee(0), ee(1), AL.subtract)
-    dmas([(ap("tb", S(2176, 5248), p=S(2 * j, 128, 16)), ee(1 + j)) for j in range(2)], 98304 * 4)
+    dmas([(ap("tb", S(2176, 5248), p=S(2 * j, 128, 16)), ee(1 + j)) for j in range(2)], 98304 * 2)
     dma(ap("nt", ALLP), ap("nbr", ALLP), 1572864 * 2)
     ops[-1]["reads"] += [ap("gt", S(1024, 1032)), ap("tb", S(2176, 2184))]
     cb = lambda j, k=ALLP: blk("cb", j, k)
@@ -221,13 +225,21 @@ def build():
     mset(ONE32, 1.0)
     sel(I, ONE, [[-1, 128]], EQ, 0.0, 0, 1)
     sel(I32, ONE32, [[-1, 128]], EQ, 0.0, 0, 1)
+    iota(cb(16), [[0, 128]], 0, 0)
+
+    def diag(out, v):
+        aff(out, I, v, eng="DAG")
+        plain = ops[-1]["emit"]
+        ops[-1]["reads"].append(cb(16))
+        ops[-1]["emit"] = lambda e: plain(e) if e != "G" else [lambda g, T: g.affine_select(real(T, out), real(T, cb(16)), [[-1, 128]], AL.not_equal, v, 0, 1)]
+
     sc, sf32 = {}, {}
-    for j, v in enumerate((1.0 / 2048, -1.0, -2.0, 2.0, 1.0 / 16, -7.0 / 16, 8.0, 0.5, -4.0, 1.0 / 32)):
+    for j, v in enumerate((1.0 / 2048, -1.0, -2.0, 2.0, 1.0 / 16, -7.0 / 16, 8.0, 0.5, -4.0, 1.0 / 32, -65536.0)):
         sc[v] = 5 + j
-        aff(cb(5 + j), I, v)
+        diag(cb(5 + j), v)
     for j, v in enumerate((-1.0, 2.0, -0.5, 0.5)):
         sf32[v] = ap("c32", 2 + j, ALLP)
-        aff(sf32[v], I32, v)
+        diag(sf32[v], v)
     Ib = lambda v, k=ALLP: cb(sc[v], k)
     If = lambda v: sf32[v]
     cl = lambda a, n=1: ap("col", S(a, a + n))
@@ -272,7 +284,7 @@ def build():
     def table():
         cur[0] = None
         for a in range(0, W, 512):
-            pv = ap(bank(a // 512 % 2), ALLP, ALLP)
+            pv = ap(bank(a // 512 % 2), ALLP)
             mm([(pv, [(I, ap("xt", S(a, a + 512))), (Ib(1.0 / 2048), ap("gt", S(a, a + 512)))])])
             aff(ap("vt", S(a, a + 512)), pv, 1.0, 128.125)
         for a in range(0, W, 1024):
@@ -291,8 +303,8 @@ def build():
         aff(cm(4), cm(3), -1.0)
         iota(cm(5), [[0, 8], [1, 16]], 0, 0)
         sel(cm(5), cm(5), [[0, 128]], EQ, 1.0, -1, 1)
-        sel(cm(6), cm(5), [[0, 128]], AL.not_equal, W - OFF, -2, 1)
-        sel(cm(5), cm(5), [[0, 128]], AL.not_equal, -2048 - OFF, -2, 1)
+        for j, v in ((6, W - OFF), (7, -4096 - OFF), (8, W + 2048 - OFF), (5, -2048 - OFF)):
+            sel(cm(j), cm(5), [[0, 128]], AL.not_equal, v, -2, 1)
         for u in range(4):
             a, b = 448.0 + TB[u] - WIN[u][0], OFF + 2176 - WIN[u][0]
             aff(cl(20 + u), cl(24), b - a, a)
@@ -303,18 +315,19 @@ def build():
         sel(cm(0), G15, [[16, 8], [1, 16]], AL.is_gt, 0.0, 0, -1)
         aff(cm(1), cm(0), 128.0)
         aff(cm(2), G15, 128.0)
-        wk = ap("wk", S(0, 1792))
-        iota(wk, [[1, 14], [0, 128]], 1, 0)
+        iota(cm(9), [[0, 128]], 16, 0)
+        sel(cm(9), cm(9), [[-16, 8], [-1, 16]], GE, -16.0, 0, 1)
+        sel(cm(9), cm(9), [[-16, 8], [0, 16]], GE, 0.0, 0, 1)
+        sel(cm(9), cm(9), [[16, 8], [0, 16]], GE, 0.0, 14, -1)
+        iota(ap("cm", S(9 * 128 + 15, 1280, 16)), [[0, 8]], 0, 0)
         for k in range(1, 15):
-            b = ap("wk", S(128 * (k - 1), 128 * k))
-            sel(b, b, [[-16, 8], [-1, 16]], GE, float(k - 15), 0, 1)
-        sel(wk, wk, [[0, 14], [-16, 8], [0, 16]], GE, 0.0, 0, 1)
-        sel(wk, wk, [[0, 14], [16, 8], [0, 16]], GE, 0.0, 14, -1)
-        iota(ap("wk", S(15, 1792, 16)), [[0, 112]], 0, 0)
+            ts(ap("wk", S(128 * (k - 1), 128 * k)), cm(9), float(k), AL.min, float(k - 15), AL.max)
         iota(cl(56, 12), [[1, 12]], 0, 0)
         ts(cl(56, 12), cl(56, 12), cl(12), EQ)
-        iota(ap("ct", ALLP, S(0, 8)), [[0, 14], [30, 8]], 15, 0)
-        iota(ap("ct", ALLP, S(8, 9)), [[0, 14]], 225, 0)
+        iota(ap("ct", ALLP, S(2, 10)), [[0, 14], [30, 8]], 15, 0)
+        iota(ap("ct", ALLP, S(10, 11)), [[0, 14]], 225, 0)
+        for j in range(2):
+            aff(ap("ct", ALLP, j), ap("c32", 1, S(0, 14)), cl(60 + j))
         iota(ap("c2", ALLP, ALLP), [[16, 14], [0, 9]], 16, 0)
         aff(cl(56, 2), cl(56, 2), 16.0)
         aff(cl(58, 4), cl(58, 4), 0.5)
@@ -322,24 +335,23 @@ def build():
         tt(cl(74, 6), ap("col", S(56, 68, 2)), ap("col", S(57, 68, 2)), AL.add)
         tt(cl(80), cl(71), cl(72), AL.add)
         ts(cl(81), cl(62), cl(64), AL.add, -240.0, AL.mult)
-        x = ap("ct", ALLP, S(0, 9))
+        x = ap("ct", ALLP, S(2, 11))
         aff(x, x, cl(80), cl(81))
         aff(ap("c2", ALLP, ALLP), ap("c2", ALLP, ALLP), cl(79))
         tt(x, x, ap("c2", ALLP, ALLP), AL.add)
         ts(cl(82), cl(68), cl(69), AL.add, -1.0, AL.mult)
         for j, (a, b) in enumerate(((-1.0, cl(70)), (1.0, cl(82)), (1.0, cl(76)), (cl(74), cl(75)))):
             if j == 3:
-                aff(ap("ct", ALLP, 12), ap("c32", 1, S(0, 14)), a, b)
+                aff(ap("ct", ALLP, 14), ap("c32", 1, S(0, 14)), a, b)
             else:
-                ts(ap("ct", ALLP, 9 + j), ap("c32", 1, S(0, 14)), b, AL.mult, a, AL.mult)
+                ts(ap("ct", ALLP, 11 + j), ap("c32", 1, S(0, 14)), b, AL.mult, a, AL.mult)
         ts(cl(83), cl(77), cl(66), AL.add, 128.0, AL.mult)
         ts(cl(83), cl(12), 6.0, AL.is_lt, cl(83), AL.add)
         tt(cl(84), cl(78), cl(67), AL.add)
-        aff(cl(88, 8), GS, cl(83))
-        aff(cl(96, 8), GS, cl(84))
+        aff(ap("cf", S(0, 210)), ap("ct", ALLP, ALLP), cl(83))
+        aff(ap("cf", S(210, 336)), x, cl(84))
         for j in range(8):
-            aff(ap("x1", S(j, 1456, 8)), ap("ct", ALLP, ALLP), cl(88 + j))
-            aff(ap("x2", S(j, 1008, 8)), x, cl(96 + j))
+            aff(ap("x1", S(j, 2688, 8)), ap("cf", ALLP), cl(32 + j))
         for h in range(2):
             aff(ap("ue%d" % h, ALLP, ALLP), ONE, 0.0)
             iota(ap("sg%d" % h, ALLP, EDG), [[0, 144]], 0, 0)
@@ -353,13 +365,14 @@ def build():
 
     def gathers(dst, win, oj, h, scale=1.0, bias=0.0):
         H, c, of, sm = names(h)
-        for a in range(0, 2048, GC):
-            aff(ap(dst, S(a, a + GC)), ind(win, of(oj, a // 16, (a + GC) // 16)), scale, bias)
+        cut = TWO if cur[1] < 0 else GC[dst[:2]]
+        for a, b in zip(cut, cut[1:]):
+            aff(ap(dst, S(a, b)), ind(win, of(oj, a // 16, b // 16)), scale, bias)
 
     def gather_add(dst, win, oj, other, h, op=AL.add):
         H, c, of, sm = names(h)
-        for a in range(0, 2048, GC):
-            tt(ap(dst, S(a, a + GC)), ind(win, of(oj, a // 16, (a + GC) // 16)), ap(other, S(a, a + GC)), op)
+        for a, b in zip(GC[other[:2] + "+"], GC[other[:2] + "+"][1:]):
+            tt(ap(dst, S(a, b)), ind(win, of(oj, a // 16, b // 16)), ap(other, S(a, b)), op)
 
     VT, NT, ET = ap("vt", ALLP), ap("nt", ALLP), ap("tb", S(2176, 5248))
 
@@ -367,20 +380,24 @@ def build():
         cur[0] = h
         H, c, of, sm = names(h)
         st, sf, sh, ed = "st" + H, "sf" + H, "sh" + H, "ed" + H
-        f, da, fd, z, y = [blk(sf, j) for j in range(5)]
-        ts(f, pin(2, h), 8.0, EQ)
-        tt(da, pin(1, h), pin(0, h), AL.subtract)
-        tt(fd, f, da, AL.mult)
-        tt(z, pin(0, h), fd, AL.add)
-        tt(y, pin(1, h), fd, AL.subtract)
-        aff(of(0, 0, 256), blk(sf, 3, w=2))
-        ts(pin(2, h), pin(2, h), 7, AL.bitwise_and)
+        a, b, f = [ap("ld0", S(256 * j + 128 * h, 256 * j + 128 * h + 128)) for j in range(3)]
+        fd = ap("rw0", S(128 * h, 128 * h + 128))
+        if h == 0:
+            cur[0] = None
+            aff(ap("ld0", S(0, 512)), ap("di0", S(0, 512)), 1.0, -OFF)
+            ts(ap("ld0", S(512, 768)), ap("di0", S(512, 768)), 8.0, EQ)
+            mm([(blk(sm, 0, w=2), [(I, ap("ld0", S(256, 512))), (Ib(-1.0), ap("ld0", S(0, 256)))])])
+            tt(ap("rw0", S(0, 256)), blk(sm, 0, w=2), ap("ld0", S(512, 768)), AL.mult)
+            ts(ap("di0", S(512, 768)), ap("di0", S(512, 768)), 7, AL.bitwise_and)
+            cur[0] = h
+        mm([(blk(sm, 0), [(I, a), (I32, fd)]), (blk(sm, 1), [(I, b), (If(-1.0), fd)])])
+        aff(of(0, 0, 256), blk(sm, 0, w=2), 1.0, OFF)
         aff(blk(sh, 0), pin(2, h), 0.125)
         gathers("t16" + H, ET, 1, h, SCL)
         gathers("g16" + H, ET, 0, h, SCL)
-        mm([(blk(sm, 2), [(y, I32)]), (blk(sm, 0), [(z, If(0.5)), (y, If(-0.5))]), (blk(sm, 1), [(f, I32)])])
-        aff(blk(st, 2), blk(sm, 2), 1.0, -OFF)
-        aff(blk(st, 0), blk(sm, 0))
+        mm([(blk(sm, 2), [(b, I), (fd, If(-1.0))]), (blk(sm, 0), [(a, I), (b, Ib(-1.0)), (fd, If(2.0))]), (blk(sm, 1), [(f, I)])])
+        aff(blk(st, 2), blk(sm, 2))
+        aff(blk(st, 0), blk(sm, 0), 0.5)
         aff(ap(ed, S(96, 112)), blk(sm, 1, EDG), 2.0, -1.0)
         aff(ap(ed, S(112, 128)), blk(sm, 1, EDG), -4.0, 2.0)
         mm([(blk(sm, 3, k), [(c("t16", k), SEH)]) for k in range(16)])
@@ -390,14 +407,13 @@ def build():
 
     def spread(h, x, p0, a):
         pl = bank(h)
-        mm([(ap(pl, ALLP, ALLP), [(ap("bk", S(128 * (a + 2 * k), 128 * (a + 2 * k) + 128)), ap(x[0], S(x[1] + p0 // 16, x[1] + p0 // 16 + 4), ALLP),
-                                   ap(pl, S(k // 4, 128, 2), k % 4)) for k in range(8)])])
-        return ap(pl, ALLP, ALLP), dict(k=(a, 2), p=S(p0, p0 + 64))
+        mm([(ap(pl, S(k, 512, 8)), [(ap("bk", S(128 * (a + 2 * k), 128 * (a + 2 * k) + 128)), ap(x[0], S(x[1] + p0 // 16, x[1] + p0 // 16 + 4), ALLP))]) for k in range(8)])
+        return ap(pl, ALLP), dict(k=(a, 2), p=S(p0, p0 + 64))
 
     def send(h, r):
         rw, sb, a = "rw%d" % h, "sb%d" % h, 2048 + HS * r
         tr = [(ap(sb, 0, ALLP), ap(rw, S(a, a + 136))), (ap(sb, 1, ALLP), ap(rw, S(a + 136, a + HS)))]
-        i = add("G", {"G": 1000.0}, [ap(sb, ALLP, ALLP)], [], None, sem="lo%d" % (2 * r + h), inc=8, late=2500.0, send=tr, arr="ar%d" % (2 * r + h))
+        i = add("G", {"G": 1000.0}, [ap(sb, ALLP, ALLP)], [], None, sem="lo%d" % (2 * r + h), inc=8, late=2500.0 if r + h else 6000.0, send=tr, arr="ar%d" % (2 * r + h))
         add("X", {"X": 0.0}, [], [ap(rw, S(a, a + HS))], None, sem="ar%d" % (2 * r + h), inc=8, late=2000.0, after=i)
 
     def step1(h, r):
@@ -409,45 +425,44 @@ def build():
         gathers("va" + H, VT, 0, h, -1.0)
         gather_add("d8" + H, VT, 1, "va" + H, h)
         if r == 0:
-            aff(ap("yh" + H, ALLP, ALLP), y, eng="DAG")
-        pb = bank(h)
-        pq = rb(pb, 0)
-        mm([(pq, [(lb, Ib(-2.0)), (Ib(2.0), ONE)]), (rb(pb, 1), [(lb, Ib(8.0))])])
+            aff(blk("yh" + H, 0), y, eng="DAG")
+        pq = rb(bank(h), 0)
+        mm([(pq, [(lb, Ib(-2.0)), (Ib(2.0), ONE)])])
         tt(pq, pq, hE, AL.mult)
-        tt(blk(sf, 0), pq, Ey, AL.add)
-        act(blk(sh, 3), rb(pb, 1), AF.Relu, -1.0, 1.0, (0.0, EQ, 1.0, AL.mult))
-        aff(ap("sb" + H, 0, S(128, 136)), blk(sf, 0, 15), eng="DAG")
-        aff(ap("sb" + H, 1, S(128, 136)), blk(sf, 0, 0), eng="DAG")
+        en = lambda k: ap("en" + H, ALLP, k)
+        tt(en(S(1, 17)), pq, Ey, AL.add)
+        aff(ap("sb" + H, 0, S(128, 136)), en(16), eng="DAG")
+        aff(ap("sb" + H, 1, S(128, 136)), en(1), eng="DAG")
+        if r == 0:
+            pb = bank(h)
+            mm([(rb(pb, j), [(ap("bk", S(128 * k, 128 * k + 128)), lb)]) for j, k in ((0, 15), (1, 0))])
+            for j, k in ((0, 15), (1, 0)):
+                tt(rb(pb, j), c("d8", k), rb(pb, j), AL.mult)
+                tt(ap("sb" + H, j, S(0, 128)), rb(pb, j), c("va", k), AL.add)
         for p0 in (0, 64):
             cols = S(16 * p0, 16 * p0 + 1024)
-            aff(ap("di" + H, cols), ap("d8" + H, cols), eng="G")
+            for a in range(16 * p0, 16 * p0 + 1024, GD):
+                aff(ap("di" + H, S(a, a + GD)), ap("d8" + H, S(a, a + GD)), eng="G")
             for a in range(2):
                 pw, ks = spread(h, (sh, 0), p0, a)
                 tt(pw, c("d8", **ks), pw, AL.mult)
                 tt(c("rw", **ks), pw, c("va", **ks), AL.add)
-            aff(ap("y16" + H, cols), ap(rw, cols), eng="DAG")
+            for a in range(16 * p0, 16 * p0 + 1024, GY):
+                aff(ap("y16" + H, S(a, a + GY)), ap(rw, S(a, a + GY)), eng="DAG")
             for a in range(2):
-                pw, ks = ap(bank(h), ALLP, ALLP), dict(k=(a, 2), p=S(p0, p0 + 64))
-                mm([(pw, [(Ib(-1.0), c("y16", **ks))])])
-                if a + p0 // 32 < GA:
-                    tt(pw, pw, c("rw", **ks), AL.add)
-                    aff(c("g16", **ks), pw)
-                else:
-                    tt(c("g16", **ks), pw, c("rw", **ks), AL.add)
-                    pw = ap(bank(h), ALLP, ALLP)
-                    mm([(pw, [(I, c("g16", **ks))])])
-                tt(c("gd", **ks), pw, c("di", **ks), AL.mult)
-        if r == 0:
-            aff(ap("sb" + H, 0, S(0, 128)), c("rw", 15), eng="DAG")
-            aff(ap("sb" + H, 1, S(0, 128)), c("rw", 0), eng="DAG")
+                pw, pg, pp = ap(bank(h), ALLP), ap(bank(h), ALLP), S(p0 + 32 * a, p0 + 32 * a + 32)
+                mm([(pw, [(Ib(-1.0), c("y16", p=pp))])])
+                tt(c("g16", p=pp), pw, c("rw", p=pp), AL.add)
+                mm([(pg, [(I, c("g16", p=pp))])])
+                tt(c("gd", p=pp), pg, c("di", p=pp), AL.mult)
         send(h, r)
-        dma(ap("d8" + H, S(0, 2048)), ap("va" + H, ALLP), 1048576, "G")
+        dma(ap("d8" + H, S(0, 2048)), ap("va" + H, S(0, 2048)), 1048576, "G")
         gathers("ld" + H, NT, 0, h, 1.0, -OFF)
         sl = 2048 + HS * r
         mo = lambda k=ALLP: ap("uf" + H, ALLP, k)
-        tt(mo(MID), blk(sf, 0, S(2, 16)), blk(sf, 0, S(0, 14)), GE)
-        tt(mo(0), blk(sf, 0, 1), ap(rw, S(sl + 128, sl + 136)), GE)
-        tt(mo(15), ap(rw, S(sl + 264, sl + 272)), blk(sf, 0, 14), GE)
+        aff(en(0), ap(rw, S(sl + 128, sl + 136)), eng="DAG")
+        aff(en(17), ap(rw, S(sl + 264, sl + 272)), eng="DAG")
+        tt(mo(), en(S(2, 18)), en(S(0, 16)), GE)
         aff(mo(0), mo(0), cl(r), 512.0)
         aff(mo(15), mo(15), cl(3 + r), -512.0)
         po = bank(h)
@@ -461,9 +476,10 @@ def build():
             aff(ap(rw, S(a, a + GB)), ap("y16" + H, S(a, a + GB)), -8.0)
             dma(ap(rw, S(a, a + GB)), ap("va" + H, S(a, a + GB)), 512 * GB, "G")
         for a in range(4):
-            pt, ks = ap(bank(h), ALLP, ALLP), (a, 4)
+            pt, ks = ap(bank(h), ALLP), (a, 4)
             ptd, pgt, ptt = newpr(), newpr(), newpr()
-            mm([(pt, [(I, c("t16", ks)), (Ib(-1.0), c("y16", ks))])])
+            mm([(pt, [(Ib(-1.0), c("y16", ks))])], end=False)
+            mm([(pt, [(I, c("t16", ks))])], begin=False)
             act(ap(ptt, ALLP, ALLP), pt, AF.Square)
             tt(ap(ptd, ALLP, ALLP), c("di", ks), pt, AL.mult)
             tt(ap(pgt, ALLP, ALLP), c("g16", ks), pt, AL.mult)
@@ -477,22 +493,24 @@ def build():
         last = r == RO - 1
         nq = 1 if last else 2
         hz, hE, y, Ey = [blk(st, j) for j in range(4)]
-        lb, eq, dn, m0 = [blk(sh, j) for j in range(4)]
-        yh = ap("yh" + H, ALLP, ALLP)
+        lb, eq, dn = [blk(sh, j) for j in range(3)]
+        yh = blk("yh" + H, 0)
         pn, pw, lh = bank(h), bank(h), lambda j: cm(j, S(0, 3))
-        mm([(rb(pn, 0), [(lh(4), lh(5 + h))] + [(c("ld", k), ap("cb", S(0, 8), k), ap(pn, S(k // 4, 32, 4), k % 4)) for k in range(16)])])
-        tt(blk(sf, 5), rb(pn, 0), m0, AL.mult)
-        mm([(rb(pw, 0), [(If(2.0), hz)]), (rb(pw, 1), [(lh(3), lh(5 + h)), (Ib(-1.0), yh), (I32, blk(sf, 5))])])
+        mm([(rb(pn, 0), [(lh(4 - h), lh(5 + h)), (lb, Ib(-65536.0))] + [(c("ld", k), Ib(-1.0, k) if h else cb(0, k), ap(pn, S(k, 128, 16))) for k in range(16)])])
+        act(blk(sf, 0), rb(pn, 0), AF.Relu, 1.0, 0.0, (0.0, AL.max, 0.0, AL.add))
+        mm([(rb(pw, 0), [(lh(3), lh(7 + h)), (Ib(-1.0), yh)]), (rb(pw, 1), [(lh(3), lh(5 + h)), (Ib(-1.0), yh), (If(-1.0) if h else I32, blk(sf, 0))])])
         aff(blk(sf, 2, w=2), blk(sm, 2, w=2))
         tt(blk(sf, 4), blk(sm, 0), blk(sf, 2), AL.mult)
         tt(blk(sm, 1), blk(sm, 1), blk(sf, 3), AL.mult)
-        tt(eq, blk(sm, 1), blk(sf, 4), EQ)
         tt(dn, blk(sm, 1), blk(sf, 4), AL.is_gt)
-        tt(blk(sf, 0, w=2), rb(pw, 0, 2), blk(sh, 1, w=2), AL.mult)
+        tt(blk(sf, 1), rb(pw, 1), dn, AL.mult)
+        tt(eq, blk(sm, 1), blk(sf, 4), EQ)
+        tt(blk(sf, 0), rb(pw, 0), eq, AL.mult)
         pu = bank(h)
-        mm([(rb(pu, 0), [(yh, I), (blk(sf, 0), I32), (blk(sf, 1), I32)])])
-        aff(of(3), rb(pu, 0), 1.0, OFF + 2048 * (1 - h))
-        gather_add("ld" + H, ap("uw", S(2048 * h, 2048 * h + 2048 + W)), 3, "rw" + H, h, AL.subtract)
+        mm([(rb(pu, 0), [(yh, I), (blk(sf, 1), I32)])], end=False)
+        mm([(rb(pu, 0), [(blk(sf, 0), I32)])], begin=False)
+        aff(of(3), rb(pu, 0), 1.0, OFF + 4096 * (1 - h))
+        gather_add("ld" + H, ap("uw", S(4096 * h, 4096 * h + 4096 + W)), 3, "rw" + H, h, AL.subtract)
         mm([(blk(sm, j), [(lb, Ib(8.0)), (Ib(-1.0), eq), (Ib(-2.0), dn)]) for j in range(1)])
         mu, ove = ap("eb" + H, S(0, 16)), ap("eb" + H, S(16, 32))
         act(ove, blk(sm, 0, EDG), AF.Relu, -1.0, -1.0, (-2.0, EQ, 1.0, AL.mult))
@@ -502,7 +520,9 @@ def build():
         for j in range(nq):
             tt(blk(sf, 3 + j), blk(sm, 0), blk(st, j), AL.mult)
         pc = bank(h)
-        mm([(rb(pc, j), [(Ey, I32) if j else (yh, I), (blk(sf, 3 + j), I32)]) for j in range(nq)])
+        if not last:
+            mm([(rb(pc, 1), [(Ey, I32)])], end=False)
+        mm([(rb(pc, 1), [(blk(sf, 4), I32)])] * (nq - 1) + [(rb(pc, 0), [(yh, I), (blk(sf, 3), I32)])], begin=last)
         aff(ap(si, S(256, 384)), rb(pc, 0))
         if not last:
             ts(ap(si, S(0, 128)), rb(pc, 1), RNDE, AL.add, -RNDE, AL.add)
@@ -510,9 +530,10 @@ def build():
         row = lambda j, u, a: ap("tb", S(TB[2 * h + u] + PW * a, TB[2 * h + u] + PW * (a + 16)), p=S(j, 128, 16))
         for u in range(2):
             dmas([(row(j, u, 1 - j % 2), ap(si, S(128 * (j // 2) + u * PW, 128 * (j // 2) + (u + 1) * PW))) for j in range(4 * last, 6)], 1024 * nq * PW)
-        er = lambda j, n=1: ap(sm, S(j, j + n), ALLP)
+        pb = bank(h)
+        er = lambda j, n=1: ap(pb, S(16 * j, 16 * (j + n))) if j < 29 else ap(sm, S(j, j + n), ALLP)
         on16, pe = ap("cb", 8, ALLP), ap(ed, S(64, 80))
-        tt(pe, blk(sf, 1, EDG), blk(sh, 3, EDG), AL.mult)
+        tt(pe, blk(sf, 1, EDG), ove, AL.mult)
         lp = [(lb, Ib(8.0, EDG)), (Ib(-1.0), blk(sh, 1, EDG)), (Ib(-2.0), blk(sh, 2, EDG)), (I, on16), (Ib(8.0), ove)]
         if not last:
             tt(ap("ue" + H, ALLP, EDG), pe, blk(st, 2, EDG), AL.add)
@@ -532,22 +553,17 @@ def build():
             tt(blk(sg, 0, EDG), er(20), ap(ed, S(112, 128)), AL.mult)
             mm([(er(24), [(I32, ap(ed, S(0, 16))), (If(0.5), pe)]), (er(25), [(I32, blk(st, 0, EDG)), (If(0.5), pe), (I32, blk(st, 2, EDG))])])
             tt(blk(st, 0, EDG), er(24), ap(ed, S(96, 112)), AL.mult)
-            aff(blk(st, 2, EDG), er(25))
+            for j, op in enumerate((AL.subtract, AL.add)):
+                tt(blk("yh" + H, j, EDG), er(25), blk(st, 0, EDG), op)
         zc = lambda k: ap("zz", S(15 - k, 143 - k))
         wk = lambda k: ap("wk", S(128 * (k - 1), 128 * k))
-        qb = lambda n, j, w=1: ap(n, S(16 * j, 16 * (j + w)), ALLP)
+        qb = lambda n, j, w=1: ap(n, S(64 * j, 64 * (j + w)))
         part = lambda n, j, p0: ap(n, S(8 * j + p0 // 16, 8 * j + (p0 + PW) // 16), ALLP)
         sn = lambda p0, k, n=1: ap("g16" + H, S(16 * p0 + PW * k, 16 * p0 + PW * (k + n)))
 
         def hops(a):
-            pd, pp, tm = ap(bank(h), ALLP, ALLP), S(a, a + 32), []
-            for x, w0, w1 in (("ld" + H, Ib(-1.0), I),):
-                tm.append((w0, fl(x, p=pp)))
-                if a % HB == HB - 32:
-                    tm += [(w1, ap(x, S(16 * a + 1, 16 * a + 509)), ap(pd[0], S(0, 127), ALLP)), (w1, ap(x, S(16 * a + 509, 16 * a + 512)), ap(pd[0], 127, S(0, 3)))]
-                else:
-                    tm.append((w1, fl(x, p=pp, shift=1)))
-            mm([(pd, tm)])
+            pd, pp = ap(bank(h), ALLP), S(a, a + 32)
+            mm([(pd, [(Ib(-1.0), c("ld", p=pp)), (I, ap("ld" + H, S(16 * a + 1, 16 * a + 512)), ap(pd[0], S(0, 511)))])])
             act(c("t16", p=pp), pd, AF.Abs, 1.0 / 128)
 
         def lengths(p0):
@@ -568,12 +584,13 @@ def build():
             act(sn(p0, b, 7), qb(pk, 0, 7), AF.Sign, 1.0, 1.0 / 256)
 
         def count(p0):
-            pc, u, pp = part(sm, 1, p0), 2 * h + p0 // PW, S(p0, p0 + PW)
+            pc, u, pp = part(sm, 1, p0) if p0 else qb(bank(h), 0), 2 * h + p0 // PW, S(p0, p0 + PW)
             b = 8 * sc[1.0 / 32] + p0 // 16
             ends = [] if last else [(ap("ue" + H, ALLP, ALLP, p=pp), ap("cb", S(b, b + 4), ALLP, p=pp))]
             mm([(pc, [(I if last else IM, ap("cb", S(24, 28), ALLP))] + ends + [(zc(k), sn(p0, k)) for k in range(1, 15)])])
             aff(of(4, p0, p0 + PW), pc, 32.0, 448.0 + TB[u] - WIN[u][0] if last else cl(20 + u))
-            aff(ap("t16" + H, S(16 * p0, 16 * p0 + 1024)), ind(ap("tb", S(*WIN[u])), of(4, p0, p0 + PW)), SCL)
+            for a, b in zip(GC["tb"], GC["tb"][1:]):
+                aff(ap("t16" + H, S(16 * p0 + a, 16 * p0 + b)), ind(ap("tb", S(*WIN[u])), of(4, p0 + a // 16, p0 + b // 16)), SCL)
 
         for f, *x in ((hops, 0), (hops, 32), (lengths, 0), (hops, 64), (rows, 0), (hops, 96), (signs, 0, 1), (lengths, 64), (signs, 0, 8),
                       (rows, 64), (count, 0), (signs, 64, 1), (signs, 64, 8), (count, 64)):
@@ -581,34 +598,41 @@ def build():
         if not last:
             mm([(ap(sm, 29, S(e, 16, 2)), [(c("t16", 15 * e), SEH)]) for e in range(2)])
             tt(blk(st, 1, EDG), er(29), blk(st, 1, EDG), AL.add)
-        for b in range(4):
+        pz, nb, (a0, ne) = bank(h), 64 if last else 72, (0, 16) if last else (88, 32)
+        x1 = lambda k, a, n: ap("x1", S(120 * (k - 1) + a, 120 * (k - 1) + a + n))
+        n = 14 // TH
+        mm([(ap(pz, S(ne * n * ((k - 1) // n) + (k - 1) % n, ne * n * ((k - 1) // n + 1), n)), [(c("t16", k), x1(k, a0, ne))]) for k in range(1, 15)])
+        for b in range(2):
             px = bank(h)
-            ks = [k for k in range(4 * b, 4 * b + 4) if 0 < k < 15]
-            k4, kk = S(ks[0] % 4, ks[-1] % 4 + 1), S(ks[0], ks[-1] + 1)
-            mm([(ap(px, S(0, 96 if last else 104), k % 4), [(c("t16", k), ap("x1", S(104 * (k - 1), 104 * k - 8 * last))),
-                                                           (c("t16", k), ap("x2", S(72 * (k - 1), 72 * k)), ap(px, S(0, 72), k % 4))]) for k in ks])
-            act(ap(sg, ALLP, kk), ap(px, S(0, 72), k4), AF.Sign, 1.0, 0.5)
+            mm([(ap(px, S(k - 1 - 7 * b, 7 * nb, 7)), [(c("t16", k), x1(k, 16, nb)), (c("t16", k), ap("x2", S(72 * (k - 1), 72 * (k - 1) + nb)))]) for k in range(1 + 7 * b, 8 + 7 * b)])
+            act(ap(sg, S(0, nb), S(1 + 7 * b, 8 + 7 * b)), ap(px, S(0, 7 * nb)), AF.Sign, 1.0, 0.5)
+        for b in range(1 if last else TH):
+            kk, a = S(1 + n * b, 1 + n * b + n), ne * n * b
             if last:
-                aff(ap(st, S(0, 24), kk), ap(px, S(72, 96), k4))
+                for a in range(TH):
+                    aff(ap("yh" + H, ALLP, S(1 + n * a, 1 + n * a + n)), ap(pz, S(16 * n * a, 16 * n * a + 16 * n)))
             else:
-                tt(ap(st, S(0, 16), kk), ap(px, S(72, 88), k4), ap(sg, S(56, 72), kk), AL.mult)
-                tt(ap(st, S(16, 32), kk), ap(px, S(88, 104), k4), ap(st, S(0, 16), kk), AL.subtract)
+                tt(ap(st, S(0, 16), kk), ap(pz, S(a, a + 16 * n)), ap(sg, S(56, 72), kk), AL.mult)
+                tt(blk("yh" + H, 0, kk), ap(pz, S(a + 16 * n, a + 24 * n)), blk(st, 0, kk), AL.subtract)
+                tt(blk(st, 3, kk), ap(pz, S(a + 24 * n, a + 32 * n)), blk(st, 1, kk), AL.subtract)
         if not last:
-            aff(yh, y, eng="DAG")
-            mm([(blk(sm, 0), [(hz, If(2.0)), (yh, I)]), (blk(sm, 1), [(yh, I)])])
-            aff(of(0, 0, 256), blk(sm, 0, w=2), 1.0, OFF)
+            aff(blk("yh" + H, 0, EDG), blk(st, 2, EDG), eng="DAG")
+            pz = bank(h)
+            mm([(rb(pz, 0), [(hz, If(2.0))])], end=False)
+            mm([(rb(pz, j), [(yh, I)]) for j in range(2)], begin=False)
+            aff(of(0, 0, 256), rb(pz, 0, 2), 1.0, OFF)
             pl = rb(bank(h), 0)
             mm([(pl, [(blk(sg, m), Ib(1.0 / 16 if m < 7 else -7.0 / 16)) for m in range(8)])])
             aff(lb, pl)
         else:
-            mm([(blk(sm, 0), [(y, I32), (hz, If(-1.0))]), (blk(sm, 1), [(y, I32), (hz, I32)])])
+            mm([(blk(sm, j), [(blk("yh" + H, j), I)]) for j in range(2)])
             aff(blk(sf, 0, w=2), blk(sm, 0, w=2), 1.0, OFF)
             dma(ap("ya", S(128 * h, 128 * h + 128)), blk(sf, 0), 65536)
             dma(ap("yb", S(128 * h, 128 * h + 128)), blk(sf, 1), 65536, "A")
             pl = rb(bank(h), 0)
             mm([(pl, [(blk(sg, m), Ib(0.5)) for m in range(8)])])
-            aff(blk(sf, 5), pl, 1.0, 4.0)
-            dma(ap("yl", S(128 * h, 128 * h + 128)), blk(sf, 5), 65536)
+            aff(blk(sf, 2), pl, 1.0, 4.0)
+            dma(ap("yl", S(128 * h, 128 * h + 128)), blk(sf, 2), 65536)
 
     for h in range(2):
         first(h)
@@ -827,6 +851,8 @@ def shorten(ops, init, iters, rng, reach=14):
         return max(t), r, rd, t, td, mp, ms
 
     cur = times()
+    if cur is None:
+        return None
     best, tb = (cur[0], list(q), list(cur[1])), {}
     for it in range(iters):
         C, r, rd, t, td, mp, ms = cur
@@ -849,6 +875,8 @@ def shorten(ops, init, iters, rng, reach=14):
             L = len(b)
             for a in range(L):
                 u = b[a]
+                if rng.random() > 0.4:
+                    continue
                 if len(ops[u]["eng"]) == 1 and (L == 1 or reach < a < L - 1 - reach):
                     continue
                 lo, hi = max([r[j] for j in pred[u]] + [-1.0]), min([r[j] for j in succ[u]] + [1e18])
@@ -970,17 +998,29 @@ def schedule(ops):
             o["deps"] = set(d)
         return x[0]
 
-    now, best, val = min(res, key=lambda x: x[0]), None, 1e18
-    for it in range(EFFORT[4]):
-        speed(*PACES[it % len(PACES)])
-        now = shorten(ops, now, 0, rng)
-        lend(ops, now)
-        now = shorten(ops, now, EFFORT[5], rng)
-        v = mean(now)
-        if v < val:
-            best, val = (now, dict(PLACE), [set(o["deps"]) for o in ops]), v
-        elif v > val + 2500.0:
-            now = back(best)
+    keep = lambda x: (x, dict(PLACE), [set(o["deps"]) for o in ops])
+
+    def turns(best, val, n):
+        now = back(best)
+        for it in range(n):
+            speed(*PACES[it % len(PACES)])
+            now = shorten(ops, now, 0, rng)
+            was = keep(now)
+            lend(ops, now)
+            if shorten(ops, now, 0, rng) is None:
+                back(was)
+            now = shorten(ops, now, EFFORT[5], rng)
+            v = mean(now)
+            if v < val:
+                best, val = keep(now), v
+            elif v > val + 2500.0:
+                now = back(best)
+        return best, val
+
+    res = [(x, 1e18) for x in [keep(x) for x in res]]
+    while len(res) > 1:
+        res = sorted([turns(x, v, len(PACES)) for x, v in res], key=lambda x: x[1])[:len(res) // 2]
+    best = turns(res[0][0], res[0][1], EFFORT[4])[0]
     speed(*PACES[0])
     now = shorten(ops, back(best), 0, rng)
     for i, o in enumerate(ops):

@@ -7,28 +7,29 @@ AF = ActivationFunctionType
 W, RO = 3072, 3
 HS = 272
 TWO, FOUR = (0, 1024, 2048), (0, 512, 1024, 1536, 2048)
-GC = {"va": (0, 512, 1024, 2048), "va+": (0, 512, 1024, 2048), "ld": TWO, "t1": FOUR, "g1": TWO, "rw+": FOUR, "tb": (0, 512, 1024)}
+GC = {"E": TWO, "va": FOUR, "va+": FOUR, "ld": FOUR, "t1": FOUR, "rw+": FOUR, "tb": (0, 512, 1024)}
 PW = 64
 NPR = 6
-HB = 32
 TH = 2
-GD, GY = 1024, 1024
+GD, GY = 1024, 512
 GB = 1024
 RND, RNDE = 1.5 * 2 ** 23, 1.5 * 2 ** 33
 OFF = 1536.0
 TB = [1088, 0, 5248, 6336]
 WIN = [(1088, 5248), (0, 5248), (2176, 6336), (2176, 7424)]
+SHARE = 0.2
 CY, PCY, GCY, LAT = 0.9, 0.42, 1.56, 140.0
-STARTS = [(a, b) for a in (10000.0, 14000.0, 18000.0, 22000.0) for b in (1.15, 1.3, 1.45)]
-PACES = [(1.0, 1.0, 1.0, 1.0), (1.0, 1.3, 1.0, 1.2), (1.0, 0.72, 1.05, 0.8), (1.2, 1.15, 1.0, 1.0), (1.0, 1.0, 1.1, 1.5), (1.3, 1.0, 1.3, 1.0)]
-EFFORT = [300, 4, 4, 200, 36, 200, 1]
+STARTS = [(a, b) for a in (8000.0, 11000.0, 14000.0, 17000.0) for b in (1.15, 1.3, 1.45)]
+PACES = [(0.92, 1.0, 1.0, 1.0), (1.2, 1.1, 1.4, 1.1), (1.0, 1.25, 1.2, 1.2), (0.95, 0.8, 1.35, 0.9), (1.2, 1.0, 1.1, 1.0), (0.95, 1.0, 1.65, 1.1)]
+EFFORT = [200, 2, 4, 150, 270, 200, 1]
 
 SCRATCH = {
     "vt": ("sbuf", [128, W], "float32"), "uw": ("sbuf", [128, W + 8192], "float32"), "xb": ("sbuf", [128, 2 * W], "bfloat16"),
     "nt": ("sbuf", [128, W], "int32"), "tb": ("sbuf", [128, W + 4 * 1088], "float32"),
     "bk": ("sbuf", [128, 2048], "bfloat16"), "ct": ("sbuf", [128, 14, 15], "bfloat16"), "c2": ("sbuf", [128, 14, 9], "bfloat16"),
-    "cb": ("sbuf", [128, 144, 16], "bfloat16"), "zz": ("sbuf", [128, 144], "bfloat16"), "c32": ("sbuf", [128, 6, 128], "float32"),
+    "cb": ("sbuf", [128, 152, 16], "bfloat16"), "zz": ("sbuf", [128, 144], "bfloat16"), "c32": ("sbuf", [128, 5, 128], "float32"),
     "cf": ("sbuf", [128, 336], "bfloat16"), "col": ("sbuf", [128, 88], "float32"), "coli": ("sbuf", [128, 8], "int32"), "se": ("sbuf", [128, 16], "bfloat16"),
+    "dg": ("sbuf", [128, 2, 128], "float16"),
 }
 BASE = {"va0": ("uw", 0), "d80": ("uw", 2048), "ut": ("uw", 4096), "d81": ("uw", 4096 + W), "va1": ("uw", 6144 + W), "xt": ("xb", 0), "gt": ("xb", W),
         "gd0": ("tb", 0), "gd1": ("tb", 5248), "wk": ("xb", 0), "x1": ("xb", 1792), "x2": ("xb", 3472), "cm": ("xb", 4480)}
@@ -37,12 +38,12 @@ for _i in range(NPR):
 for _h in range(2):
     for _n, _s, _t in (("di", [2048], "int32"), ("rw", [2048 + RO * HS], "float32"),
                        ("g16", [2048], "float16"), ("t16", [2048], "float16"), ("ld", [2048], "float16"), ("y16", [2048], "float16"),
-                       ("si", [896], "float32"), ("of", [640], "uint16"), ("st", [32, 16], "float32"), ("sf", [40, 16], "float32"),
+                       ("si", [896], "float32"), ("of", [640], "uint16"), ("st", [24, 16], "float32"), ("sf", [40, 16], "float32"),
                        ("sh", [48, 16], "bfloat16"), ("yh", [16, 16], "float16"), ("uf", [8, 16], "float16"), ("ue", [8, 16], "float16"), ("en", [8, 18], "float32"),
                        ("sg", [72, 16], "bfloat16"), ("ed", [128], "float32"), ("eb", [32], "bfloat16"), ("sb", [2, 136], "float32")):
         SCRATCH["%s%d" % (_n, _h)] = ("sbuf", [128] + _s, _t)
-    for _i in range(3):
-        SCRATCH["ps%d" % (4 * _h + _i)] = ("psum", [128, 512], "float32")
+    for _i in range(3 * _h, 3 * _h + 3):
+        SCRATCH["bn%d" % _i] = ("psum", [128, 512], "float32")
     SCRATCH["ps%d" % (4 * _h + 3)] = ("psum", [128, 32, 16], "float32")
 NDMA = 72
 SEMAPHORES = ["cD", "cA", "cP", "cG"] + ["dm%d" % i for i in range(NDMA)] \
@@ -72,7 +73,7 @@ def ind(win, off):
 
 
 def spec(name):
-    return SCRATCH.get(PLACE.get(name, name))
+    return SCRATCH.get({"vb": "bn0", "vp": "pr0"}.get(name[:2], name))
 
 
 def region(a):
@@ -165,7 +166,7 @@ def build():
             for i, tm in enumerate(terms):
                 l, r = tm[0], tm[1]
                 o = tm[2] if len(tm) > 2 else out
-                cost += max(64, nel(r)) * (1 if two(l) else 4) * PCY
+                cost += max(64, nel(r) * (1 if two(l) else 4)) * PCY
                 rd += [l, r]
                 fs.append(lambda g, T, o=o, l=l, r=r, a=(i == 0 and (begin or len(wr) > 1)), b=(end and i == len(terms) - 1): g.tensor.matmul(real(T, o), real(T, l), real(T, r), a, b))
         add("P", {"P": cost}, rd, wr, lambda e: fs)
@@ -198,7 +199,7 @@ def build():
         add("S", {"S": 80.0 * len(lst)}, [a for o, a in lst], [o for o, a in lst], lambda e: fs, sem="dm%d" % (nd[0] - 1), inc=16, late=2200 + nbytes / 250.0)
 
     EQ, GE = AL.is_equal, AL.is_ge
-    MID, EDG = S(1, 15), S(0, 16, 15)
+    EDG = S(0, 16, 15)
     blk = lambda n, j, k=ALLP, w=1: ap(n, S(8 * j, 8 * (j + w)), k)
     rb = lambda n, j, w=1: ap(n, S(128 * j, 128 * (j + w)))
     pin = lambda j, h: ap("di0", S(256 * j + 128 * h, 256 * j + 128 * h + 128))
@@ -234,10 +235,11 @@ def build():
         ops[-1]["emit"] = lambda e: plain(e) if e != "G" else [lambda g, T: g.affine_select(real(T, out), real(T, cb(16)), [[-1, 128]], AL.not_equal, v, 0, 1)]
 
     sc, sf32 = {}, {}
-    for j, v in enumerate((1.0 / 2048, -1.0, -2.0, 2.0, 1.0 / 16, -7.0 / 16, 8.0, 0.5, -4.0, 1.0 / 32, -65536.0)):
-        sc[v] = 5 + j
-        diag(cb(5 + j), v)
-    for j, v in enumerate((-1.0, 2.0, -0.5, 0.5)):
+    sc[1.0] = 0
+    for j, v in enumerate((1.0 / 512, -1.0, -2.0, 2.0, 1.0 / 16, -7.0 / 16, 8.0, 0.5, -4.0, 1.0 / 32, -65536.0, 0.125)):
+        sc[v] = 5 + j if j < 11 else 18
+        diag(cb(sc[v]), v)
+    for j, v in enumerate((-1.0, 2.0, -0.5)):
         sf32[v] = ap("c32", 2 + j, ALLP)
         diag(sf32[v], v)
     Ib = lambda v, k=ALLP: cb(sc[v], k)
@@ -273,20 +275,18 @@ def build():
 
     def bank(h):
         rot[h] += 1
-        PLACE["vb%d" % (2 * rot[h] + h)] = "ps%d" % (4 * h + rot[h] % 3)
         return "vb%d" % (2 * rot[h] + h)
 
     def newpr():
         prn[0] += 1
-        PLACE["vp%d" % prn[0]] = "pr%d" % (prn[0] % NPR)
         return "vp%d" % prn[0]
 
     def table():
         cur[0] = None
         for a in range(0, W, 512):
             pv = ap(bank(a // 512 % 2), ALLP)
-            mm([(pv, [(I, ap("xt", S(a, a + 512))), (Ib(1.0 / 2048), ap("gt", S(a, a + 512)))])])
-            aff(ap("vt", S(a, a + 512)), pv, 1.0, 128.125)
+            mm([(pv, [(Ib(8.0), ap("xt", S(a, a + 512))), (Ib(1.0 / 512), ap("gt", S(a, a + 512)))])])
+            aff(ap("vt", S(a, a + 512)), pv, 1.0, 1025.0)
         for a in range(0, W, 1024):
             aff(ap("ut", S(a, a + 1024)), ap("vt", S(a, a + 1024)), -1.0)
 
@@ -300,11 +300,17 @@ def build():
         aff(IM, I, cl(26))
         iota(cm(3), [[16, 128]], 0, 0)
         sel(cm(3), cm(3), [[0, 128]], EQ, 1.0, 0, 1)
-        aff(cm(4), cm(3), -1.0)
+        diag(cm(4), 65536.0)
         iota(cm(5), [[0, 8], [1, 16]], 0, 0)
         sel(cm(5), cm(5), [[0, 128]], EQ, 1.0, -1, 1)
-        for j, v in ((6, W - OFF), (7, -4096 - OFF), (8, W + 2048 - OFF), (5, -2048 - OFF)):
+        for j, v in ((7, -4096 - OFF), (8, W + 2048 - OFF)):
             sel(cm(j), cm(5), [[0, 128]], AL.not_equal, v, -2, 1)
+        iota(cm(6), [[0, 8], [-1, 16]], 0, 0)
+        sel(cm(6), cm(6), [[0, 128]], EQ, 0.0, -1, 1)
+        iota(cl(85, 2), [[W + 2048, 2]], -2048 - int(OFF), 16)
+        iota(cl(28, 2), [[-W - 6144, 2]], 4096 + int(OFF), -16)
+        for h in range(2):
+            aff(ap("dg", h, ALLP), I, cl(28 + h))
         for u in range(4):
             a, b = 448.0 + TB[u] - WIN[u][0], OFF + 2176 - WIN[u][0]
             aff(cl(20 + u), cl(24), b - a, a)
@@ -342,16 +348,16 @@ def build():
         ts(cl(82), cl(68), cl(69), AL.add, -1.0, AL.mult)
         for j, (a, b) in enumerate(((-1.0, cl(70)), (1.0, cl(82)), (1.0, cl(76)), (cl(74), cl(75)))):
             if j == 3:
-                aff(ap("ct", ALLP, 14), ap("c32", 1, S(0, 14)), a, b)
+                aff(ap("ct", ALLP, 13), ap("c32", 1, S(0, 14)), a, b)
             else:
-                ts(ap("ct", ALLP, 11 + j), ap("c32", 1, S(0, 14)), b, AL.mult, a, AL.mult)
+                ts(ap("ct", ALLP, (11, 12, 14)[j]), ap("c32", 1, S(0, 14)), b, AL.mult, a, AL.mult)
         ts(cl(83), cl(77), cl(66), AL.add, 128.0, AL.mult)
         ts(cl(83), cl(12), 6.0, AL.is_lt, cl(83), AL.add)
         tt(cl(84), cl(78), cl(67), AL.add)
         aff(ap("cf", S(0, 210)), ap("ct", ALLP, ALLP), cl(83))
         aff(ap("cf", S(210, 336)), x, cl(84))
         for j in range(8):
-            aff(ap("x1", S(j, 2688, 8)), ap("cf", ALLP), cl(32 + j))
+            aff(ap("x1", S(j, 2688, 8)), ap("cf", ALLP), cl(32 + j), eng="AD")
         for h in range(2):
             aff(ap("ue%d" % h, ALLP, ALLP), ONE, 0.0)
             iota(ap("sg%d" % h, ALLP, EDG), [[0, 144]], 0, 0)
@@ -365,7 +371,7 @@ def build():
 
     def gathers(dst, win, oj, h, scale=1.0, bias=0.0):
         H, c, of, sm = names(h)
-        cut = TWO if cur[1] < 0 else GC[dst[:2]]
+        cut = GC["E" if cur[1] < 0 else dst[:2]]
         for a, b in zip(cut, cut[1:]):
             aff(ap(dst, S(a, b)), ind(win, of(oj, a // 16, b // 16)), scale, bias)
 
@@ -394,15 +400,15 @@ def build():
         aff(of(0, 0, 256), blk(sm, 0, w=2), 1.0, OFF)
         aff(blk(sh, 0), pin(2, h), 0.125)
         gathers("t16" + H, ET, 1, h, SCL)
-        gathers("g16" + H, ET, 0, h, SCL)
+        gathers("y16" + H, ET, 0, h, SCL)
         mm([(blk(sm, 2), [(b, I), (fd, If(-1.0))]), (blk(sm, 0), [(a, I), (b, Ib(-1.0)), (fd, If(2.0))]), (blk(sm, 1), [(f, I)])])
-        aff(blk(st, 2), blk(sm, 2))
+        aff(blk("yh" + H, 0), blk(sm, 2))
         aff(blk(st, 0), blk(sm, 0), 0.5)
         aff(ap(ed, S(96, 112)), blk(sm, 1, EDG), 2.0, -1.0)
         aff(ap(ed, S(112, 128)), blk(sm, 1, EDG), -4.0, 2.0)
         mm([(blk(sm, 3, k), [(c("t16", k), SEH)]) for k in range(16)])
-        aff(blk(st, 3), blk(sm, 3), 2.0)
-        mm([(blk(sm, 1, k), [(c("g16", k), SEH), (c("t16", k), SEN)]) for k in range(16)])
+        aff(blk(st, 2), blk(sm, 3), 2.0)
+        mm([(blk(sm, 1, k), [(c("y16", k), SEH), (c("t16", k), SEN)]) for k in range(16)])
         aff(blk(st, 1), blk(sm, 1))
 
     def spread(h, x, p0, a):
@@ -412,22 +418,20 @@ def build():
 
     def send(h, r):
         rw, sb, a = "rw%d" % h, "sb%d" % h, 2048 + HS * r
-        tr = [(ap(sb, 0, ALLP), ap(rw, S(a, a + 136))), (ap(sb, 1, ALLP), ap(rw, S(a + 136, a + HS)))]
-        i = add("G", {"G": 1000.0}, [ap(sb, ALLP, ALLP)], [], None, sem="lo%d" % (2 * r + h), inc=8, late=2500.0 if r + h else 6000.0, send=tr, arr="ar%d" % (2 * r + h))
-        add("X", {"X": 0.0}, [], [ap(rw, S(a, a + HS))], None, sem="ar%d" % (2 * r + h), inc=8, late=2000.0, after=i)
+        u, tr = 2 * r + h, [(ap(sb, j, ALLP), ap(rw, S(a + 136 * j, a + 136 * j + 136))) for j in range(2)]
+        i = add("G", {"G": 1000.0}, [ap(sb, ALLP, ALLP)], [], None, sem="lo%d" % u, inc=8, late=2500.0 if u else 6000.0, send=tr, arr="ar%d" % u)
+        add("X", {"X": 0.0}, [], [x[1] for x in tr], None, sem="ar%d" % u, inc=8, late=2000.0, after=i)
 
     def step1(h, r):
         cur[0] = h
         H, c, of, sm = names(h)
         st, sf, sh, rw = "st" + H, "sf" + H, "sh" + H, "rw" + H
-        hz, hE, y, Ey = [blk(st, j) for j in range(4)]
+        hz, hE, Ey = [blk(st, j) for j in range(3)]
         lb = blk(sh, 0)
         gathers("va" + H, VT, 0, h, -1.0)
         gather_add("d8" + H, VT, 1, "va" + H, h)
-        if r == 0:
-            aff(blk("yh" + H, 0), y, eng="DAG")
         pq = rb(bank(h), 0)
-        mm([(pq, [(lb, Ib(-2.0)), (Ib(2.0), ONE)])])
+        mm([(pq, [(Ib(2.0), ONE), (lb, Ib(-2.0))])])
         tt(pq, pq, hE, AL.mult)
         en = lambda k: ap("en" + H, ALLP, k)
         tt(en(S(1, 17)), pq, Ey, AL.add)
@@ -440,7 +444,6 @@ def build():
                 tt(rb(pb, j), c("d8", k), rb(pb, j), AL.mult)
                 tt(ap("sb" + H, j, S(0, 128)), rb(pb, j), c("va", k), AL.add)
         for p0 in (0, 64):
-            cols = S(16 * p0, 16 * p0 + 1024)
             for a in range(16 * p0, 16 * p0 + 1024, GD):
                 aff(ap("di" + H, S(a, a + GD)), ap("d8" + H, S(a, a + GD)), eng="G")
             for a in range(2):
@@ -448,10 +451,10 @@ def build():
                 tt(pw, c("d8", **ks), pw, AL.mult)
                 tt(c("rw", **ks), pw, c("va", **ks), AL.add)
             for a in range(16 * p0, 16 * p0 + 1024, GY):
-                aff(ap("y16" + H, S(a, a + GY)), ap(rw, S(a, a + GY)), eng="DAG")
+                aff(ap("y16" + H, S(a, a + GY)), ap(rw, S(a, a + GY)), -8.0)
             for a in range(2):
                 pw, pg, pp = ap(bank(h), ALLP), ap(bank(h), ALLP), S(p0 + 32 * a, p0 + 32 * a + 32)
-                mm([(pw, [(Ib(-1.0), c("y16", p=pp))])])
+                mm([(pw, [(Ib(0.125), c("y16", p=pp))])])
                 tt(c("g16", p=pp), pw, c("rw", p=pp), AL.add)
                 mm([(pg, [(I, c("g16", p=pp))])])
                 tt(c("gd", p=pp), pg, c("di", p=pp), AL.mult)
@@ -462,23 +465,23 @@ def build():
         mo = lambda k=ALLP: ap("uf" + H, ALLP, k)
         aff(en(0), ap(rw, S(sl + 128, sl + 136)), eng="DAG")
         aff(en(17), ap(rw, S(sl + 264, sl + 272)), eng="DAG")
+        po = bank(h)
         tt(mo(), en(S(2, 18)), en(S(0, 16)), GE)
         aff(mo(0), mo(0), cl(r), 512.0)
         aff(mo(15), mo(15), cl(3 + r), -512.0)
-        po = bank(h)
-        mm([(rb(po, 0), [(mo(), Ib(2.0)), (I, BC)])])
+        mm([(rb(po, 0), [(I, BC), (mo(), Ib(2.0))])])
         aff(of(2), rb(po, 0), 1.0, cl(16 + r))
         red = lambda j, pr, a: mm([(blk(sm, j, a + 4 * k), [(ap(pr, ALLP, k), GS)]) for k in range(4)])
         for a in range(4):
             mm([(blk(sm, 0, k), [(c("gd", k), GS)]) for k in range(a, 16, 4)])
-        gathers("t16" + H, ap(rw, S(0, sl + HS)), 2, h)
+        gathers("t16" + H, ap(rw, S(0, sl + HS)), 2, h, 8.0)
         for a in range(0, 2048, GB):
-            aff(ap(rw, S(a, a + GB)), ap("y16" + H, S(a, a + GB)), -8.0)
+            aff(ap(rw, S(a, a + GB)), ap("y16" + H, S(a, a + GB)), eng="DAG")
             dma(ap(rw, S(a, a + GB)), ap("va" + H, S(a, a + GB)), 512 * GB, "G")
         for a in range(4):
             pt, ks = ap(bank(h), ALLP), (a, 4)
             ptd, pgt, ptt = newpr(), newpr(), newpr()
-            mm([(pt, [(Ib(-1.0), c("y16", ks))])], end=False)
+            mm([(pt, [(I, c("y16", ks))])], end=False)
             mm([(pt, [(I, c("t16", ks))])], begin=False)
             act(ap(ptt, ALLP, ALLP), pt, AF.Square)
             tt(ap(ptd, ALLP, ALLP), c("di", ks), pt, AL.mult)
@@ -492,31 +495,31 @@ def build():
         st, sf, sh, ed, sg, si = "st" + H, "sf" + H, "sh" + H, "ed" + H, "sg" + H, "si" + H
         last = r == RO - 1
         nq = 1 if last else 2
-        hz, hE, y, Ey = [blk(st, j) for j in range(4)]
-        lb, eq, dn = [blk(sh, j) for j in range(3)]
+        hz, hE, Ey = [blk(st, j) for j in range(3)]
+        lb, up, dn = [blk(sh, j) for j in range(3)]
         yh = blk("yh" + H, 0)
-        pn, pw, lh = bank(h), bank(h), lambda j: cm(j, S(0, 3))
-        mm([(rb(pn, 0), [(lh(4 - h), lh(5 + h)), (lb, Ib(-65536.0))] + [(c("ld", k), Ib(-1.0, k) if h else cb(0, k), ap(pn, S(k, 128, 16))) for k in range(16)])])
-        act(blk(sf, 0), rb(pn, 0), AF.Relu, 1.0, 0.0, (0.0, AL.max, 0.0, AL.add))
-        mm([(rb(pw, 0), [(lh(3), lh(7 + h)), (Ib(-1.0), yh)]), (rb(pw, 1), [(lh(3), lh(5 + h)), (Ib(-1.0), yh), (If(-1.0) if h else I32, blk(sf, 0))])])
+        pn, lh, u1, u2 = bank(h), lambda j: cm(j, S(0, 3)), blk("yh" + H, 1), ap("uf" + H, ALLP, ALLP)
+        mm([(rb(pn, 1), [(lh(3), lh(6)), (I, yh)]),
+            (rb(pn, 0), [(lh(3), lh(6)), (lb, cm(4) if h else Ib(-65536.0))] + [(c("ld", k), cb(0, k), ap(pn, S(k, 128, 16))) for k in range(16)])])
+        ts(rb(pn, 0), rb(pn, 0), cl(85 + h), AL.min if h else AL.max)
         aff(blk(sf, 2, w=2), blk(sm, 2, w=2))
         tt(blk(sf, 4), blk(sm, 0), blk(sf, 2), AL.mult)
         tt(blk(sm, 1), blk(sm, 1), blk(sf, 3), AL.mult)
         tt(dn, blk(sm, 1), blk(sf, 4), AL.is_gt)
-        tt(blk(sf, 1), rb(pw, 1), dn, AL.mult)
-        tt(eq, blk(sm, 1), blk(sf, 4), EQ)
-        tt(blk(sf, 0), rb(pw, 0), eq, AL.mult)
+        tt(u2, rb(pn, 0), dn, AL.mult)
+        tt(up, blk(sm, 1), blk(sf, 4), AL.is_lt)
+        tt(u1, rb(pn, 1), up, AL.mult)
         pu = bank(h)
-        mm([(rb(pu, 0), [(yh, I), (blk(sf, 1), I32)])], end=False)
-        mm([(rb(pu, 0), [(blk(sf, 0), I32)])], begin=False)
+        mm([(rb(pu, 0), [(lh(7 + h), lh(3)), (dn, ap("dg", h, ALLP)), (u2, I)])], end=False)
+        mm([(rb(pu, 0), [(up, ap("dg", h, ALLP)), (u1, I)])], begin=False)
         aff(of(3), rb(pu, 0), 1.0, OFF + 4096 * (1 - h))
         gather_add("ld" + H, ap("uw", S(4096 * h, 4096 * h + 4096 + W)), 3, "rw" + H, h, AL.subtract)
-        mm([(blk(sm, j), [(lb, Ib(8.0)), (Ib(-1.0), eq), (Ib(-2.0), dn)]) for j in range(1)])
+        mm([(blk(sm, 0), [(lb, Ib(8.0)), (Ib(-1.0), dn), (I, up)])])
         mu, ove = ap("eb" + H, S(0, 16)), ap("eb" + H, S(16, 32))
-        act(ove, blk(sm, 0, EDG), AF.Relu, -1.0, -1.0, (-2.0, EQ, 1.0, AL.mult))
+        act(ove, blk(sm, 0, EDG), AF.Relu, -1.0, 0.0, (-1.0, EQ, 1.0, AL.mult))
         if not last:
-            act(mu, blk(sm, 0, EDG), AF.Relu, 2.0, -12.0, (7.0, EQ, 2.0, AL.mult))
-        ts(blk(sm, 0), blk(sm, 0), 4.0, AL.is_lt, 2.0, AL.mult)
+            act(mu, blk(sm, 0, EDG), AF.Relu, 2.0, -14.0, (8.0, EQ, 2.0, AL.mult))
+        ts(blk(sm, 0), blk(sm, 0), 5.0, AL.is_lt, 2.0, AL.mult)
         for j in range(nq):
             tt(blk(sf, 3 + j), blk(sm, 0), blk(st, j), AL.mult)
         pc = bank(h)
@@ -533,25 +536,28 @@ def build():
         pb = bank(h)
         er = lambda j, n=1: ap(pb, S(16 * j, 16 * (j + n))) if j < 29 else ap(sm, S(j, j + n), ALLP)
         on16, pe = ap("cb", 8, ALLP), ap(ed, S(64, 80))
-        tt(pe, blk(sf, 1, EDG), ove, AL.mult)
-        lp = [(lb, Ib(8.0, EDG)), (Ib(-1.0), blk(sh, 1, EDG)), (Ib(-2.0), blk(sh, 2, EDG)), (I, on16), (Ib(8.0), ove)]
+        mm([(er(23), [(I, blk("yh" + H, 0, EDG)), (Ib(-1.0), ap("uf" + H, ALLP, EDG)), (lh(3), ap("cm", S(783, 896, 16), p=S(0, 3)), ap(pb, S(369, 384, 2)))])])
+        tt(pe, er(23), ove, AL.mult)
+        lp = [(lb, Ib(8.0, EDG)), (I, blk(sh, 1, EDG)), (Ib(-1.0), blk(sh, 2, EDG)), (Ib(8.0), ove)]
         if not last:
-            tt(ap("ue" + H, ALLP, EDG), pe, blk(st, 2, EDG), AL.add)
+            tt(ap("ue" + H, ALLP, EDG), blk("yh" + H, 0, EDG), pe, AL.subtract)
             for j, k in ((0, 15), (1, 0)):
                 aff(ap("sb" + H, j, S(0, 128)), c("ld", k), 0.125)
-            mm([(er(16 + j), [(I, on16), (Ib(-2.0), ove), (Ib(-1.0), mu)]) for j in range(2)] + [(er(18 + j), [(Ib(2.0), ove), (I, mu)]) for j in range(2)]
+            mm([(er(16 + j), [(I, on16), (Ib(-2.0), ove), (Ib(-1.0), mu)]) for j in range(2)]
                + [(er(20), lp + [(Ib(-4.0), mu)])] + [(er(21 + j), [(I, on16), (Ib(-1.0), mu)]) for j in range(2)])
-            for j in range(2):
-                tt(ap(ed, S(32 * j, 32 * j + 32)), er(16 + 2 * j, 2), blk(st, 0, EDG, 2), AL.mult)
+            tt(ap(ed, S(0, 32)), er(16, 2), blk(st, 0, EDG, 2), AL.mult)
             tt(ap(ed, S(96, 128)), er(21, 2), ap(ed, S(96, 128)), AL.mult)
             aff(blk(sg, 0, EDG), er(20), 2.0)
-            mm([(er(24, 4), [(I32, ap(ed, S(0, 64))), (If(0.5), pe, er(24)), (I32, blk(st, 2, EDG, 2), er(26, 2)), (If(-0.5), blk(st, 3, EDG), er(25))])])
-            aff(ap(st, ALLP, EDG), er(24, 4))
+            eg = lambda j, w=1: blk(st, j, EDG, w)
+            mm([(er(24, 2), [(I32, ap(ed, S(0, 32))), (If(-0.5), pe, er(24)), (If(-0.5), eg(2), er(25))]),
+                (er(26), [(I32, eg(1)), (I32, eg(2)), (If(-1.0), ap(ed, S(16, 32)))]), (er(27), [(I32, eg(0)), (I, blk("yh" + H, 0, EDG)), (If(-1.0), ap(ed, S(0, 16)))])])
+            aff(eg(0, 3), er(24, 3))
+            aff(blk("yh" + H, 0, EDG), er(27))
         else:
             mm([(er(16), [(I, on16), (Ib(-2.0), ove)]), (er(20), lp + [(Ib(-4.0), on16)])])
             tt(ap(ed, S(0, 16)), er(16), blk(st, 0, EDG), AL.mult)
             tt(blk(sg, 0, EDG), er(20), ap(ed, S(112, 128)), AL.mult)
-            mm([(er(24), [(I32, ap(ed, S(0, 16))), (If(0.5), pe)]), (er(25), [(I32, blk(st, 0, EDG)), (If(0.5), pe), (I32, blk(st, 2, EDG))])])
+            mm([(er(24), [(I32, ap(ed, S(0, 16))), (If(-0.5), pe)]), (er(25), [(I32, blk(st, 0, EDG)), (If(-0.5), pe), (I, blk("yh" + H, 0, EDG))])])
             tt(blk(st, 0, EDG), er(24), ap(ed, S(96, 112)), AL.mult)
             for j, op in enumerate((AL.subtract, AL.add)):
                 tt(blk("yh" + H, j, EDG), er(25), blk(st, 0, EDG), op)
@@ -564,7 +570,7 @@ def build():
         def hops(a):
             pd, pp = ap(bank(h), ALLP), S(a, a + 32)
             mm([(pd, [(Ib(-1.0), c("ld", p=pp)), (I, ap("ld" + H, S(16 * a + 1, 16 * a + 512)), ap(pd[0], S(0, 511)))])])
-            act(c("t16", p=pp), pd, AF.Abs, 1.0 / 128)
+            act(c("t16", p=pp), pd, AF.Abs, 1.0 / 1024)
 
         def lengths(p0):
             ph = part(sm, 0, p0)
@@ -613,10 +619,9 @@ def build():
                     aff(ap("yh" + H, ALLP, S(1 + n * a, 1 + n * a + n)), ap(pz, S(16 * n * a, 16 * n * a + 16 * n)))
             else:
                 tt(ap(st, S(0, 16), kk), ap(pz, S(a, a + 16 * n)), ap(sg, S(56, 72), kk), AL.mult)
-                tt(blk("yh" + H, 0, kk), ap(pz, S(a + 16 * n, a + 24 * n)), blk(st, 0, kk), AL.subtract)
-                tt(blk(st, 3, kk), ap(pz, S(a + 24 * n, a + 32 * n)), blk(st, 1, kk), AL.subtract)
+                tt(blk("yh" + H, 0, kk), ap(pz, S(a + 24 * n, a + 32 * n)), blk(st, 0, kk), AL.subtract)
+                tt(blk(st, 2, kk), ap(pz, S(a + 16 * n, a + 24 * n)), blk(st, 1, kk), AL.subtract)
         if not last:
-            aff(blk("yh" + H, 0, EDG), blk(st, 2, EDG), eng="DAG")
             pz = bank(h)
             mm([(rb(pz, 0), [(hz, If(2.0))])], end=False)
             mm([(rb(pz, j), [(yh, I)]) for j in range(2)], begin=False)
@@ -712,15 +717,14 @@ def lend(ops, at=None):
         for n in sorted(set(a[0] for a in o["reads"] + o["writes"] if a[0][:2] in ("vb", "vp"))):
             uses.setdefault(n, []).append(i)
     names = sorted(uses, key=lambda n: uses[n][0] if at is None else (at[2][uses[n][0]], uses[n][0]))
-    free = {"vb": {"ps%d" % j: -1.0 for j in range(8) if j % 4 < 3}, "vp": {"pr%d" % j: -1.0 for j in range(NPR)}}
-    last = {}
+    free, last = {}, {}
     for n in names:
-        if at is not None:
-            f = free[n[:2]]
-            PLACE[n] = min(f, key=f.get)
-            f[PLACE[n]] = max(at[2][i] + ops[i]["cost"][at[1][i]] for i in uses[n])
-        ops[uses[n][0]]["deps"].update(last.get(PLACE[n], []))
-        last[PLACE[n]] = uses[n]
+        h = int(n[2:]) % 2
+        can = ["pr%d" % j for j in range(NPR)] if n[1] == "p" else ["bn%d" % j for j in (range(6) if at else range(3 * h, 3 * h + 3))]
+        y = PLACE[n] = min(can, key=lambda y: free.get(y, -1.0))
+        free[y] = max(at[2][i] + ops[i]["cost"][at[1][i]] for i in uses[n]) if at else uses[n][-1]
+        ops[uses[n][0]]["deps"].update(last.get(y, []))
+        last[y] = uses[n]
 
 
 def graph(ops):
@@ -848,34 +852,89 @@ def shorten(ops, init, iters, rng, reach=14):
             if j >= 0 and t[j] > m:
                 m = t[j]
             t[i] = m + p[i]
-        return max(t), r, rd, t, td, mp, ms
+        return max(t), r, rd, t, td, mp, ms, order
 
     cur = times()
     if cur is None:
         return None
-    best, tb = (cur[0], list(q), list(cur[1])), {}
+    C, r, rd, t, td, mp, ms, order = cur
+    best, tb = (C, list(q), list(r)), {}
+    pos, fin = [0] * n, [r[i] + p[i] + late[i] for i in range(n)]
+    for k, i in enumerate(order):
+        pos[i] = k
+    heads = [i for i in range(n) if not npred[i]]
+
+    def link(u, a, b):
+        x, y = mp[u], ms[u]
+        if x >= 0:
+            ms[x] = y
+        if y >= 0:
+            mp[y] = x
+        mp[u], ms[u] = a, b
+        if a >= 0:
+            ms[a] = u
+        if b >= 0:
+            mp[b] = u
+
+    def again(u):
+        lo = min(pos[u], pos[ms[u]]) if ms[u] >= 0 else pos[u]
+        hi = max(pos[u], pos[mp[u]]) if mp[u] >= 0 else pos[u]
+        seg = order[lo:hi + 1]
+        left = {i: sum(1 for j in pred[i] if pos[j] >= lo) + (mp[i] >= 0 and pos[mp[i]] >= lo) for i in seg}
+        new = [i for i in seg if not left[i]]
+        for i in new:
+            for j in succ[i] + [ms[i]]:
+                if j in left:
+                    left[j] -= 1
+                    if not left[j]:
+                        new.append(j)
+        if len(new) < len(seg):
+            return False
+        order[lo:hi + 1] = new
+        for k, i in enumerate(new):
+            pos[i] = lo + k
+        for i in order[lo:]:
+            m = 0.0
+            for j in pred[i]:
+                if fin[j] > m:
+                    m = fin[j]
+            rd[i], j = m, mp[i]
+            if j >= 0 and r[j] + p[j] > m:
+                m = r[j] + p[j]
+            r[i], fin[i] = m, m + p[i] + late[i]
+        for i in order[hi::-1]:
+            m = 0.0
+            for j in succ[i]:
+                if t[j] > m:
+                    m = t[j]
+            m += late[i]
+            td[i], j = m, ms[i]
+            if j >= 0 and t[j] > m:
+                m = t[j]
+            t[i] = m + p[i]
+        return True
+
     for it in range(iters):
-        C, r, rd, t, td, mp, ms = cur
-        c0 = [i for i in range(n) if r[i] == 0.0 and t[i] > C - 1e-6]
+        c0 = [i for i in heads if r[i] == 0.0 and t[i] > C - 1e-6]
         i = c0[int(rng.integers(len(c0)))]
         blocks = [[i]]
         while True:
-            nx = [j for j in succ[i] if abs(t[j] + late[i] + p[i] - t[i]) < 1e-6]
             j = ms[i]
-            if j >= 0 and abs(t[j] + p[i] - t[i]) < 1e-6 and (not nx or rng.random() < 0.5):
+            if j >= 0 and (t[j] > td[i] or (t[j] == td[i] and rng.random() < 0.5)):
                 blocks[-1].append(j)
                 i = j
-            elif nx:
-                i = nx[int(rng.integers(len(nx)))]
-                blocks.append([i])
-            else:
+                continue
+            nx = [j for j in succ[i] if t[j] + late[i] == td[i]]
+            if not nx:
                 break
-        cand = []
+            i = nx[int(rng.integers(len(nx)))] if len(nx) > 1 else nx[0]
+            blocks.append([i])
+        cand, pick = [], (rng.random(n) < SHARE).tolist()
         for b in blocks:
             L = len(b)
             for a in range(L):
                 u = b[a]
-                if rng.random() > 0.4:
+                if not pick[u]:
                     continue
                 if len(ops[u]["eng"]) == 1 and (L == 1 or reach < a < L - 1 - reach):
                     continue
@@ -933,28 +992,32 @@ def shorten(ops, init, iters, rng, reach=14):
             s, old = seq[q[u]], q[u]
             a = s.index(u)
             s.pop(a)
+            was = (mp[u], ms[u])
             if kind == 2:
                 seq[v].insert(k, u)
                 q[u], p[u], back = v, ops[u]["cost"][v], [(u, old)]
             else:
                 b = s.index(v)
-                s.insert(b + (1 - kind), u)
+                k = b + (1 - kind)
+                s.insert(k, u)
                 back = [(w, u) for w in s[a:b + 1]] if kind == 0 else [(u, w) for w in s[b + 1:a + 1]]
-            nw = times()
-            if nw is None:
-                seq[q[u]].remove(u)
+            x = seq[q[u]]
+            link(u, x[k - 1] if k else -1, x[k + 1] if k + 1 < len(x) else -1)
+            if not again(u):
+                x.pop(k)
+                link(u, *was)
                 q[u], p[u] = old, ops[u]["cost"][old]
                 s.insert(a, u)
                 continue
             ten = it + 100 + int(rng.integers(100))
             for kk in back:
                 tb[kk] = ten
-            cur, done = nw, True
+            C, done = max(t[i] for i in heads), True
             break
         if not done:
             tb = {}
-        if cur[0] < best[0] - 1e-6:
-            best = (cur[0], list(q), list(cur[1]))
+        if C < best[0] - 1e-6:
+            best = (C, list(q), list(r))
     return best
 
 
@@ -969,14 +1032,19 @@ def schedule(ops):
     depend(one)
     t = shorten(one, pack(one, None, EFFORT[1], rng), EFFORT[0], rng)[2]
     pair = list(zip([i for i, o in enumerate(ops) if o["half"] == 0], [i for i, o in enumerate(ops) if o["half"] == 1]))
-    res = [pack(ops, None, EFFORT[1], rng)]
+    res, keep = [], lambda x: (x, dict(PLACE), [set(o["deps"]) for o in ops])
     for lag, pace in STARTS:
         key = [t[at[i]] * pace if i in at else 0.0 for i in range(len(ops))]
         for a, b in pair:
             key[b] = key[a] + (lag if t[at[a]] > 9000 else 500.0)
-        res.append(pack(ops, key, EFFORT[1], rng))
-    res = [shorten(ops, x, EFFORT[3], rng) for x in sorted(res, key=lambda x: x[0])[:EFFORT[2]]]
-    plain = [(o["cost"], o.get("late")) for o in ops]
+        lend(ops)
+        x = pack(ops, key, 2, rng)
+        for it in range(EFFORT[1]):
+            lend(ops, x)
+            x = pack(ops, x[2], 2, rng)
+        res.append(keep(shorten(ops, x, EFFORT[3], rng)))
+    res = sorted(res, key=lambda x: x[0][0])[:EFFORT[2]]
+    plain, norm = [(o["cost"], o.get("late")) for o in ops], {}
 
     def speed(fv, fg, fp, fd):
         for o, (c, late) in zip(ops, plain):
@@ -989,7 +1057,8 @@ def schedule(ops):
         tot = 0.0
         for s in PACES:
             speed(*s)
-            tot += shorten(ops, x, 0, rng)[0] / s[0]
+            v = shorten(ops, x, 0, rng)[0]
+            tot += v * norm.setdefault(s, 170000.0 / v)
         return tot / len(PACES)
 
     def back(x):
@@ -997,8 +1066,6 @@ def schedule(ops):
         for o, d in zip(ops, x[2]):
             o["deps"] = set(d)
         return x[0]
-
-    keep = lambda x: (x, dict(PLACE), [set(o["deps"]) for o in ops])
 
     def turns(best, val, n):
         now = back(best)
@@ -1017,7 +1084,7 @@ def schedule(ops):
                 now = back(best)
         return best, val
 
-    res = [(x, 1e18) for x in [keep(x) for x in res]]
+    res = [(x, 1e18) for x in res]
     while len(res) > 1:
         res = sorted([turns(x, v, len(PACES)) for x, v in res], key=lambda x: x[1])[:len(res) // 2]
     best = turns(res[0][0], res[0][1], EFFORT[4])[0]

import numpy as np
from concourse.bass import DstId, RemoteDMATransfer
from concourse.mybir import AluOpType, ActivationFunctionType

AL = AluOpType
AF = ActivationFunctionType
W, RO = 3072, 3
HS = 272
TWO, FOUR = (0, 1024, 2048), (0, 512, 1024, 1536, 2048)
GC = {"E": TWO, "va": FOUR, "va+": FOUR, "ld": FOUR, "t1": FOUR, "rw+": FOUR, "tb": (0, 512, 1024)}
PW = 64
NPR = 6
TH = 2
GD, GY = 1024, 512
GB = 1024
RND, RNDE = 1.5 * 2 ** 23, 1.5 * 2 ** 33
OFF = 1536.0
TB = [1088, 0, 5248, 6336]
WIN = [(1088, 5248), (0, 5248), (2176, 6336), (2176, 7424)]
SHARE = 0.2
CY, PCY, GCY, LAT = 0.9, 0.42, 1.56, 140.0
STARTS = [(a, b) for a in (8000.0, 11000.0, 14000.0, 17000.0) for b in (1.15, 1.3, 1.45)]
PACES = [(0.92, 1.0, 1.0, 1.0), (1.2, 1.1, 1.4, 1.1), (1.0, 1.25, 1.2, 1.2), (0.95, 0.8, 1.35, 0.9), (1.2, 1.0, 1.1, 1.0), (0.95, 1.0, 1.65, 1.1)]
EFFORT = [200, 2, 4, 150, 270, 200, 1]

SCRATCH = {
    "vt": ("sbuf", [128, W], "float32"), "uw": ("sbuf", [128, W + 8192], "float32"), "xb": ("sbuf", [128, 2 * W], "bfloat16"),
    "nt": ("sbuf", [128, W], "int32"), "tb": ("sbuf", [128, W + 4 * 1088], "float32"),
    "bk": ("sbuf", [128, 2048], "bfloat16"), "ct": ("sbuf", [128, 14, 15], "bfloat16"), "c2": ("sbuf", [128, 14, 9], "bfloat16"),
    "cb": ("sbuf", [128, 152, 16], "bfloat16"), "zz": ("sbuf", [128, 144], "bfloat16"), "c32": ("sbuf", [128, 5, 128], "float32"),
    "cf": ("sbuf", [128, 336], "bfloat16"), "col": ("sbuf", [128, 88], "float32"), "coli": ("sbuf", [128, 8], "int32"), "se": ("sbuf", [128, 16], "bfloat16"),
    "dg": ("sbuf", [128, 2, 128], "float16"),
}
BASE = {"va0": ("uw", 0), "d80": ("uw", 2048), "ut": ("uw", 4096), "d81": ("uw", 4096 + W), "va1": ("uw", 6144 + W), "xt": ("xb", 0), "gt": ("xb", W),
        "gd0": ("tb", 0), "gd1": ("tb", 5248), "wk": ("xb", 0), "x1": ("xb", 1792), "x2": ("xb", 3472), "cm": ("xb", 4480)}
for _i in range(NPR):
    SCRATCH["pr%d" % _i] = ("sbuf", [128, 128, 4], "float32")
for _h in range(2):
    for _n, _s, _t in (("di", [2048], "int32"), ("rw", [2048 + RO * HS], "float32"),
                       ("g16", [2048], "float16"), ("t16", [2048], "float16"), ("ld", [2048], "float16"), ("y16", [2048], "float16"),
                       ("si", [896], "float32"), ("of", [640], "uint16"), ("st", [24, 16], "float32"), ("sf", [40, 16], "float32"),
                       ("sh", [48, 16], "bfloat16"), ("yh", [16, 16], "float16"), ("uf", [8, 16], "float16"), ("ue", [8, 16], "float16"), ("en", [8, 18], "float32"),
                       ("sg", [72, 16], "bfloat16"), ("ed", [128], "float32"), ("eb", [32], "bfloat16"), ("sb", [2, 136], "float32")):
        SCRATCH["%s%d" % (_n, _h)] = ("sbuf", [128] + _s, _t)
    for _i in range(3 * _h, 3 * _h + 3):
        SCRATCH["bn%d" % _i] = ("psum", [128, 512], "float32")
    SCRATCH["ps%d" % (4 * _h + 3)] = ("psum", [128, 32, 16], "float32")
NDMA = 72
SEMAPHORES = ["cD", "cA", "cP", "cG"] + ["dm%d" % i for i in range(NDMA)] \
    + ["ar%d" % i for i in range(2 * RO)] + ["lo%d" % i for i in range(2 * RO)]

S = slice
ALLP = S(None)
_IDX, PLACE = {}, {}


def ap(name, *idx, p=ALLP):
    if name in BASE:
        (name, b), s = BASE[name], idx[0]
        idx = (S(s.start + b, s.stop + b, s.step),)
    return (name, (p,) + idx)


def fl(name, k=ALLP, p=S(0, 128), shift=0):
    a, b = 16 * p.start, 16 * p.stop
    if isinstance(k, tuple):
        return ap(name, S(a + k[0], b, k[1]))
    return ap(name, S(a + shift, b + shift)) if k == ALLP else ap(name, S(a + k, b, 16))


def ind(win, off):
    return ("IND", win, off)


def spec(name):
    return SCRATCH.get({"vb": "bn0", "vp": "pr0"}.get(name[:2], name))


def region(a):
    name, idx = a
    if spec(name) is None:
        return None
    if name not in _IDX:
        fs = spec(name)[1][1:]
        _IDX[name] = np.arange(int(np.prod(fs))).reshape(fs)
    return _IDX[name][idx[1:]].ravel()


def nel(a):
    return len(region(a[2])) * 16 if a[0] == "IND" else len(region(a))


def two(a):
    return a[0] != "IND" and spec(a[0])[2] in ("bfloat16", "float16", "uint16")


def psum(a):
    return a[0] != "IND" and spec(a[0])[0] == "psum"


def real(T, a):
    if not isinstance(a, tuple):
        return a
    if a[0] == "IND":
        return real(T, a[1]).indirect(real(T, a[2]))
    return T[PLACE.get(a[0], a[0])][a[1]]


def parts(a):
    if not isinstance(a, tuple):
        return []
    return [a[1], a[2]] if a[0] == "IND" else [a]


def build():
    ops, cur, nd = [], [None, -1], [0]

    def add(eng, cost, reads, writes, emit, **kw):
        o = dict(eng=eng, cost=cost, reads=[x for r in reads for x in parts(r)], writes=writes, emit=emit, half=cur[0], rnd=cur[1])
        o.update(kw)
        ops.append(o)
        return len(ops) - 1

    def vcost(n, k):
        return 60 + max(64, n * k) * CY

    def tt(out, a, b, op):
        k = GCY if a[0] == "IND" else 1 if psum(a) or psum(b) else 2
        add("D", {"D": vcost(nel(a), k)}, [a, b], [out], lambda e: [lambda g, T: g.vector.tensor_tensor(real(T, out), real(T, a), real(T, b), op)])

    def tsf(out, a, s1, op0, s2, op1):
        if op1 is None:
            return lambda g, T: g.vector.tensor_scalar(real(T, out), real(T, a), real(T, s1), None, op0)
        return lambda g, T: g.vector.tensor_scalar(real(T, out), real(T, a), real(T, s1), real(T, s2), op0, op1)

    def ts(out, a, s1, op0, s2=None, op1=None):
        k = 0.5 if two(a) and two(out) else 1
        add("D", {"D": vcost(nel(a), k)}, [a, s1, s2], [out], lambda e: [tsf(out, a, s1, op0, s2, op1)])

    def mset(out, v):
        fs = {"D": lambda g, T: g.vector.memset(real(T, out), v),
              "G": lambda g, T: g.iota(real(T, out), [[0, nel(out)]], int(v), 0, allow_small_or_imprecise_dtypes=True)}
        add("GD", {"D": vcost(nel(out), 0.5 if two(out) else 1), "G": 130 + 2 * nel(out) * CY}, [], [out], lambda e: [fs[e]])

    def act(out, a, fn, scale=1.0, bias=0.0, alt=None, eng="DA"):
        k = GCY if a[0] == "IND" else 1

        def emit(e):
            if e == "A":
                return [lambda g, T: g.scalar.activation(real(T, out), real(T, a), fn, bias=real(T, bias), scale=real(T, scale))]
            if e == "G":
                return [lambda g, T: g.affine_select(real(T, out), real(T, a), [[0, nel(a)]], AL.is_equal, 0.0, 0, 0)]
            if alt == ():
                return [lambda g, T: g.vector.tensor_copy(real(T, out), real(T, a))]
            return [tsf(out, a, *alt)]
        kd = 0.5 if two(a) and two(out) else k
        add("A" if alt is None else eng, {"D": vcost(nel(a), kd), "A": vcost(nel(a), k), "G": 170 + 2 * nel(a) * CY}, [a, scale, bias], [out], emit)

    def aff(out, a, scale=1.0, bias=0.0, eng="DA"):
        act(out, a, AF.Identity, scale, bias, () if scale == 1.0 and bias == 0.0 else (scale, AL.mult, bias, AL.add), eng)

    def mm(lst, begin=True, end=True):
        fs, cost, rd, wr = [], 30, [] if begin else [lst[0][0]], []
        for out, terms in lst:
            wr.append(out)
            for i, tm in enumerate(terms):
                l, r = tm[0], tm[1]
                o = tm[2] if len(tm) > 2 else out
                cost += max(64, nel(r) * (1 if two(l) else 4)) * PCY
                rd += [l, r]
                fs.append(lambda g, T, o=o, l=l, r=r, a=(i == 0 and (begin or len(wr) > 1)), b=(end and i == len(terms) - 1): g.tensor.matmul(real(T, o), real(T, l), real(T, r), a, b))
        add("P", {"P": cost}, rd, wr, lambda e: fs)

    def iota(out, pat, base, cm):
        if SCRATCH[out[0]][2] == "int32":
            f = lambda g, T: g.iota(real(T, out), pat, base, cm)
        else:
            f = lambda g, T: g.iota(real(T, out), pat, base, cm, allow_small_or_imprecise_dtypes=True)
        add("G", {"G": 130 + 2 * nel(out) * CY}, [], [out], lambda e: [f])

    def sel(out, a, pat, cmp, fill, base, cm):
        add("G", {"G": 170 + 2 * nel(a) * CY}, [a], [out], lambda e: [lambda g, T: g.affine_select(real(T, out), real(T, a), pat, cmp, fill, base, cm)])

    def dma(out, a, nbytes, q="S"):
        sem = "dm%d" % nd[0]
        nd[0] += 1
        if q == "G":
            f = lambda g, T: g.dma_start(real(T, out), real(T, a), accum_op=AL.add)
            return add(q, {q: 1000.0}, [a, out], [out], lambda e: [f], sem=sem, inc=16, late=2500 + nbytes / 150.0)
        if q == "S":
            f = lambda g, T: g.sync.dma_start(real(T, out), real(T, a))
        else:
            f = lambda g, T: g.scalar.dma_start(real(T, out), real(T, a))
        add(q, {q: 80.0}, [a], [out], lambda e: [f], sem=sem, inc=16, late=2000 + nbytes / 250.0)

    def dmas(lst, nbytes):
        nd[0] += 1
        fs = [lambda g, T, o=o, a=a: g.sync.dma_start(real(T, o), real(T, a)) for o, a in lst]
        add("S", {"S": 80.0 * len(lst)}, [a for o, a in lst], [o for o, a in lst], lambda e: fs, sem="dm%d" % (nd[0] - 1), inc=16, late=2200 + nbytes / 250.0)

    EQ, GE = AL.is_equal, AL.is_ge
    EDG = S(0, 16, 15)
    blk = lambda n, j, k=ALLP, w=1: ap(n, S(8 * j, 8 * (j + w)), k)
    rb = lambda n, j, w=1: ap(n, S(128 * j, 128 * (j + w)))
    pin = lambda j, h: ap("di0", S(256 * j + 128 * h, 256 * j + 128 * h + 128))
    dma(ap("di0", S(0, 256)), ap("pa", ALLP), 131072)
    dma(ap("di0", S(256, 512)), ap("pb", ALLP), 131072, "A")
    dma(ap("di0", S(512, 768)), ap("lam", ALLP), 131072)
    for a in range(0, W, 1024):
        dma(ap("xt", S(a, a + 1024)), ap("xrec", S(a, a + 1024)), 400000 + 512 * (a + 1024), "A")
        dma(ap("gt", S(a, a + 1024)), ap("grec", S(a, a + 1024)), 400000 + 512 * (a + 1024))
    for a in range(2176, 5248, 768):
        mset(ap("tb", S(a, a + 768)), 0)
    ee = lambda j: ap("va1" if j else "di1", S(192 * j, 192 * j + 192))
    dma(ee(0), ap("erec", ALLP), 98304, "A")
    ts(ee(1), ee(0), RNDE, AL.add, -RNDE, AL.add)
    tt(ee(2), ee(0), ee(1), AL.subtract)
    dmas([(ap("tb", S(2176, 5248), p=S(2 * j, 128, 16)), ee(1 + j)) for j in range(2)], 98304 * 2)
    dma(ap("nt", ALLP), ap("nbr", ALLP), 1572864 * 2)
    ops[-1]["reads"] += [ap("gt", S(1024, 1032)), ap("tb", S(2176, 2184))]
    cb = lambda j, k=ALLP: blk("cb", j, k)
    I, ONE, BC, P32, G15, IM = [cb(j) for j in (0, 1, 2, 3, 4, 17)]
    cm = lambda j, p=ALLP: ap("cm", S(128 * j, 128 * j + 128), p=p)
    I32, ONE32 = ap("c32", 0, ALLP), ap("c32", 1, ALLP)
    mset(ONE, 1.0)
    mset(ONE32, 1.0)
    sel(I, ONE, [[-1, 128]], EQ, 0.0, 0, 1)
    sel(I32, ONE32, [[-1, 128]], EQ, 0.0, 0, 1)
    iota(cb(16), [[0, 128]], 0, 0)

    def diag(out, v):
        aff(out, I, v, eng="DAG")
        plain = ops[-1]["emit"]
        ops[-1]["reads"].append(cb(16))
        ops[-1]["emit"] = lambda e: plain(e) if e != "G" else [lambda g, T: g.affine_select(real(T, out), real(T, cb(16)), [[-1, 128]], AL.not_equal, v, 0, 1)]

    sc, sf32 = {}, {}
    sc[1.0] = 0
    for j, v in enumerate((1.0 / 512, -1.0, -2.0, 2.0, 1.0 / 16, -7.0 / 16, 8.0, 0.5, -4.0, 1.0 / 32, -65536.0, 0.125)):
        sc[v] = 5 + j if j < 11 else 18
        diag(cb(sc[v]), v)
    for j, v in enumerate((-1.0, 2.0, -0.5)):
        sf32[v] = ap("c32", 2 + j, ALLP)
        diag(sf32[v], v)
    Ib = lambda v, k=ALLP: cb(sc[v], k)
    If = lambda v: sf32[v]
    cl = lambda a, n=1: ap("col", S(a, a + n))
    GS, SCL = cl(32, 8), cl(27)
    SEH, SEN = ap("se", S(0, 8)), ap("se", S(8, 16))
    aff(cl(40, 8), ap("c32", 0, S(0, 128, 16)), 16.0)
    tt(SEH, cl(40, 8), ap("cb", S(8 * sc[0.5], 8 * sc[0.5] + 8), 2), AL.add)
    aff(SEN, SEH, -1.0)
    sel(GS, ap("c32", 1, S(0, 8)), [[-16, 8]], GE, 0.0, 0, 1)
    sel(GS, GS, [[16, 8]], GE, 0.0, 15, -1)
    mset(ap("bk", ALLP), -1.0)
    sel(ap("bk", ALLP), ap("bk", ALLP), [[-1, 16], [-16, 8], [0, 16]], EQ, 0.0, 0, 1)
    iota(P32, [[1, 128]], 0, 0)
    iota(ap("coli", S(0, 1)), [[0, 1]], 0, 1)
    iota(cl(0, 3), [[-HS, 3]], 1 - 2048, 15)
    iota(cl(3, 3), [[HS, 3]], 2048 + 136 - 14, -15)
    iota(cl(6, 3), [[HS, 3]], 1025, 0)
    aff(cl(0, 6), cl(0, 6), 0.5)
    ts(ap("coli", S(4, 5)), ap("coli", S(0, 1)), 15, AL.bitwise_and)
    aff(cl(12), ap("coli", S(4, 5)), eng="D")
    ts(cl(13), cl(12), 0.0, EQ)
    ts(SCL, cl(12), 2.0, GE, 1.0 / 32, AL.max)
    ts(cl(14), cl(12), 15.0, EQ, 1024.0, AL.mult)
    ts(cl(14), cl(14), cl(12), AL.add, -1.0, AL.add)
    ts(cl(16, 3), cl(6, 3), cl(13), AL.mult, cl(14), AL.add)
    aff(cl(15), cl(13), -15.0, 16.0)
    aff(BC, P32, cl(15))
    aff(P32, P32, 1.0 / 32)

    rot, prn = [0, 0], [0]

    def bank(h):
        rot[h] += 1
        return "vb%d" % (2 * rot[h] + h)

    def newpr():
        prn[0] += 1
        return "vp%d" % prn[0]

    def table():
        cur[0] = None
        for a in range(0, W, 512):
            pv = ap(bank(a // 512 % 2), ALLP)
            mm([(pv, [(Ib(8.0), ap("xt", S(a, a + 512))), (Ib(1.0 / 512), ap("gt", S(a, a + 512)))])])
            aff(ap("vt", S(a, a + 512)), pv, 1.0, 1025.0)
        for a in range(0, W, 1024):
            aff(ap("ut", S(a, a + 1024)), ap("vt", S(a, a + 1024)), -1.0)

    def late_consts():
        cur[0] = None
        zz = ap("zz", ALLP)
        iota(zz, [[0, 144]], 1, 0)
        sel(zz, zz, [[0, 9], [1, 16]], EQ, 0.0, -15, 0)
        ts(cl(24), cl(12), 15.0, EQ, cl(13), AL.add)
        aff(cl(26), cl(24), -1.0, 1.0)
        aff(IM, I, cl(26))
        iota(cm(3), [[16, 128]], 0, 0)
        sel(cm(3), cm(3), [[0, 128]], EQ, 1.0, 0, 1)
        diag(cm(4), 65536.0)
        iota(cm(5), [[0, 8], [1, 16]], 0, 0)
        sel(cm(5), cm(5), [[0, 128]], EQ, 1.0, -1, 1)
        for j, v in ((7, -4096 - OFF), (8, W + 2048 - OFF)):
            sel(cm(j), cm(5), [[0, 128]], AL.not_equal, v, -2, 1)
        iota(cm(6), [[0, 8], [-1, 16]], 0, 0)
        sel(cm(6), cm(6), [[0, 128]], EQ, 0.0, -1, 1)
        iota(cl(85, 2), [[W + 2048, 2]], -2048 - int(OFF), 16)
        iota(cl(28, 2), [[-W - 6144, 2]], 4096 + int(OFF), -16)
        for h in range(2):
            aff(ap("dg", h, ALLP), I, cl(28 + h))
        for u in range(4):
            a, b = 448.0 + TB[u] - WIN[u][0], OFF + 2176 - WIN[u][0]
            aff(cl(20 + u), cl(24), b - a, a)
        sel(zz, zz, [[-16, 9], [0, 16]], GE, 0.0, 0, 1)
        sel(zz, zz, [[16, 9], [0, 16]], GE, 0.0, 15, -1)
        sel(G15, ONE, [[-16, 8], [0, 16]], GE, 0.0, 0, 1)
        sel(G15, G15, [[16, 8], [0, 16]], GE, 0.0, 14, -1)
        sel(cm(0), G15, [[16, 8], [1, 16]], AL.is_gt, 0.0, 0, -1)
        aff(cm(1), cm(0), 128.0)
        aff(cm(2), G15, 128.0)
        iota(cm(9), [[0, 128]], 16, 0)
        sel(cm(9), cm(9), [[-16, 8], [-1, 16]], GE, -16.0, 0, 1)
        sel(cm(9), cm(9), [[-16, 8], [0, 16]], GE, 0.0, 0, 1)
        sel(cm(9), cm(9), [[16, 8], [0, 16]], GE, 0.0, 14, -1)
        iota(ap("cm", S(9 * 128 + 15, 1280, 16)), [[0, 8]], 0, 0)
        for k in range(1, 15):
            ts(ap("wk", S(128 * (k - 1), 128 * k)), cm(9), float(k), AL.min, float(k - 15), AL.max)
        iota(cl(56, 12), [[1, 12]], 0, 0)
        ts(cl(56, 12), cl(56, 12), cl(12), EQ)
        iota(ap("ct", ALLP, S(2, 10)), [[0, 14], [30, 8]], 15, 0)
        iota(ap("ct", ALLP, S(10, 11)), [[0, 14]], 225, 0)
        for j in range(2):
            aff(ap("ct", ALLP, j), ap("c32", 1, S(0, 14)), cl(60 + j))
        iota(ap("c2", ALLP, ALLP), [[16, 14], [0, 9]], 16, 0)
        aff(cl(56, 2), cl(56, 2), 16.0)
        aff(cl(58, 4), cl(58, 4), 0.5)
        tt(cl(68, 6), ap("col", S(56, 68, 2)), ap("col", S(57, 68, 2)), AL.subtract)
        tt(cl(74, 6), ap("col", S(56, 68, 2)), ap("col", S(57, 68, 2)), AL.add)
        tt(cl(80), cl(71), cl(72), AL.add)
        ts(cl(81), cl(62), cl(64), AL.add, -240.0, AL.mult)
        x = ap("ct", ALLP, S(2, 11))
        aff(x, x, cl(80), cl(81))
        aff(ap("c2", ALLP, ALLP), ap("c2", ALLP, ALLP), cl(79))
        tt(x, x, ap("c2", ALLP, ALLP), AL.add)
        ts(cl(82), cl(68), cl(69), AL.add, -1.0, AL.mult)
        for j, (a, b) in enumerate(((-1.0, cl(70)), (1.0, cl(82)), (1.0, cl(76)), (cl(74), cl(75)))):
            if j == 3:
                aff(ap("ct", ALLP, 13), ap("c32", 1, S(0, 14)), a, b)
            else:
                ts(ap("ct", ALLP, (11, 12, 14)[j]), ap("c32", 1, S(0, 14)), b, AL.mult, a, AL.mult)
        ts(cl(83), cl(77), cl(66), AL.add, 128.0, AL.mult)
        ts(cl(83), cl(12), 6.0, AL.is_lt, cl(83), AL.add)
        tt(cl(84), cl(78), cl(67), AL.add)
        aff(ap("cf", S(0, 210)), ap("ct", ALLP, ALLP), cl(83))
        aff(ap("cf", S(210, 336)), x, cl(84))
        for j in range(8):
            aff(ap("x1", S(j, 2688, 8)), ap("cf", ALLP), cl(32 + j), eng="AD")
        for h in range(2):
            aff(ap("ue%d" % h, ALLP, ALLP), ONE, 0.0)
            iota(ap("sg%d" % h, ALLP, EDG), [[0, 144]], 0, 0)
            iota(ap("tb", S(5248 * h + 2048, 5248 * h + 2176)), [[0, 128]], 0, 0)

    def names(h):
        H = str(h)
        c = lambda n, k=ALLP, p=S(0, 128), shift=0: fl(n + H, k, p, shift)
        of = lambda j, a=0, b=128: ap("of" + H, S(128 * j + a, 128 * j + b))
        return H, c, of, "ps%d" % (4 * h + 3)

    def gathers(dst, win, oj, h, scale=1.0, bias=0.0):
        H, c, of, sm = names(h)
        cut = GC["E" if cur[1] < 0 else dst[:2]]
        for a, b in zip(cut, cut[1:]):
            aff(ap(dst, S(a, b)), ind(win, of(oj, a // 16, b // 16)), scale, bias)

    def gather_add(dst, win, oj, other, h, op=AL.add):
        H, c, of, sm = names(h)
        for a, b in zip(GC[other[:2] + "+"], GC[other[:2] + "+"][1:]):
            tt(ap(dst, S(a, b)), ind(win, of(oj, a // 16, b // 16)), ap(other, S(a, b)), op)

    VT, NT, ET = ap("vt", ALLP), ap("nt", ALLP), ap("tb", S(2176, 5248))

    def first(h):
        cur[0] = h
        H, c, of, sm = names(h)
        st, sf, sh, ed = "st" + H, "sf" + H, "sh" + H, "ed" + H
        a, b, f = [ap("ld0", S(256 * j + 128 * h, 256 * j + 128 * h + 128)) for j in range(3)]
        fd = ap("rw0", S(128 * h, 128 * h + 128))
        if h == 0:
            cur[0] = None
            aff(ap("ld0", S(0, 512)), ap("di0", S(0, 512)), 1.0, -OFF)
            ts(ap("ld0", S(512, 768)), ap("di0", S(512, 768)), 8.0, EQ)
            mm([(blk(sm, 0, w=2), [(I, ap("ld0", S(256, 512))), (Ib(-1.0), ap("ld0", S(0, 256)))])])
            tt(ap("rw0", S(0, 256)), blk(sm, 0, w=2), ap("ld0", S(512, 768)), AL.mult)
            ts(ap("di0", S(512, 768)), ap("di0", S(512, 768)), 7, AL.bitwise_and)
            cur[0] = h
        mm([(blk(sm, 0), [(I, a), (I32, fd)]), (blk(sm, 1), [(I, b), (If(-1.0), fd)])])
        aff(of(0, 0, 256), blk(sm, 0, w=2), 1.0, OFF)
        aff(blk(sh, 0), pin(2, h), 0.125)
        gathers("t16" + H, ET, 1, h, SCL)
        gathers("y16" + H, ET, 0, h, SCL)
        mm([(blk(sm, 2), [(b, I), (fd, If(-1.0))]), (blk(sm, 0), [(a, I), (b, Ib(-1.0)), (fd, If(2.0))]), (blk(sm, 1), [(f, I)])])
        aff(blk("yh" + H, 0), blk(sm, 2))
        aff(blk(st, 0), blk(sm, 0), 0.5)
        aff(ap(ed, S(96, 112)), blk(sm, 1, EDG), 2.0, -1.0)
        aff(ap(ed, S(112, 128)), blk(sm, 1, EDG), -4.0, 2.0)
        mm([(blk(sm, 3, k), [(c("t16", k), SEH)]) for k in range(16)])
        aff(blk(st, 2), blk(sm, 3), 2.0)
        mm([(blk(sm, 1, k), [(c("y16", k), SEH), (c("t16", k), SEN)]) for k in range(16)])
        aff(blk(st, 1), blk(sm, 1))

    def spread(h, x, p0, a):
        pl = bank(h)
        mm([(ap(pl, S(k, 512, 8)), [(ap("bk", S(128 * (a + 2 * k), 128 * (a + 2 * k) + 128)), ap(x[0], S(x[1] + p0 // 16, x[1] + p0 // 16 + 4), ALLP))]) for k in range(8)])
        return ap(pl, ALLP), dict(k=(a, 2), p=S(p0, p0 + 64))

    def send(h, r):
        rw, sb, a = "rw%d" % h, "sb%d" % h, 2048 + HS * r
        u, tr = 2 * r + h, [(ap(sb, j, ALLP), ap(rw, S(a + 136 * j, a + 136 * j + 136))) for j in range(2)]
        i = add("G", {"G": 1000.0}, [ap(sb, ALLP, ALLP)], [], None, sem="lo%d" % u, inc=8, late=2500.0 if u else 6000.0, send=tr, arr="ar%d" % u)
        add("X", {"X": 0.0}, [], [x[1] for x in tr], None, sem="ar%d" % u, inc=8, late=2000.0, after=i)

    def step1(h, r):
        cur[0] = h
        H, c, of, sm = names(h)
        st, sf, sh, rw = "st" + H, "sf" + H, "sh" + H, "rw" + H
        hz, hE, Ey = [blk(st, j) for j in range(3)]
        lb = blk(sh, 0)
        gathers("va" + H, VT, 0, h, -1.0)
        gather_add("d8" + H, VT, 1, "va" + H, h)
        pq = rb(bank(h), 0)
        mm([(pq, [(Ib(2.0), ONE), (lb, Ib(-2.0))])])
        tt(pq, pq, hE, AL.mult)
        en = lambda k: ap("en" + H, ALLP, k)
        tt(en(S(1, 17)), pq, Ey, AL.add)
        aff(ap("sb" + H, 0, S(128, 136)), en(16), eng="DAG")
        aff(ap("sb" + H, 1, S(128, 136)), en(1), eng="DAG")
        if r == 0:
            pb = bank(h)
            mm([(rb(pb, j), [(ap("bk", S(128 * k, 128 * k + 128)), lb)]) for j, k in ((0, 15), (1, 0))])
            for j, k in ((0, 15), (1, 0)):
                tt(rb(pb, j), c("d8", k), rb(pb, j), AL.mult)
                tt(ap("sb" + H, j, S(0, 128)), rb(pb, j), c("va", k), AL.add)
        for p0 in (0, 64):
            for a in range(16 * p0, 16 * p0 + 1024, GD):
                aff(ap("di" + H, S(a, a + GD)), ap("d8" + H, S(a, a + GD)), eng="G")
            for a in range(2):
                pw, ks = spread(h, (sh, 0), p0, a)
                tt(pw, c("d8", **ks), pw, AL.mult)
                tt(c("rw", **ks), pw, c("va", **ks), AL.add)
            for a in range(16 * p0, 16 * p0 + 1024, GY):
                aff(ap("y16" + H, S(a, a + GY)), ap(rw, S(a, a + GY)), -8.0)
            for a in range(2):
                pw, pg, pp = ap(bank(h), ALLP), ap(bank(h), ALLP), S(p0 + 32 * a, p0 + 32 * a + 32)
                mm([(pw, [(Ib(0.125), c("y16", p=pp))])])
                tt(c("g16", p=pp), pw, c("rw", p=pp), AL.add)
                mm([(pg, [(I, c("g16", p=pp))])])
                tt(c("gd", p=pp), pg, c("di", p=pp), AL.mult)
        send(h, r)
        dma(ap("d8" + H, S(0, 2048)), ap("va" + H, S(0, 2048)), 1048576, "G")
        gathers("ld" + H, NT, 0, h, 1.0, -OFF)
        sl = 2048 + HS * r
        mo = lambda k=ALLP: ap("uf" + H, ALLP, k)
        aff(en(0), ap(rw, S(sl + 128, sl + 136)), eng="DAG")
        aff(en(17), ap(rw, S(sl + 264, sl + 272)), eng="DAG")
        po = bank(h)
        tt(mo(), en(S(2, 18)), en(S(0, 16)), GE)
        aff(mo(0), mo(0), cl(r), 512.0)
        aff(mo(15), mo(15), cl(3 + r), -512.0)
        mm([(rb(po, 0), [(I, BC), (mo(), Ib(2.0))])])
        aff(of(2), rb(po, 0), 1.0, cl(16 + r))
        red = lambda j, pr, a: mm([(blk(sm, j, a + 4 * k), [(ap(pr, ALLP, k), GS)]) for k in range(4)])
        for a in range(4):
            mm([(blk(sm, 0, k), [(c("gd", k), GS)]) for k in range(a, 16, 4)])
        gathers("t16" + H, ap(rw, S(0, sl + HS)), 2, h, 8.0)
        for a in range(0, 2048, GB):
            aff(ap(rw, S(a, a + GB)), ap("y16" + H, S(a, a + GB)), eng="DAG")
            dma(ap(rw, S(a, a + GB)), ap("va" + H, S(a, a + GB)), 512 * GB, "G")
        for a in range(4):
            pt, ks = ap(bank(h), ALLP), (a, 4)
            ptd, pgt, ptt = newpr(), newpr(), newpr()
            mm([(pt, [(I, c("y16", ks))])], end=False)
            mm([(pt, [(I, c("t16", ks))])], begin=False)
            act(ap(ptt, ALLP, ALLP), pt, AF.Square)
            tt(ap(ptd, ALLP, ALLP), c("di", ks), pt, AL.mult)
            tt(ap(pgt, ALLP, ALLP), c("g16", ks), pt, AL.mult)
            for j, pr in ((2, ptt), (3, ptd), (1, pgt)):
                red(j, pr, a)

    def step23(h, r):
        cur[0] = h
        H, c, of, sm = names(h)
        st, sf, sh, ed, sg, si = "st" + H, "sf" + H, "sh" + H, "ed" + H, "sg" + H, "si" + H
        last = r == RO - 1
        nq = 1 if last else 2
        hz, hE, Ey = [blk(st, j) for j in range(3)]
        lb, up, dn = [blk(sh, j) for j in range(3)]
        yh = blk("yh" + H, 0)
        pn, lh, u1, u2 = bank(h), lambda j: cm(j, S(0, 3)), blk("yh" + H, 1), ap("uf" + H, ALLP, ALLP)
        mm([(rb(pn, 1), [(lh(3), lh(6)), (I, yh)]),
            (rb(pn, 0), [(lh(3), lh(6)), (lb, cm(4) if h else Ib(-65536.0))] + [(c("ld", k), cb(0, k), ap(pn, S(k, 128, 16))) for k in range(16)])])
        ts(rb(pn, 0), rb(pn, 0), cl(85 + h), AL.min if h else AL.max)
        aff(blk(sf, 2, w=2), blk(sm, 2, w=2))
        tt(blk(sf, 4), blk(sm, 0), blk(sf, 2), AL.mult)
        tt(blk(sm, 1), blk(sm, 1), blk(sf, 3), AL.mult)
        tt(dn, blk(sm, 1), blk(sf, 4), AL.is_gt)
        tt(u2, rb(pn, 0), dn, AL.mult)
        tt(up, blk(sm, 1), blk(sf, 4), AL.is_lt)
        tt(u1, rb(pn, 1), up, AL.mult)
        pu = bank(h)
        mm([(rb(pu, 0), [(lh(7 + h), lh(3)), (dn, ap("dg", h, ALLP)), (u2, I)])], end=False)
        mm([(rb(pu, 0), [(up, ap("dg", h, ALLP)), (u1, I)])], begin=False)
        aff(of(3), rb(pu, 0), 1.0, OFF + 4096 * (1 - h))
        gather_add("ld" + H, ap("uw", S(4096 * h, 4096 * h + 4096 + W)), 3, "rw" + H, h, AL.subtract)
        mm([(blk(sm, 0), [(lb, Ib(8.0)), (Ib(-1.0), dn), (I, up)])])
        mu, ove = ap("eb" + H, S(0, 16)), ap("eb" + H, S(16, 32))
        act(ove, blk(sm, 0, EDG), AF.Relu, -1.0, 0.0, (-1.0, EQ, 1.0, AL.mult))
        if not last:
            act(mu, blk(sm, 0, EDG), AF.Relu, 2.0, -14.0, (8.0, EQ, 2.0, AL.mult))
        ts(blk(sm, 0), blk(sm, 0), 5.0, AL.is_lt, 2.0, AL.mult)
        for j in range(nq):
            tt(blk(sf, 3 + j), blk(sm, 0), blk(st, j), AL.mult)
        pc = bank(h)
        if not last:
            mm([(rb(pc, 1), [(Ey, I32)])], end=False)
        mm([(rb(pc, 1), [(blk(sf, 4), I32)])] * (nq - 1) + [(rb(pc, 0), [(yh, I), (blk(sf, 3), I32)])], begin=last)
        aff(ap(si, S(256, 384)), rb(pc, 0))
        if not last:
            ts(ap(si, S(0, 128)), rb(pc, 1), RNDE, AL.add, -RNDE, AL.add)
            tt(ap(si, S(128, 256)), rb(pc, 1), ap(si, S(0, 128)), AL.subtract)
        row = lambda j, u, a: ap("tb", S(TB[2 * h + u] + PW * a, TB[2 * h + u] + PW * (a + 16)), p=S(j, 128, 16))
        for u in range(2):
            dmas([(row(j, u, 1 - j % 2), ap(si, S(128 * (j // 2) + u * PW, 128 * (j // 2) + (u + 1) * PW))) for j in range(4 * last, 6)], 1024 * nq * PW)
        pb = bank(h)
        er = lambda j, n=1: ap(pb, S(16 * j, 16 * (j + n))) if j < 29 else ap(sm, S(j, j + n), ALLP)
        on16, pe = ap("cb", 8, ALLP), ap(ed, S(64, 80))
        mm([(er(23), [(I, blk("yh" + H, 0, EDG)), (Ib(-1.0), ap("uf" + H, ALLP, EDG)), (lh(3), ap("cm", S(783, 896, 16), p=S(0, 3)), ap(pb, S(369, 384, 2)))])])
        tt(pe, er(23), ove, AL.mult)
        lp = [(lb, Ib(8.0, EDG)), (I, blk(sh, 1, EDG)), (Ib(-1.0), blk(sh, 2, EDG)), (Ib(8.0), ove)]
        if not last:
            tt(ap("ue" + H, ALLP, EDG), blk("yh" + H, 0, EDG), pe, AL.subtract)
            for j, k in ((0, 15), (1, 0)):
                aff(ap("sb" + H, j, S(0, 128)), c("ld", k), 0.125)
            mm([(er(16 + j), [(I, on16), (Ib(-2.0), ove), (Ib(-1.0), mu)]) for j in range(2)]
               + [(er(20), lp + [(Ib(-4.0), mu)])] + [(er(21 + j), [(I, on16), (Ib(-1.0), mu)]) for j in range(2)])
            tt(ap(ed, S(0, 32)), er(16, 2), blk(st, 0, EDG, 2), AL.mult)
            tt(ap(ed, S(96, 128)), er(21, 2), ap(ed, S(96, 128)), AL.mult)
            aff(blk(sg, 0, EDG), er(20), 2.0)
            eg = lambda j, w=1: blk(st, j, EDG, w)
            mm([(er(24, 2), [(I32, ap(ed, S(0, 32))), (If(-0.5), pe, er(24)), (If(-0.5), eg(2), er(25))]),
                (er(26), [(I32, eg(1)), (I32, eg(2)), (If(-1.0), ap(ed, S(16, 32)))]), (er(27), [(I32, eg(0)), (I, blk("yh" + H, 0, EDG)), (If(-1.0), ap(ed, S(0, 16)))])])
            aff(eg(0, 3), er(24, 3))
            aff(blk("yh" + H, 0, EDG), er(27))
        else:
            mm([(er(16), [(I, on16), (Ib(-2.0), ove)]), (er(20), lp + [(Ib(-4.0), on16)])])
            tt(ap(ed, S(0, 16)), er(16), blk(st, 0, EDG), AL.mult)
            tt(blk(sg, 0, EDG), er(20), ap(ed, S(112, 128)), AL.mult)
            mm([(er(24), [(I32, ap(ed, S(0, 16))), (If(-0.5), pe)]), (er(25), [(I32, blk(st, 0, EDG)), (If(-0.5), pe), (I, blk("yh" + H, 0, EDG))])])
            tt(blk(st, 0, EDG), er(24), ap(ed, S(96, 112)), AL.mult)
            for j, op in enumerate((AL.subtract, AL.add)):
                tt(blk("yh" + H, j, EDG), er(25), blk(st, 0, EDG), op)
        zc = lambda k: ap("zz", S(15 - k, 143 - k))
        wk = lambda k: ap("wk", S(128 * (k - 1), 128 * k))
        qb = lambda n, j, w=1: ap(n, S(64 * j, 64 * (j + w)))
        part = lambda n, j, p0: ap(n, S(8 * j + p0 // 16, 8 * j + (p0 + PW) // 16), ALLP)
        sn = lambda p0, k, n=1: ap("g16" + H, S(16 * p0 + PW * k, 16 * p0 + PW * (k + n)))

        def hops(a):
            pd, pp = ap(bank(h), ALLP), S(a, a + 32)
            mm([(pd, [(Ib(-1.0), c("ld", p=pp)), (I, ap("ld" + H, S(16 * a + 1, 16 * a + 512)), ap(pd[0], S(0, 511)))])])
            act(c("t16", p=pp), pd, AF.Abs, 1.0 / 1024)

        def lengths(p0):
            ph = part(sm, 0, p0)
            mm([(ph, [(zc(k), c("t16", k, S(p0, p0 + PW))) for k in range(15)])])
            ts(part(sh, 4, p0), ph, RND, AL.add, -RND, AL.add)
            tt(part(sh, 5, p0), ph, part(sh, 4, p0), AL.subtract)

        def rows(p0):
            pq, s0 = bank(h), 384 + 4 * p0
            mm([(qb(pq, j), [(w, part(sh, 4 + j % 2, p0))]) for j, w in enumerate((cm(0), cm(1), G15, cm(2)))])
            aff(ap(si, S(s0, s0 + 4 * PW)), qb(pq, 0, 4))
            dmas([(row(6 + j, p0 // PW, a), ap(si, S(s0 + b * PW, s0 + (b + 1) * PW))) for j, (a, b) in enumerate(((1, 0), (0, 0), (1, 1), (0, 1), (1, 2), (1, 3)))], 3072 * PW)

        def signs(p0, b):
            pk = bank(h)
            mm([(qb(pk, j), [(wk(b + j), part(sh, 4, p0)), (wk(b + j), part(sh, 5, p0))]) for j in range(7)])
            act(sn(p0, b, 7), qb(pk, 0, 7), AF.Sign, 1.0, 1.0 / 256)

        def count(p0):
            pc, u, pp = part(sm, 1, p0) if p0 else qb(bank(h), 0), 2 * h + p0 // PW, S(p0, p0 + PW)
            b = 8 * sc[1.0 / 32] + p0 // 16
            ends = [] if last else [(ap("ue" + H, ALLP, ALLP, p=pp), ap("cb", S(b, b + 4), ALLP, p=pp))]
            mm([(pc, [(I if last else IM, ap("cb", S(24, 28), ALLP))] + ends + [(zc(k), sn(p0, k)) for k in range(1, 15)])])
            aff(of(4, p0, p0 + PW), pc, 32.0, 448.0 + TB[u] - WIN[u][0] if last else cl(20 + u))
            for a, b in zip(GC["tb"], GC["tb"][1:]):
                aff(ap("t16" + H, S(16 * p0 + a, 16 * p0 + b)), ind(ap("tb", S(*WIN[u])), of(4, p0 + a // 16, p0 + b // 16)), SCL)

        for f, *x in ((hops, 0), (hops, 32), (lengths, 0), (hops, 64), (rows, 0), (hops, 96), (signs, 0, 1), (lengths, 64), (signs, 0, 8),
                      (rows, 64), (count, 0), (signs, 64, 1), (signs, 64, 8), (count, 64)):
            f(*x)
        if not last:
            mm([(ap(sm, 29, S(e, 16, 2)), [(c("t16", 15 * e), SEH)]) for e in range(2)])
            tt(blk(st, 1, EDG), er(29), blk(st, 1, EDG), AL.add)
        pz, nb, (a0, ne) = bank(h), 64 if last else 72, (0, 16) if last else (88, 32)
        x1 = lambda k, a, n: ap("x1", S(120 * (k - 1) + a, 120 * (k - 1) + a + n))
        n = 14 // TH
        mm([(ap(pz, S(ne * n * ((k - 1) // n) + (k - 1) % n, ne * n * ((k - 1) // n + 1), n)), [(c("t16", k), x1(k, a0, ne))]) for k in range(1, 15)])
        for b in range(2):
            px = bank(h)
            mm([(ap(px, S(k - 1 - 7 * b, 7 * nb, 7)), [(c("t16", k), x1(k, 16, nb)), (c("t16", k), ap("x2", S(72 * (k - 1), 72 * (k - 1) + nb)))]) for k in range(1 + 7 * b, 8 + 7 * b)])
            act(ap(sg, S(0, nb), S(1 + 7 * b, 8 + 7 * b)), ap(px, S(0, 7 * nb)), AF.Sign, 1.0, 0.5)
        for b in range(1 if last else TH):
            kk, a = S(1 + n * b, 1 + n * b + n), ne * n * b
            if last:
                for a in range(TH):
                    aff(ap("yh" + H, ALLP, S(1 + n * a, 1 + n * a + n)), ap(pz, S(16 * n * a, 16 * n * a + 16 * n)))
            else:
                tt(ap(st, S(0, 16), kk), ap(pz, S(a, a + 16 * n)), ap(sg, S(56, 72), kk), AL.mult)
                tt(blk("yh" + H, 0, kk), ap(pz, S(a + 24 * n, a + 32 * n)), blk(st, 0, kk), AL.subtract)
                tt(blk(st, 2, kk), ap(pz, S(a + 16 * n, a + 24 * n)), blk(st, 1, kk), AL.subtract)
        if not last:
            pz = bank(h)
            mm([(rb(pz, 0), [(hz, If(2.0))])], end=False)
            mm([(rb(pz, j), [(yh, I)]) for j in range(2)], begin=False)
            aff(of(0, 0, 256), rb(pz, 0, 2), 1.0, OFF)
            pl = rb(bank(h), 0)
            mm([(pl, [(blk(sg, m), Ib(1.0 / 16 if m < 7 else -7.0 / 16)) for m in range(8)])])
            aff(lb, pl)
        else:
            mm([(blk(sm, j), [(blk("yh" + H, j), I)]) for j in range(2)])
            aff(blk(sf, 0, w=2), blk(sm, 0, w=2), 1.0, OFF)
            dma(ap("ya", S(128 * h, 128 * h + 128)), blk(sf, 0), 65536)
            dma(ap("yb", S(128 * h, 128 * h + 128)), blk(sf, 1), 65536, "A")
            pl = rb(bank(h), 0)
            mm([(pl, [(blk(sg, m), Ib(0.5)) for m in range(8)])])
            aff(blk(sf, 2), pl, 1.0, 4.0)
            dma(ap("yl", S(128 * h, 128 * h + 128)), blk(sf, 2), 65536)

    for h in range(2):
        first(h)
    table()
    for r in range(RO):
        cur[1] = r
        for h in range(2):
            step1(h, r)
        if r == 0:
            late_consts()
        for h in range(2):
            step23(h, r)
    return ops


def depend(ops):
    lastw, readers, bankacc, some = {}, {}, {}, {}
    for i, o in enumerate(ops):
        d = set()
        for a in o["reads"]:
            if a[0] in lastw:
                d.update(int(x) for x in np.unique(lastw[a[0]][region(a)]) if x >= 0)
        for a in o["writes"]:
            rg, n = region(a), a[0]
            if rg is None:
                continue
            if n not in lastw:
                lastw[n] = np.full(_IDX[n].size, -1)
            rows = a[1][0] != ALLP
            d.update(int(x) for x in np.unique(lastw[n][rg]) if x >= 0)
            m = np.zeros(_IDX[n].size, bool)
            m[rg] = True
            keep = []
            for j, mj in readers.get(n, []):
                if (mj & m).any():
                    d.add(j)
                    if not rows:
                        mj = mj & ~m
                if mj.any():
                    keep.append((j, mj))
            readers[n] = keep
        for a in o["reads"]:
            d.update(j for j, rg in some.get(a[0], []) if np.intersect1d(rg, region(a)).size)
        for a in o["writes"]:
            if region(a) is not None:
                if a[1][0] != ALLP:
                    some.setdefault(a[0], []).append((i, region(a)))
                else:
                    lastw[a[0]][region(a)] = i
        rd = {}
        for a in o["reads"]:
            if region(a) is not None:
                rd.setdefault(a[0], np.zeros(_IDX[a[0]].size, bool))[region(a)] = True
        for n, m in rd.items():
            readers.setdefault(n, []).append((i, m))
        for n in set(a[0] for a in o["reads"] + o["writes"] if a[0][:2] in ("ps", "vb")):
            acc = bankacc.setdefault(n, [None, [], []])
            if acc[0] != o["eng"] or len(o["eng"]) > 1:
                acc[:] = [o["eng"], [], acc[1]]
            d.update(acc[2])
            acc[1].append(i)
        d.discard(i)
        anc = 0
        for j in d:
            anc |= ops[j]["anc"]
        o["data"] = set(j for j in d if not anc >> j & 1)
        for j in d:
            anc |= 1 << j
        o["anc"] = anc
    lend(ops)


def lend(ops, at=None):
    uses = {}
    for i, o in enumerate(ops):
        o["deps"] = set(o["data"])
        for n in sorted(set(a[0] for a in o["reads"] + o["writes"] if a[0][:2] in ("vb", "vp"))):
            uses.setdefault(n, []).append(i)
    names = sorted(uses, key=lambda n: uses[n][0] if at is None else (at[2][uses[n][0]], uses[n][0]))
    free, last = {}, {}
    for n in names:
        h = int(n[2:]) % 2
        can = ["pr%d" % j for j in range(NPR)] if n[1] == "p" else ["bn%d" % j for j in (range(6) if at else range(3 * h, 3 * h + 3))]
        y = PLACE[n] = min(can, key=lambda y: free.get(y, -1.0))
        free[y] = max(at[2][i] + ops[i]["cost"][at[1][i]] for i in uses[n]) if at else uses[n][-1]
        ops[uses[n][0]]["deps"].update(last.get(y, []))
        last[y] = uses[n]


def graph(ops):
    pred = [sorted(set(o["deps"]) | ({o["after"]} if "after" in o else set())) for o in ops]
    succ = [[] for _ in ops]
    for i, x in enumerate(pred):
        for j in x:
            succ[j].append(i)
    return pred, succ, [o.get("late", LAT) for o in ops]


def rightof(s, v, key=None):
    a, b = 0, len(s)
    while a < b:
        m = (a + b) // 2
        if (s[m] if key is None else key[s[m]]) > v:
            b = m
        else:
            a = m + 1
    return a


def pack(ops, key, iters, rng):
    n = len(ops)
    pred, succ, late = graph(ops)
    engs = [[(x, o["cost"][x]) for x in o["eng"]] for o in ops]

    def place(key, back=False):
        before, after = (succ, pred) if back else (pred, succ)
        left, rdy = [len(x) for x in before], [0.0] * n
        byrank = [int(j) for j in np.argsort(np.array(key), kind="stable")]
        rank = [0] * n
        for k, j in enumerate(byrank):
            rank[j] = k
        ready = set(rank[i] for i in range(n) if not left[i])
        bs, be = {e: [] for e in "DAPGSX"}, {e: [] for e in "DAPGSX"}
        q, t0, t1 = [None] * n, [0.0] * n, [0.0] * n
        while ready:
            k = min(ready)
            ready.remove(k)
            i, best = byrank[k], None
            for x, c in engs[i]:
                s, e, st = bs[x], be[x], rdy[i] + (late[i] if back else 0.0)
                k, m = rightof(e, st), len(s)
                while k < m and s[k] < st + c:
                    st = e[k]
                    k += 1
                f = st + c * (1.0 if x == engs[i][-1][0] else 3.0 if x == "D" else 6.0)
                if best is None or f < best[0]:
                    best = (f, st, x, k, c)
            f, st, x, k, c = best
            bs[x].insert(k, st)
            be[x].insert(k, st + c)
            q[i], t0[i] = x, st
            f = t1[i] = st + c + (0.0 if back else late[i])
            for j in after[i]:
                if f > rdy[j]:
                    rdy[j] = f
                left[j] -= 1
                if not left[j]:
                    ready.add(rank[j])
        return max(t1), q, t0, t1

    if key is None:
        key = [0.0] * n
        for i in range(n - 1, -1, -1):
            key[i] = min([key[j] for j in succ[i]] + [0.0]) - min(c for x, c in engs[i]) - late[i]
    now = best = place(key)
    for it in range(iters):
        z = rng.normal(0, 120.0, (2, n))
        b = place([-x + float(y) for x, y in zip(now[3], z[0])], True)
        c = place([-x + float(y) for x, y in zip(b[3], z[1])])
        if c[0] < best[0]:
            best = c
        now = c if c[0] < best[0] * 1.003 else best
    return best[:3]


def shorten(ops, init, iters, rng, reach=14):
    n = len(ops)
    pred, succ, late = graph(ops)
    q = list(init[1])
    p = [ops[i]["cost"][q[i]] for i in range(n)]
    seq = {e: [] for e in "DAPGSX"}
    for i in sorted(range(n), key=lambda i: (init[2][i], i)):
        seq[q[i]].append(i)
    npred = [len(x) for x in pred]

    def times():
        mp, ms, left = [-1] * n, [-1] * n, list(npred)
        for e in "DAPGS":
            s = seq[e]
            for a, b in zip(s, s[1:]):
                mp[b], ms[a] = a, b
                left[b] += 1
        r, rd = [0.0] * n, [0.0] * n
        order = [i for i in range(n) if not left[i]]
        for i in order:
            f, j = r[i] + p[i], ms[i]
            if j >= 0:
                if f > r[j]:
                    r[j] = f
                left[j] -= 1
                if not left[j]:
                    order.append(j)
            f += late[i]
            for j in succ[i]:
                if f > rd[j]:
                    rd[j] = f
                    if f > r[j]:
                        r[j] = f
                left[j] -= 1
                if not left[j]:
                    order.append(j)
        if len(order) < n:
            return None
        t, td = [0.0] * n, [0.0] * n
        for i in reversed(order):
            m = 0.0
            for j in succ[i]:
                if t[j] > m:
                    m = t[j]
            m += late[i]
            td[i], j = m, ms[i]
            if j >= 0 and t[j] > m:
                m = t[j]
            t[i] = m + p[i]
        return max(t), r, rd, t, td, mp, ms, order

    cur = times()
    if cur is None:
        return None
    C, r, rd, t, td, mp, ms, order = cur
    best, tb = (C, list(q), list(r)), {}
    pos, fin = [0] * n, [r[i] + p[i] + late[i] for i in range(n)]
    for k, i in enumerate(order):
        pos[i] = k
    heads = [i for i in range(n) if not npred[i]]

    def link(u, a, b):
        x, y = mp[u], ms[u]
        if x >= 0:
            ms[x] = y
        if y >= 0:
            mp[y] = x
        mp[u], ms[u] = a, b
        if a >= 0:
            ms[a] = u
        if b >= 0:
            mp[b] = u

    def again(u):
        lo = min(pos[u], pos[ms[u]]) if ms[u] >= 0 else pos[u]
        hi = max(pos[u], pos[mp[u]]) if mp[u] >= 0 else pos[u]
        seg = order[lo:hi + 1]
        left = {i: sum(1 for j in pred[i] if pos[j] >= lo) + (mp[i] >= 0 and pos[mp[i]] >= lo) for i in seg}
        new = [i for i in seg if not left[i]]
        for i in new:
            for j in succ[i] + [ms[i]]:
                if j in left:
                    left[j] -= 1
                    if not left[j]:
                        new.append(j)
        if len(new) < len(seg):
            return False
        order[lo:hi + 1] = new
        for k, i in enumerate(new):
            pos[i] = lo + k
        for i in order[lo:]:
            m = 0.0
            for j in pred[i]:
                if fin[j] > m:
                    m = fin[j]
            rd[i], j = m, mp[i]
            if j >= 0 and r[j] + p[j] > m:
                m = r[j] + p[j]
            r[i], fin[i] = m, m + p[i] + late[i]
        for i in order[hi::-1]:
            m = 0.0
            for j in succ[i]:
                if t[j] > m:
                    m = t[j]
            m += late[i]
            td[i], j = m, ms[i]
            if j >= 0 and t[j] > m:
                m = t[j]
            t[i] = m + p[i]
        return True

    for it in range(iters):
        c0 = [i for i in heads if r[i] == 0.0 and t[i] > C - 1e-6]
        i = c0[int(rng.integers(len(c0)))]
        blocks = [[i]]
        while True:
            j = ms[i]
            if j >= 0 and (t[j] > td[i] or (t[j] == td[i] and rng.random() < 0.5)):
                blocks[-1].append(j)
                i = j
                continue
            nx = [j for j in succ[i] if t[j] + late[i] == td[i]]
            if not nx:
                break
            i = nx[int(rng.integers(len(nx)))] if len(nx) > 1 else nx[0]
            blocks.append([i])
        cand, pick = [], (rng.random(n) < SHARE).tolist()
        for b in blocks:
            L = len(b)
            for a in range(L):
                u = b[a]
                if not pick[u]:
                    continue
                if len(ops[u]["eng"]) == 1 and (L == 1 or reach < a < L - 1 - reach):
                    continue
                lo, hi = max([r[j] for j in pred[u]] + [-1.0]), min([r[j] for j in succ[u]] + [1e18])
                for x in ops[u]["eng"]:
                    if x == q[u]:
                        continue
                    s, c, bp = seq[x], ops[u]["cost"][x], None
                    k = rightof(s, lo, r)
                    while k <= len(s) and not (k and r[s[k - 1]] >= hi):
                        v = max(rd[u], r[s[k - 1]] + p[s[k - 1]] if k else 0.0) + c + max(td[u], t[s[k]] if k < len(s) else 0.0)
                        if bp is None or v < bp[0]:
                            bp = (v, k)
                        elif v > bp[0] + 3000:
                            break
                        k += 1
                    if bp:
                        cand.append((bp[0], 2, u, x, bp[1]))
                h, hs = (r[mp[u]] + p[mp[u]] if mp[u] >= 0 else 0.0), []
                for k in range(a + 1, min(L, a + reach + 1) if a == 0 or a + reach >= L - 1 else 0):
                    v = b[k]
                    if r[v] >= hi:
                        break
                    h = max(h, rd[v])
                    hs.append(h)
                    h += p[v]
                    if k == L - 1 or a == 0:
                        tl = p[u] + max(td[u], t[ms[v]] if ms[v] >= 0 else 0.0)
                        est = max(h, rd[u]) + tl
                        for m in range(k, a, -1):
                            tl = p[b[m]] + max(td[b[m]], tl)
                            est = max(est, hs[m - a - 1] + tl)
                        cand.append((est, 0, u, v, 0))
                tl, ts_ = (t[ms[u]] if ms[u] >= 0 else 0.0), []
                for k in range(a - 1, max(-1, a - reach - 1) if a == L - 1 or a <= reach else a, -1):
                    v = b[k]
                    if r[v] <= lo:
                        break
                    tl = p[v] + max(td[v], tl)
                    ts_.append(tl)
                    if (k == 0 or a == L - 1) and (k < a - 1 or (k > 0 and a < L - 1)):
                        h = max(rd[u], r[mp[v]] + p[mp[v]] if mp[v] >= 0 else 0.0)
                        est = h + p[u] + max(td[u], tl)
                        h += p[u]
                        for m in range(k, a):
                            h = max(h, rd[b[m]])
                            est = max(est, h + ts_[a - 1 - m])
                            h += p[b[m]]
                        cand.append((est, 1, u, v, 0))
        done = False
        for m in np.argsort(np.array([c[0] for c in cand]) + rng.random(len(cand)) * 200.0):
            est, kind, u, v, k = cand[m]
            if tb.get((u, v) if kind != 1 else (v, u), -1) >= it and est >= best[0]:
                continue
            s, old = seq[q[u]], q[u]
            a = s.index(u)
            s.pop(a)
            was = (mp[u], ms[u])
            if kind == 2:
                seq[v].insert(k, u)
                q[u], p[u], back = v, ops[u]["cost"][v], [(u, old)]
            else:
                b = s.index(v)
                k = b + (1 - kind)
                s.insert(k, u)
                back = [(w, u) for w in s[a:b + 1]] if kind == 0 else [(u, w) for w in s[b + 1:a + 1]]
            x = seq[q[u]]
            link(u, x[k - 1] if k else -1, x[k + 1] if k + 1 < len(x) else -1)
            if not again(u):
                x.pop(k)
                link(u, *was)
                q[u], p[u] = old, ops[u]["cost"][old]
                s.insert(a, u)
                continue
            ten = it + 100 + int(rng.integers(100))
            for kk in back:
                tb[kk] = ten
            C, done = max(t[i] for i in heads), True
            break
        if not done:
            tb = {}
        if C < best[0] - 1e-6:
            best = (C, list(q), list(r))
    return best


def schedule(ops):
    rng = np.random.default_rng(EFFORT[6])
    idx = [i for i, o in enumerate(ops) if o["half"] != 1]
    at = {j: k for k, j in enumerate(idx)}
    one = [dict(ops[i]) for i in idx]
    for o in one:
        if "after" in o:
            o["after"] = at[o["after"]]
    depend(one)
    t = shorten(one, pack(one, None, EFFORT[1], rng), EFFORT[0], rng)[2]
    pair = list(zip([i for i, o in enumerate(ops) if o["half"] == 0], [i for i, o in enumerate(ops) if o["half"] == 1]))
    res, keep = [], lambda x: (x, dict(PLACE), [set(o["deps"]) for o in ops])
    for lag, pace in STARTS:
        key = [t[at[i]] * pace if i in at else 0.0 for i in range(len(ops))]
        for a, b in pair:
            key[b] = key[a] + (lag if t[at[a]] > 9000 else 500.0)
        lend(ops)
        x = pack(ops, key, 2, rng)
        for it in range(EFFORT[1]):
            lend(ops, x)
            x = pack(ops, x[2], 2, rng)
        res.append(keep(shorten(ops, x, EFFORT[3], rng)))
    res = sorted(res, key=lambda x: x[0][0])[:EFFORT[2]]
    plain, norm = [(o["cost"], o.get("late")) for o in ops], {}

    def speed(fv, fg, fp, fd):
        for o, (c, late) in zip(ops, plain):
            g = fg if any(a[0][:2] == "of" for a in o["reads"]) else 1.0
            o["cost"] = c if late else {e: v * (fp if e == "P" else fv * g) for e, v in c.items()}
            if late:
                o["late"] = late * fd

    def mean(x):
        tot = 0.0
        for s in PACES:
            speed(*s)
            v = shorten(ops, x, 0, rng)[0]
            tot += v * norm.setdefault(s, 170000.0 / v)
        return tot / len(PACES)

    def back(x):
        PLACE.update(x[1])
        for o, d in zip(ops, x[2]):
            o["deps"] = set(d)
        return x[0]

    def turns(best, val, n):
        now = back(best)
        for it in range(n):
            speed(*PACES[it % len(PACES)])
            now = shorten(ops, now, 0, rng)
            was = keep(now)
            lend(ops, now)
            if shorten(ops, now, 0, rng) is None:
                back(was)
            now = shorten(ops, now, EFFORT[5], rng)
            v = mean(now)
            if v < val:
                best, val = keep(now), v
            elif v > val + 2500.0:
                now = back(best)
        return best, val

    res = [(x, 1e18) for x in res]
    while len(res) > 1:
        res = sorted([turns(x, v, len(PACES)) for x, v in res], key=lambda x: x[1])[:len(res) // 2]
    best = turns(res[0][0], res[0][1], EFFORT[4])[0]
    speed(*PACES[0])
    now = shorten(ops, back(best), 0, rng)
    for i, o in enumerate(ops):
        o["q"], o["t0"] = now[1][i], now[2][i]
        o["t1"] = o["t0"] + o["cost"][o["q"]] + o.get("late", LAT)
    return sorted(range(len(ops)), key=lambda i: (now[2][i], i))


def plan():
    ops = build()
    depend(ops)
    order = schedule(ops)
    cnt, known, prog = {}, {e: {} for e in "DAPGSX"}, []
    for i in order:
        o = ops[i]
        q = o["q"]
        kn = known[q]
        waits = {}
        for j in sorted(o["deps"], key=lambda j: -ops[j]["t1"]):
            p = ops[j]
            if q == "P" and p["q"] == "P":
                continue
            s, c = p["mark"]
            if kn.get(s, 0) < c:
                waits[s] = max(waits.get(s, 0), c)
                for s2, c2 in p["clock"].items():
                    kn[s2] = max(kn.get(s2, 0), c2)
        fs = o["emit"](q) if o["emit"] else [None]
        s = o.get("sem", "c" + q)
        cnt[s] = cnt.get(s, 0) + o.get("inc", 1) * len(fs)
        o["mark"] = (s, cnt[s])
        o["clock"] = dict(kn) if q != "X" else {}
        o["clock"][s] = cnt[s]
        prog.append((q, waits, fs, s, o))
    return prog, cnt, ops


_PLAN = []


def rank_program(g, core, T, topo):
    rank = T.rank_of(core)
    if rank is None:
        return
    if not _PLAN:
        _PLAN.append(plan())
    prog, cnt, _ = _PLAN[0]
    Q = {"D": g.vector, "A": g.scalar, "P": g.tensor, "G": g, "S": g.sync}
    n = len(T.cores)
    nxt, prv = T.cores[(rank + 1) % n], T.cores[(rank - 1) % n]
    for q, waits, fs, s, o in prog:
        if q == "X":
            continue
        for w, c in waits.items():
            Q[q].wait_ge(T.sem[w], c)
        if "send" in o:
            trs = []
            for j, dst in enumerate((nxt, prv)):
                rid, pid, _ = topo.addr(dst)
                eng = topo.engines(core, dst)
                k = len(eng) // 2
                mask = sum(1 << e for e in eng[j * k:j * k + 4])
                trs.append(RemoteDMATransfer(dst_ids=[DstId(rid=rid, pnc=pid)], dma_engine_mask=mask, remote_sem=T.sem[o["arr"]],
                                             src=real(T, o["send"][j][0]), dst=real(T, o["send"][j][1])))
            g.remote_dma_fused(trs, local_sem=T.sem[s])
            continue
        for f in fs:
            f(g, T).then_inc(T.sem[s], o.get("inc", 1))
    for s, c in cnt.items():
        g.wait_ge(T.sem[s], c)
